import numpy as np, ml_dtypes
CORES = [242,247,114,119]
N = 4
BF = ml_dtypes.bfloat16
W, S, H, R, CAP, HOP, ST = 2048, 256, 1024, 3, 192, 4, 467
P, E = W + R * S, S // N
AT = np.arange(W)
def hashed(u, lo, A):
    m = (61 * np.arange(16) + 7)[:, None]; u = u[:, :, None, :]
    return lo + (((u * u >> 5) + m * u + A[:, :, None, None]) & (W - 1))
def older(rng, *shape):
    return AT - 1 - np.minimum((AT * rng.random(shape + (W,)) ** 2).astype(np.int64), np.maximum(AT - 1, 0))
def parts(rng):
    off = rng.integers(-12, 9, (N, 8, 1, 1))
    X = np.clip(70 + rng.integers(-20, 21, (N, 8, 1, W)) + rng.integers(-60, 61, (N, 8, 16, W)), 0, 255)
    a = 2 * (70 + off + rng.integers(-20, 21, (N, 8, 1, S)) + rng.integers(-60, 61, (N, 8, 16, S))) + rng.integers(0, 2, (N, 8, 16, S))
    b = 80 + off + rng.integers(-50, 51, (N, 8, 1, (R - 1) * S)) + rng.integers(-100, 101, (N, 8, 16, (R - 1) * S))
    D = np.where(rng.random((N, 8, 16, W)) < 0.75, older(rng, N, 8, 16), -1); C = np.where(rng.random((N, 8, W)) < 0.9, older(rng, N, 8), -1)
    n = np.clip(W + S - 1 - ((W + S) * rng.random((N, 8, (R - 1) * S)) ** 2).astype(np.int64), 0, W + S - 1)
    return X, np.clip(np.concatenate([a, b], axis=3), 0, 255), D, C, n
def pack(X, a, D, C, n):
    return {"x0": X.reshape(N, 128, W).astype(np.float32).astype(BF), "come": a.reshape(N, 128, R * S).astype(np.float32).astype(BF),
            "dl0": np.ascontiguousarray(D[..., W - H:]).reshape(N, 128, H).astype(np.int32), "cd0": C.astype(np.int32), "age": n.astype(np.int32)}
def setup_inputs(rng):
    return pack(*parts(rng))
def setup_inputs_spread(rng):
    X = (256 * rng.random((N, 8, 16, W)) * np.exp2(-rng.integers(0, 7, (N, 8, 1, W)))).astype(np.int64)
    a = (256 * rng.random((N, 8, 16, R * S)) * np.exp2(-rng.integers(0, 5, (N, 8, 1, R * S)))).astype(np.int64)
    D = np.minimum(((AT + 1) * rng.random((N, 8, 16, W))).astype(np.int64), AT) - 1; C = np.minimum(((AT + 1) * rng.random((N, 8, W))).astype(np.int64), AT) - 1
    return pack(np.clip(X, 0, 255), np.clip(a, 0, 255), D, C, rng.integers(0, W + S, (N, 8, (R - 1) * S)))
def setup_inputs_ends(rng):
    X, a, D, C, n = parts(rng)
    def two(k):
        kind = rng.integers(0, 4, (N, 8, 1, k))
        return 255 * np.where(kind == 0, 0, np.where(kind == 1, 1, rng.integers(0, 2, (N, 8, 16, k))))
    X, a = two(W), two(R * S)
    r = rng.random(D.shape); D = np.where(r < 0.64, -1, np.where(r < 0.84, AT - 1, D))
    r = rng.random(C.shape); C = np.where(r < 0.64, -1, np.where(r < 0.84, AT - 1, C))
    n = (W + S - 1) * rng.integers(0, 2, n.shape)
    c = hashed(np.full((N, 8, 1), 16 * 127), 0, np.zeros((N, 8), np.int64))[0, 0, :, 0]
    X[..., c] = 255; C[..., c] = -1; X[:, 7, :, 0] = 255; X[:, 7, :, W - 1] = 255
    D[..., W - 1] = np.where(np.arange(16) % 2 == 0, W - 2, -1); C[:, ::2, W - 1] = -1; C[:, 1::2, W - 1] = W - 2
    last = np.arange(E - 1, S, E); a[..., last] = 255; a[..., S + last] = 255; n[..., last] = W + S - 1
    X[:, 5] = 0; X[:, 6] = 0; X[:, 6, :, W - 1] = 255; X[0, 7] = 0
    s = 4000 + np.array([11, 21, 27, 37, 43, 53, 59, 69]); h = hashed(np.zeros((N, 8, 8), np.int64) + s, S, np.zeros((N, 8), np.int64))[0, 0]
    good = h[15][h[15] < W]; half = 255 * (np.arange(16) % 2 == 0).astype(np.int64)[:, None]
    X4 = X[:, 4]; X4[:, :6] = 255; X4[..., h[h < W]] = half; X4[..., S] = half[:, 0]; X4[..., good] = 255
    C[:, 4, good] = -1; C[:, 4, int(np.min(good))] = S
    a[:, 4, :, :S] = 255; n[:, 4, :S] = W + S - 1; n[:, 4, S + 1:2 * S:2] = W + S - 1
    u = rng.integers(3841, 4075, (N, S)); u[:, 1::2] = s[np.arange(S // 2) & 7]; short = 4080 - u
    lack = (short >> 4)[:, None, :] + (((np.arange(16)[:, None] + np.arange(S)) & 15) < (short & 15)[:, None, :]).astype(np.int64)
    a[:, 4, :, S:2 * S] = 255 - 2 * lack
    a[:, 4, :6, 2 * S:] = 0; a[:, 4, :, 2 * S + 1:3 * S:2] = 255; a[:, 4, :6, 2 * S + 1:3 * S:2] = 253
    return pack(X, a, D, C, n)
def setup_inputs_corners(rng):
    X, a, D, C, n = parts(rng); X = 128 + (X >> 1); F = W // 8
    kind = rng.integers(0, 4, (N, 8, 1, W))
    D = np.where(kind == 0, -1, np.where(kind == 1, D[:, :, :1], D)); C[:, 1::3] = AT - 1
    edge = np.array([W - 1, ST - 1, ST])
    for q in range(N):
        for g in range(8):
            xg, dg, cg = X[q, g], D[q, g], C[q, g]
            dead = np.unique(np.append(rng.integers(1, F, 7), 0)); xg[:, dead] = 0
            cg[np.isin(cg, dead)] = -1
            k = (0, 1, CAP - 1, CAP, CAP + 1, W - F, CAP, CAP + 1)[(g + q) % 8]
            o = np.append(edge, rng.permutation(np.setdiff1d(np.arange(F, W), edge)))[:k]
            cg[o] = rng.choice(dead, len(o))
            gone = np.flatnonzero(kind[q, g, 0] == 2); gone = gone[gone >= F]; dg[:, gone] = rng.choice(dead, (16, len(gone)))
    x = a[..., :S] >> 1; c = hashed(np.add.reduce(x, axis=2), 0, np.zeros((N, 8), np.int64))
    live = np.max(X, axis=2) > 0; ok = np.take_along_axis(live, c.reshape(N, 8, 16 * S), 2).reshape(c.shape)
    up = np.max(np.where(ok, c, -1), axis=2); up2 = np.take_along_axis(C, np.maximum(up, 0), 2)
    y, y2 = W + S - 1 - up, W + S - 1 - up2
    n[..., :S] = np.clip(np.choose(rng.integers(0, 6, up.shape), [y, y - 1, y2, y2 - 1, 0 * y, 0 * y + W + S - 1]), 0, W + S - 1)
    return pack(X, a, D, C, n)
def setup_inputs_crowd(rng):
    X, a, D, C, n = parts(rng)
    for q in range(N):
        for g in range(8):
            k = (g + q) % 8; xg, ag, dg, cg = X[q, g], a[q, g], D[q, g], C[q, g]
            if k == 0: xg[:] = 0
            elif k == 1:
                xg[:] = 0; xg[:, int(rng.choice(np.array([0, 1, W - 2, W - 1])))] = 255
            elif k == 2 or k == 3:
                e = q & 1
                xg[:] = 128 + (xg >> 1); xg[:, e] = 0; xg[:, 1 - e] = 255; cg[1 + e:] = e; dg[:, 2:] = 1 - e
                if e == 1: cg[2:W >> 1] = -1
                if k == 3:
                    cg[W - 1] = -1; dg[:15, 2:] = -1
            elif k == 4:
                ag[:] = np.repeat(ag[:, ::S], S, axis=1); n[q, g] = W + S - 1
            elif k == 5:
                b = int(rng.integers(0, S)); us = rng.permutation(np.arange(400, 3600)); tab = np.zeros(S, np.int64)
                tab[(us * us >> 5) & (S - 1)] = us; u = tab[(b - AT) & (S - 1)]
                xg[:] = (u >> 4) + (np.arange(16)[:, None] < (u & 15)).astype(np.int64)
            elif k == 6:
                cg[:] = AT - 1; dg[:] = AT - 1
            else:
                xg[:] = 60 + (xg >> 2); ag[:, :S] = ag[:, :S] >> 2; ag[:, S:2 * S] = 254; ag[:, 2 * S:3 * S] = 0
                if q & 1: xg[:, int(rng.choice(np.array([S, W - 1])))] = 255
    return pack(X, a, D, C, n)
def setup_inputs_ties(rng):
    X, a, D, C, n = parts(rng)
    X = 60 + rng.integers(0, 2, (N, 8, 1, 1)) + rng.integers(0, 4, X.shape); a = 60 + rng.integers(0, 4, a.shape)
    a[..., :S] = 120 + rng.integers(0, 8, (N, 8, 16, S))
    o = np.argsort(rng.random((N, 2, 16, S)), axis=2); k = rng.integers(4, 8, (N, 2, 1, S))
    X[:, 2:4] = 62
    lower = 62 - (o[:, 0] < k[:, 0]).astype(np.int64)
    both = 62 + (o[:, 1] < k[:, 1]).astype(np.int64) - (o[:, 1] >= 10).astype(np.int64)
    a[:, 2, :, :S] = 2 * lower + rng.integers(0, 2, lower.shape); a[:, 3, :, :S] = 2 * both + rng.integers(0, 2, both.shape)
    return pack(X, a, D, C, n)
def check_inputs(d):
    bad = []
    for k, lo, hi in (("x0", 0, 255), ("come", 0, 255), ("dl0", -1, W - 2), ("cd0", -1, W - 2), ("age", 0, W + S - 1)):
        v = np.asarray(d[k]).astype(np.float64)
        if not np.all((v >= lo) & (v <= hi)): bad.append("range of " + k)
        elif not np.all(v == np.floor(v)): bad.append("whole numbers in " + k)
    if np.any(np.asarray(d["dl0"]) >= np.arange(W - H, W)): bad.append("the witnesses in dl0 are older places")
    if np.any(np.asarray(d["cd0"]) >= np.arange(W)): bad.append("the parents in cd0 are older places")
    return bad
def judge(X, live, c, y):
    k = c.shape[-1]; i = np.maximum(c, 0).reshape(N, 8, 16 * k)
    v = np.take_along_axis(X, i[:, :, None, :], 3).reshape(N, 8, 16, 16, k)
    more = np.add.reduce((v >= y[:, :, :, None, :]).astype(np.int32), axis=2)
    return (c >= 0) & (more >= 11) & np.take_along_axis(live, i, 2).reshape(N, 8, 16, k)
def reference(x0, come, dl0, cd0, age):
    X = np.zeros((N, 8, 16, P), np.int64); X[..., :W] = x0.astype(np.float32).astype(np.int64).reshape(N, 8, 16, W)
    D = np.full((N, 8, 16, P), -1, np.int64); D[..., W - H:W] = dl0.reshape(N, 8, 16, H)
    C = np.full((N, 8, P), -1, np.int64); C[..., :W] = cd0
    a = come.astype(np.float32).astype(np.int64).reshape(N, 8, 16, R, S); n = age.astype(np.int64).reshape(N, 8, R - 1, S)
    live = np.zeros((N, 8, P), bool); live[..., :W] = True
    z = np.zeros((N, 8, 16, S), np.int64); A = np.zeros((N, 8), np.int64)
    for t in range(R):
        lo = S * t; B = W + S * t
        live[..., :lo] = False
        x = (a[:, :, :, t] + z) >> 1; X[..., B:B + S] = x
        old = X[..., lo:B]; u = np.add.reduce(old, axis=2)
        who = ((u * u >> 5) + np.arange(lo, B)) & (S - 1)
        over = np.add.reduce((np.take_along_axis(x, who[:, :, None, :], 3) >= old).astype(np.int32), axis=2)
        die = live[..., lo:B] & (over >= 11); live[..., lo:B] = live[..., lo:B] & ~die
        c = hashed(np.add.reduce(x, axis=2), lo, A)
        c = np.where(judge(X, live, c, x), c, -1)
        D[..., B:B + S] = c; C[..., B:B + S] = np.max(c, axis=2); live[..., B:B + S] = True
        A = np.add.reduce(die.astype(np.int64), axis=2)
        cd = C[..., lo:B]
        orphan = live[..., lo:B] & (cd >= 0) & ~np.take_along_axis(live, np.maximum(cd, 0), 2)
        turn = np.roll(orphan, -ST * (t + 1), axis=2)
        turn = turn & (np.add.accumulate(turn.astype(np.int64), axis=2) <= CAP)
        taken = np.roll(turn, ST * (t + 1), axis=2)
        o = np.argsort(~taken, axis=2, kind="stable")[..., :CAP]; use = np.take_along_axis(taken, o, 2); o = o + lo
        y = np.take_along_axis(X, o[:, :, None, :], 3); d = np.take_along_axis(D, o[:, :, None, :], 3)
        left = np.where(judge(X, live, d, y), d, -1); b = np.max(left, axis=2)
        xb = np.take_along_axis(X, np.maximum(b, 0)[:, :, None, :], 3)
        y = np.where((use & (b >= 0))[:, :, None, :], (y + xb) >> 1, y)
        b = np.where(use, b, np.take_along_axis(C, o, 2)); d = np.where(use[:, :, None, :], left, d)
        np.put_along_axis(X, o[:, :, None, :], y, 3); np.put_along_axis(D, o[:, :, None, :], d, 3); np.put_along_axis(C, o, b, 2)
        if t < R - 1:
            w = np.zeros((N, 8, S), np.int64) + np.arange(B, B + S)
            for h in range(HOP):
                up = np.take_along_axis(C, w, 2)
                w = np.where((up >= 0) & (B + S - 1 - up <= n[:, :, t]), up, w)
            out = np.take_along_axis(X, w[:, :, None, :], 3).reshape(N, 8, 16, N, E)
            z = np.ascontiguousarray(out.transpose(3, 1, 2, 0, 4)).reshape(N, 8, 16, S)
    lo = S * (R - 1)
    return {"yx": np.ascontiguousarray(X[..., lo:]).reshape(N, 128, W + S).astype(np.float32).astype(BF), "yc": C[..., lo:].astype(np.float32), "ya": live[..., lo:].astype(np.float32)}

@@ -1,0 +1,670 @@
+from concourse.bass import DstId, RemoteDMATransfer
+from concourse.mybir import AluOpType as ALU, ActivationFunctionType as AF, AxisListType as AX
+
+W, S, R, CAP, ST, NR = 2048, 256, 3, 192, 467, 4
+OFF = 16
+NT = OFF + W + R * S
+NW = NT + CAP
+f32, b16, i32, u16 = "float32", "bfloat16", "int32", "uint16"
+
+_SB = dict(
+    X=(NW, b16), XJ=(NW, b16), C=(NW, f32), D=(NW, i32), cm=(768, b16),
+    cin=(128, i32), cinf=(128, f32), cw=(128, f32), blk=(128, i32), blkf=(128, f32),
+    ag=(32, i32), agf=(32, f32), agt=(32, f32), thr=(160, f32), a5=(160, f32), zv=(144, b16), nih=(128, b16), ahf=(16, f32),
+    ones=(160, b16), bow=(144, b16), bow0=(144, b16), z1=(144, b16), zk=(144, b16), zs=(144, b16), iw=(160, b16), ni=(128, b16),
+    bom=(128, b16), bof=(128, f32), idf=(128, f32), tri=(128, b16), iwe=(160, f32), iwo=(160, f32),
+    pi=(4, i32), pj=(4, i32), pc=(8, f32), j16=(256, f32), dm=(256, f32), kp=(256, f32), coef=(256, f32), kr=(192, f32),
+    pw0=(128, f32), pw=(128, f32), c16=(16, f32), kw=(12, f32), l16=(16, u16), l15=(12, u16), lc=(16, u16), h0=(32, f32), l512=(32, u16),
+    lm=(16, u16), bv=(512, b16), bs=(512, b16), bk=(128, b16), onesf=(256, f32), rmask=(8, f32),
+    xi=(256, i32), x2=(512, b16), wh=(128, f32), whi=(128, i32), whm=(128, i32), who=(128, u16),
+    g2=(2048, b16), cmpd=(2048, b16), sg=(128, b16), acc=(16, f32), ar=(1, f32), acol=(3, f32),
+    offp=(130, u16), thr0=(129, b16), pg=(2064, b16), F=(141, b16), P=(144, f32), Q=(141, f32),
+    junk=(12 * 144, b16), lv=(12, f32), cu=(12, u16), base=(36, f32), cmp2=(192, b16),
+    offo=(12, u16), offg=(12, u16), offd=(12, u16), ogf=(12, f32), offw=(192, u16), dp=(192, f32), y=(192, b16),
+    G=(3072, b16), cmpo=(3072, b16), left=(192, f32), lt=(192, f32), ls=(192, f32), bb=(192, f32), br=(192, f32),
+    w1=(12, f32), w2=(12, f32), w3=(12, f32), offx=(12, u16), xh=(192, f32), yn=(192, i32), dn=(192, i32),
+    asq=(16, f32), au=(16, f32), ah=(16, i32), at=(256, f32), ati=(256, i32), atm=(256, i32), offa=(256, u16),
+    cmpa=(4096, b16), lfa=(256, f32), tr=(256, f32), a1=(16, f32), E=(256, f32), din=(512, f32), dout=(512, f32),
+    offh=(48, u16), H=(768, f32), hs=(768, f32), q1=(80, f32), q2=(80, f32), offq=(16, u16),
+    sb=(512, b16), Z=(512, b16), aw=(128, f32), awt=(128, f32),
+)
+_AT = {}
+SCRATCH = {}
+for _k, (_n, _d) in _SB.items():
+    if _n <= 36 and _d in (f32, u16):
+        _w = SCRATCH.get("pack_" + _d, (0, [0, 0]))[1][1]
+        _AT[_k] = ("pack_" + _d, _w)
+        SCRATCH["pack_" + _d] = ("sbuf", [128, _w + (_n + 15) // 16 * 16], _d)
+    else:
+        _AT[_k] = (_k, 0)
+        SCRATCH[_k] = ("sbuf", [128, _n], _d)
+for _k in range(8):
+    SCRATCH["ps%d" % _k] = ("psum", [128, 512], f32)
+NDMA = 40
+SEMAPHORES = ["cV", "cS", "cP", "cG", "sent", "arr0", "arr1"] + ["d%d" % k for k in range(NDMA)]
+
+PRM = dict(cyc=1.04, pe=0.52, g=1.56, sc=3.8, same=60.0, cross=110.0, dma=2000.0, comm=3500.0)
+OPT = dict(arr_s=[(6, 7)] * 3, pg=[((0, 50, "S"), (50, 100, "S"), (100, 129, "S"))] * 3, orph_v=[(1,)] * 3, die_v=[(0, 1)] * 3,
+           c_s=[0] * 3, bb_s=[1] * 3, xj_s=[()] * 3, orph_sign=[(2,)] * 3, seed=7, jit=4000.0, moves=8, iters=1200)
+VARIANTS = [{}, dict(g=1.1, sc=2.0), dict(g=2.0, sc=5.5), dict(same=120.0, cross=220.0), dict(pe=0.9), dict(comm=5000.0, dma=2500.0)]
+WAIT_ALL = True
+
+
+def a(name, c0=0, c1=None, st=1, p=None):
+    if c1 is None:
+        c1 = _SB[name][0] if name in _SB else 512
+    return ("ap", name, c0, c1, st, p)
+
+
+def ind(win, off):
+    return ("ind", win, off)
+
+
+def ext(name, idx):
+    return ("ext", name, idx)
+
+
+def n_of(d):
+    if d[0] == "ind":
+        return 16 * n_of(d[2])
+    return len(range(d[2], d[3], d[4]))
+
+
+def spans(d):
+    if not isinstance(d, tuple) or d[0] == "ext":
+        return []
+    if d[0] == "ind":
+        return spans(d[1]) + spans(d[2])
+    return [(d[1], d[2], d[3])]
+
+
+def wide(d):
+    return d[0] == "ap" and (d[1] not in _SB or _SB[d[1]][1] in (f32, i32))
+
+
+def psum(d):
+    return d[0] == "ap" and d[1] not in _SB
+
+
+def build(me):
+    ops = []
+
+    def add(eng, kind, args, outs, ins, cost):
+        rd, wr = [], []
+        for o in outs:
+            if o[0] == "ind":
+                wr += spans(o[1]); rd += spans(o[2])
+            else:
+                wr += spans(o)
+        for i in ins:
+            rd += spans(i)
+        ops.append(dict(eng=eng, kind=kind, args=args, rd=rd, wr=wr, cost=cost))
+
+    def vcost(out, in0, k):
+        if out[0] == "ind":
+            return ("sc", n_of(out))
+        if in0[0] == "ind":
+            return ("g", n_of(in0))
+        return ("c", max(64, k * n_of(out)))
+
+    def half(out, in0):
+        return 1.0 if wide(out) or wide(in0) else 0.5
+
+    def tt(out, x, y, op):
+        add("V", "tt", (out, x, y, op), [out], [x, y], vcost(out, x, 1 if psum(x) or psum(y) else 2))
+
+    def ts(out, x, s1, op0, s2=None, op1=None):
+        add("V", "ts", (out, x, s1, s2, op0, op1), [out], [x, s1, s2], vcost(out, x, half(out, x)))
+
+    def cp(out, x):
+        add("V", "cp", (out, x), [out], [x], vcost(out, x, half(out, x)))
+
+    def ms(out, v):
+        add("V", "ms", (out, v), [out], [], ("c", max(64, n_of(out) * (1.0 if wide(out) else 0.5))))
+
+    def scan(out, d0, d1, op0, op1):
+        add("V", "scan", (out, d0, d1, 0.0, op0, op1), [out], [d0, d1], ("c", max(64, n_of(out))))
+
+    def trn(out, x):
+        add("V", "trn", (out, x), [out], [x], ("c", max(64, n_of(out))))
+
+    def red(out, x):
+        add("V", "red", (out, x), [out], [x], ("c", 64))
+
+    def act(out, x, func=AF.Identity, bias=0.0, scale=1.0, accum=None):
+        c = ("g", n_of(x)) if x[0] == "ind" else ("c", max(64, n_of(x)) + (20 if accum else 0))
+        add("S", "act", (out, x, func, bias, scale, accum), [out] + ([accum] if accum else []), [x, bias, scale], c)
+
+    def mm(lst, start=True, stop=True):
+        cyc = sum(max(64, n_of(r)) * (4 if wide(r) else 1) for o, l, r in lst)
+        add("P", "mm", (lst, start, stop), [o for o, l, r in lst], [l for o, l, r in lst] + [r for o, l, r in lst], ("pe", cyc))
+
+    def iota(out, pat, base, cm=0):
+        add("G", "iota", (out, pat, base, cm), [out], [], ("c", 130 + 2 * n_of(out)))
+
+    def sel(out, x, pat, op, base, cm):
+        add("G", "sel", (out, x, pat, op, base, cm), [out], [x], ("c", 170 + 2 * n_of(out)))
+
+    def dma(q, pairs, extra=0.0):
+        add(q, "dma", pairs, [o for o, i in pairs], [i for o, i in pairs], ("dma", len(pairs), extra))
+
+    def wrap(out, z, src, c0, n, first=()):
+        mm(list(first) + [(out, a(z, 15 - r, 143 - r), a(src, c0 + r, c0 + 16 * n, 16)) for r in range(16)])
+
+    I = a("iw", 16, 144)
+    pm, pm2, par, npar, p32, pm16 = [a("pc", k, k + 1) for k in range(6)]
+
+    dma("Y", [(a("X", OFF, OFF + 1024), ext("x0", (slice(None), slice(0, 1024))))], 700.0)
+    dma("S", [(a("X", OFF + 1024, OFF + W), ext("x0", (slice(None), slice(1024, W))))], 700.0)
+    dma("Y", [(a("cm"), ext("come", (slice(None), slice(None))))], 500.0)
+    dma("Y", [(a("cin", 32 * b + 16 * h, 32 * b + 16 * h + 16), ext("cd0", (slice(h, 8, 2), slice(512 * b, 512 * b + 512))))
+              for b in range(4) for h in range(2)], 500.0)
+    dma("Y", [(a("blk"), ext("cd0", (slice(None), slice(None))))])
+    dma("Y", [(a("D", OFF + 1024, OFF + W), ext("dl0", (slice(None), slice(None))))], 1500.0)
+    dma("Y", [(a("ag", 16 * h, 16 * h + 16), ext("age", (slice(h, 8, 2), slice(None)))) for h in range(2)])
+    iota(a("ones"), [[0, 160]], 1)
+    sel(a("bow0"), a("ones", 0, 144), [[-16, 9], [0, 16]], ALU.is_ge, 0, 1)
+    sel(a("bow"), a("bow0"), [[16, 9], [0, 16]], ALU.is_ge, 15, -1)
+    sel(a("z1"), a("bow"), [[0, 9], [1, 16]], ALU.is_equal, -15, 0)
+    iota(a("pi"), [[0, 4]], 0, 1)
+    iota(a("pw0"), [[0, 8], [32, 16]], 0)
+    sel(a("iw"), a("ones"), [[-1, 160]], ALU.is_equal, 16, 1)
+    iota(a("coef"), [[61, 16], [0, 16]], 7)
+    iota(a("c16"), [[16, 16]], 0)
+    sel(a("tri"), a("bow", 0, 128), [[1, 128]], ALU.is_ge, 0, -1)
+    iota(a("kr"), [[1, 192]], 0)
+    iota(a("j16"), [[0, 16], [1, 16]], 0)
+    iota(a("h0"), [[1, 16], [0, 2]], 0)
+    iota(a("onesf"), [[0, 256]], 1)
+    ts(a("pj", 0, 1), a("pi", 0, 1), 15, ALU.bitwise_and)
+    ts(a("pj", 1, 2), a("pi", 0, 1), 31, ALU.bitwise_and)
+    cp(pm, a("pj", 0, 1))
+    cp(p32, a("pj", 1, 2))
+    ts(pm2, a("pj", 0, 1), 2.0, ALU.mult, -0.75, ALU.add)
+    ts(pm16, a("pj", 0, 1), 16.0, ALU.mult)
+    ts(par, a("pj", 1, 2), 16.0, ALU.is_ge)
+    ts(npar, a("pj", 1, 2), 16.0, ALU.is_lt)
+    ts(a("pw"), a("pw0"), pm2, ALU.add)
+    ms(a("bv"), 5376.0); ms(a("bs"), 2816.0); ms(a("bk", 64, 128), -86016.0); ms(a("bk", 0, 64), -40960.0)
+    ms(a("X", 0, OFF), 0.0); ms(a("XJ", 0, OFF), -1.0); ms(a("C", 0, OFF), -1.0); ms(a("D", 1024, 1024 + OFF), -1)
+    ms(a("F", 129, 141), 1.0); ms(a("P", 0, 4), 0.0); ms(a("acol", 0, 1), -0.375)
+    act(a("ni"), I, scale=-1.0)
+    act(a("bom"), a("bow", 0, 128), scale=-512.0)
+    act(a("zk"), a("z1"), scale=8192.0)
+    act(a("zs"), a("z1"), scale=1.0 / 32)
+    if any(e == "V" for pg in OPT["pg"] for c0, c1, e in pg):
+        act(a("zv"), a("z1"), scale=1.0 / 16)
+        act(a("nih"), I, scale=-0.5)
+    act(a("bof"), a("bow", 0, 128))
+    act(a("idf"), I)
+    act(a("iwe"), a("iw"), scale=npar)
+    act(a("iwo"), a("iw"), scale=par)
+    ts(a("dm"), a("j16"), pm, ALU.is_equal)
+    ts(a("kp"), a("j16"), 0.5, ALU.is_ge)
+    ts(a("kw"), a("c16", 0, 12), pm, ALU.add, 0.5, ALU.add)
+    ts(a("l16"), a("c16"), 0.0, ALU.mult, pm, ALU.add)
+    ts(a("l15"), a("c16", 0, 12), 15.0, ALU.add)
+    ts(a("lc"), a("c16"), 1.0 / 16, ALU.mult)
+    ts(a("l512"), a("h0"), pm16, ALU.add)
+    ts(a("lm"), a("c16"), 2.0, ALU.mult, p32, ALU.add)
+    for t in range(R):
+        rs = float((ST * (t + 1)) % 16)
+        ts(a("rmask", 2 * t, 2 * t + 1), pm, rs, ALU.is_lt, 4096.0, ALU.mult)
+        ts(a("rmask", 2 * t + 1, 2 * t + 2), pm, rs, ALU.is_ge, 4096.0, ALU.mult)
+    for t in range(R - 1):
+        ts(a("a5", 80 * t, 80 * t + 80, 5), a("c16"), pm, ALU.add, float(W + S * t), ALU.add)
+    ms(a("thr"), 0.0)
+    iota(a("C", OFF + W, OFF + W + 2 * S), [[0, 2 * S]], -1)
+    cp(a("cinf"), a("cin"))
+    cp(a("blkf"), a("blk"))
+    dma("Y", [(a("C", OFF, OFF + W, 1, slice(m, 128, 16)), a("blkf")) for m in range(16)], 4000.0)
+    cp(a("agf"), a("ag"))
+    trn(a("agt"), a("agf"))
+    for t in range(R - 1):
+        for k in range(1, 5):
+            act(a("thr", 80 * t + k, 80 * t + 80, 5), a("agt", 16 * t, 16 * t + 16), bias=float(W + S * t + S - 1), scale=-1.0)
+
+    for t in range(R):
+        lo = S * t; B = W + lo; L = OFF + lo; BB = OFF + B
+        last = t == R - 1
+        cs = (ST * (t + 1)) // 16; n1 = 128 - cs
+        old = "X" if t == 0 else "XJ"
+        for c0, c1, pn in ((0, 64, "ps4"), (64, 128, "ps5")) if t == 0 else ((0, 128, "ps4"),):
+            wrap(a(pn, 0, c1 - c0), "z1", "X", L + 16 * c0, c1 - c0)
+            act(a(pn, 256, 256 + c1 - c0), a(pn, 0, c1 - c0), AF.Square, scale=0.25)
+            tt(a("wh", c0, c1), a(pn, 256, 256 + c1 - c0), a("pw", c0, c1), ALU.add)
+            ts(a("whi", c0, c1), a("wh", c0, c1), 0.5, ALU.mult)
+            ts(a("whm", c0, c1), a("whi", c0, c1), 255, ALU.bitwise_and)
+            cp(a("who", c0, c1), a("whm", c0, c1))
+        if t > 0:
+            act(a("ps7", S, 2 * S), a("cm", S * t, S * t + S), bias=-0.25, scale=0.5)
+            ms(a("XJ", L - S, L), -1.0)
+        trn(a("cw"), a("cinf"))
+        if t > 0:
+            act(a("cw", 112, 128), a("a1"))
+        ts(a("offp", 0, n1), a("cw", cs, 128), float(OFF), ALU.add)
+        ts(a("offp", n1, 129), a("cw", 0, cs + 1), float(OFF), ALU.add)
+        act(a("thr0", 1, n1), a("cw", cs + 1, 128), AF.Relu, scale=-1.0)
+        act(a("thr0", n1, 128), a("cw", 0, cs), AF.Relu, scale=-1.0)
+        act(a("thr0", 0, 1), a("cw", cs, cs + 1), AF.Relu, scale=-1.0, bias=a("rmask", 2 * t, 2 * t + 1))
+        act(a("thr0", 128, 129), a("cw", cs, cs + 1), AF.Relu, scale=-1.0, bias=a("rmask", 2 * t + 1, 2 * t + 2))
+        dv = OPT["die_v"][t]; ds = [q for q in range(4) if q not in dv]
+        for q in dv:
+            mm([(a("ps%d" % q), I, a("bv"))], True, False)
+        if t == 0:
+            ts(a("xi"), a("cm", 0, S), 0.5, ALU.mult, -0.25, ALU.add)
+        else:
+            add("V", "recv", t - 1, [a("Z", S * (t - 1), S * t)], [a("Z", S * (t - 1), S * t)], ("c", 0))
+            tt(a("xi"), a("Z", S * (t - 1), S * t), a("ps7", S, 2 * S), ALU.add)
+        cp(a("x2", 0, S), a("xi"))
+        for q in ds:
+            mm([(a("ps%d" % q), a("ni"), a(old, L + 512 * q, L + 512 * q + 512))], True, False)
+            act(a("g2", 512 * q, 512 * q + 512), ind(a("x2", 0, S), a("who", 32 * q, 32 * q + 32)))
+            mm([(a("ps%d" % q), I, a("g2", 512 * q, 512 * q + 512))], False, True)
+        for q in dv:
+            tt(a("cmpd", 512 * q, 512 * q + 512), ind(a("xi"), a("who", 32 * q, 32 * q + 32)), a(old, L + 512 * q, L + 512 * q + 512), ALU.is_ge)
+            mm([(a("ps%d" % q), a("bom"), a("cmpd", 512 * q, 512 * q + 512))], False, True)
+        for q in ds:
+            act(a("cmpd", 512 * q, 512 * q + 512), a("ps%d" % q), AF.Sign, bias=0.5)
+            mm([(a("ps%d" % q), I, a("bs"))], True, False)
+            mm([(a("ps%d" % q), a("bom"), a("cmpd", 512 * q, 512 * q + 512))], False, True)
+        for q in range(4):
+            if q in OPT["xj_s"][t]:
+                act(a("g2", 512 * q, 512 * q + 512), a("ps%d" % q), AF.Relu, scale=-2.0)
+                mm([(a("ps%d" % q), I, a(old, L + 512 * q, L + 512 * q + 512)), (a("ps%d" % q), a("ni"), a("g2", 512 * q, 512 * q + 512))])
+                act(a("XJ", L + 512 * q, L + 512 * q + 512), a("ps%d" % q))
+            else:
+                tt(a("XJ", L + 512 * q, L + 512 * q + 512), a("ps%d" % q), a(old, L + 512 * q, L + 512 * q + 512), ALU.min)
+        wrap(a("ps4", 0, 64), "z1", "cmpd", 0, 64)
+        wrap(a("ps4", 64, 128), "z1", "cmpd", 1024, 64)
+        cuts = sorted(set([0, 128] + ([16] if t == 0 else []) + [32 * q for q in range(1, 4) if (q in dv) != (q - 1 in dv)]))
+        for k in range(len(cuts) - 1):
+            c0, c1 = cuts[k], cuts[k + 1]
+            act(a("sg", c0, c1), a("ps4", c0, c1), AF.Sign, bias=-10.5 if c0 // 32 in dv else -5.0, accum=None if last else a("acc", 8 * t + k + 1, 8 * t + k + 2))
+        wrap(a("ps6", 0, 16), "z1", "x2", 0, 16)
+        act(a("asq"), a("ps6", 0, 16), AF.Square, scale=0.25)
+        act(a("au"), a("ps6", 0, 16))
+        act(a("x2", S, 2 * S), a("x2", 0, S))
+        ts(a("ah"), a("asq"), 0.5, ALU.mult, a("acol", t, t + 1), ALU.add)
+        if OPT["c_s"][t]:
+            cp(a("ahf"), a("ah"))
+            for k in range(16):
+                act(a("at", k, S, 16), a("coef", 0, S, 16), bias=a("ahf", k, k + 1), scale=a("au", k, k + 1))
+            cp(a("ati"), a("at"))
+        else:
+            tt(a("at"), ind(a("au"), a("l16")), a("coef"), ALU.mult)
+            tt(a("ati"), ind(a("ah"), a("l16")), a("at"), ALU.add)
+        ts(a("atm"), a("ati"), W - 1, ALU.bitwise_and)
+        cp(a("offa"), a("atm"))
+        for h in range(2):
+            for q in range(4 * h, 4 * h + 4):
+                src = ind(a("XJ", L, BB), a("offa", 32 * q, 32 * q + 32))
+                if q in OPT["arr_s"][t]:
+                    gq = a("g2", 512 * (q % 2), 512 * (q % 2) + 512); pq = a("ps%d" % (2 + q % 2))
+                    mm([(pq, a("ni"), a("x2"))], True, False)
+                    act(gq, src)
+                    mm([(pq, I, gq)], False, True)
+                    act(a("cmpa", 512 * q, 512 * q + 512), pq, AF.Sign, bias=0.5)
+                else:
+                    tt(a("cmpa", 512 * q, 512 * q + 512), src, a("x2"), ALU.is_ge)
+            pn = "ps%d" % (6 + h)
+            o = a(pn, 0, 128)
+            wrap(o, "zk", "cmpa", 2048 * h, 128, [(a(pn, 32 * k, 32 * k + 32), I, a("bk", 32, 64) if 4 * h + k in OPT["arr_s"][t] else a("bk", 64, 96)) for k in range(4)])
+            tt(a("lfa", 128 * h, 128 * h + 128), o, a("atm", 128 * h, 128 * h + 128), ALU.min)
+        tt(a("tr", 0, 128), a("lfa", 0, 128), a("lfa", 128, 256), ALU.max)
+        tt(a("tr", 128, 192), a("tr", 0, 64), a("tr", 64, 128), ALU.max)
+        tt(a("tr", 192, 224), a("tr", 128, 160), a("tr", 160, 192), ALU.max)
+        tt(a("tr", 224, 240), a("tr", 192, 208), a("tr", 208, 224), ALU.max)
+        ts(a("a1"), a("tr", 224, 240), float(lo), ALU.add, -1.0, ALU.max)
+        act(a("X", BB, BB + S), a("x2", 0, S))
+
+        def parents_row():
+            tt(a("E"), ind(a("a1"), a("lc")), a("dm"), ALU.mult)
+            mm([(a("ps6", 0, S), a("bof"), a("E"))])
+            act(a("C", BB, BB + S), a("ps6", 0, S))
+        if last:
+            parents_row()
+            dma("Y", [(ext("yx", (slice(None), slice(W, W + S))), a("X", BB, BB + S)),
+                      (ext("ya", (slice(None), slice(W, W + S))), a("onesf", 0, S, 1, slice(0, 8)))])
+            act(a("aw"), a("sg"), bias=0.5, scale=-0.5)
+            trn(a("awt"), a("aw"))
+            dma("Y", [(ext("ya", (slice(h, 8, 2), slice(512 * b, 512 * b + 512))), a("awt", 32 * b + 16 * h, 32 * b + 16 * h + 16))
+                      for b in range(4) for h in range(2)])
+        else:
+            ts(a("offh", 0, 16), a("tr", 224, 240), float(L), ALU.add, float(OFF - 1), ALU.max)
+            act(a("a5", 80 * t + 1, 80 * t + 80, 5), a("a1"))
+        mm([(a("ps5", 0, 129), a("ni"), a("thr0"))], True, False)
+        for c0, c1, e in OPT["pg"][t]:
+            if c1 == 129:
+                mm([(a("ps5", 0, n1), a("ni"), a("sg", cs, 128)), (a("ps5", n1, 129), a("ni"), a("sg", 0, cs + 1))], False, False)
+            if e == "S":
+                act(a("pg", 16 * c0, 16 * c1), ind(a("XJ", 0, BB), a("offp", c0, c1)), AF.Sign, bias=-0.5, scale=-1.0)
+            else:
+                ts(a("pg", 16 * c0, 16 * c1), ind(a("XJ", 0, BB), a("offp", c0, c1)), 0.0, ALU.is_lt)
+            mm([(a("ps5", c0, c1), a("zs" if e == "S" else "zv", 15 - r, 143 - r), a("pg", 16 * c0 + r, 16 * c1, 16)) for r in range(16)]
+               + ([] if e == "S" else [(a("ps5", c0, c1), a("nih"), a("ones", 0, c1 - c0))]), False, c1 == 129)
+        act(a("F", 0, 129), a("ps5", 0, 129), AF.Relu, bias=-2.0, scale=2.0)
+        mm([(a("ps5", 0, 141), a("bow", 0, 128), a("F"))])
+        mm([(a("ps5", 256, 397), a("tri"), a("F"))])
+        scan(a("P", 1, 142), a("onesf", 0, 141), a("ps5", 0, 141), ALU.mult, ALU.add)
+        tt(a("Q"), a("ps5", 256, 397), a("P", 0, 141), ALU.add)
+        for k in range(12):
+            act(a("junk", 144 * k, 144 * k + 141), a("P", 1, 142), AF.Sign, bias=a("kw", k, k + 1), scale=-1.0, accum=a("lv", k, k + 1))
+        ts(a("cu"), a("lv"), 0.5, ALU.mult, 70.5, ALU.add)
+        k0 = L + 16 * cs
+        ts(a("base", 0, 12), a("lv"), 8.0, ALU.mult, float(8 * 141 + k0), ALU.add)
+        ts(a("base", 12, 24), a("lv"), float(2 * n1 - 141), ALU.is_ge, float(-W), ALU.mult)
+        ts(a("base", 24, 36), a("lv"), float(2 * 129 - 141), ALU.is_ge, float(NT - 16 * 129 - k0 + W), ALU.mult)
+        tt(a("cmp2"), ind(a("Q"), a("cu")), a("kr"), ALU.is_le)
+        o = a("ps5", 0, 12)
+        mm([(o, a("idf"), a("base", 12 * k, 12 * k + 12)) for k in range(3)], True, False)
+        mm([(o, a("z1", 15 - r, 143 - r), a("cmp2", r, 192, 16)) for r in range(16)], False, True)
+        ts(a("offd"), o, -1024.0, ALU.add, float(BB - 1 - 1024), ALU.min)
+        ts(a("offg"), o, float(BB - 1), ALU.min)
+        cp(a("offo"), o)
+        ts(a("ogf"), o, float(BB - 1), ALU.min, float(1 - OFF), ALU.add)
+        ts(a("offw"), ind(a("D", 1024, BB), a("offd")), float(OFF), ALU.add)
+        act(a("y"), ind(a("X", 0, BB), a("offg")))
+        mm([(a("ps0", 0, 192), I, a("y"))])
+        ts(a("dp"), a("offw"), float(1 - OFF), ALU.add)
+        for c in range(3):
+            gsrc = ind(a("XJ", 0, BB), a("offw", 64 * c, 64 * c + 64))
+            if c in OPT["orph_v"][t]:
+                cp(a("G", 1024 * c, 1024 * c + 1024), gsrc)
+            else:
+                act(a("G", 1024 * c, 1024 * c + 1024), gsrc)
+            o = a("ps1", 64 * c, 64 * c + 64)
+            if c in OPT["orph_sign"][t]:
+                for h in range(2):
+                    k = 1024 * c + 512 * h; pn = "ps%d" % (2 + h)
+                    mm([(a(pn, m, 512, 16), a("ni"), a("y", 64 * c + 32 * h, 64 * c + 32 * h + 32)) for m in range(16)], True, False)
+                    mm([(a(pn), I, a("G", k, k + 512))], False, True)
+                    act(a("cmpo", k, k + 512), a(pn), AF.Sign, bias=0.5)
+                mm([(o, I, a("bk", 0, 64))] + [(o, a("zk", 15 - m, 143 - m), a("cmpo", 1024 * c + m, 1024 * c + 1024, 16)) for m in range(16)])
+            else:
+                for h in range(2):
+                    for m in range(8 * h, 8 * h + 8):
+                        k = 1024 * c + 64 * m
+                        tt(a("cmpo", k, k + 64), a("G", 1024 * c + m, 1024 * c + 1024, 16), a("ps0", 64 * c, 64 * c + 64), ALU.is_ge)
+                    mm(([(o, I, a("bk", 64, 128))] if h == 0 else []) +
+                       [(o, a("zk", 15 - m, 143 - m), a("cmpo", 1024 * c + 64 * m, 1024 * c + 64 * m + 64)) for m in range(8 * h, 8 * h + 8)], h == 0, h == 1)
+            tt(a("left", 64 * c, 64 * c + 64), o, a("dp", 64 * c, 64 * c + 64), ALU.min)
+        trn(a("lt"), a("left"))
+        scan(a("ls"), a("kp", 0, 192), a("lt"), ALU.mult, ALU.max)
+        if OPT["bb_s"][t]:
+            act(a("bb"), ind(a("ls"), a("l15")))
+        else:
+            cp(a("bb"), ind(a("ls"), a("l15")))
+        trn(a("br"), a("bb"))
+        ts(ind(a("C"), a("offo")), a("br"), 1.0, ALU.mult, -1.0, ALU.add)
+        if not last:
+            dma("Y", [(a("cinf", 32 * b + 16 * h, 32 * b + 16 * h + 16), a("C", L + S + 512 * b, L + S + 512 * b + 512, 1, slice(16 * h, 128, 32)))
+                      for b in range(4) for h in range(2)], 500.0)
+        for ih in range(2):
+            src = "iwo" if ih else "iwe"
+            mm([(a("ps5", ih, 12, 2), a(src, 16 + 16 * (ih - gh), 144 + 16 * (ih - gh)), a("ls", 16 * gh + 15, 192, 32)) for gh in range(2)])
+        ts(a("w1"), a("ps5", 0, 12), 0.5, ALU.is_lt, 8192.0, ALU.mult)
+        tt(a("w2"), a("ps5", 0, 12), a("w1"), ALU.add)
+        tt(a("w3"), a("w2"), a("ogf"), ALU.min)
+        ts(a("offx"), a("w3"), float(OFF - 1), ALU.add)
+        act(a("ps4", 256, 448), a("y"), bias=-0.25, scale=0.5)
+        act(a("xh"), ind(a("X", 0, BB), a("offx")), scale=0.5)
+        tt(a("yn"), a("xh"), a("ps4", 256, 448), ALU.add)
+        cp(ind(a("X"), a("offo")), a("yn"))
+        if last:
+            dma("Y", [(ext("yc", (slice(None), slice(None))), a("C", L, BB + S, 1, slice(0, 128, 16)))], 300.0)
+            dma("Y", [(ext("yx", (slice(None), slice(0, 1024))), a("X", L, L + 1024))], 700.0)
+            dma("S", [(ext("yx", (slice(None), slice(1024, W))), a("X", L + 1024, BB))], 700.0)
+            break
+        for k in range(3):
+            tt(a("H", S * k, S * k + S), ind(a("C", 0, BB), a("offh", 16 * k, 16 * k + 16)), a("dm"), ALU.mult)
+            scan(a("hs", S * k, S * k + S), a("kp"), a("H", S * k, S * k + S), ALU.mult, ALU.add)
+            ak = a("hs", S * k + 15, S * k + S, 16)
+            if k < 2:
+                ts(a("offh", 16 * k + 16, 16 * k + 32), ak, float(OFF), ALU.add)
+                act(a("a5", 80 * t + k + 2, 80 * t + 80, 5), ak)
+            else:
+                cp(a("a5", 80 * t + 4, 80 * t + 80, 5), ak)
+        tt(a("q1"), a("a5", 80 * t, 80 * t + 80), a("thr", 80 * t, 80 * t + 80), ALU.is_lt)
+        scan(a("q2"), a("q1"), a("a5", 80 * t, 80 * t + 80), ALU.mult, ALU.max)
+        ts(a("offq"), a("q2", 4, 80, 5), float(OFF), ALU.add)
+        ts(a("sb", S * t, S * t + S), ind(a("X", 0, BB + S), a("offq")), 0.5, ALU.mult)
+        add("G", "send", t, [], [a("sb", S * t, S * t + S)], ("c", 300))
+        act(a("Z", S * t + 64 * me, S * t + 64 * me + 64), a("sb", S * t + 64 * me, S * t + 64 * me + 64))
+        cp(ind(a("XJ"), a("offo")), a("yn"))
+        act(a("XJ", BB, BB + S), a("x2", 0, S))
+        ts(a("dn"), a("left"), 0.0, ALU.max, -1.0, ALU.add)
+        cp(ind(a("D"), a("offo")), a("dn"))
+        act(a("din"), ind(a("lfa"), a("l512")))
+        trn(a("dout"), a("din"))
+        ts(a("D", BB, BB + S), ind(a("dout"), a("lm")), float(lo), ALU.add, -1.0, ALU.max)
+        parents_row()
+        if t == 0:
+            red(a("ar"), a("acc", 1, len(cuts)))
+            red(a("acc", 0, 1), a("acc", 2, len(cuts)))
+            act(a("acc", 8, 9), a("acc", 0, 1), scale=-1.0)
+        else:
+            red(a("ar"), a("acc", 8, 8 + len(cuts)))
+        mm([(a("ps7", 0, 1), a("bof"), a("ar"))])
+        ts(a("acol", t + 1, t + 2), a("ps7", 0, 1), 0.5, ALU.mult, (1024.0 if t == 0 else 128.0) - 0.375, ALU.add)
+    return ops
+
+
+def link(ops):
+    hist = {}
+    deps = []
+    sends = {}
+    for j, o in enumerate(ops):
+        d = {}
+        for acc_w, lst in ((False, o["rd"]), (True, o["wr"])):
+            for name, c0, c1 in lst:
+                bank = name not in _SB
+                for i, w, e0, e1 in hist.get(name, []):
+                    if i == j or not (bank or ((w or acc_w) and e0 < c1 and c0 < e1)):
+                        continue
+                    p = ops[i]
+                    same = p["eng"] == o["eng"] and p["kind"] not in ("dma", "send") and o["kind"] not in ("dma", "send")
+                    raw = w and not acc_w and e0 < c1 and c0 < e1
+                    need = (not same) or raw or (WAIT_ALL and o["eng"] != "P" and (w or acc_w) and e0 < c1 and c0 < e1)
+                    if p["kind"] == "recv" and same:
+                        need = False
+                    d[i] = d.get(i, False) or need
+        for acc_w, lst in ((False, o["rd"]), (True, o["wr"])):
+            for name, c0, c1 in lst:
+                hist.setdefault(name, []).append((j, acc_w, c0, c1))
+        if o["kind"] == "send":
+            sends[o["args"]] = j
+        if o["kind"] == "recv":
+            d[sends[o["args"]]] = None
+        deps.append(d)
+    return deps
+
+
+def sizes(ops, prm):
+    out = []
+    for o in ops:
+        c = o["cost"]
+        if c[0] == "c": v = c[1] * prm["cyc"]
+        elif c[0] == "g": v = 60 + c[1] * prm["cyc"] * prm["g"]
+        elif c[0] == "sc": v = 60 + c[1] * prm["cyc"] * prm["sc"]
+        elif c[0] == "pe": v = c[1] * prm["pe"]
+        else: v = 60.0 * c[1]
+        out.append((v, v + (prm["dma"] + c[2] if c[0] == "dma" else 0.0)))
+    return out
+
+
+def gap(ops, i, j, need, prm):
+    if need is None: return prm["comm"]
+    if not need: return 0.0
+    return prm["same"] if ops[i]["eng"] == ops[j]["eng"] else prm["cross"]
+
+
+def schedule(ops, deps, prm):
+    n = len(ops); eng = [o["eng"] for o in ops]
+
+    def graph(p):
+        sz = sizes(ops, p); d = [max(s[0], 1e-3) for s in sz]
+        lag = [[(i, (sz[i][1] if need is not False else d[i]) + gap(ops, i, j, need, p) + 1e-3) for i, need in deps[j].items()] for j in range(n)]
+        return d, [s[1] for s in sz], lag
+
+    def place(seq, pred, first, d):
+        busy = {e: ([], []) for e in "VSPGY"}
+        start = [0.0] * n
+        for j in seq:
+            t = first[j]
+            for i, l in pred[j]:
+                if start[i] + l > t: t = start[i] + l
+            bs, be = busy[eng[j]]; k = len(be)
+            while k > 0 and be[k - 1] > t: k -= 1
+            while k < len(bs) and t + d[j] > bs[k]:
+                if be[k] > t: t = be[k]
+                k += 1
+            start[j] = t; bs.insert(k, t); be.insert(k, t + d[j])
+        return start
+
+    def span(seq, gr):
+        d, full, lag = gr; free = {e: 0.0 for e in "VSPGY"}; st = [0.0] * n; end = 0.0
+        for j in seq:
+            t = free[eng[j]]
+            for i, l in lag[j]:
+                if st[i] + l > t: t = st[i] + l
+            st[j] = t; free[eng[j]] = t + d[j]
+            if t + full[j] > end: end = t + full[j]
+        return end
+
+    others = [graph(dict(prm, **v)) for v in VARIANTS]
+    d, full, lag = others[0]
+    back = [[] for j in range(n)]
+    for j in range(n):
+        for i, l in lag[j]: back[i].append((j, d[j] + l - d[i]))
+    tail = [full[j] - d[j] for j in range(n)]; zero = [0.0] * n
+    level = list(full)
+    for j in range(n - 1, -1, -1):
+        for i, l in lag[j]: level[i] = max(level[i], l + level[j])
+    key = [-v for v in level]
+    x = OPT["seed"]; best = None; ref = None
+    for it in range(OPT["iters"]):
+        st = place(sorted(range(n), key=lambda k: (key[k], k)), lag, zero, d)
+        for rep in range(2):
+            sb = place(sorted(range(n), key=lambda k: (-st[k], -k)), back, tail, d)
+            st = place(sorted(range(n), key=lambda k: (-sb[k] - d[k], k)), lag, zero, d)
+        seq = sorted(range(n), key=lambda k: (st[k], k))
+        tm = [span(seq, gr) for gr in others]
+        if ref is None: ref = tm
+        score = sum(u / v for u, v in zip(tm, ref))
+        if best is None or score < best[0]: best = (score, seq, st)
+        key = list(best[2])
+        for k in range(OPT["moves"]):
+            x = (x * 1103515245 + 12345) % 2147483648; j = (x >> 8) % n
+            x = (x * 1103515245 + 12345) % 2147483648
+            key[j] += OPT["jit"] * (x / 1073741824.0 - 1.0)
+        for j in range(n):
+            for i, l in lag[j]:
+                if key[j] <= key[i]: key[j] = key[i] + 1e-3
+    return best[1]
+
+
+_PLAN = {}
+
+
+def masks(src, cores, topo):
+    peers = sorted([c for c in cores if c != src], key=lambda c: len(topo.engines(src, c)))
+    used = []; out = {}
+    for c in peers:
+        e = [k for k in topo.engines(src, c) if k not in used][:4]
+        used += e; out[c] = e
+    return out
+
+
+def rank_program(g, core, T, topo):
+    me = T.rank_of(core)
+    if me is None:
+        return
+    cores = list(T.cores)
+    ops = build(me); deps = link(ops)
+    if "order" not in _PLAN:
+        _PLAN["order"] = schedule(ops, deps, PRM)
+    order = _PLAN["order"]
+    Q = dict(V=g.vector, S=g.scalar, P=g.tensor, G=g, Y=g.sync)
+    pos = {j: n for n, j in enumerate(order)}
+    key = lambda i: ops[i]["eng"] if ops[i]["kind"] not in ("dma", "send", "recv") else i
+    know = {e: {} for e in Q}; clock = {}; needed = set()
+    for j in order:
+        kn = know[ops[j]["eng"]]
+        for i in sorted([i for i, need in deps[j].items() if need], key=lambda i: -pos[i]):
+            if kn.get(key(i), -1) >= pos[i]:
+                deps[j][i] = False
+                continue
+            needed.add(i)
+            for k2, v in clock[i].items(): kn[k2] = max(kn.get(k2, -1), v)
+            kn[key(i)] = pos[i]
+        if ops[j]["kind"] == "recv": kn[j] = pos[j]
+        clock[j] = dict(kn)
+    mark = {}; cnt = dict(V=0, S=0, P=0, G=0); nd = 0
+    for j in order:
+        o = ops[j]
+        if o["kind"] == "dma":
+            mark[j] = ("d%d" % nd, 16 * len(o["args"])); nd += 1
+        elif o["kind"] == "send":
+            mark[j] = ("sent", (o["args"] + 1) * sum(len(e) for e in masks(core, cores, topo).values()))
+        elif j in needed and o["kind"] != "recv":
+            cnt[o["eng"]] += 1; mark[j] = ("c" + o["eng"], cnt[o["eng"]])
+
+    def ap(d):
+        if not isinstance(d, tuple): return d
+        if d[0] == "ind": return ap(d[1]).indirect(ap(d[2]))
+        if d[0] == "ext": return T[d[1]][d[2]]
+        p = slice(None) if d[5] is None else d[5]
+        nm, o0 = _AT.get(d[1], (d[1], 0))
+        return T[nm][p, o0 + d[2]:o0 + d[3]] if d[4] == 1 else T[nm][p, o0 + d[2]:o0 + d[3]:d[4]]
+
+    seen = {e: {} for e in Q}
+    for j in order:
+        o = ops[j]; e = o["eng"]; q = Q[e]; k = o["kind"]; x = o["args"]
+        want = {}
+        for i, need in deps[j].items():
+            if need and i in mark:
+                s, v = mark[i]; want[s] = max(want.get(s, 0), v)
+            if need and ops[i]["kind"] == "recv":
+                want["arr%d" % ops[i]["args"]] = sum(len(masks(c, cores, topo)[core]) for c in cores if c != core)
+        if k == "recv":
+            want["arr%d" % x] = sum(len(masks(c, cores, topo)[core]) for c in cores if c != core)
+        for s, v in want.items():
+            if seen[e].get(s, 0) < v:
+                q.wait_ge(T.sem[s], v); seen[e][s] = v
+        ins = None
+        if k == "tt": ins = q.tensor_tensor(ap(x[0]), ap(x[1]), ap(x[2]), x[3])
+        elif k == "ts":
+            if x[5] is None: ins = q.tensor_scalar(ap(x[0]), ap(x[1]), ap(x[2]), None, x[4])
+            else: ins = q.tensor_scalar(ap(x[0]), ap(x[1]), ap(x[2]), ap(x[3]), x[4], x[5])
+        elif k == "cp": ins = q.tensor_copy(ap(x[0]), ap(x[1]))
+        elif k == "ms": ins = q.memset(ap(x[0]), x[1])
+        elif k == "scan": ins = q.tensor_tensor_scan(ap(x[0]), ap(x[1]), ap(x[2]), x[3], x[4], x[5])
+        elif k == "trn": ins = q.transpose(ap(x[0]), ap(x[1]))
+        elif k == "red": ins = q.tensor_reduce(ap(x[0]), ap(x[1]), AX.X, ALU.add)
+        elif k == "act": ins = q.activation(ap(x[0]), ap(x[1]), x[2], bias=ap(x[3]), scale=ap(x[4]), accum_out=ap(x[5]))
+        elif k == "mm":
+            for n, (po, l, r) in enumerate(x[0]):
+                ins = q.matmul(ap(po), ap(l), ap(r), x[1] and n == 0, x[2] and n == len(x[0]) - 1)
+        elif k == "iota":
+            if _SB[x[0][1]][1] == i32: ins = q.iota(ap(x[0]), x[1], x[2], x[3])
+            else: ins = q.iota(ap(x[0]), x[1], x[2], x[3], allow_small_or_imprecise_dtypes=True)
+        elif k == "sel": ins = q.affine_select(ap(x[0]), ap(x[1]), x[2], x[3], 0.0, x[4], x[5])
+        elif k == "dma":
+            for po, pi in x:
+                q.dma_start(ap(po), ap(pi)).then_inc(T.sem[mark[j][0]], 16)
+        elif k == "send":
+            trs = []
+            for c, eng in masks(core, cores, topo).items():
+                b = cores.index(c); rid, pid = topo.addr(c, core)
+                trs.append(RemoteDMATransfer(dst_ids=[DstId(rid=rid, pnc=pid)], dma_engine_mask=sum(1 << n for n in eng), remote_sem=T.sem["arr%d" % x],
+                                             src=T.sb[:, S * x + 64 * b:S * x + 64 * b + 64], dst=T.Z[:, S * x + 64 * me:S * x + 64 * me + 64]))
+            q.remote_dma_fused(trs, local_sem=T.sem.sent)
+        if ins is not None and j in mark:
+            ins.then_inc(T.sem[mark[j][0]], 1)
+    last = {}
+    for s, v in mark.values():
+        last[s] = max(last.get(s, 0), v)
+    for s, v in last.items():
+        if not any(seen[e].get(s, 0) >= v for e in Q):
+            g.wait_ge(T.sem[s], v)

@@ -2,27 +2,29 @@ from concourse.bass import DstId, RemoteDMATransfer
 from concourse.mybir import AluOpType as ALU, ActivationFunctionType as AF, AxisListType as AX
 
 W, S, R, CAP, ST, NR = 2048, 256, 3, 192, 467, 4
-OFF = 16
-NT = OFF + W + R * S
-NW = NT + CAP
+OFF = 2 * CAP + 16
+W0 = OFF - 16
+NW = OFF + W + R * S
+BIG = 8192.0
 f32, b16, i32, u16 = "float32", "bfloat16", "int32", "uint16"
 
 _SB = dict(
-    X=(NW, b16), XJ=(NW, b16), C=(NW, f32), D=(NW, i32), cm=(768, b16),
-    cin=(128, i32), cinf=(128, f32), cw=(128, f32), blk=(128, i32), blkf=(128, f32),
-    ag=(32, i32), agf=(32, f32), agt=(32, f32), thr=(160, f32), a5=(160, f32), zv=(144, b16), nih=(128, b16), ahf=(16, f32),
-    ones=(160, b16), bow=(144, b16), bow0=(144, b16), z1=(144, b16), zk=(144, b16), zs=(144, b16), iw=(160, b16), ni=(128, b16),
-    bom=(128, b16), bof=(128, f32), idf=(128, f32), tri=(128, b16), iwe=(160, f32), iwo=(160, f32),
-    pi=(4, i32), pj=(4, i32), pc=(8, f32), j16=(256, f32), dm=(256, f32), kp=(256, f32), coef=(256, f32), kr=(192, f32),
-    pw0=(128, f32), pw=(128, f32), c16=(16, f32), kw=(12, f32), l16=(16, u16), l15=(12, u16), lc=(16, u16), h0=(32, f32), l512=(32, u16),
-    lm=(16, u16), bv=(512, b16), bs=(512, b16), bk=(128, b16), onesf=(256, f32), rmask=(8, f32),
-    xi=(256, i32), x2=(512, b16), wh=(128, f32), whi=(128, i32), whm=(128, i32), who=(128, u16),
-    g2=(2048, b16), cmpd=(2048, b16), sg=(128, b16), acc=(16, f32), ar=(1, f32), acol=(3, f32),
-    offp=(130, u16), thr0=(129, b16), pg=(2064, b16), F=(141, b16), P=(144, f32), Q=(141, f32),
-    junk=(12 * 144, b16), lv=(12, f32), cu=(12, u16), base=(36, f32), cmp2=(192, b16),
-    offo=(12, u16), offg=(12, u16), offd=(12, u16), ogf=(12, f32), offw=(192, u16), dp=(192, f32), y=(192, b16),
+    X=(NW, b16), XJ=(NW, b16), C=(NW, f32), D=(NW, i32), CD=(16 + W + 2 * S, b16), cm=(768, b16),
+    cin=(128, i32), cinf=(128, f32), blk=(128, i32), blkf=(128, f32),
+    ag=(32, i32), agf=(32, f32), agt=(32, f32), thr=(160, f32), a5=(160, f32), ahf=(16, f32),
+    ones=(160, b16), bow=(144, b16), bow0=(144, b16), z1=(144, b16), zk=(144, b16), iw=(160, b16), ni=(128, b16), ni16=(128, b16), ih=(128, b16),
+    bom=(128, b16), bof=(128, f32), tri=(128, b16), iwe=(160, f32), iwo=(160, f32), nkr=(128, b16),
+    pi=(4, i32), pj=(4, i32), pc=(12, f32), j16=(256, f32), dm=(256, f32), kp=(256, b16), coef=(256, f32), kr=(192, b16),
+    Mh=(256, f32), idf=(128, f32), mk=(16, b16), wv=(16, b16), kc=(36, f32), ky=(12, f32),
+    pw0=(128, f32), pw=(128, f32), c16=(16, f32), kw=(12, f32), l16=(16, u16), l15=(12, u16), lc=(16, u16), lp=(8, u16), h0=(32, f32), l512=(32, u16),
+    U=(2048, b16), c16b=(16, f32), lm=(16, u16), bv=(512, b16), bk=(128, b16), onesf=(256, f32),
+    xi=(256, i32), x2=(512, b16), wh=(128, i32), whm=(128, i32), who=(128, u16),
+    g2=(1024, b16), sg=(128, b16), acc=(16, f32), ar=(1, f32), acol=(3, f32),
+    offp=(128, u16), pg=(2048, b16), F=(144, b16), Fp=(144, b16), Q=(144, b16), vb=(128, b16), M=(12 * 128, b16),
+    cu=(12, u16), uf=(12, f32), uu=(12, f32), cmp2=(192, b16),
+    offo=(12, u16), offw=(192, u16), dp=(192, f32), y=(192, b16),
     G=(3072, b16), cmpo=(3072, b16), left=(192, f32), lt=(192, f32), ls=(192, f32), bb=(192, f32), br=(192, f32),
-    w1=(12, f32), w2=(12, f32), w3=(12, f32), offx=(12, u16), xh=(192, f32), yn=(192, i32), dn=(192, i32),
+    w1=(12, f32), offx=(12, u16), xh=(192, f32), yn=(192, i32), dn=(192, i32),
     asq=(16, f32), au=(16, f32), ah=(16, i32), at=(256, f32), ati=(256, i32), atm=(256, i32), offa=(256, u16),
     cmpa=(4096, b16), lfa=(256, f32), tr=(256, f32), a1=(16, f32), E=(256, f32), din=(512, f32), dout=(512, f32),
     offh=(48, u16), H=(768, f32), hs=(768, f32), q1=(80, f32), q2=(80, f32), offq=(16, u16),
@@ -31,7 +33,7 @@ _SB = dict(
 _AT = {}
 SCRATCH = {}
 for _k, (_n, _d) in _SB.items():
-    if _n <= 36 and _d in (f32, u16):
+    if _n <= 36 and _d in (f32, u16, b16):
         _w = SCRATCH.get("pack_" + _d, (0, [0, 0]))[1][1]
         _AT[_k] = ("pack_" + _d, _w)
         SCRATCH["pack_" + _d] = ("sbuf", [128, _w + (_n + 15) // 16 * 16], _d)
@@ -43,10 +45,21 @@ for _k in range(8):
 NDMA = 40
 SEMAPHORES = ["cV", "cS", "cP", "cG", "sent", "arr0", "arr1"] + ["d%d" % k for k in range(NDMA)]
 
-PRM = dict(cyc=1.04, pe=0.52, g=1.56, sc=3.8, same=60.0, cross=110.0, dma=2000.0, comm=3500.0)
-OPT = dict(arr_s=[(6, 7)] * 3, pg=[((0, 50, "S"), (50, 100, "S"), (100, 129, "S"))] * 3, orph_v=[(1,)] * 3, die_v=[(0, 1)] * 3,
-           c_s=[0] * 3, bb_s=[1] * 3, xj_s=[()] * 3, orph_sign=[(2,)] * 3, seed=7, jit=4000.0, moves=8, iters=1200)
-VARIANTS = [{}, dict(g=1.1, sc=2.0), dict(g=2.0, sc=5.5), dict(same=120.0, cross=220.0), dict(pe=0.9), dict(comm=5000.0, dma=2500.0)]
+PRM = dict(cyc=0.9, pe=0.46, g=1.56, sc=3.8, same=100.0, cross=150.0, dma=2300.0, comm=4500.0)
+VARIANTS = [{}, dict(cyc=1.04, pe=0.52, same=60.0, cross=110.0, dma=2000.0, comm=3500.0), dict(cyc=0.83, pe=0.42, same=150.0, cross=200.0),
+            dict(cyc=0.83, pe=0.42, same=60.0, cross=110.0, dma=3000.0, comm=6500.0), dict(g=1.1, sc=2.0), dict(cyc=1.2, pe=0.6, g=2.0, sc=5.5)]
+OPT = dict(
+    x_parts=((0, 32), (32, 64), (64, 96), (96, 128)), s_xi=0,
+    die=[((0, 32, "V"), (32, 64, "S"), (64, 96, "V"), (96, 112, "S"), (112, 128, "V"))]
+    + [((0, 32, "V"), (96, 128, "S"), (32, 64, "V"), (80, 96, "S"), (64, 80, "V"))] * 2,
+    par=[((0, 4, "S"), (4, 8, "S"), (8, 12, "S"), (12, 14, "S"), (14, 16, "S"))] * 3,
+    xj_s=[()] * 3, e_s=[1] * 3, c_s=[0] * 3, f_s=[0] * 3, cnt_s=[(8, 9, 10, 11)] * 3,
+    arr=[tuple((e, int(w)) for e, w in "S2 S2 V1 V1 V2 V1 V1 V2 V2 V1 S1".split())] * 3,
+    og=[((0, 64, "S"), (64, 128, "S"), (128, 160, "S"), (160, 192, "S"))] * 3,
+    oc=[((0, 64, "V", 8, 1), (64, 128, "V", 8, 5), (128, 192, "S", (2, 3), 1))] * 3, bb_s=[(0, 64)] * 3,
+    ox=[((0, 192, (0, 64, 128, 192)),)] * 2 + [((0, 128, (0, 128)), (128, 192, (128, 192)))],
+    hop=[((0, 8, "SSS"), (8, 16, "SSS"))] * 2, snd=[((0, 8, "S"), (8, 16, "S"))] * 2, gcopy=1,
+    seed=7, jit=4000.0, moves=8, iters=1000, steps=12000, heat=0.004, soft=0.0)
 WAIT_ALL = True
 
 
@@ -75,7 +88,13 @@ def spans(d):
         return []
     if d[0] == "ind":
         return spans(d[1]) + spans(d[2])
-    return [(d[1], d[2], d[3])]
+    return [(d[1], d[2], d[3], d[4])]
+
+
+def meet(x, y):
+    if x[2] == y[2] and (x[0] - y[0]) % x[2]:
+        return False
+    return x[0] < y[1] and y[0] < x[1]
 
 
 def wide(d):
@@ -88,6 +107,7 @@ def psum(d):
 
 def build(me):
     ops = []
+    table = [1500.0]
 
     def add(eng, kind, args, outs, ins, cost):
         rd, wr = [], []
@@ -107,8 +127,8 @@ def build(me):
             return ("g", n_of(in0))
         return ("c", max(64, k * n_of(out)))
 
-    def half(out, in0):
-        return 1.0 if wide(out) or wide(in0) else 0.5
+    def half(*aps):
+        return 1.0 if any(wide(d) for d in aps) else 0.5
 
     def tt(out, x, y, op):
         add("V", "tt", (out, x, y, op), [out], [x, y], vcost(out, x, 1 if psum(x) or psum(y) else 2))
@@ -120,20 +140,22 @@ def build(me):
         add("V", "cp", (out, x), [out], [x], vcost(out, x, half(out, x)))
 
     def ms(out, v):
-        add("V", "ms", (out, v), [out], [], ("c", max(64, n_of(out) * (1.0 if wide(out) else 0.5))))
+        add("V", "ms", (out, v), [out], [], ("c", max(64, n_of(out) * half(out))))
 
-    def scan(out, d0, d1, op0, op1):
-        add("V", "scan", (out, d0, d1, 0.0, op0, op1), [out], [d0, d1], ("c", max(64, n_of(out))))
+    def scan(out, d0, d1, op0, op1, first=0.0):
+        add("V", "scan", (out, d0, d1, first, op0, op1), [out], [d0, d1], ("c", max(64, n_of(out) * half(out, d0, d1))))
 
     def trn(out, x):
         add("V", "trn", (out, x), [out], [x], ("c", max(64, n_of(out))))
 
-    def red(out, x):
-        add("V", "red", (out, x), [out], [x], ("c", 64))
-
     def act(out, x, func=AF.Identity, bias=0.0, scale=1.0, accum=None):
         c = ("g", n_of(x)) if x[0] == "ind" else ("c", max(64, n_of(x)) + (20 if accum else 0))
+        if func == AF.Sigmoid and table[0]:
+            c = ("c", c[1] + table[0]); table[0] = 0.0
         add("S", "act", (out, x, func, bias, scale, accum), [out] + ([accum] if accum else []), [x, bias, scale], c)
+
+    def step(out, x, at, sign=1.0):
+        act(out, x, AF.Sigmoid, bias=-256.0 * sign * at, scale=256.0 * sign)
 
     def mm(lst, start=True, stop=True):
         cyc = sum(max(64, n_of(r)) * (4 if wide(r) else 1) for o, l, r in lst)
@@ -145,23 +167,45 @@ def build(me):
     def sel(out, x, pat, op, base, cm):
         add("G", "sel", (out, x, pat, op, base, cm), [out], [x], ("c", 170 + 2 * n_of(out)))
 
+    def move(out, x):
+        if OPT["gcopy"]:
+            sel(out, x, [[0, n_of(x)]], ALU.is_ge, 0, 0)
+        else:
+            act(out, x)
+
+    def fill(out, v):
+        if OPT["gcopy"]:
+            iota(out, [[0, n_of(out)]], int(v))
+        else:
+            ms(out, v)
+
+    def take(e, out, src):
+        if e == "S":
+            act(out, src)
+        else:
+            cp(out, src)
+
     def dma(q, pairs, extra=0.0):
         add(q, "dma", pairs, [o for o, i in pairs], [i for o, i in pairs], ("dma", len(pairs), extra))
 
     def wrap(out, z, src, c0, n, first=()):
         mm(list(first) + [(out, a(z, 15 - r, 143 - r), a(src, c0 + r, c0 + 16 * n, 16)) for r in range(16)])
 
-    I = a("iw", 16, 144)
-    pm, pm2, par, npar, p32, pm16 = [a("pc", k, k + 1) for k in range(6)]
+    I = a("iw", 16, 144); BOW = a("bow", 0, 128)
+    pm, pm2, par, npar, p32, pm16, pf, p8, pq = [a("pc", k, k + 1) for k in range(9)]
 
-    dma("Y", [(a("X", OFF, OFF + 1024), ext("x0", (slice(None), slice(0, 1024))))], 700.0)
-    dma("S", [(a("X", OFF + 1024, OFF + W), ext("x0", (slice(None), slice(1024, W))))], 700.0)
-    dma("Y", [(a("cm"), ext("come", (slice(None), slice(None))))], 500.0)
-    dma("Y", [(a("cin", 32 * b + 16 * h, 32 * b + 16 * h + 16), ext("cd0", (slice(h, 8, 2), slice(512 * b, 512 * b + 512))))
-              for b in range(4) for h in range(2)], 500.0)
-    dma("Y", [(a("blk"), ext("cd0", (slice(None), slice(None))))])
-    dma("Y", [(a("D", OFF + 1024, OFF + W), ext("dl0", (slice(None), slice(None))))], 1500.0)
-    dma("Y", [(a("ag", 16 * h, 16 * h + 16), ext("age", (slice(h, 8, 2), slice(None)))) for h in range(2)])
+    parts = OPT["x_parts"]
+    for k, (c0, c1) in enumerate(parts):
+        dma("Y", [(a("X", OFF + 16 * c0, OFF + 16 * c1), ext("x0", (slice(None), slice(16 * c0, 16 * c1))))], 11.0 * c1 + (150.0 if k else 0.0))
+        if k == 0:
+            dma("Y", [(a("cm", 0, S), ext("come", (slice(None), slice(0, S))))], 11.0 * c1 + 150.0)
+    dma("Y", [(a("cin", 16 * b, 16 * b + 16), ext("cd0", (slice(None), slice(256 * b, 256 * b + 256)))) for b in range(8)], 1700.0)
+    dma("Y", [(a("blk"), ext("cd0", (slice(None), slice(None))))], 1700.0)
+    dma("Y", [(a("D", OFF + 1024, OFF + W), ext("dl0", (slice(None), slice(None))))], 3000.0)
+    dma("Y", [(a("cm", S, 3 * S), ext("come", (slice(None), slice(S, 3 * S))))], 3300.0)
+    dma("Y", [(a("ag", 16 * h, 16 * h + 16), ext("age", (slice(h, 8, 2), slice(None)))) for h in range(2)], 3300.0)
+    for k in range(1, len(ops)):
+        ops[k]["after"] = k - 1
     iota(a("ones"), [[0, 160]], 1)
     sel(a("bow0"), a("ones", 0, 144), [[-16, 9], [0, 16]], ALU.is_ge, 0, 1)
     sel(a("bow"), a("bow0"), [[16, 9], [0, 16]], ALU.is_ge, 15, -1)
@@ -169,53 +213,65 @@ def build(me):
     iota(a("pi"), [[0, 4]], 0, 1)
     iota(a("pw0"), [[0, 8], [32, 16]], 0)
     sel(a("iw"), a("ones"), [[-1, 160]], ALU.is_equal, 16, 1)
+    iota(a("j16"), [[0, 16], [1, 16]], 0)
     iota(a("coef"), [[61, 16], [0, 16]], 7)
     iota(a("c16"), [[16, 16]], 0)
-    sel(a("tri"), a("bow", 0, 128), [[1, 128]], ALU.is_ge, 0, -1)
+    sel(a("tri"), BOW, [[1, 128]], ALU.is_ge, 0, -1)
     iota(a("kr"), [[1, 192]], 0)
-    iota(a("j16"), [[0, 16], [1, 16]], 0)
     iota(a("h0"), [[1, 16], [0, 2]], 0)
-    iota(a("onesf"), [[0, 256]], 1)
     ts(a("pj", 0, 1), a("pi", 0, 1), 15, ALU.bitwise_and)
     ts(a("pj", 1, 2), a("pi", 0, 1), 31, ALU.bitwise_and)
     cp(pm, a("pj", 0, 1))
     cp(p32, a("pj", 1, 2))
-    ts(pm2, a("pj", 0, 1), 2.0, ALU.mult, -0.75, ALU.add)
+    cp(pf, a("pi", 0, 1))
+    ts(pm2, a("pj", 0, 1), 2.0, ALU.mult, -0.3125, ALU.add)
     ts(pm16, a("pj", 0, 1), 16.0, ALU.mult)
     ts(par, a("pj", 1, 2), 16.0, ALU.is_ge)
     ts(npar, a("pj", 1, 2), 16.0, ALU.is_lt)
+    ts(p8, a("pj", 0, 1), 8.0, ALU.is_ge, -127.0, ALU.mult)
+    tt(pq, p8, pm16, ALU.add)
     ts(a("pw"), a("pw0"), pm2, ALU.add)
-    ms(a("bv"), 5376.0); ms(a("bs"), 2816.0); ms(a("bk", 64, 128), -86016.0); ms(a("bk", 0, 64), -40960.0)
-    ms(a("X", 0, OFF), 0.0); ms(a("XJ", 0, OFF), -1.0); ms(a("C", 0, OFF), -1.0); ms(a("D", 1024, 1024 + OFF), -1)
-    ms(a("F", 129, 141), 1.0); ms(a("P", 0, 4), 0.0); ms(a("acol", 0, 1), -0.375)
+    ms(a("bv"), 5376.0); ms(a("bk"), -86016.0); ms(a("onesf"), 1.0)
+    ms(a("X", 0, OFF), 0.0); ms(a("XJ", W0, OFF), -1.0); ms(a("C", W0, OFF), -1.0); ms(a("D", 0, OFF + 1024), -1); ms(a("CD", 0, 16), 0.0)
+    ms(a("Fp", 0, 1), 0.0); ms(a("acol", 0, 1), -0.375); ms(a("wv", 0, 6, 2), 1.0)
+    step(a("kp"), a("j16"), 0.5)
     act(a("ni"), I, scale=-1.0)
-    act(a("bom"), a("bow", 0, 128), scale=-512.0)
+    act(a("ni16"), I, scale=-16.0)
+    act(a("ih"), I, scale=0.5)
+    act(a("bom"), BOW, scale=-512.0)
     act(a("zk"), a("z1"), scale=8192.0)
-    act(a("zs"), a("z1"), scale=1.0 / 32)
-    if any(e == "V" for pg in OPT["pg"] for c0, c1, e in pg):
-        act(a("zv"), a("z1"), scale=1.0 / 16)
-        act(a("nih"), I, scale=-0.5)
-    act(a("bof"), a("bow", 0, 128))
-    act(a("idf"), I)
+    act(a("nkr"), a("j16", 0, 128), scale=-1.0)
+    act(a("bof"), BOW)
     act(a("iwe"), a("iw"), scale=npar)
     act(a("iwo"), a("iw"), scale=par)
     ts(a("dm"), a("j16"), pm, ALU.is_equal)
-    ts(a("kp"), a("j16"), 0.5, ALU.is_ge)
-    ts(a("kw"), a("c16", 0, 12), pm, ALU.add, 0.5, ALU.add)
+    if any(OPT["xj_s"]):
+        ts(a("c16b"), a("dm", 0, 16), 0.5, ALU.mult)
+        for r in range(16):
+            act(a("U", 128 * r, 128 * r + 128), a("bom"), scale=a("c16b", r, r + 1))
+    ts(a("H", 0, S), a("j16"), pm, ALU.is_lt, -BIG, ALU.mult)
+    act(a("H", S, 2 * S), a("dm"), scale=BIG)
+    tt(a("Mh"), a("H", 0, S), a("H", S, 2 * S), ALU.add)
+    ts(a("Mh", 15, S, 16), a("Mh", 15, S, 16), -2 * BIG, ALU.add)
+    act(a("idf"), I)
+    ts(a("kw"), a("c16", 0, 12), pm, ALU.add)
+    ts(a("ky"), a("kw"), float(CAP), ALU.add)
     ts(a("l16"), a("c16"), 0.0, ALU.mult, pm, ALU.add)
     ts(a("l15"), a("c16", 0, 12), 15.0, ALU.add)
     ts(a("lc"), a("c16"), 1.0 / 16, ALU.mult)
+    ts(a("lp"), a("c16", 0, 8), 1.0 / 8, ALU.mult, pq, ALU.add)
     ts(a("l512"), a("h0"), pm16, ALU.add)
     ts(a("lm"), a("c16"), 2.0, ALU.mult, p32, ALU.add)
     for t in range(R):
-        rs = float((ST * (t + 1)) % 16)
-        ts(a("rmask", 2 * t, 2 * t + 1), pm, rs, ALU.is_lt, 4096.0, ALU.mult)
-        ts(a("rmask", 2 * t + 1, 2 * t + 2), pm, rs, ALU.is_ge, 4096.0, ALU.mult)
+        rs = float((ST * (t + 1)) % 16); cs = (ST * (t + 1)) // 16
+        ts(a("mk", 2 * t, 2 * t + 1), pm, rs, ALU.is_lt, -64.0, ALU.mult)
+        ts(a("mk", 2 * t + 1, 2 * t + 2), pm, rs, ALU.is_ge, -64.0, ALU.mult)
+        ts(a("pc", 9 + t, 10 + t), pf, float(127 - cs), ALU.is_equal, float(-W), ALU.mult)
+        ts(a("wv", 2 * t + 1, 2 * t + 2), a("pc", 9 + t, 10 + t), 16.0, ALU.add)
+        ts(a("kc", 12 * t, 12 * t + 12), a("kw"), float(-16 - OFF - S * t - 16 * cs), ALU.add)
     for t in range(R - 1):
         ts(a("a5", 80 * t, 80 * t + 80, 5), a("c16"), pm, ALU.add, float(W + S * t), ALU.add)
     ms(a("thr"), 0.0)
-    iota(a("C", OFF + W, OFF + W + 2 * S), [[0, 2 * S]], -1)
-    cp(a("cinf"), a("cin"))
     cp(a("blkf"), a("blk"))
     dma("Y", [(a("C", OFF, OFF + W, 1, slice(m, 128, 16)), a("blkf")) for m in range(16)], 4000.0)
     cp(a("agf"), a("ag"))
@@ -225,66 +281,95 @@ def build(me):
             act(a("thr", 80 * t + k, 80 * t + 80, 5), a("agt", 16 * t, 16 * t + 16), bias=float(W + S * t + S - 1), scale=-1.0)
 
     for t in range(R):
-        lo = S * t; B = W + lo; L = OFF + lo; BB = OFF + B
+        lo = S * t; B = W + lo; L = OFF + lo; BB = OFF + B; K0 = 16 + lo
         last = t == R - 1
         cs = (ST * (t + 1)) // 16; n1 = 128 - cs
         old = "X" if t == 0 else "XJ"
-        for c0, c1, pn in ((0, 64, "ps4"), (64, 128, "ps5")) if t == 0 else ((0, 128, "ps4"),):
+        for k, (c0, c1) in enumerate(parts if t == 0 else ((0, 128),)):
+            pn = "ps%d" % (4 + k % 2)
             wrap(a(pn, 0, c1 - c0), "z1", "X", L + 16 * c0, c1 - c0)
-            act(a(pn, 256, 256 + c1 - c0), a(pn, 0, c1 - c0), AF.Square, scale=0.25)
-            tt(a("wh", c0, c1), a(pn, 256, 256 + c1 - c0), a("pw", c0, c1), ALU.add)
-            ts(a("whi", c0, c1), a("wh", c0, c1), 0.5, ALU.mult)
-            ts(a("whm", c0, c1), a("whi", c0, c1), 255, ALU.bitwise_and)
+            act(a(pn, 128, 128 + c1 - c0), a(pn, 0, c1 - c0), AF.Square, scale=0.25)
+            tt(a("wh", c0, c1), a(pn, 128, 128 + c1 - c0), a("pw", c0, c1), ALU.add)
+            ts(a("whm", c0, c1), a("wh", c0, c1), 1, ALU.arith_shift_right, 255, ALU.bitwise_and)
             cp(a("who", c0, c1), a("whm", c0, c1))
         if t > 0:
-            act(a("ps7", S, 2 * S), a("cm", S * t, S * t + S), bias=-0.25, scale=0.5)
-            ms(a("XJ", L - S, L), -1.0)
-        trn(a("cw"), a("cinf"))
-        if t > 0:
-            act(a("cw", 112, 128), a("a1"))
-        ts(a("offp", 0, n1), a("cw", cs, 128), float(OFF), ALU.add)
-        ts(a("offp", n1, 129), a("cw", 0, cs + 1), float(OFF), ALU.add)
-        act(a("thr0", 1, n1), a("cw", cs + 1, 128), AF.Relu, scale=-1.0)
-        act(a("thr0", n1, 128), a("cw", 0, cs), AF.Relu, scale=-1.0)
-        act(a("thr0", 0, 1), a("cw", cs, cs + 1), AF.Relu, scale=-1.0, bias=a("rmask", 2 * t, 2 * t + 1))
-        act(a("thr0", 128, 129), a("cw", cs, cs + 1), AF.Relu, scale=-1.0, bias=a("rmask", 2 * t + 1, 2 * t + 2))
-        dv = OPT["die_v"][t]; ds = [q for q in range(4) if q not in dv]
-        for q in dv:
-            mm([(a("ps%d" % q), I, a("bv"))], True, False)
+            act(a("ps4", S, 2 * S), a("cm", S * t, S * t + S), bias=-0.25, scale=0.5)
+            fill(a("XJ", L - S, L), -1.0)
+            fill(a("CD", K0 - S, K0), 1.0)
+        ts(a("offp"), ind(a("cin" if t == 0 else "cinf"), a("lp")), 16.0, ALU.add)
+        for q in range(4):
+            mm([(a("ps%d" % q), I, a(old, L + 512 * q, L + 512 * q + 512) if q in OPT["xj_s"][t] else a("bv"))], True, False)
+        ds = [(c0, c1) for c0, c1, e in OPT["die"][t] if e == "S"]
+        for k, (c0, c1) in enumerate(ds[:2]):
+            mm([(a("ps%d" % (6 + k), 0, 16 * (c1 - c0)), a("ni"), a(old, L + 16 * c0, L + 16 * c1))], True, False)
         if t == 0:
             ts(a("xi"), a("cm", 0, S), 0.5, ALU.mult, -0.25, ALU.add)
         else:
             add("V", "recv", t - 1, [a("Z", S * (t - 1), S * t)], [a("Z", S * (t - 1), S * t)], ("c", 0))
-            tt(a("xi"), a("Z", S * (t - 1), S * t), a("ps7", S, 2 * S), ALU.add)
+            tt(a("xi"), a("Z", S * (t - 1), S * t), a("ps4", S, 2 * S), ALU.add)
         cp(a("x2", 0, S), a("xi"))
-        for q in ds:
-            mm([(a("ps%d" % q), a("ni"), a(old, L + 512 * q, L + 512 * q + 512))], True, False)
-            act(a("g2", 512 * q, 512 * q + 512), ind(a("x2", 0, S), a("who", 32 * q, 32 * q + 32)))
-            mm([(a("ps%d" % q), I, a("g2", 512 * q, 512 * q + 512))], False, True)
-        for q in dv:
-            tt(a("cmpd", 512 * q, 512 * q + 512), ind(a("xi"), a("who", 32 * q, 32 * q + 32)), a(old, L + 512 * q, L + 512 * q + 512), ALU.is_ge)
-            mm([(a("ps%d" % q), a("bom"), a("cmpd", 512 * q, 512 * q + 512))], False, True)
-        for q in ds:
-            act(a("cmpd", 512 * q, 512 * q + 512), a("ps%d" % q), AF.Sign, bias=0.5)
-            mm([(a("ps%d" % q), I, a("bs"))], True, False)
-            mm([(a("ps%d" % q), a("bom"), a("cmpd", 512 * q, 512 * q + 512))], False, True)
+        for c0, c1, e in OPT["die"][t]:
+            o = a("CD", K0 + 16 * c0, K0 + 16 * c1); n = 16 * (c1 - c0)
+            if e == "S":
+                k = ds.index((c0, c1)); pq2 = a("ps%d" % (6 + k), 0, n); gq = a("g2", 512 * k, 512 * k + n)
+                act(gq, ind(a("xi") if OPT["s_xi"] else a("x2", 0, S), a("who", c0, c1)))
+                mm([(pq2, I, gq)], False, True)
+                step(o, pq2, -0.5)
+            else:
+                tt(o, ind(a("xi"), a("who", c0, c1)), a(old, L + 16 * c0, L + 16 * c1), ALU.is_ge)
+        wrap(a("ps5", 256, 272), "z1", "x2", 0, 16)
+        act(a("asq"), a("ps5", 256, 272), AF.Square, scale=0.25)
+        act(a("au"), a("ps5", 256, 272))
+        wrap(a("ps4", 0, 64), "z1", "CD", K0, 64)
+        wrap(a("ps4", 64, 128), "z1", "CD", K0 + 1024, 64)
+        cuts = [0, 16, 128] if t == 0 else [0, 128]
+        for k in range(len(cuts) - 1):
+            act(a("sg", cuts[k], cuts[k + 1]), a("ps4", cuts[k], cuts[k + 1]), AF.Sign, bias=-10.5,
+                accum=None if last else a("acc", 2 * t + k, 2 * t + k + 1))
         for q in range(4):
             if q in OPT["xj_s"][t]:
-                act(a("g2", 512 * q, 512 * q + 512), a("ps%d" % q), AF.Relu, scale=-2.0)
-                mm([(a("ps%d" % q), I, a(old, L + 512 * q, L + 512 * q + 512)), (a("ps%d" % q), a("ni"), a("g2", 512 * q, 512 * q + 512))])
-                act(a("XJ", L + 512 * q, L + 512 * q + 512), a("ps%d" % q))
+                mm([(a("ps%d" % q, r, 512, 16), a("U", 128 * r, 128 * r + 128), a("sg", 32 * q, 32 * q + 32)) for r in range(16)], False, True)
+                act(a("XJ", L + 512 * q, L + 512 * q + 512), a("ps%d" % q), bias=-256.0)
             else:
+                mm([(a("ps%d" % q), a("bom"), a("CD", K0 + 512 * q, K0 + 512 * q + 512))], False, True)
                 tt(a("XJ", L + 512 * q, L + 512 * q + 512), a("ps%d" % q), a(old, L + 512 * q, L + 512 * q + 512), ALU.min)
-        wrap(a("ps4", 0, 64), "z1", "cmpd", 0, 64)
-        wrap(a("ps4", 64, 128), "z1", "cmpd", 1024, 64)
-        cuts = sorted(set([0, 128] + ([16] if t == 0 else []) + [32 * q for q in range(1, 4) if (q in dv) != (q - 1 in dv)]))
-        for k in range(len(cuts) - 1):
-            c0, c1 = cuts[k], cuts[k + 1]
-            act(a("sg", c0, c1), a("ps4", c0, c1), AF.Sign, bias=-10.5 if c0 // 32 in dv else -5.0, accum=None if last else a("acc", 8 * t + k + 1, 8 * t + k + 2))
-        wrap(a("ps6", 0, 16), "z1", "x2", 0, 16)
-        act(a("asq"), a("ps6", 0, 16), AF.Square, scale=0.25)
-        act(a("au"), a("ps6", 0, 16))
-        act(a("x2", S, 2 * S), a("x2", 0, S))
+        for k, (r0, r1, e) in enumerate(OPT["par"][t]):
+            end = k == len(OPT["par"][t]) - 1
+            if end:
+                mm([(a("ps5", 0, n1), a("ni16"), a("sg", cs, 128)), (a("ps5", n1, 129), a("ni16"), a("sg", 0, cs + 1)),
+                    (a("ps5", 0, 129, 128), I, a("mk", 2 * t, 2 * t + 2))], False, False)
+            take(e, a("pg", 128 * r0, 128 * r1), ind(a("CD", 0, 16 + B), a("offp", 8 * r0, 8 * r1)))
+            mm([x for r in range(r0, r1) for x in ((a("ps5", 0, n1), a("z1", 15 - r, 143 - r), a("pg", 128 * r + cs, 128 * r + 128)),
+                                                   (a("ps5", n1, 129), a("z1", 15 - r, 143 - r), a("pg", 128 * r, 128 * r + cs + 1)))], k == 0, end)
+        if OPT["f_s"][t]:
+            step(a("F", 0, 129), a("ps5", 0, 129), 26.5)
+        else:
+            ts(a("F", 0, 129), a("ps5", 0, 129), 26.5, ALU.is_ge)
+        mm([(a("ps4", 0, 128), I, a("nkr"))], True, False)
+        scan(a("Fp", 1, 130), a("ones", 0, 129), a("F", 0, 129), ALU.mult, ALU.add)
+        mm([(a("ps4", 0, 128), a("Fp", 1, 129), BOW)], False, True)
+        mm([(a("ps5", 256, 386), BOW, a("Fp", 0, 130)), (a("ps5", 256, 385), a("tri"), a("F", 0, 129))])
+        act(a("Q", 0, 130), a("ps5", 256, 386))
+        ts(a("uf"), a("kw"), a("Q", 129, 130), ALU.is_ge, -4096.0, ALU.mult)
+        tt(a("uu"), a("uf"), a("kc", 12 * t, 12 * t + 12), ALU.max)
+        cs_ = OPT["cnt_s"][t]
+        if len(cs_) < 12:
+            cp(a("vb"), a("ps4", 0, 128))
+        for k in range(12):
+            if k in cs_:
+                step(a("M", 128 * k, 128 * k + 128), a("vb") if len(cs_) < 12 else a("ps4", 0, 128), 16 * k + 0.5, -1.0)
+            else:
+                ts(a("M", 128 * k, 128 * k + 128), a("vb"), 16 * k + 0.5, ALU.is_lt)
+        for k in range(12):
+            mm([(a("ps5", k, k + 1), a("M", 128 * k, 128 * k + 128), a("wv", 2 * t, 2 * t + 1))], k == 0, k == 11)
+        cp(a("cu"), a("ps5", 0, 12))
+        o = a("ps4", 0, 12)
+        mm([(a("ps4", k, k + 1), a("M", 128 * k, 128 * k + 128), a("wv", 2 * t + 1, 2 * t + 2)) for k in range(12)], True, False)
+        mm([(o, a("idf"), a("uu"))], False, False)
+        tt(a("cmp2"), ind(a("Q", 0, 130), a("cu")), a("kr"), ALU.is_le)
+        mm([(o, a("z1", 15 - r, 143 - r), a("cmp2", r, CAP, 16)) for r in range(16)], False, True)
+        ts(a("offo"), o, float(L + 16 * cs), ALU.add)
+        move(a("x2", S, 2 * S), a("x2", 0, S))
         ts(a("ah"), a("asq"), 0.5, ALU.mult, a("acol", t, t + 1), ALU.add)
         if OPT["c_s"][t]:
             cp(a("ahf"), a("ah"))
@@ -296,34 +381,37 @@ def build(me):
             tt(a("ati"), ind(a("ah"), a("l16")), a("at"), ALU.add)
         ts(a("atm"), a("ati"), W - 1, ALU.bitwise_and)
         cp(a("offa"), a("atm"))
-        for h in range(2):
-            for q in range(4 * h, 4 * h + 4):
-                src = ind(a("XJ", L, BB), a("offa", 32 * q, 32 * q + 32))
-                if q in OPT["arr_s"][t]:
-                    gq = a("g2", 512 * (q % 2), 512 * (q % 2) + 512); pq = a("ps%d" % (2 + q % 2))
-                    mm([(pq, a("ni"), a("x2"))], True, False)
-                    act(gq, src)
-                    mm([(pq, I, gq)], False, True)
-                    act(a("cmpa", 512 * q, 512 * q + 512), pq, AF.Sign, bias=0.5)
-                else:
-                    tt(a("cmpa", 512 * q, 512 * q + 512), src, a("x2"), ALU.is_ge)
-            pn = "ps%d" % (6 + h)
-            o = a(pn, 0, 128)
-            wrap(o, "zk", "cmpa", 2048 * h, 128, [(a(pn, 32 * k, 32 * k + 32), I, a("bk", 32, 64) if 4 * h + k in OPT["arr_s"][t] else a("bk", 64, 96)) for k in range(4)])
-            tt(a("lfa", 128 * h, 128 * h + 128), o, a("atm", 128 * h, 128 * h + 128), ALU.min)
+        m0 = 0; k = 0
+        for e, w in OPT["arr"][t]:
+            n = S * w; src = ind(a("XJ", L, BB), a("offa", 16 * m0, 16 * (m0 + w))); o = a("cmpa", S * m0, S * m0 + n)
+            if e == "S":
+                gq = a("g2", 512 * k, 512 * k + n); pq2 = a("ps%d" % (2 + k), 0, n); k = 1 - k
+                mm([(pq2, a("ni"), a("x2", 0, n))], True, False)
+                act(gq, src)
+                mm([(pq2, I, gq)], False, True)
+                step(o, pq2, -0.5)
+            else:
+                tt(o, src, a("x2", 0, n), ALU.is_ge)
+            m0 += w
+            if m0 % 4 == 0:
+                o = a("ps%d" % (6 + (m0 - 4) // 8), 16 * ((m0 - 4) % 8), 16 * ((m0 - 4) % 8) + 64)
+                wrap(o, "zk", "cmpa", S * (m0 - 4), 64, [(o, I, a("bk", 0, 64))])
+            if m0 % 8 == 0:
+                tt(a("lfa", 16 * m0 - 128, 16 * m0), a("ps%d" % (5 + m0 // 8), 0, 128), a("atm", 16 * m0 - 128, 16 * m0), ALU.min)
         tt(a("tr", 0, 128), a("lfa", 0, 128), a("lfa", 128, 256), ALU.max)
         tt(a("tr", 128, 192), a("tr", 0, 64), a("tr", 64, 128), ALU.max)
         tt(a("tr", 192, 224), a("tr", 128, 160), a("tr", 160, 192), ALU.max)
         tt(a("tr", 224, 240), a("tr", 192, 208), a("tr", 208, 224), ALU.max)
         ts(a("a1"), a("tr", 224, 240), float(lo), ALU.add, -1.0, ALU.max)
-        act(a("X", BB, BB + S), a("x2", 0, S))
-
-        def parents_row():
+        move(a("X", BB, BB + S), a("x2", 0, S))
+        if OPT["e_s"][t]:
+            for k in range(16):
+                act(a("E", 16 * k, 16 * k + 16), a("dm", 0, 16), scale=a("a1", k, k + 1))
+        else:
             tt(a("E"), ind(a("a1"), a("lc")), a("dm"), ALU.mult)
-            mm([(a("ps6", 0, S), a("bof"), a("E"))])
-            act(a("C", BB, BB + S), a("ps6", 0, S))
+        mm([(a("ps6", 0, S), a("bof"), a("E"))])
+        act(a("C", BB, BB + S), a("ps6", 0, S))
         if last:
-            parents_row()
             dma("Y", [(ext("yx", (slice(None), slice(W, W + S))), a("X", BB, BB + S)),
                       (ext("ya", (slice(None), slice(W, W + S))), a("onesf", 0, S, 1, slice(0, 8)))])
             act(a("aw"), a("sg"), bias=0.5, scale=-0.5)
@@ -331,120 +419,92 @@ def build(me):
             dma("Y", [(ext("ya", (slice(h, 8, 2), slice(512 * b, 512 * b + 512))), a("awt", 32 * b + 16 * h, 32 * b + 16 * h + 16))
                       for b in range(4) for h in range(2)])
         else:
-            ts(a("offh", 0, 16), a("tr", 224, 240), float(L), ALU.add, float(OFF - 1), ALU.max)
+            ts(a("offh", 0, 16), a("tr", 224, 240), float(K0), ALU.add, 15.0, ALU.max)
             act(a("a5", 80 * t + 1, 80 * t + 80, 5), a("a1"))
-        mm([(a("ps5", 0, 129), a("ni"), a("thr0"))], True, False)
-        for c0, c1, e in OPT["pg"][t]:
-            if c1 == 129:
-                mm([(a("ps5", 0, n1), a("ni"), a("sg", cs, 128)), (a("ps5", n1, 129), a("ni"), a("sg", 0, cs + 1))], False, False)
+        ts(a("offw"), ind(a("D", 0, BB), a("offo")), 16.0, ALU.add)
+        act(a("y"), ind(a("X", 0, BB), a("offo")))
+        mm([(a("ps0", 0, CAP), I, a("y")), (a("ps0", 256, 256 + CAP), a("ih"), a("y"))])
+        act(a("XJ", CAP, 2 * CAP), a("y"))
+        ts(a("dp"), a("offw"), float(W0), ALU.add)
+        for j0, j1, e in OPT["og"][t]:
+            take(e, a("G", 16 * j0, 16 * j1), ind(a("XJ", W0, BB), a("offw", j0, j1)))
+        for j0, j1, e, by, bank in OPT["oc"][t]:
+            n = j1 - j0; o = a("ps%d" % bank, j0, j1)
             if e == "S":
-                act(a("pg", 16 * c0, 16 * c1), ind(a("XJ", 0, BB), a("offp", c0, c1)), AF.Sign, bias=-0.5, scale=-1.0)
-            else:
-                ts(a("pg", 16 * c0, 16 * c1), ind(a("XJ", 0, BB), a("offp", c0, c1)), 0.0, ALU.is_lt)
-            mm([(a("ps5", c0, c1), a("zs" if e == "S" else "zv", 15 - r, 143 - r), a("pg", 16 * c0 + r, 16 * c1, 16)) for r in range(16)]
-               + ([] if e == "S" else [(a("ps5", c0, c1), a("nih"), a("ones", 0, c1 - c0))]), False, c1 == 129)
-        act(a("F", 0, 129), a("ps5", 0, 129), AF.Relu, bias=-2.0, scale=2.0)
-        mm([(a("ps5", 0, 141), a("bow", 0, 128), a("F"))])
-        mm([(a("ps5", 256, 397), a("tri"), a("F"))])
-        scan(a("P", 1, 142), a("onesf", 0, 141), a("ps5", 0, 141), ALU.mult, ALU.add)
-        tt(a("Q"), a("ps5", 256, 397), a("P", 0, 141), ALU.add)
-        for k in range(12):
-            act(a("junk", 144 * k, 144 * k + 141), a("P", 1, 142), AF.Sign, bias=a("kw", k, k + 1), scale=-1.0, accum=a("lv", k, k + 1))
-        ts(a("cu"), a("lv"), 0.5, ALU.mult, 70.5, ALU.add)
-        k0 = L + 16 * cs
-        ts(a("base", 0, 12), a("lv"), 8.0, ALU.mult, float(8 * 141 + k0), ALU.add)
-        ts(a("base", 12, 24), a("lv"), float(2 * n1 - 141), ALU.is_ge, float(-W), ALU.mult)
-        ts(a("base", 24, 36), a("lv"), float(2 * 129 - 141), ALU.is_ge, float(NT - 16 * 129 - k0 + W), ALU.mult)
-        tt(a("cmp2"), ind(a("Q"), a("cu")), a("kr"), ALU.is_le)
-        o = a("ps5", 0, 12)
-        mm([(o, a("idf"), a("base", 12 * k, 12 * k + 12)) for k in range(3)], True, False)
-        mm([(o, a("z1", 15 - r, 143 - r), a("cmp2", r, 192, 16)) for r in range(16)], False, True)
-        ts(a("offd"), o, -1024.0, ALU.add, float(BB - 1 - 1024), ALU.min)
-        ts(a("offg"), o, float(BB - 1), ALU.min)
-        cp(a("offo"), o)
-        ts(a("ogf"), o, float(BB - 1), ALU.min, float(1 - OFF), ALU.add)
-        ts(a("offw"), ind(a("D", 1024, BB), a("offd")), float(OFF), ALU.add)
-        act(a("y"), ind(a("X", 0, BB), a("offg")))
-        mm([(a("ps0", 0, 192), I, a("y"))])
-        ts(a("dp"), a("offw"), float(1 - OFF), ALU.add)
-        for c in range(3):
-            gsrc = ind(a("XJ", 0, BB), a("offw", 64 * c, 64 * c + 64))
-            if c in OPT["orph_v"][t]:
-                cp(a("G", 1024 * c, 1024 * c + 1024), gsrc)
-            else:
-                act(a("G", 1024 * c, 1024 * c + 1024), gsrc)
-            o = a("ps1", 64 * c, 64 * c + 64)
-            if c in OPT["orph_sign"][t]:
-                for h in range(2):
-                    k = 1024 * c + 512 * h; pn = "ps%d" % (2 + h)
-                    mm([(a(pn, m, 512, 16), a("ni"), a("y", 64 * c + 32 * h, 64 * c + 32 * h + 32)) for m in range(16)], True, False)
+                for h in range(n // 32):
+                    k = 16 * j0 + 512 * h; pn = "ps%d" % by[h]
+                    mm([(a(pn, m, 512, 16), a("ni"), a("y", j0 + 32 * h, j0 + 32 * h + 32)) for m in range(16)], True, False)
                     mm([(a(pn), I, a("G", k, k + 512))], False, True)
-                    act(a("cmpo", k, k + 512), a(pn), AF.Sign, bias=0.5)
-                mm([(o, I, a("bk", 0, 64))] + [(o, a("zk", 15 - m, 143 - m), a("cmpo", 1024 * c + m, 1024 * c + 1024, 16)) for m in range(16)])
+                    step(a("cmpo", k, k + 512), a(pn), -0.5)
+                mm([(o, I, a("bk", 0, n))] + [(o, a("zk", 15 - m, 143 - m), a("cmpo", 16 * j0 + m, 16 * j1, 16)) for m in range(16)])
             else:
-                for h in range(2):
-                    for m in range(8 * h, 8 * h + 8):
-                        k = 1024 * c + 64 * m
-                        tt(a("cmpo", k, k + 64), a("G", 1024 * c + m, 1024 * c + 1024, 16), a("ps0", 64 * c, 64 * c + 64), ALU.is_ge)
-                    mm(([(o, I, a("bk", 64, 128))] if h == 0 else []) +
-                       [(o, a("zk", 15 - m, 143 - m), a("cmpo", 1024 * c + 64 * m, 1024 * c + 64 * m + 64)) for m in range(8 * h, 8 * h + 8)], h == 0, h == 1)
-            tt(a("left", 64 * c, 64 * c + 64), o, a("dp", 64 * c, 64 * c + 64), ALU.min)
-        trn(a("lt"), a("left"))
-        scan(a("ls"), a("kp", 0, 192), a("lt"), ALU.mult, ALU.max)
-        if OPT["bb_s"][t]:
-            act(a("bb"), ind(a("ls"), a("l15")))
-        else:
-            cp(a("bb"), ind(a("ls"), a("l15")))
-        trn(a("br"), a("bb"))
-        ts(ind(a("C"), a("offo")), a("br"), 1.0, ALU.mult, -1.0, ALU.add)
+                mm([(o, I, a("bk", 0, n))], True, False)
+                for h in range(0, 16, by):
+                    for m in range(h, h + by):
+                        tt(a("cmpo", 16 * j0 + n * m, 16 * j0 + n * m + n), a("G", 16 * j0 + m, 16 * j1, 16), a("ps0", j0, j1), ALU.is_ge)
+                    mm([(o, a("zk", 15 - m, 143 - m), a("cmpo", 16 * j0 + n * m, 16 * j0 + n * m + n)) for m in range(h, h + by)], False, h + by == 16)
+            tt(a("left", j0, j1), o, a("dp", j0, j1), ALU.min)
+            trn(a("lt", j0, j1), a("left", j0, j1))
+            scan(a("ls", j0, j1), a("kp", 0, n), a("lt", j0, j1), ALU.mult, ALU.max)
+            src = ind(a("ls", j0, j1), a("l15", 0, n // 16))
+            if j0 in OPT["bb_s"][t]:
+                act(a("bb", j0, j1), src, AF.Relu, bias=float(1 - OFF))
+            else:
+                ts(a("bb", j0, j1), src, float(1 - OFF), ALU.add, 0.0, ALU.max)
+            trn(a("br", j0, j1), a("bb", j0, j1))
+            ts(ind(a("C", 0, BB), a("offo", j0 // 16, j1 // 16)), a("br", j0, j1), 1.0, ALU.mult, -1.0, ALU.add)
         if not last:
-            dma("Y", [(a("cinf", 32 * b + 16 * h, 32 * b + 16 * h + 16), a("C", L + S + 512 * b, L + S + 512 * b + 512, 1, slice(16 * h, 128, 32)))
-                      for b in range(4) for h in range(2)], 500.0)
-        for ih in range(2):
-            src = "iwo" if ih else "iwe"
-            mm([(a("ps5", ih, 12, 2), a(src, 16 + 16 * (ih - gh), 144 + 16 * (ih - gh)), a("ls", 16 * gh + 15, 192, 32)) for gh in range(2)])
-        ts(a("w1"), a("ps5", 0, 12), 0.5, ALU.is_lt, 8192.0, ALU.mult)
-        tt(a("w2"), a("ps5", 0, 12), a("w1"), ALU.add)
-        tt(a("w3"), a("w2"), a("ogf"), ALU.min)
-        ts(a("offx"), a("w3"), float(OFF - 1), ALU.add)
-        act(a("ps4", 256, 448), a("y"), bias=-0.25, scale=0.5)
-        act(a("xh"), ind(a("X", 0, BB), a("offx")), scale=0.5)
-        tt(a("yn"), a("xh"), a("ps4", 256, 448), ALU.add)
-        cp(ind(a("X"), a("offo")), a("yn"))
+            dma("Y", [(a("cinf", 16 * b, 16 * b + 16), a("C", L + S + 256 * b, L + S + 256 * b + 256, 1, slice(0, 128, 16))) for b in range(8)], 500.0)
+        for j0, j1, k0 in OPT["ox"][t]:
+            c0, c1 = j0 // 16, j1 // 16
+            mm([(a("ps4", c0 + ih, c1, 2), a("iwo" if ih else "iwe", 16 + 16 * (ih - gh), 144 + 16 * (ih - gh)), a("ls", j0 + 16 * gh + 15, j1, 32))
+                for ih in range(2) for gh in range(2)])
+            tt(a("w1", c0, c1), a("ps4", c0, c1), a("ky", c0, c1), ALU.max)
+            ts(a("offx", c0, c1), a("w1", c0, c1), float(-CAP), ALU.add)
+            act(a("xh", j0, j1), ind(a("XJ", CAP, BB), a("offx", c0, c1)), bias=-0.25, scale=0.5)
+            tt(a("yn", j0, j1), a("xh", j0, j1), a("ps0", 256 + j0, 256 + j1), ALU.add)
+            for k in range(len(k0) - 1):
+                cp(ind(a("X", 0, BB), a("offo", k0[k] // 16, k0[k + 1] // 16)), a("yn", k0[k], k0[k + 1]))
         if last:
             dma("Y", [(ext("yc", (slice(None), slice(None))), a("C", L, BB + S, 1, slice(0, 128, 16)))], 300.0)
             dma("Y", [(ext("yx", (slice(None), slice(0, 1024))), a("X", L, L + 1024))], 700.0)
             dma("S", [(ext("yx", (slice(None), slice(1024, W))), a("X", L + 1024, BB))], 700.0)
             break
         for k in range(3):
-            tt(a("H", S * k, S * k + S), ind(a("C", 0, BB), a("offh", 16 * k, 16 * k + 16)), a("dm"), ALU.mult)
-            scan(a("hs", S * k, S * k + S), a("kp"), a("H", S * k, S * k + S), ALU.mult, ALU.add)
-            ak = a("hs", S * k + 15, S * k + S, 16)
-            if k < 2:
-                ts(a("offh", 16 * k + 16, 16 * k + 32), ak, float(OFF), ALU.add)
-                act(a("a5", 80 * t + k + 2, 80 * t + 80, 5), ak)
+            for c0, c1, e in OPT["hop"][t]:
+                p0, p1 = S * k + 16 * c0, S * k + 16 * c1
+                take(e[k], a("H", p0, p1), ind(a("C", W0, BB), a("offh", 16 * k + c0, 16 * k + c1)))
+                scan(a("hs", p0, p1), a("H", p0, p1), a("Mh", 0, p1 - p0), ALU.max, ALU.add, -BIG)
+                ak = a("hs", p0 + 15, p1, 16); dst = a("a5", 80 * t + 5 * c0 + k + 2, 80 * t + 5 * c1, 5)
+                if k < 2:
+                    ts(a("offh", 16 * k + 16 + c0, 16 * k + 16 + c1), ak, BIG + 16, ALU.add)
+                    act(dst, ak, bias=BIG)
+                else:
+                    ts(dst, ak, BIG, ALU.add)
+        for c0, c1, e in OPT["hop"][t]:
+            p0, p1 = 80 * t + 5 * c0, 80 * t + 5 * c1
+            tt(a("q1", 5 * c0, 5 * c1), a("a5", p0, p1), a("thr", p0, p1), ALU.is_lt)
+            scan(a("q2", 5 * c0, 5 * c1), a("q1", 5 * c0, 5 * c1), a("a5", p0, p1), ALU.mult, ALU.max)
+            ts(a("offq", c0, c1), a("q2", 5 * c0 + 4, 5 * c1, 5), 16.0, ALU.add)
+        for c0, c1, e in OPT["snd"][t]:
+            o = a("sb", S * t + 16 * c0, S * t + 16 * c1); src = ind(a("X", W0, BB + S), a("offq", c0, c1))
+            if e == "S":
+                act(o, src, scale=0.5)
             else:
-                cp(a("a5", 80 * t + 4, 80 * t + 80, 5), ak)
-        tt(a("q1"), a("a5", 80 * t, 80 * t + 80), a("thr", 80 * t, 80 * t + 80), ALU.is_lt)
-        scan(a("q2"), a("q1"), a("a5", 80 * t, 80 * t + 80), ALU.mult, ALU.max)
-        ts(a("offq"), a("q2", 4, 80, 5), float(OFF), ALU.add)
-        ts(a("sb", S * t, S * t + S), ind(a("X", 0, BB + S), a("offq")), 0.5, ALU.mult)
+                ts(o, src, 0.5, ALU.mult)
         add("G", "send", t, [], [a("sb", S * t, S * t + S)], ("c", 300))
         act(a("Z", S * t + 64 * me, S * t + 64 * me + 64), a("sb", S * t + 64 * me, S * t + 64 * me + 64))
-        cp(ind(a("XJ"), a("offo")), a("yn"))
+        cp(ind(a("XJ", 0, BB), a("offo")), a("yn"))
         act(a("XJ", BB, BB + S), a("x2", 0, S))
-        ts(a("dn"), a("left"), 0.0, ALU.max, -1.0, ALU.add)
-        cp(ind(a("D"), a("offo")), a("dn"))
+        ts(a("dn"), a("left"), float(OFF - 1), ALU.max, float(-OFF), ALU.add)
+        cp(ind(a("D", 0, BB), a("offo")), a("dn"))
         act(a("din"), ind(a("lfa"), a("l512")))
         trn(a("dout"), a("din"))
         ts(a("D", BB, BB + S), ind(a("dout"), a("lm")), float(lo), ALU.add, -1.0, ALU.max)
-        parents_row()
         if t == 0:
-            red(a("ar"), a("acc", 1, len(cuts)))
-            red(a("acc", 0, 1), a("acc", 2, len(cuts)))
-            act(a("acc", 8, 9), a("acc", 0, 1), scale=-1.0)
+            tt(a("ar"), a("acc", 0, 1), a("acc", 1, 2), ALU.add)
         else:
-            red(a("ar"), a("acc", 8, 8 + len(cuts)))
+            tt(a("ar"), a("acc", 2, 3), a("acc", 1, 2), ALU.subtract)
         mm([(a("ps7", 0, 1), a("bof"), a("ar"))])
         ts(a("acol", t + 1, t + 2), a("ps7", 0, 1), 0.5, ALU.mult, (1024.0 if t == 0 else 128.0) - 0.375, ALU.add)
     return ops
@@ -457,21 +517,25 @@ def link(ops):
     for j, o in enumerate(ops):
         d = {}
         for acc_w, lst in ((False, o["rd"]), (True, o["wr"])):
-            for name, c0, c1 in lst:
-                bank = name not in _SB
-                for i, w, e0, e1 in hist.get(name, []):
-                    if i == j or not (bank or ((w or acc_w) and e0 < c1 and c0 < e1)):
+            for sp in lst:
+                bank = sp[0] not in _SB
+                for i, w, run in hist.get(sp[0], []):
+                    hit = (w or acc_w) and meet(run, sp[1:])
+                    if i == j or not (bank or hit):
                         continue
                     p = ops[i]
                     same = p["eng"] == o["eng"] and p["kind"] not in ("dma", "send") and o["kind"] not in ("dma", "send")
-                    raw = w and not acc_w and e0 < c1 and c0 < e1
-                    need = (not same) or raw or (WAIT_ALL and o["eng"] != "P" and (w or acc_w) and e0 < c1 and c0 < e1)
+                    if bank and same and o["eng"] != "P" and not hit:
+                        continue
+                    need = (not same) or (hit and w and not acc_w) or (WAIT_ALL and o["eng"] != "P" and hit)
                     if p["kind"] == "recv" and same:
                         need = False
                     d[i] = d.get(i, False) or need
         for acc_w, lst in ((False, o["rd"]), (True, o["wr"])):
-            for name, c0, c1 in lst:
-                hist.setdefault(name, []).append((j, acc_w, c0, c1))
+            for sp in lst:
+                hist.setdefault(sp[0], []).append((j, acc_w, sp[1:]))
+        if "after" in o:
+            d.setdefault(o["after"], False)
         if o["kind"] == "send":
             sends[o["args"]] = j
         if o["kind"] == "recv":
@@ -561,6 +625,79 @@ def schedule(ops, deps, prm):
         for j in range(n):
             for i, l in lag[j]:
                 if key[j] <= key[i]: key[j] = key[i] + 1e-3
+    anc = [0] * n; keep = []
+    for j in range(n):
+        up = 0
+        for i in deps[j]: up |= anc[i]
+        keep.append([i for i in deps[j] if not up >> i & 1])
+        for i in deps[j]: up |= 1 << i
+        anc[j] = up
+    slim = [(g[0], g[1], [[(i, l) for i, l in g[2][j] if i in keep[j]] for j in range(n)]) for g in others]
+
+    def run(seq, p0, old):
+        lastop = {}
+        for k in range(p0 - 1, -1, -1):
+            if eng[seq[k]] not in lastop:
+                lastop[eng[seq[k]]] = seq[k]
+                if len(lastop) == 5: break
+        out = []; tail_seq = seq[p0:]
+        for (d, full, lag), o in zip(slim, old):
+            st = list(o); free = {e: (st[lastop[e]] + d[lastop[e]] if e in lastop else 0.0) for e in "VSPGY"}
+            for j in tail_seq:
+                e = eng[j]; t = free[e]
+                for i, l in lag[j]:
+                    u = st[i] + l
+                    if u > t: t = u
+                st[j] = t; free[e] = t + d[j]
+            out.append(st)
+        return out
+
+    ends = [j for j in range(n) if ops[j]["kind"] == "dma"]
+    soft = OPT["soft"] / n
+    value = lambda sts: sum((max(st[j] + g[1][j] for j in ends) + soft * sum(st)) / v for st, g, v in zip(sts, slim, ref))
+    seq = best[1]; sts = run(seq, 0, [zero] * len(slim)); cur = value(sts); best = (cur, seq); chain = None
+    for it in range(OPT["steps"]):
+        if chain is None:
+            pos = [0] * n; before = [None] * n; lastq = {}
+            for k, j in enumerate(seq):
+                pos[j] = k; before[j] = lastq.get(eng[j]); lastq[eng[j]] = j
+            chain = {}
+        x = (x * 1103515245 + 12345) % 2147483648; v = (x >> 8) % len(slim)
+        if v not in chain:
+            st = sts[v]; d, full, lag = slim[v]; j = max(ends, key=lambda k: st[k] + full[k]); c = []
+            while j is not None:
+                b = before[j]
+                if b is not None and st[b] + d[b] >= st[j] - 1e-6:
+                    if not anc[j] >> b & 1: c.append(j)
+                    j = b
+                else:
+                    j = next((i for i, l in lag[j] if st[i] + l >= st[j] - 1e-6), None)
+            chain[v] = c
+        x = (x * 1103515245 + 12345) % 2147483648
+        j = chain[v][(x >> 8) % len(chain[v])] if chain[v] and x % 8 else (x >> 8) % n
+        i = before[j]
+        if i is None: continue
+        x = (x * 1103515245 + 12345) % 2147483648; far = (0, 0, 0, 1, 2, 4, 8, 16)[(x >> 8) % 8]
+        if x >> 20 & 1:
+            while far and before[i] is not None: i = before[i]; far -= 1
+            mid = seq[pos[i]:pos[j] + 1]
+            go = [k for k in mid if k == j or anc[j] >> k & 1]
+            if go[0] == i: continue
+            new = seq[:pos[i]] + go + [k for k in mid if not (k == j or anc[j] >> k & 1)] + seq[pos[j] + 1:]
+        else:
+            k = pos[j] + 1
+            while far and k < n:
+                if eng[seq[k]] == eng[j]: j = seq[k]; far -= 1
+                k += 1
+            mid = seq[pos[i]:pos[j] + 1]
+            go = [k for k in mid if k == i or anc[k] >> i & 1]
+            if go[-1] == j: continue
+            new = seq[:pos[i]] + [k for k in mid if not (k == i or anc[k] >> i & 1)] + go + seq[pos[j] + 1:]
+        s2 = run(new, pos[i], sts); val = value(s2)
+        x = (x * 1103515245 + 12345) % 2147483648
+        if val <= cur + OPT["heat"] * (1.0 - it / OPT["steps"]) * (x / 2147483648.0) ** 2:
+            seq = new; sts = s2; cur = val; chain = None
+            if cur < best[0]: best = (cur, seq)
     return best[1]
 
 
@@ -641,7 +778,6 @@ def rank_program(g, core, T, topo):
         elif k == "ms": ins = q.memset(ap(x[0]), x[1])
         elif k == "scan": ins = q.tensor_tensor_scan(ap(x[0]), ap(x[1]), ap(x[2]), x[3], x[4], x[5])
         elif k == "trn": ins = q.transpose(ap(x[0]), ap(x[1]))
-        elif k == "red": ins = q.tensor_reduce(ap(x[0]), ap(x[1]), AX.X, ALU.add)
         elif k == "act": ins = q.activation(ap(x[0]), ap(x[1]), x[2], bias=ap(x[3]), scale=ap(x[4]), accum_out=ap(x[5]))
         elif k == "mm":
             for n, (po, l, r) in enumerate(x[0]):

@@ -1,3 +1,4 @@
+import math
 from concourse.bass import DstId, RemoteDMATransfer
 from concourse.mybir import AluOpType as ALU, ActivationFunctionType as AF, AxisListType as AX
 
@@ -5,29 +6,33 @@ W, S, R, CAP, ST, NR = 2048, 256, 3, 192, 467, 4
 OFF = 2 * CAP + 16
 W0 = OFF - 16
 NW = OFF + W + R * S
+NA = S - S // NR
 BIG = 8192.0
+KD = 65536.0
 f32, b16, i32, u16 = "float32", "bfloat16", "int32", "uint16"
 
 _SB = dict(
     X=(NW, b16), XJ=(NW, b16), C=(NW, f32), D=(NW, i32), CD=(16 + W + 2 * S, b16), cm=(768, b16),
-    cin=(128, i32), cinf=(128, f32), blk=(128, i32), blkf=(128, f32),
-    ag=(32, i32), agf=(32, f32), agt=(32, f32), thr=(160, f32), a5=(160, f32), ahf=(16, f32),
-    ones=(160, b16), bow=(144, b16), bow0=(144, b16), z1=(144, b16), zk=(144, b16), iw=(160, b16), ni=(128, b16), ni16=(128, b16), ih=(128, b16),
-    bom=(128, b16), bof=(128, f32), tri=(128, b16), iwe=(160, f32), iwo=(160, f32), nkr=(128, b16),
-    pi=(4, i32), pj=(4, i32), pc=(12, f32), j16=(256, f32), dm=(256, f32), kp=(256, b16), coef=(256, f32), kr=(192, b16),
-    Mh=(256, f32), idf=(128, f32), mk=(16, b16), wv=(16, b16), kc=(36, f32), ky=(12, f32),
-    pw0=(128, f32), pw=(128, f32), c16=(16, f32), kw=(12, f32), l16=(16, u16), l15=(12, u16), lc=(16, u16), lp=(8, u16), h0=(32, f32), l512=(32, u16),
-    U=(2048, b16), c16b=(16, f32), lm=(16, u16), bv=(512, b16), bk=(128, b16), onesf=(256, f32),
-    xi=(256, i32), x2=(512, b16), wh=(128, i32), whm=(128, i32), who=(128, u16),
-    g2=(1024, b16), sg=(128, b16), acc=(16, f32), ar=(1, f32), acol=(3, f32),
-    offp=(128, u16), pg=(2048, b16), F=(144, b16), Fp=(144, b16), Q=(144, b16), vb=(128, b16), M=(12 * 128, b16),
+    blk=(160, i32), blkf=(160, f32), bti=(288, i32), bt=(288, f32),
+    ag=(32, i32), agf=(32, f32), agt=(32, f32), agr=(32, f32), thr=(160, f32), ahf=(16, f32),
+    ones=(160, b16), bow=(128, b16), bow0=(128, b16), gi=(9, b16), z1=(144, b16), zk=(144, b16), iw=(160, b16),
+    ni=(128, b16), ni32=(128, b16), i32=(128, b16), ih=(128, b16), rs=(9, f32),
+    bom=(128, b16), bof=(128, f32), tri=(128, b16), tri2=(128, b16), iwe=(160, f32), iwo=(160, f32), nkr=(128, b16),
+    pi=(4, i32), pj=(8, i32), pc=(18, f32), j16=(192, f32), dm=(256, f32), kp=(192, b16), coef=(256, f32), cfm=(16, f32), kr=(192, b16),
+    Mh=(192, f32), idf=(128, f32), mk=(16, b16), wv=(16, b16), kc=(36, f32), ky=(12, f32), c32=(32, f32), kq=(16, f32),
+    pw0=(128, f32), pw=(128, f32), kw=(16, f32), l16=(16, u16), l12=(12, f32), l15=(12, u16), lc=(16, u16), lk=(16, u16),
+    lq=(16, u16), lr=(2, u16), ln=(2, u16), lo1=(2, u16), lid=(16, u16),
+    lm=(16, u16), bv=(512, b16), bk=(256, b16), onesf=(256, f32), U=(2048, b16),
+    xi=(256, i32), x2=(256, b16), xa=(512, b16), xb=(256, b16), wh=(128, i32), whm=(128, i32), who=(128, u16),
+    g2=(1024, b16), sg=(144, b16), junk=(128, b16), acc=(16, f32), ar=(1, f32), acol=(3, f32),
+    offp=(128, u16), pg=(2048, b16), F=(144, b16), Fp=(144, b16), Q=(144, b16), Lf=(144, b16), vb=(128, b16), M=(12 * 128, b16),
     cu=(12, u16), uf=(12, f32), uu=(12, f32), cmp2=(192, b16),
     offo=(12, u16), offw=(192, u16), dp=(192, f32), y=(192, b16),
     G=(3072, b16), cmpo=(3072, b16), left=(192, f32), lt=(192, f32), ls=(192, f32), bb=(192, f32), br=(192, f32),
     w1=(12, f32), offx=(12, u16), xh=(192, f32), yn=(192, i32), dn=(192, i32),
-    asq=(16, f32), au=(16, f32), ah=(16, i32), at=(256, f32), ati=(256, i32), atm=(256, i32), offa=(256, u16),
-    cmpa=(4096, b16), lfa=(256, f32), tr=(256, f32), a1=(16, f32), E=(256, f32), din=(512, f32), dout=(512, f32),
-    offh=(48, u16), H=(768, f32), hs=(768, f32), q1=(80, f32), q2=(80, f32), offq=(16, u16),
+    tq=(128, f32), tu=(128, f32), ti=(128, i32), th=(128, f32), cu0=(256, f32), cu1=(256, f32), asq=(16, f32), au=(16, f32), ah=(16, i32), at=(256, f32), ati=(256, i32), atm=(256, i32), offa=(256, u16),
+    cmpa=(4096, b16), lfa=(256, f32), tr=(256, f32), a1=(16, f32), E=(256, f32), din=(288, f32), dout=(544, f32),
+    offh=(48, u16), H=(768, f32), hs=(1600, f32), q1=(80, f32), q2=(80, f32), offq=(16, u16),
     sb=(512, b16), Z=(512, b16), aw=(128, f32), awt=(128, f32),
 )
 _AT = {}
@@ -45,21 +50,38 @@ for _k in range(8):
 NDMA = 40
 SEMAPHORES = ["cV", "cS", "cP", "cG", "sent", "arr0", "arr1"] + ["d%d" % k for k in range(NDMA)]
 
-PRM = dict(cyc=0.9, pe=0.46, g=1.56, sc=3.8, same=100.0, cross=150.0, dma=2300.0, comm=4500.0)
-VARIANTS = [{}, dict(cyc=1.04, pe=0.52, same=60.0, cross=110.0, dma=2000.0, comm=3500.0), dict(cyc=0.83, pe=0.42, same=150.0, cross=200.0),
-            dict(cyc=0.83, pe=0.42, same=60.0, cross=110.0, dma=3000.0, comm=6500.0), dict(g=1.1, sc=2.0), dict(cyc=1.2, pe=0.6, g=2.0, sc=5.5)]
+PRM = dict(cyc=0.92, pe=0.46, g=1.56, sc=3.8, same=150.0, cross=160.0, dma=2000.0, comm=2400.0, pool=1.3)
+VARIANTS = [{}, dict(cyc=1.0, pe=0.5, same=100.0, cross=150.0, dma=1500.0, pool=1.0),
+            dict(cyc=0.85, pe=0.42, same=180.0, cross=190.0, dma=2500.0, comm=3800.0, pool=1.6), dict(g=1.2, sc=2.5), dict(cyc=1.2, pe=0.6, g=2.0, sc=5.5)]
+
+
+def _pieces(text):
+    return tuple((e, int(w)) for e, w in text.split())
+
+
 OPT = dict(
-    x_parts=((0, 32), (32, 64), (64, 96), (96, 128)), s_xi=0,
-    die=[((0, 32, "V"), (32, 64, "S"), (64, 96, "V"), (96, 112, "S"), (112, 128, "V"))]
-    + [((0, 32, "V"), (96, 128, "S"), (32, 64, "V"), (80, 96, "S"), (64, 80, "V"))] * 2,
-    par=[((0, 4, "S"), (4, 8, "S"), (8, 12, "S"), (12, 14, "S"), (14, 16, "S"))] * 3,
-    xj_s=[()] * 3, e_s=[1] * 3, c_s=[0] * 3, f_s=[0] * 3, cnt_s=[(8, 9, 10, 11)] * 3,
-    arr=[tuple((e, int(w)) for e, w in "S2 S2 V1 V1 V2 V1 V1 V2 V2 V1 S1".split())] * 3,
-    og=[((0, 64, "S"), (64, 128, "S"), (128, 160, "S"), (160, 192, "S"))] * 3,
-    oc=[((0, 64, "V", 8, 1), (64, 128, "V", 8, 5), (128, 192, "S", (2, 3), 1))] * 3, bb_s=[(0, 64)] * 3,
-    ox=[((0, 192, (0, 64, 128, 192)),)] * 2 + [((0, 128, (0, 128)), (128, 192, (128, 192)))],
-    hop=[((0, 8, "SSS"), (8, 16, "SSS"))] * 2, snd=[((0, 8, "S"), (8, 16, "S"))] * 2, gcopy=1,
-    seed=7, jit=4000.0, moves=8, iters=1000, steps=12000, heat=0.004, soft=0.0)
+    x_parts=((0, 32), (32, 64), (64, 96), (96, 128)), x2_s=1, one_m=0, late=0, both=[0] * 3, first=[()] * 3, t_e=["SS"] * 3, cut=[99] * 3, bkl=[(6, 7, 6, 7)] * 3, na=192, xj_s=[()] * 3, sg2=[7, 0, 0], bka=[(2, 3, 6, 7), (1, 2, 6, 7), (1, 4, 6, 7)], bkb=[(2, 3, 6, 7), (7, 6, 7, 7), (4, 7, 6, 6)],
+    die=[((0, 32, "V"), (32, 64, "V"), (64, 96, "V"), (96, 128, "V"))] * 2 + [((0, 32, "V"), (32, 64, "V"), (64, 104, "V"), (104, 128, "S"))],
+    par=[((0, 32, "S"), (32, 64, "S"), (64, 96, "S"), (96, 128, "S"))] + [((0, 16, "S"), (16, 48, "S"), (48, 96, "S"), (96, 128, "S"))] * 2,
+    sgp=[((0, 64), (64, 128))] * 3, parw=[(), (), (64,)],
+    sg_last=[0, 1, 0], dp_s=[0] * 3, e_s=[2, 2, 2], c_s=[1, 1, 1], cb_s=[1, 1, 1], f_s=[1, 1, 0], cnt_s=[(), (6, 7, 8, 9, 10, 11), (10, 11)], y_e=["S"] * 3,
+    arr=[_pieces("S2 S2 S2 V2 V2 V2 V2 V2"), _pieces("V2 V2 S2 S2 V2 V2 V2 V2"), _pieces("S2 S2 V2 V2 V2 V2 V2 V2")], cha=[(8, 16)] * 3,
+    brr=[_pieces("S8 S8")] * 3,
+    og=[((0, 32, "V"), (32, 64, "S"), (64, 128, "S"), (128, 192, "S")), ((0, 32, "S"), (32, 64, "V"), (64, 128, "S"), (128, 160, "S"), (160, 192, "S")),
+        ((0, 64, "S"), (64, 128, "S"), (128, 160, "S"), (160, 192, "V"))],
+    oc=[((0, 64, "V", 8, 1), (64, 128, "S", (2, 3), 5), (128, 192, "V", 8, 1))] + [((0, 64, "V", 4, 1), (64, 128, "V", 4, 5), (128, 192, "S", (2, 3), 1))] * 2,
+    bb_s=[(), (0,), (0, 128)],
+    ox=[((0, 192, (0, 64, 128, 192)),), ((0, 192, (0, 96, 192)),), ((0, 192, (0, 192)),)],
+    hop=[((0, 6, "SSS"), (6, 12, "SSS"), (12, 16, "SSS")), ((0, 6, "SVS"), (6, 12, "SSS"), (12, 16, "SSS"))],
+    snd=[((0, 6, "S"), (6, 12, "V"), (12, 16, "S")), ((0, 6, "S"), (6, 12, "V"), (12, 16, "S"))],
+    jit=1500.0, moves=4, tries=2, iters=100, steps=60000, polish=8000, heat=0.006)
+for _t, _d in enumerate((
+        dict(bb_s=(0, 128), sg_last=1, sgp=((0, 96), (96, 128))),
+        dict(),
+        dict(arr=_pieces("S2 V1 V1 V1 V1 V2 V2 V2 S2 S2"), cut=5, og=((0, 32, "V"), (32, 64, "S"), (64, 96, "V"), (96, 128, "S"), (128, 192, "S")),
+             oc=((0, 64, "V", 4, 1), (64, 128, "S", (2, 3), 5), (128, 192, "V", 4, 1)), c_s=0, bkb=(6, 7, 6, 7), cha=(16,), brr=_pieces("V4 V4 S8"), f_s=1))):
+    for _k, _v in _d.items():
+        OPT[_k][_t] = _v
 WAIT_ALL = True
 
 
@@ -92,7 +114,7 @@ def spans(d):
 
 
 def meet(x, y):
-    if x[2] == y[2] and (x[0] - y[0]) % x[2]:
+    if (x[0] - y[0]) % math.gcd(x[2], y[2]):
         return False
     return x[0] < y[1] and y[0] < x[1]
 
@@ -103,6 +125,18 @@ def wide(d):
 
 def psum(d):
     return d[0] == "ap" and d[1] not in _SB
+
+
+def transfers(o, me):
+    t = o["args"]; out = []
+    for q in range(NR - 1):
+        b = (q + me + 1) % NR; z = S * t + 64 * ((me - b - 1) % NR)
+        out.append((b, a("sb", S * t + 64 * q, S * t + 64 * q + 64), a("Z", z, z + 64)))
+    return out
+
+
+def recv_needs(o, me):
+    return [(b, o["args"]) for b in range(NR) if b != me]
 
 
 def build(me):
@@ -156,28 +190,26 @@ def build(me):
 
     def step(out, x, at, sign=1.0):
         act(out, x, AF.Sigmoid, bias=-256.0 * sign * at, scale=256.0 * sign)
+        if len(table) > 1:
+            ops[-1]["after"] = table[1]
+        else:
+            table.append(len(ops) - 1)
 
     def mm(lst, start=True, stop=True):
-        cyc = sum(max(64, n_of(r)) * (4 if wide(r) else 1) for o, l, r in lst)
+        cyc = sum(max(min(64, n_of(l)), n_of(r)) * (4 if wide(r) else 1) for o, l, r in lst)
         add("P", "mm", (lst, start, stop), [o for o, l, r in lst], [l for o, l, r in lst] + [r for o, l, r in lst], ("pe", cyc))
 
     def iota(out, pat, base, cm=0):
         add("G", "iota", (out, pat, base, cm), [out], [], ("c", 130 + 2 * n_of(out)))
 
-    def sel(out, x, pat, op, base, cm):
-        add("G", "sel", (out, x, pat, op, base, cm), [out], [x], ("c", 170 + 2 * n_of(out)))
+    def sel(out, x, pat, op, base, cm, other=0.0):
+        add("G", "sel", (out, x, pat, op, base, cm, other), [out], [x], ("c", 170 + 2 * n_of(out)))
 
     def move(out, x):
-        if OPT["gcopy"]:
-            sel(out, x, [[0, n_of(x)]], ALU.is_ge, 0, 0)
-        else:
-            act(out, x)
+        sel(out, x, [[0, n_of(x)]], ALU.is_ge, 0, 0)
 
     def fill(out, v):
-        if OPT["gcopy"]:
-            iota(out, [[0, n_of(out)]], int(v))
-        else:
-            ms(out, v)
+        iota(out, [[0, n_of(out)]], int(v))
 
     def take(e, out, src):
         if e == "S":
@@ -192,165 +224,276 @@ def build(me):
         mm(list(first) + [(out, a(z, 15 - r, 143 - r), a(src, c0 + r, c0 + 16 * n, 16)) for r in range(16)])
 
     I = a("iw", 16, 144); BOW = a("bow", 0, 128)
-    pm, pm2, par, npar, p32, pm16, pf, p8, pq = [a("pc", k, k + 1) for k in range(9)]
+    pm, pr, pn, pm_, p32, p3, par, p8, pf, pm2, npar, pq, pm12, pm4, p16, pa, pb, pd = [a("pc", k, k + 1) for k in range(18)]
+    s4 = 4 * (me + 1); na = OPT["na"]
+    nat = [(q + me + 1) % NR for q in range(NR)]
 
     parts = OPT["x_parts"]
     for k, (c0, c1) in enumerate(parts):
-        dma("Y", [(a("X", OFF + 16 * c0, OFF + 16 * c1), ext("x0", (slice(None), slice(16 * c0, 16 * c1))))], 11.0 * c1 + (150.0 if k else 0.0))
+        dma("Y", [(a("X", OFF + 16 * c0, OFF + 16 * c1), ext("x0", (slice(None), slice(16 * c0, 16 * c1))))], 11.0 * c1 + (300.0 if k else 0.0))
         if k == 0:
             dma("Y", [(a("cm", 0, S), ext("come", (slice(None), slice(0, S))))], 11.0 * c1 + 150.0)
-    dma("Y", [(a("cin", 16 * b, 16 * b + 16), ext("cd0", (slice(None), slice(256 * b, 256 * b + 256)))) for b in range(8)], 1700.0)
-    dma("Y", [(a("blk"), ext("cd0", (slice(None), slice(None))))], 1700.0)
+            dma("Y", [(a("blk", 16, 144), ext("cd0", (slice(None), slice(None))))], 11.0 * c1 + 300.0)
     dma("Y", [(a("D", OFF + 1024, OFF + W), ext("dl0", (slice(None), slice(None))))], 3000.0)
     dma("Y", [(a("cm", S, 3 * S), ext("come", (slice(None), slice(S, 3 * S))))], 3300.0)
     dma("Y", [(a("ag", 16 * h, 16 * h + 16), ext("age", (slice(h, 8, 2), slice(None)))) for h in range(2)], 3300.0)
     for k in range(1, len(ops)):
         ops[k]["after"] = k - 1
-    iota(a("ones"), [[0, 160]], 1)
-    sel(a("bow0"), a("ones", 0, 144), [[-16, 9], [0, 16]], ALU.is_ge, 0, 1)
-    sel(a("bow"), a("bow0"), [[16, 9], [0, 16]], ALU.is_ge, 15, -1)
-    sel(a("z1"), a("bow"), [[0, 9], [1, 16]], ALU.is_equal, -15, 0)
-    iota(a("pi"), [[0, 4]], 0, 1)
+    ms(a("bv"), 21 * KD); ms(a("ones"), 1.0); ms(a("z1"), 0.0); ms(a("bk", 0, 128 if all(len(c) > 1 and c[0] * na <= 2048 for c in OPT["cha"]) else 256), -86016.0)
+    step(a("onesf"), a("bv", 0, S), 0.5)
+    iota(a("pi"), [[16 - s4, 2], [s4, 2]], 0, 1)
+    sel(a("gi"), a("ones", 0, 9), [[-16, 9]], ALU.is_ge, 0, 1)
+    sel(a("z1", 15, 144, 16), a("gi"), [[16, 9]], ALU.is_ge, 15, -1)
+    sel(a("bow0"), a("ones", 0, 128), [[-16, 8], [0, 16]], ALU.is_ge, 0, 1)
+    sel(a("bow"), a("bow0"), [[16, 8], [0, 16]], ALU.is_ge, 15, -1)
     iota(a("pw0"), [[0, 8], [32, 16]], 0)
     sel(a("iw"), a("ones"), [[-1, 160]], ALU.is_equal, 16, 1)
-    iota(a("j16"), [[0, 16], [1, 16]], 0)
-    iota(a("coef"), [[61, 16], [0, 16]], 7)
-    iota(a("c16"), [[16, 16]], 0)
+    iota(a("j16"), [[0, 12], [1, 16]], 0)
+    if not all(OPT["c_s"]) or 2 in OPT["c_s"]:
+        iota(a("coef", 0, na), [[61, 16], [0, na // 16]], 7)
+    if na < S and (not all(OPT["cb_s"]) or 2 in OPT["c_s"]):
+        iota(a("coef", NA, S), [[61, 16], [0, 4]], 7)
+    if 2 in OPT["c_s"]:
+        for u, v, k0 in ((0, na, 0), (na, S, 12))[:1 + (na < S)]:
+            for dst, src in (("cu1", "coef"), ("cu0", "onesf")):
+                sel(a(dst, u, v, 1, slice(0, 16)), a(src, u, v, 1, slice(0, 16)), [[0, 16], [1, (v - u) // 16]], ALU.is_equal, k0, -1)
+    iota(a("c32"), [[0, 2], [32, 16]], 0)
     sel(a("tri"), BOW, [[1, 128]], ALU.is_ge, 0, -1)
+    sel(a("tri2"), a("tri"), [[1, 128]], ALU.not_equal, 0, -1, 4096.0)
     iota(a("kr"), [[1, 192]], 0)
-    iota(a("h0"), [[1, 16], [0, 2]], 0)
-    ts(a("pj", 0, 1), a("pi", 0, 1), 15, ALU.bitwise_and)
-    ts(a("pj", 1, 2), a("pi", 0, 1), 31, ALU.bitwise_and)
-    cp(pm, a("pj", 0, 1))
-    cp(p32, a("pj", 1, 2))
+    iota(a("rs", 0, 3), [[ST % 16, 3]], ST % 16)
+    iota(a("rs", 3, 6), [[-(ST // 16), 3]], 127 - ST // 16)
+    n4 = (OFF + 1024) // 4
+    ms(a("D", 0, n4), -1)
+    dma("Y", [(a("D", n4 * k, n4 * k + n4), a("D", 0, n4)) for k in range(1, 4)], 3500.0)
+    ts(a("pj", 0, 3), a("pi", 0, 3), 15, ALU.bitwise_and)
+    ts(a("pj", 4, 5), a("pi", 0, 1), 31, ALU.bitwise_and)
+    ts(a("pj", 5, 6), a("pi", 0, 1), 3, ALU.bitwise_and)
+    ts(a("pj", 6, 7), a("pi", 0, 1), 4, ALU.arith_shift_right, 1, ALU.bitwise_and)
+    ts(a("pj", 7, 8), a("pi", 0, 1), 3, ALU.arith_shift_right, 1, ALU.bitwise_and)
+    ts(a("pj", 3, 4), a("pi", 0, 1), 1, ALU.bitwise_and)
+    cp(a("pc", 0, 8), a("pj"))
     cp(pf, a("pi", 0, 1))
-    ts(pm2, a("pj", 0, 1), 2.0, ALU.mult, -0.3125, ALU.add)
-    ts(pm16, a("pj", 0, 1), 16.0, ALU.mult)
-    ts(par, a("pj", 1, 2), 16.0, ALU.is_ge)
-    ts(npar, a("pj", 1, 2), 16.0, ALU.is_lt)
-    ts(p8, a("pj", 0, 1), 8.0, ALU.is_ge, -127.0, ALU.mult)
-    tt(pq, p8, pm16, ALU.add)
-    ts(a("pw"), a("pw0"), pm2, ALU.add)
-    ms(a("bv"), 5376.0); ms(a("bk"), -86016.0); ms(a("onesf"), 1.0)
-    ms(a("X", 0, OFF), 0.0); ms(a("XJ", W0, OFF), -1.0); ms(a("C", W0, OFF), -1.0); ms(a("D", 0, OFF + 1024), -1); ms(a("CD", 0, 16), 0.0)
-    ms(a("Fp", 0, 1), 0.0); ms(a("acol", 0, 1), -0.375); ms(a("wv", 0, 6, 2), 1.0)
-    step(a("kp"), a("j16"), 0.5)
+    ms(a("blk", 0, 16), 0); ms(a("blk", 144, 160), 0); ms(a("din", 0, 16), 0.0); ms(a("din", 272, 288), 0.0)
+    act(pm2, pm, scale=2.0, bias=2.0 * (S - 16 * s4) - 0.3125)
+    act(a("pw"), a("pw0"), bias=pm2)
+    ts(p16, pm_, par, ALU.not_equal, 9.0, ALU.mult)
+    ts(pa, p16, pm, ALU.add, 16.0, ALU.mult)
+    act(pq, p8, scale=-127.0, bias=pa)
+    act(npar, par, scale=-1.0, bias=1.0)
+    act(pb, par, scale=272.0, bias=pm)
+    act(pd, npar, scale=272.0, bias=pm)
+    act(pm12, pm, scale=na / 16.0)
+    if na < S:
+        act(pm4, pm, scale=4.0, bias=180.0)
+    ts(a("lq", 0, 8), a("c32", 0, 8), 1.0 / 16, ALU.mult, pq, ALU.add)
+    ts(a("lq", 8, 15), a("c32", 1, 8), 1.0 / 16, ALU.mult, pq, ALU.add)
+    ms(a("X", 0, OFF), 0.0); ms(a("XJ", W0, OFF), -1.0); ms(a("C", W0, OFF), -1.0); ms(a("CD", 0, 16), 0.0)
+    ms(a("Fp", 0, 1), 0.0); ms(a("acol", 0, 1), -0.375); ms(a("wv", 0, 6, 2), 1.0); ms(a("sg", 128, 144), -1.0); ms(a("thr", 0, 160, 5), 0.0)
+    nk = max(j1 - j0 for t in range(R) for j0, j1, e, by, bank in OPT["oc"][t])
+    ts(a("kp", 0, nk), a("j16", 0, nk), 0.5, ALU.is_lt, -16 * BIG, ALU.mult)
     act(a("ni"), I, scale=-1.0)
-    act(a("ni16"), I, scale=-16.0)
+    act(a("ni32"), I, scale=-32.0)
+    act(a("i32"), I, scale=32.0)
     act(a("ih"), I, scale=0.5)
-    act(a("bom"), BOW, scale=-512.0)
+    act(a("bom"), BOW, scale=-2 * KD)
     act(a("zk"), a("z1"), scale=8192.0)
     act(a("nkr"), a("j16", 0, 128), scale=-1.0)
     act(a("bof"), BOW)
     act(a("iwe"), a("iw"), scale=npar)
     act(a("iwo"), a("iw"), scale=par)
-    ts(a("dm"), a("j16"), pm, ALU.is_equal)
-    if any(OPT["xj_s"]):
-        ts(a("c16b"), a("dm", 0, 16), 0.5, ALU.mult)
-        for r in range(16):
-            act(a("U", 128 * r, 128 * r + 128), a("bom"), scale=a("c16b", r, r + 1))
-    ts(a("H", 0, S), a("j16"), pm, ALU.is_lt, -BIG, ALU.mult)
-    act(a("H", S, 2 * S), a("dm"), scale=BIG)
-    tt(a("Mh"), a("H", 0, S), a("H", S, 2 * S), ALU.add)
-    ts(a("Mh", 15, S, 16), a("Mh", 15, S, 16), -2 * BIG, ALU.add)
+    nh = 16 * max(c1 - c0 for c0, c1, e in OPT["hop"][0] + OPT["hop"][1])
+    nd = nh if all(OPT["e_s"][:2]) else S
+    ts(a("dm", 0, min(nd, NA)), a("j16", 0, min(nd, NA)), pm, ALU.is_equal)
+    if nd > NA:
+        move(a("dm", NA, S), a("dm", 0, S - NA))
+    ts(a("H", 0, nh), a("j16", 0, nh), pm, ALU.is_lt, BIG, ALU.mult)
+    act(a("H", S, S + nh), a("dm", 0, nh), scale=-BIG)
+    tt(a("Mh", 0, nh), a("H", 0, nh), a("H", S, S + nh), ALU.add)
+    act(a("Mh", 15, nh, 16), a("Mh", 15, nh, 16), bias=2 * BIG)
     act(a("idf"), I)
-    ts(a("kw"), a("c16", 0, 12), pm, ALU.add)
-    ts(a("ky"), a("kw"), float(CAP), ALU.add)
-    ts(a("l16"), a("c16"), 0.0, ALU.mult, pm, ALU.add)
-    ts(a("l15"), a("c16", 0, 12), 15.0, ALU.add)
-    ts(a("lc"), a("c16"), 1.0 / 16, ALU.mult)
-    ts(a("lp"), a("c16", 0, 8), 1.0 / 8, ALU.mult, pq, ALU.add)
-    ts(a("l512"), a("h0"), pm16, ALU.add)
-    ts(a("lm"), a("c16"), 2.0, ALU.mult, p32, ALU.add)
+    act(a("kw"), a("c32", 0, 16), scale=0.5, bias=pm)
+    act(a("ky"), a("kw", 0, 12), bias=float(CAP - OFF))
+    if na == S and not all(OPT["c_s"]):
+        ts(a("l16"), a("X", 0, 16), pm, ALU.add)
+    elif not all(OPT["c_s"]):
+        iota(a("l12"), [[0, 4], [4, 3]], 0)
+        act(a("uf"), a("l12"), bias=pm)
+        ts(a("uu"), a("uf"), 12.0, ALU.is_ge, -12.0, ALU.mult)
+        tt(a("l12"), a("uf"), a("uu"), ALU.add)
+        cp(a("l16", 0, 12), a("l12"))
+    if na < S and not all(OPT["cb_s"]):
+        ts(a("l16", 12, 16), a("bv", 0, 4), 4.0, ALU.min, p3, ALU.add)
+    if any(OPT["c_s"]) or any(OPT["cb_s"]):
+        iota(a("cfm"), [[61, 16]], 7)
+    if OPT["x2_s"] == 1:
+        cp(a("lid"), a("kw"))
+    ts(a("l15"), a("c32", 0, 12), 0.5, ALU.mult, 15.0, ALU.add)
+    if not all(OPT["e_s"][:2]):
+        ts(a("lc"), a("c32", 16 - s4, 32 - s4), 1.0 / 32, ALU.mult)
+    ts(a("lk", 0, na // 16), a("c32", 0, na // 16), 1.0 / 32, ALU.mult, pm12, ALU.add)
+    if na < S:
+        ts(a("lk", 12, 16), a("c32", 12, 16), 1.0 / 32, ALU.mult, pm4, ALU.add)
+    if any(OPT["xj_s"]):
+        for r in range(16):
+            ts(a("U", 128 * r, 128 * r + 128), a("bom"), a("dm", r, r + 1), ALU.mult, 0.5, ALU.mult)
+    ts(a("lm", 0, 16, 2), a("c32", 16 - s4, 32 - s4, 2), 0.5, ALU.mult, pb, ALU.add)
+    ts(a("lm", 1, 16, 2), a("c32", 17 - s4, 32 - s4, 2), 0.5, ALU.mult, pd, ALU.add)
+    ts(a("lr"), a("c32", 0, 2), 0.5, ALU.mult, pr, ALU.add)
+    ts(a("ln"), a("X", 0, 2), pn, ALU.add)
+    cp(a("lo1", 0, 1), p32)
+    act(a("kq"), a("c32", s4, s4 + 16), scale=0.5, bias=pm)
+    ts(a("mk", 0, 6, 2), a("rs", 0, 3), pm, ALU.is_gt, -64.0, ALU.mult)
+    ts(a("mk", 1, 6, 2), a("rs", 0, 3), pm, ALU.is_le, -64.0, ALU.mult)
+    ts(a("rs", 6, 9), a("rs", 3, 6), pf, ALU.is_equal, float(-W), ALU.mult)
+    act(a("wv", 1, 6, 2), a("rs", 6, 9), bias=16.0)
     for t in range(R):
-        rs = float((ST * (t + 1)) % 16); cs = (ST * (t + 1)) // 16
-        ts(a("mk", 2 * t, 2 * t + 1), pm, rs, ALU.is_lt, -64.0, ALU.mult)
-        ts(a("mk", 2 * t + 1, 2 * t + 2), pm, rs, ALU.is_ge, -64.0, ALU.mult)
-        ts(a("pc", 9 + t, 10 + t), pf, float(127 - cs), ALU.is_equal, float(-W), ALU.mult)
-        ts(a("wv", 2 * t + 1, 2 * t + 2), a("pc", 9 + t, 10 + t), 16.0, ALU.add)
-        ts(a("kc", 12 * t, 12 * t + 12), a("kw"), float(-16 - OFF - S * t - 16 * cs), ALU.add)
-    for t in range(R - 1):
-        ts(a("a5", 80 * t, 80 * t + 80, 5), a("c16"), pm, ALU.add, float(W + S * t), ALU.add)
-    ms(a("thr"), 0.0)
+        act(a("kc", 12 * t, 12 * t + 12), a("kw", 0, 12), bias=float(-16 - OFF - S * t - 16 * ((ST * (t + 1)) // 16)))
     cp(a("blkf"), a("blk"))
-    dma("Y", [(a("C", OFF, OFF + W, 1, slice(m, 128, 16)), a("blkf")) for m in range(16)], 4000.0)
+    dma("Y", [(a("C", OFF, OFF + W, 1, slice(0, 128, 16)), a("blkf", 16, 144))], 1500.0)
+    dma("Y", [(a("C", OFF, OFF + W, 1, slice(m, 128, 16)), a("C", OFF, OFF + W, 1, slice(0, 128, 16))) for m in range(1, 16)], 7000.0)
     cp(a("agf"), a("ag"))
     trn(a("agt"), a("agf"))
+    act(a("agr"), ind(a("agt"), a("lr")))
     for t in range(R - 1):
         for k in range(1, 5):
-            act(a("thr", 80 * t + k, 80 * t + 80, 5), a("agt", 16 * t, 16 * t + 16), bias=float(W + S * t + S - 1), scale=-1.0)
+            act(a("thr", 80 * t + k, 80 * t + 80, 5), a("agr", 16 * t, 16 * t + 16), bias=BIG + W + S * t + S - 1, scale=-1.0)
+    trn(a("bti", 0, 128), a("blk", 16, 144))
+    trn(a("bti", 128, 288), a("blk"))
+    ts(a("offp"), ind(a("bti"), a("lq", 0, 8)), 16.0, ALU.add)
+
+    for o in ops[table[1] + 1:]:
+        if o["eng"] == "S": o["after"] = table[1]
 
     for t in range(R):
         lo = S * t; B = W + lo; L = OFF + lo; BB = OFF + B; K0 = 16 + lo
         last = t == R - 1
         cs = (ST * (t + 1)) // 16; n1 = 128 - cs
-        old = "X" if t == 0 else "XJ"
+
+        def turned(c0, c1, cs=cs):
+            runs = [(max(c0, cs), c1, max(c0, cs) - cs), (c0, min(c1, cs + 1), 128 - cs + c0)]
+            return [x for x in runs if x[0] < x[1]]
+
         for k, (c0, c1) in enumerate(parts if t == 0 else ((0, 128),)):
-            pn = "ps%d" % (4 + k % 2)
-            wrap(a(pn, 0, c1 - c0), "z1", "X", L + 16 * c0, c1 - c0)
-            act(a(pn, 128, 128 + c1 - c0), a(pn, 0, c1 - c0), AF.Square, scale=0.25)
-            tt(a("wh", c0, c1), a(pn, 128, 128 + c1 - c0), a("pw", c0, c1), ALU.add)
+            pn_ = "ps%d" % (4 + k % 2)
+            wrap(a(pn_, 0, c1 - c0), "z1", "X", L + 16 * c0, c1 - c0)
+            act(a(pn_, 128, 128 + c1 - c0), a(pn_, 0, c1 - c0), AF.Square, scale=0.25)
+            tt(a("wh", c0, c1), a(pn_, 128, 128 + c1 - c0), a("pw", c0, c1), ALU.add)
             ts(a("whm", c0, c1), a("wh", c0, c1), 1, ALU.arith_shift_right, 255, ALU.bitwise_and)
             cp(a("who", c0, c1), a("whm", c0, c1))
         if t > 0:
-            act(a("ps4", S, 2 * S), a("cm", S * t, S * t + S), bias=-0.25, scale=0.5)
+            for q in range(NR):
+                act(a("ps6", 64 * q, 64 * q + 64), a("cm", S * t + 64 * nat[q], S * t + 64 * nat[q] + 64), bias=-0.25, scale=0.5)
             fill(a("XJ", L - S, L), -1.0)
             fill(a("CD", K0 - S, K0), 1.0)
-        ts(a("offp"), ind(a("cin" if t == 0 else "cinf"), a("lp")), 16.0, ALU.add)
         for q in range(4):
-            mm([(a("ps%d" % q), I, a(old, L + 512 * q, L + 512 * q + 512) if q in OPT["xj_s"][t] else a("bv"))], True, False)
-        ds = [(c0, c1) for c0, c1, e in OPT["die"][t] if e == "S"]
-        for k, (c0, c1) in enumerate(ds[:2]):
-            mm([(a("ps%d" % (6 + k), 0, 16 * (c1 - c0)), a("ni"), a(old, L + 16 * c0, L + 16 * c1))], True, False)
+            n = 512 if q < 3 else 512 - S
+            if q in OPT["xj_s"][t]:
+                mm([(a("ps%d" % q), I, a("X", L + 512 * q, L + 512 * q + 512))], True, False)
+            else:
+                mm([(a("ps%d" % q), I, a("bv"))] + [(a("ps%d" % q, 0, n), a("i32"), a("XJ", L + 512 * q, L + 512 * q + n))] * (t > 0), True, False)
+        for c0, c1, e in OPT["die"][t]:
+            if e == "S":
+                mm([(a("ps7", 0, 16 * (c1 - c0)), a("ni"), a("X", L + 16 * c0, L + 16 * c1))], True, False)
+        was = [] if t == 0 else [(a("ps5", w, w + v - u), a("i32"), a("Lf", w0 + u + 16 - u0, w0 + v + 16 - u0))
+                                 for u0, v0, w0 in turned(16, 128, (ST * t) // 16) for u, v, w in turned(u0 - 16, v0 - 16)]
+        mm([(a("ps5", 0, 129), I, a("X", CAP, CAP + 129)), (a("ps5", 0, 129, 128), I, a("mk", 2 * t, 2 * t + 2))] + was, True, False)
+        if t > 0 and OPT["sg2"][t]:
+            for k, (c0, c1) in enumerate(OPT["sgp"][t]):
+                mm([(a("ps%d" % (OPT["sg2"][t] if k else 4), c0, c1), a("i32"), a("sg", 16 + c0, 16 + c1))], True, False)
+        elif t > 0:
+            mm([(a("ps4", 0, 128), a("i32"), a("sg", 16, 144))], True, False)
         if t == 0:
-            ts(a("xi"), a("cm", 0, S), 0.5, ALU.mult, -0.25, ALU.add)
+            for q in range(NR):
+                ts(a("xi", 64 * q, 64 * q + 64), a("cm", 64 * nat[q], 64 * nat[q] + 64), 0.5, ALU.mult, -0.25, ALU.add)
         else:
-            add("V", "recv", t - 1, [a("Z", S * (t - 1), S * t)], [a("Z", S * (t - 1), S * t)], ("c", 0))
-            tt(a("xi"), a("Z", S * (t - 1), S * t), a("ps4", S, 2 * S), ALU.add)
-        cp(a("x2", 0, S), a("xi"))
+            z = S * (t - 1)
+            tt(a("xi", NA, S), a("Z", z + NA, z + S), a("ps6", NA, S), ALU.add)
+            add("V", "recv", t - 1, [a("Z", z, z + NA)], [a("Z", z, z + NA)], ("c", 0))
+            tt(a("xi", 0, NA), a("Z", z, z + NA), a("ps6", 0, NA), ALU.add)
+        if OPT["x2_s"] == 0:
+            cp(a("x2"), a("xi"))
+        elif OPT["x2_s"] == 1:
+            act(a("x2"), ind(a("xi"), a("lid")))
+        else:
+            act(a("x2"), a("xi"))
+        if OPT["c_s"][t] == 2:
+            low = slice(0, 16)
+            mm([(a("ps6", 256 + r, 384, 16, low), a("x2", r, S, 16), a("z1", 15, 143, 16)) for r in range(16)])
+            act(a("tq", 0, 128, 1, low), a("ps6", 256, 384, 1, low), AF.Square, scale=0.25)
+            act(a("tu", 0, 128, 1, low), a("ps6", 256, 384, 1, low))
+            ts(a("ti", 0, 128, 1, low), a("tq", 0, 128, 1, low), 0.5, ALU.mult, -0.375, ALU.add)
+            cp(a("th", 0, 128, 1, low), a("ti", 0, 128, 1, low))
+        else:
+            wrap(a("ps6", 256, 272), "z1", "x2", 0, 16)
+            act(a("asq"), a("ps6", 256, 272), AF.Square, scale=0.25)
+            act(a("au"), a("ps6", 256, 272))
+            ts(a("ah"), a("asq"), 0.5, ALU.mult, a("acol", t, t + 1), ALU.add)
+            if OPT["c_s"][t] or OPT["cb_s"][t]:
+                cp(a("ahf"), a("ah"))
+
+        def hashes(i0, n, on_s):
+            w = n // 16; k0 = i0 // 16
+            if OPT["c_s"][t] == 2:
+                low = slice(0, 16); o = a("ps6", 0, n)
+                mm([(o, a("tu", 0, 128, 1, low), a("cu1", i0, i0 + n, 1, low)), (o, a("th", 0, 128, 1, low), a("cu0", i0, i0 + n, 1, low))])
+                ts(a("ati", i0, i0 + n), o, a("acol", t, t + 1), ALU.add, 0.375, ALU.add)
+            elif on_s:
+                for k in range(w):
+                    act(a("at", i0 + k, i0 + n, w), a("cfm"), bias=a("ahf", k0 + k, k0 + k + 1), scale=a("au", k0 + k, k0 + k + 1))
+                cp(a("ati", i0, i0 + n), a("at", i0, i0 + n))
+            else:
+                tt(a("at", i0, i0 + n), ind(a("au", k0 // 8 * 8, 16), a("l16", k0, k0 + w)), a("coef", i0, i0 + n), ALU.mult)
+                tt(a("ati", i0, i0 + n), ind(a("ah", k0 // 8 * 8, 16), a("l16", k0, k0 + w)), a("at", i0, i0 + n), ALU.add)
+            ts(a("atm", i0, i0 + n), a("ati", i0, i0 + n), W - 1, ALU.bitwise_and)
+            cp(a("offa", i0, i0 + n), a("atm", i0, i0 + n))
+
+        both = OPT["c_s"][t] == 2 and OPT["both"][t]
+        hashes(0, S if both else na, OPT["c_s"][t])
         for c0, c1, e in OPT["die"][t]:
             o = a("CD", K0 + 16 * c0, K0 + 16 * c1); n = 16 * (c1 - c0)
             if e == "S":
-                k = ds.index((c0, c1)); pq2 = a("ps%d" % (6 + k), 0, n); gq = a("g2", 512 * k, 512 * k + n)
-                act(gq, ind(a("xi") if OPT["s_xi"] else a("x2", 0, S), a("who", c0, c1)))
-                mm([(pq2, I, gq)], False, True)
-                step(o, pq2, -0.5)
+                act(a("g2", 0, n), ind(a("xi"), a("who", c0, c1)))
+                mm([(a("ps7", 0, n), I, a("g2", 0, n))], False, True)
+                step(o, a("ps7", 0, n), -0.5)
             else:
-                tt(o, ind(a("xi"), a("who", c0, c1)), a(old, L + 16 * c0, L + 16 * c1), ALU.is_ge)
-        wrap(a("ps5", 256, 272), "z1", "x2", 0, 16)
-        act(a("asq"), a("ps5", 256, 272), AF.Square, scale=0.25)
-        act(a("au"), a("ps5", 256, 272))
-        wrap(a("ps4", 0, 64), "z1", "CD", K0, 64)
-        wrap(a("ps4", 64, 128), "z1", "CD", K0 + 1024, 64)
-        cuts = [0, 16, 128] if t == 0 else [0, 128]
-        for k in range(len(cuts) - 1):
-            act(a("sg", cuts[k], cuts[k + 1]), a("ps4", cuts[k], cuts[k + 1]), AF.Sign, bias=-10.5,
-                accum=None if last else a("acc", 2 * t + k, 2 * t + k + 1))
+                tt(o, ind(a("xi"), a("who", c0, c1)), a("X", L + 16 * c0, L + 16 * c1), ALU.is_ge)
+        for k, (c0, c1) in enumerate(OPT["sgp"][t]):
+            pn2 = "ps%d" % (4 if k == 0 or not OPT["sg2"][t] else OPT["sg2"][t]); end = OPT["sg2"][t] or k == len(OPT["sgp"][t]) - 1
+            mm([(a(pn2, c0, c1), a("z1", 15 - r, 143 - r), a("CD", K0 + 16 * c0 + r, K0 + 16 * c1, 16)) for r in range(16)],
+               t == 0 and (k == 0 or bool(OPT["sg2"][t])), bool(end))
+            if end:
+                u = c0 if OPT["sg2"][t] else 0
+                act(a("sg", u, c1), a(pn2, u, c1), AF.Sign, bias=-10.5 if t == 0 else 21.5)
         for q in range(4):
             if q in OPT["xj_s"][t]:
                 mm([(a("ps%d" % q, r, 512, 16), a("U", 128 * r, 128 * r + 128), a("sg", 32 * q, 32 * q + 32)) for r in range(16)], False, True)
-                act(a("XJ", L + 512 * q, L + 512 * q + 512), a("ps%d" % q), bias=-256.0)
+                act(a("XJ", L + 512 * q, L + 512 * q + 512), a("ps%d" % q), bias=-KD)
             else:
                 mm([(a("ps%d" % q), a("bom"), a("CD", K0 + 512 * q, K0 + 512 * q + 512))], False, True)
-                tt(a("XJ", L + 512 * q, L + 512 * q + 512), a("ps%d" % q), a(old, L + 512 * q, L + 512 * q + 512), ALU.min)
-        for k, (r0, r1, e) in enumerate(OPT["par"][t]):
-            end = k == len(OPT["par"][t]) - 1
-            if end:
-                mm([(a("ps5", 0, n1), a("ni16"), a("sg", cs, 128)), (a("ps5", n1, 129), a("ni16"), a("sg", 0, cs + 1)),
-                    (a("ps5", 0, 129, 128), I, a("mk", 2 * t, 2 * t + 2))], False, False)
-            take(e, a("pg", 128 * r0, 128 * r1), ind(a("CD", 0, 16 + B), a("offp", 8 * r0, 8 * r1)))
-            mm([x for r in range(r0, r1) for x in ((a("ps5", 0, n1), a("z1", 15 - r, 143 - r), a("pg", 128 * r + cs, 128 * r + 128)),
-                                                   (a("ps5", n1, 129), a("z1", 15 - r, 143 - r), a("pg", 128 * r, 128 * r + cs + 1)))], k == 0, end)
+                tt(a("XJ", L + 512 * q, L + 512 * q + 512), a("ps%d" % q), a("X", L + 512 * q, L + 512 * q + 512), ALU.min)
+        for c0, c1, e in OPT["par"][t]:
+            take(e, a("pg", 16 * c0, 16 * c1), ind(a("CD", 0, K0 + 16 * c1), a("offp", c0, c1)))
+        cuts = [0] + [c for c in OPT["parw"][t] if c < cs - 8] + [cs + 1, cs] + [c for c in OPT["parw"][t] if c > cs + 8] + [128]
+        runs = [(u, v) for u, v in zip(cuts, cuts[1:]) if u < v]
+        own = [(a("ps5", w, w + v - u), a("ni32"), a("sg", u, v)) for u, v, w in turned(0, 128)]
+        for k, (u, v) in enumerate(runs):
+            end = k == len(runs) - 1; w = u - cs if u >= cs else n1 + u
+            if end and not OPT["sg_last"][t]:
+                mm(own, False, False)
+            mm([(a("ps5", w, w + v - u), a("z1", 15 - r, 143 - r), a("pg", 16 * u + r, 16 * v, 16)) for r in range(16)], False, end and not OPT["sg_last"][t])
+        if OPT["sg_last"][t]:
+            mm(own, False, True)
         if OPT["f_s"][t]:
-            step(a("F", 0, 129), a("ps5", 0, 129), 26.5)
+            step(a("F", 0, 129), a("ps5", 0, 129), 42.5)
         else:
-            ts(a("F", 0, 129), a("ps5", 0, 129), 26.5, ALU.is_ge)
+            ts(a("F", 0, 129), a("ps5", 0, 129), 42.5, ALU.is_ge)
         mm([(a("ps4", 0, 128), I, a("nkr"))], True, False)
         scan(a("Fp", 1, 130), a("ones", 0, 129), a("F", 0, 129), ALU.mult, ALU.add)
         mm([(a("ps4", 0, 128), a("Fp", 1, 129), BOW)], False, True)
         mm([(a("ps5", 256, 386), BOW, a("Fp", 0, 130)), (a("ps5", 256, 385), a("tri"), a("F", 0, 129))])
         act(a("Q", 0, 130), a("ps5", 256, 386))
-        ts(a("uf"), a("kw"), a("Q", 129, 130), ALU.is_ge, -4096.0, ALU.mult)
+        ts(a("uf"), a("kw", 0, 12), a("Q", 129, 130), ALU.is_ge, -4096.0, ALU.mult)
         tt(a("uu"), a("uf"), a("kc", 12 * t, 12 * t + 12), ALU.max)
         cs_ = OPT["cnt_s"][t]
         if len(cs_) < 12:
@@ -360,82 +503,116 @@ def build(me):
                 step(a("M", 128 * k, 128 * k + 128), a("vb") if len(cs_) < 12 else a("ps4", 0, 128), 16 * k + 0.5, -1.0)
             else:
                 ts(a("M", 128 * k, 128 * k + 128), a("vb"), 16 * k + 0.5, ALU.is_lt)
-        for k in range(12):
-            mm([(a("ps5", k, k + 1), a("M", 128 * k, 128 * k + 128), a("wv", 2 * t, 2 * t + 1))], k == 0, k == 11)
-        cp(a("cu"), a("ps5", 0, 12))
-        o = a("ps4", 0, 12)
-        mm([(a("ps4", k, k + 1), a("M", 128 * k, 128 * k + 128), a("wv", 2 * t + 1, 2 * t + 2)) for k in range(12)], True, False)
+        if OPT["one_m"]:
+            for k in range(12):
+                mm([(a("ps5", k, k + 17, 16), a("M", 128 * k, 128 * k + 128), a("wv", 2 * t, 2 * t + 2))], k == 0, False)
+            cp(a("cu"), a("ps5", 0, 12))
+            o = a("ps5", 16, 28)
+        else:
+            for k in range(12):
+                mm([(a("ps5", k, k + 1), a("M", 128 * k, 128 * k + 128), a("wv", 2 * t, 2 * t + 1))], k == 0, k == 11)
+            cp(a("cu"), a("ps5", 0, 12))
+            o = a("ps4", 0, 12)
+            mm([(a("ps4", k, k + 1), a("M", 128 * k, 128 * k + 128), a("wv", 2 * t + 1, 2 * t + 2)) for k in range(12)], True, False)
         mm([(o, a("idf"), a("uu"))], False, False)
         tt(a("cmp2"), ind(a("Q", 0, 130), a("cu")), a("kr"), ALU.is_le)
         mm([(o, a("z1", 15 - r, 143 - r), a("cmp2", r, CAP, 16)) for r in range(16)], False, True)
         ts(a("offo"), o, float(L + 16 * cs), ALU.add)
-        move(a("x2", S, 2 * S), a("x2", 0, S))
-        ts(a("ah"), a("asq"), 0.5, ALU.mult, a("acol", t, t + 1), ALU.add)
-        if OPT["c_s"][t]:
-            cp(a("ahf"), a("ah"))
-            for k in range(16):
-                act(a("at", k, S, 16), a("coef", 0, S, 16), bias=a("ahf", k, k + 1), scale=a("au", k, k + 1))
-            cp(a("ati"), a("at"))
-        else:
-            tt(a("at"), ind(a("au"), a("l16")), a("coef"), ALU.mult)
-            tt(a("ati"), ind(a("ah"), a("l16")), a("at"), ALU.add)
-        ts(a("atm"), a("ati"), W - 1, ALU.bitwise_and)
-        cp(a("offa"), a("atm"))
-        m0 = 0; k = 0
-        for e, w in OPT["arr"][t]:
-            n = S * w; src = ind(a("XJ", L, BB), a("offa", 16 * m0, 16 * (m0 + w))); o = a("cmpa", S * m0, S * m0 + n)
-            if e == "S":
-                gq = a("g2", 512 * k, 512 * k + n); pq2 = a("ps%d" % (2 + k), 0, n); k = 1 - k
-                mm([(pq2, a("ni"), a("x2", 0, n))], True, False)
-                act(gq, src)
-                mm([(pq2, I, gq)], False, True)
-                step(o, pq2, -0.5)
+
+        def arrivals(i0, n, pieces, ends, rep, on_s, t0, banks, cut=99):
+            w = n // 16; k0 = i0 // 16; g0 = 16 * i0
+            m0 = 0; k = 0; done = 0
+            for p, (e, d) in enumerate(pieces):
+                if p == cut:
+                    yield
+                    banks = OPT["bkl"][t]
+                src = ind(a("XJ", L, BB), a("offa", i0 + w * m0, i0 + w * (m0 + d))); o = a("cmpa", g0 + n * m0, g0 + n * (m0 + d))
+                if e == "S":
+                    gq = a("g2", 512 * k, 512 * k + n * d); pn2 = "ps%d" % banks[k]; k = 1 - k
+                    mm([(a(pn2, n * j, n * j + n), a("ni"), a("x2", i0, i0 + n)) for j in range(d)], True, False)
+                    act(gq, src)
+                    mm([(a(pn2, 0, n * d), I, gq)], False, True)
+                    step(o, a(pn2, 0, n * d), -0.5)
+                else:
+                    tt(o, src, a("xi", i0, i0 + n) if d == 1 else a(rep, 0, n * d), ALU.is_ge)
+                m0 += d
+                if m0 in ends:
+                    o = a("ps%d" % banks[2 + ends.index(m0) % 2], 0, w * (m0 - done))
+                    wrap(o, "zk", "cmpa", g0 + n * done, w * (m0 - done), [(o, I, a("bk", 0, w * (m0 - done)))])
+                    tt(a("lfa", i0 + w * done, i0 + w * m0), o, a("atm", i0 + w * done, i0 + w * m0), ALU.min)
+                    done = m0
+            src = ("lfa", i0); h = n // 2
+            while h >= w:
+                tt(a("tr", t0, t0 + h), a(src[0], src[1], src[1] + h), a(src[0], src[1] + h, src[1] + 2 * h), ALU.max)
+                src = ("tr", t0); t0 += h; h //= 2
+            top = a("tr", src[1], src[1] + w)
+            ts(a("a1", k0, k0 + w), top, float(lo), ALU.add, -1.0, ALU.max)
+            if not last:
+                ts(a("offh", k0, k0 + w), top, float(K0), ALU.add, 15.0, ALU.max)
+
+        if any(e == "V" and d > 1 for e, d in OPT["arr"][t]):
+            move(a("xa", 0, na), a("x2", 0, na)); move(a("xa", na, 2 * na), a("x2", 0, na))
+        for q in range(NR):
+            move(a("X", BB + 64 * nat[q], BB + 64 * nat[q] + 64), a("x2", 64 * q, 64 * q + 64))
+        leaving = arrivals(0, na, OPT["arr"][t], OPT["cha"][t], "xa", OPT["c_s"][t], 0, OPT["bka"][t], OPT["cut"][t])
+        next(leaving, None)
+
+        def rest():
+            if na < S and any(e == "V" for e, d in OPT["brr"][t]):
+                move(a("xb", 0, 64), a("x2", NA, S)); move(a("xb", 64, 128), a("x2", NA, S)); move(a("xb", 128, S), a("xb", 0, 128))
+            if na < S:
+                if not both:
+                    hashes(NA, S - NA, OPT["cb_s"][t])
+                next(arrivals(NA, S - NA, OPT["brr"][t], (16,), "xb", OPT["cb_s"][t], 180, OPT["bkb"][t]), None)
+            if last or OPT["e_s"][t] == 2:
+                take(OPT["t_e"][t][0], a("E", 0, 32), ind(a("a1"), a("ln")))
+                trn(a("E", 32, 64), a("E", 0, 32))
+                take(OPT["t_e"][t][1], a("E", 64, 80), ind(a("E", 32, 64), a("lo1", 0, 1)))
+                if last:
+                    dma("Y", [(ext("yc", (slice(None), slice(W, W + S))), a("E", 64, 80))])
+                else:
+                    row = lambda m: a("C", BB, BB + S, 1, slice(m, 128, 16))
+                    dma("Y", [(row(0), a("E", 64, 80))], 500.0)
+                    ops[-1]["behind"] = sent[0]
+                    dma("Y", [(row(m), row(0)) for m in range(1, 16)], 2000.0)
+                    ops[-1]["later"] = ops[-2]["later"] = True
+                return
+            if OPT["e_s"][t]:
+                for k in range(16):
+                    kk = (k - s4) % 16
+                    act(a("E", 16 * k, 16 * k + 16), a("dm", 0, 16), scale=a("a1", kk, kk + 1))
             else:
-                tt(o, src, a("x2", 0, n), ALU.is_ge)
-            m0 += w
-            if m0 % 4 == 0:
-                o = a("ps%d" % (6 + (m0 - 4) // 8), 16 * ((m0 - 4) % 8), 16 * ((m0 - 4) % 8) + 64)
-                wrap(o, "zk", "cmpa", S * (m0 - 4), 64, [(o, I, a("bk", 0, 64))])
-            if m0 % 8 == 0:
-                tt(a("lfa", 16 * m0 - 128, 16 * m0), a("ps%d" % (5 + m0 // 8), 0, 128), a("atm", 16 * m0 - 128, 16 * m0), ALU.min)
-        tt(a("tr", 0, 128), a("lfa", 0, 128), a("lfa", 128, 256), ALU.max)
-        tt(a("tr", 128, 192), a("tr", 0, 64), a("tr", 64, 128), ALU.max)
-        tt(a("tr", 192, 224), a("tr", 128, 160), a("tr", 160, 192), ALU.max)
-        tt(a("tr", 224, 240), a("tr", 192, 208), a("tr", 208, 224), ALU.max)
-        ts(a("a1"), a("tr", 224, 240), float(lo), ALU.add, -1.0, ALU.max)
-        move(a("X", BB, BB + S), a("x2", 0, S))
-        if OPT["e_s"][t]:
-            for k in range(16):
-                act(a("E", 16 * k, 16 * k + 16), a("dm", 0, 16), scale=a("a1", k, k + 1))
-        else:
-            tt(a("E"), ind(a("a1"), a("lc")), a("dm"), ALU.mult)
-        mm([(a("ps6", 0, S), a("bof"), a("E"))])
-        act(a("C", BB, BB + S), a("ps6", 0, S))
+                tt(a("E"), ind(a("a1"), a("lc")), a("dm"), ALU.mult)
+            mm([(a("ps6", 0, S), a("bof"), a("E"))])
+            act(a("C", BB, BB + S), a("ps6", 0, S))
+
         if last:
+            if not (OPT["late"] or OPT["cut"][t] < 99):
+                rest()
             dma("Y", [(ext("yx", (slice(None), slice(W, W + S))), a("X", BB, BB + S)),
-                      (ext("ya", (slice(None), slice(W, W + S))), a("onesf", 0, S, 1, slice(0, 8)))])
-            act(a("aw"), a("sg"), bias=0.5, scale=-0.5)
+                      (ext("ya", (slice(None), slice(W, W + S))), a("onesf", 0, S, 1, slice(0, 8)))], 10000.0)
+            act(a("aw"), a("sg", 0, 128), bias=0.5, scale=-0.5)
             trn(a("awt"), a("aw"))
             dma("Y", [(ext("ya", (slice(h, 8, 2), slice(512 * b, 512 * b + 512))), a("awt", 32 * b + 16 * h, 32 * b + 16 * h + 16))
-                      for b in range(4) for h in range(2)])
-        else:
-            ts(a("offh", 0, 16), a("tr", 224, 240), float(K0), ALU.add, 15.0, ALU.max)
-            act(a("a5", 80 * t + 1, 80 * t + 80, 5), a("a1"))
+                      for b in range(4) for h in range(2)], 10000.0)
         ts(a("offw"), ind(a("D", 0, BB), a("offo")), 16.0, ALU.add)
-        act(a("y"), ind(a("X", 0, BB), a("offo")))
+        take(OPT["y_e"][t], a("y"), ind(a("X", 0, BB), a("offo")))
         mm([(a("ps0", 0, CAP), I, a("y")), (a("ps0", 256, 256 + CAP), a("ih"), a("y"))])
-        act(a("XJ", CAP, 2 * CAP), a("y"))
-        ts(a("dp"), a("offw"), float(W0), ALU.add)
+        move(a("XJ", CAP, 2 * CAP), a("y"))
+        if OPT["dp_s"][t]:
+            act(a("dp"), ind(a("D", 0, BB), a("offo")))
+        else:
+            ts(a("dp"), a("offw"), -16.0, ALU.add)
         for j0, j1, e in OPT["og"][t]:
             take(e, a("G", 16 * j0, 16 * j1), ind(a("XJ", W0, BB), a("offw", j0, j1)))
         for j0, j1, e, by, bank in OPT["oc"][t]:
             n = j1 - j0; o = a("ps%d" % bank, j0, j1)
             if e == "S":
                 for h in range(n // 32):
-                    k = 16 * j0 + 512 * h; pn = "ps%d" % by[h]
-                    mm([(a(pn, m, 512, 16), a("ni"), a("y", j0 + 32 * h, j0 + 32 * h + 32)) for m in range(16)], True, False)
-                    mm([(a(pn), I, a("G", k, k + 512))], False, True)
-                    step(a("cmpo", k, k + 512), a(pn), -0.5)
+                    k = 16 * j0 + 512 * h; pn2 = "ps%d" % by[h % len(by)]
+                    mm([(a(pn2, m, 512, 16), a("ni"), a("y", j0 + 32 * h, j0 + 32 * h + 32)) for m in range(16)], True, False)
+                    mm([(a(pn2), I, a("G", k, k + 512))], False, True)
+                    step(a("cmpo", k, k + 512), a(pn2), -0.5)
                 mm([(o, I, a("bk", 0, n))] + [(o, a("zk", 15 - m, 143 - m), a("cmpo", 16 * j0 + m, 16 * j1, 16)) for m in range(16)])
             else:
                 mm([(o, I, a("bk", 0, n))], True, False)
@@ -445,68 +622,89 @@ def build(me):
                     mm([(o, a("zk", 15 - m, 143 - m), a("cmpo", 16 * j0 + n * m, 16 * j0 + n * m + n)) for m in range(h, h + by)], False, h + by == 16)
             tt(a("left", j0, j1), o, a("dp", j0, j1), ALU.min)
             trn(a("lt", j0, j1), a("left", j0, j1))
-            scan(a("ls", j0, j1), a("kp", 0, n), a("lt", j0, j1), ALU.mult, ALU.max)
+            scan(a("ls", j0, j1), a("kp", 0, n), a("lt", j0, j1), ALU.add, ALU.max)
             src = ind(a("ls", j0, j1), a("l15", 0, n // 16))
             if j0 in OPT["bb_s"][t]:
-                act(a("bb", j0, j1), src, AF.Relu, bias=float(1 - OFF))
+                act(a("bb", j0, j1), src, AF.Relu, bias=1.0)
             else:
-                ts(a("bb", j0, j1), src, float(1 - OFF), ALU.add, 0.0, ALU.max)
+                ts(a("bb", j0, j1), src, 1.0, ALU.add, 0.0, ALU.max)
             trn(a("br", j0, j1), a("bb", j0, j1))
             ts(ind(a("C", 0, BB), a("offo", j0 // 16, j1 // 16)), a("br", j0, j1), 1.0, ALU.mult, -1.0, ALU.add)
-        if not last:
-            dma("Y", [(a("cinf", 16 * b, 16 * b + 16), a("C", L + S + 256 * b, L + S + 256 * b + 256, 1, slice(0, 128, 16))) for b in range(8)], 500.0)
         for j0, j1, k0 in OPT["ox"][t]:
             c0, c1 = j0 // 16, j1 // 16
             mm([(a("ps4", c0 + ih, c1, 2), a("iwo" if ih else "iwe", 16 + 16 * (ih - gh), 144 + 16 * (ih - gh)), a("ls", j0 + 16 * gh + 15, j1, 32))
                 for ih in range(2) for gh in range(2)])
             tt(a("w1", c0, c1), a("ps4", c0, c1), a("ky", c0, c1), ALU.max)
-            ts(a("offx", c0, c1), a("w1", c0, c1), float(-CAP), ALU.add)
+            ts(a("offx", c0, c1), a("w1", c0, c1), float(OFF - CAP), ALU.add)
             act(a("xh", j0, j1), ind(a("XJ", CAP, BB), a("offx", c0, c1)), bias=-0.25, scale=0.5)
             tt(a("yn", j0, j1), a("xh", j0, j1), a("ps0", 256 + j0, 256 + j1), ALU.add)
             for k in range(len(k0) - 1):
                 cp(ind(a("X", 0, BB), a("offo", k0[k] // 16, k0[k + 1] // 16)), a("yn", k0[k], k0[k + 1]))
+        next(leaving, None)
         if last:
-            dma("Y", [(ext("yc", (slice(None), slice(None))), a("C", L, BB + S, 1, slice(0, 128, 16)))], 300.0)
+            if OPT["late"] or OPT["cut"][t] < 99:
+                rest()
+            dma("Y", [(ext("yc", (slice(None), slice(0, W))), a("C", L, BB, 1, slice(0, 128, 16)))], 300.0)
             dma("Y", [(ext("yx", (slice(None), slice(0, 1024))), a("X", L, L + 1024))], 700.0)
             dma("S", [(ext("yx", (slice(None), slice(1024, W))), a("X", L + 1024, BB))], 700.0)
             break
-        for k in range(3):
-            for c0, c1, e in OPT["hop"][t]:
-                p0, p1 = S * k + 16 * c0, S * k + 16 * c1
-                take(e[k], a("H", p0, p1), ind(a("C", W0, BB), a("offh", 16 * k + c0, 16 * k + c1)))
-                scan(a("hs", p0, p1), a("H", p0, p1), a("Mh", 0, p1 - p0), ALU.max, ALU.add, -BIG)
-                ak = a("hs", p0 + 15, p1, 16); dst = a("a5", 80 * t + 5 * c0 + k + 2, 80 * t + 5 * c1, 5)
-                if k < 2:
-                    ts(a("offh", 16 * k + 16 + c0, 16 * k + 16 + c1), ak, BIG + 16, ALU.add)
-                    act(dst, ak, bias=BIG)
+        dma("Y", [(a("blkf", 16, 144), a("C", L, BB, 1, slice(0, 128, 16)))], 200.0)
+        trn(a("bt", 0, 128), a("blkf", 16, 144))
+        trn(a("bt", 128, 288), a("blkf"))
+        ts(a("offp", 0, 112), ind(a("bt"), a("lq", 8, 15)), 16.0, ALU.add)
+
+        def queries(pieces, snd):
+            base = {c0: 80 * c0 + 64 * k + (128 if c0 == 12 else 0) for k, (c0, c1, e) in enumerate(pieces)}
+            for c0, c1, e in pieces:
+                h0 = base[c0]; n = 80 * (c1 - c0)
+                act(a("hs", h0 + 75, h0 + n, 80), a("kq", c0, c1), bias=BIG + B)
+                act(a("hs", h0 + 91, h0 + n + 16, 80), a("a1", c0, c1), bias=BIG)
+            for k in range(3):
+                for c0, c1, e in pieces:
+                    p0, p1 = S * k + 16 * c0, S * k + 16 * c1; h0 = base[c0] + 16 * (k + 2); n = 80 * (c1 - c0)
+                    take(e[k], a("H", p0, p1), ind(a("C", W0, BB), a("offh", 16 * k + c0, 16 * k + c1)))
+                    scan(a("hs", h0, h0 + n, 5), a("H", p0, p1), a("Mh", 0, p1 - p0), ALU.min, ALU.add, BIG)
+                    if k < 2:
+                        ts(a("offh", 16 * k + 16 + c0, 16 * k + 16 + c1), a("hs", h0 + 75, h0 + n, 80), 16 - BIG, ALU.add)
+            for c0, c1, e in pieces:
+                five = a("hs", base[c0] + 75, base[c0] + 80 * (c1 - c0) + 60, 16)
+                tt(a("q1", 5 * c0, 5 * c1), five, a("thr", 80 * t + 5 * c0, 80 * t + 5 * c1), ALU.is_lt)
+                scan(a("q2", 5 * c0, 5 * c1), a("q1", 5 * c0, 5 * c1), five, ALU.mult, ALU.max)
+                ts(a("offq", c0, c1), a("q2", 5 * c0 + 4, 5 * c1, 5), 16 - BIG, ALU.add)
+            for c0, c1, e in snd:
+                o = a("sb" if c0 < 12 else "Z", S * t + 16 * c0, S * t + 16 * c1); src = ind(a("X", W0, BB + S), a("offq", c0, c1))
+                if e == "S":
+                    act(o, src, scale=0.5)
                 else:
-                    ts(dst, ak, BIG, ALU.add)
-        for c0, c1, e in OPT["hop"][t]:
-            p0, p1 = 80 * t + 5 * c0, 80 * t + 5 * c1
-            tt(a("q1", 5 * c0, 5 * c1), a("a5", p0, p1), a("thr", p0, p1), ALU.is_lt)
-            scan(a("q2", 5 * c0, 5 * c1), a("q1", 5 * c0, 5 * c1), a("a5", p0, p1), ALU.mult, ALU.max)
-            ts(a("offq", c0, c1), a("q2", 5 * c0 + 4, 5 * c1, 5), 16.0, ALU.add)
-        for c0, c1, e in OPT["snd"][t]:
-            o = a("sb", S * t + 16 * c0, S * t + 16 * c1); src = ind(a("X", W0, BB + S), a("offq", c0, c1))
-            if e == "S":
-                act(o, src, scale=0.5)
-            else:
-                ts(o, src, 0.5, ALU.mult)
-        add("G", "send", t, [], [a("sb", S * t, S * t + S)], ("c", 300))
-        act(a("Z", S * t + 64 * me, S * t + 64 * me + 64), a("sb", S * t + 64 * me, S * t + 64 * me + 64))
-        cp(ind(a("XJ", 0, BB), a("offo")), a("yn"))
-        act(a("XJ", BB, BB + S), a("x2", 0, S))
-        ts(a("dn"), a("left"), float(OFF - 1), ALU.max, float(-OFF), ALU.add)
-        cp(ind(a("D", 0, BB), a("offo")), a("dn"))
-        act(a("din"), ind(a("lfa"), a("l512")))
-        trn(a("dout"), a("din"))
+                    ts(o, src, 0.5, ALU.mult)
+
+        queries([p for p in OPT["hop"][t] if p[0] < 12], [p for p in OPT["snd"][t] if p[0] < 12])
+        add("G", "send", t, [], [a("sb", S * t, S * t + NA)], ("c", 300))
+        sent = [len(ops) - 1]
+        rest()
+        queries([p for p in OPT["hop"][t] if p[0] >= 12], [p for p in OPT["snd"][t] if p[0] >= 12])
+        ts(a("offp", 112, 128), ind(a("a1"), a("ln", 0, 1)), 16.0, ALU.add)
+        mm([(a("ps5", 0, 129), BOW, a("Fp", 0, 129)), (a("ps5", 0, 129), a("tri2"), a("F", 0, 129))])
+        step(a("Lf", 0, 129), a("ps5", 0, 129), 4096 + CAP - 0.5)
+        cp(ind(a("D", 0, BB), a("offo")), a("left"))
+        act(a("din", 16, 272), ind(a("lfa"), a("lk")))
+        trn(a("dout", 0, 256), a("din", 16, 272))
+        trn(a("dout", 256, 544), a("din"))
         ts(a("D", BB, BB + S), ind(a("dout"), a("lm")), float(lo), ALU.add, -1.0, ALU.max)
         if t == 0:
+            act(a("junk", 0, 16), a("sg", 0, 16), accum=a("acc", 0, 1))
+            act(a("junk", 16, 128), a("sg", 16, 128), accum=a("acc", 1, 2))
             tt(a("ar"), a("acc", 0, 1), a("acc", 1, 2), ALU.add)
         else:
+            act(a("junk"), a("sg", 0, 128), accum=a("acc", 2, 3))
             tt(a("ar"), a("acc", 2, 3), a("acc", 1, 2), ALU.subtract)
         mm([(a("ps7", 0, 1), a("bof"), a("ar"))])
         ts(a("acol", t + 1, t + 2), a("ps7", 0, 1), 0.5, ALU.mult, (1024.0 if t == 0 else 128.0) - 0.375, ALU.add)
+    cuts = [0] + [j for j, o in enumerate(ops) if o["kind"] == "recv"] + [len(ops)]
+    for t in range(R):
+        for x, m, y, n in OPT["first"][t]:
+            nth = lambda name, k: [j for j in range(cuts[t], cuts[t + 1]) if ops[j]["wr"] and ops[j]["wr"][0][0] == name and ops[j]["eng"] in "VS"][k]
+            ops[nth(y, n)]["after"] = nth(x, m)
     return ops
 
 
@@ -536,6 +734,8 @@ def link(ops):
                 hist.setdefault(sp[0], []).append((j, acc_w, sp[1:]))
         if "after" in o:
             d.setdefault(o["after"], False)
+        if "behind" in o:
+            d[o["behind"]] = True
         if o["kind"] == "send":
             sends[o["args"]] = j
         if o["kind"] == "recv":
@@ -548,12 +748,12 @@ def sizes(ops, prm):
     out = []
     for o in ops:
         c = o["cost"]
-        if c[0] == "c": v = c[1] * prm["cyc"]
+        if c[0] == "c": v = c[1] * prm["cyc"] * (prm["pool"] if o["eng"] == "G" else 1.0)
         elif c[0] == "g": v = 60 + c[1] * prm["cyc"] * prm["g"]
         elif c[0] == "sc": v = 60 + c[1] * prm["cyc"] * prm["sc"]
         elif c[0] == "pe": v = c[1] * prm["pe"]
         else: v = 60.0 * c[1]
-        out.append((v, v + (prm["dma"] + c[2] if c[0] == "dma" else 0.0)))
+        out.append((v, v + (prm["dma"] + c[2] if c[0] == "dma" and not ("later" in o and prm.get("part")) else 0.0)))
     return out
 
 
@@ -563,12 +763,19 @@ def gap(ops, i, j, need, prm):
     return prm["same"] if ops[i]["eng"] == ops[j]["eng"] else prm["cross"]
 
 
-def schedule(ops, deps, prm):
+def schedule(ops, deps, prm, iters, steps, start=None, seed=7):
     n = len(ops); eng = [o["eng"] for o in ops]
+    anc = [0] * n; keep = []
+    for j in range(n):
+        up = 0
+        for i in deps[j]: up |= anc[i]
+        keep.append([i for i in deps[j] if not up >> i & 1 or ops[i]["kind"] in ("dma", "send")])
+        for i in deps[j]: up |= 1 << i
+        anc[j] = up
 
     def graph(p):
         sz = sizes(ops, p); d = [max(s[0], 1e-3) for s in sz]
-        lag = [[(i, (sz[i][1] if need is not False else d[i]) + gap(ops, i, j, need, p) + 1e-3) for i, need in deps[j].items()] for j in range(n)]
+        lag = [[(i, (sz[i][1] if deps[j][i] is not False else d[i]) + gap(ops, i, j, deps[j][i], p) + 1e-3) for i in keep[j]] for j in range(n)]
         return d, [s[1] for s in sz], lag
 
     def place(seq, pred, first, d):
@@ -606,17 +813,21 @@ def schedule(ops, deps, prm):
     for j in range(n - 1, -1, -1):
         for i, l in lag[j]: level[i] = max(level[i], l + level[j])
     key = [-v for v in level]
-    x = OPT["seed"]; best = None; ref = None
-    for it in range(OPT["iters"]):
+    x = seed; best = None; ref = None
+    if start:
+        ref = [span(start, gr) for gr in others]; best = (0.0, start)
+    for it in range(iters):
         st = place(sorted(range(n), key=lambda k: (key[k], k)), lag, zero, d)
         for rep in range(2):
             sb = place(sorted(range(n), key=lambda k: (-st[k], -k)), back, tail, d)
             st = place(sorted(range(n), key=lambda k: (-sb[k] - d[k], k)), lag, zero, d)
         seq = sorted(range(n), key=lambda k: (st[k], k))
-        tm = [span(seq, gr) for gr in others]
-        if ref is None: ref = tm
-        score = sum(u / v for u, v in zip(tm, ref))
-        if best is None or score < best[0]: best = (score, seq, st)
+        first = span(seq, others[0])
+        if best is None or first < 1.01 * best[3]:
+            tm = [first] + [span(seq, gr) for gr in others[1:]]
+            if ref is None: ref = tm
+            score = sum(u / v for u, v in zip(tm, ref))
+            if best is None or score < best[0]: best = (score, seq, st, first)
         key = list(best[2])
         for k in range(OPT["moves"]):
             x = (x * 1103515245 + 12345) % 2147483648; j = (x >> 8) % n
@@ -625,16 +836,9 @@ def schedule(ops, deps, prm):
         for j in range(n):
             for i, l in lag[j]:
                 if key[j] <= key[i]: key[j] = key[i] + 1e-3
-    anc = [0] * n; keep = []
-    for j in range(n):
-        up = 0
-        for i in deps[j]: up |= anc[i]
-        keep.append([i for i in deps[j] if not up >> i & 1])
-        for i in deps[j]: up |= 1 << i
-        anc[j] = up
-    slim = [(g[0], g[1], [[(i, l) for i, l in g[2][j] if i in keep[j]] for j in range(n)]) for g in others]
+    slim = others; full0 = others[0][1]
 
-    def run(seq, p0, old):
+    def run(seq, p0, old, most=None):
         lastop = {}
         for k in range(p0 - 1, -1, -1):
             if eng[seq[k]] not in lastop:
@@ -649,19 +853,20 @@ def schedule(ops, deps, prm):
                     u = st[i] + l
                     if u > t: t = u
                 st[j] = t; free[e] = t + d[j]
+            if most and not out and max(st[j] + full[j] for j in ends) > most:
+                return None
             out.append(st)
         return out
 
-    ends = [j for j in range(n) if ops[j]["kind"] == "dma"]
-    soft = OPT["soft"] / n
-    value = lambda sts: sum((max(st[j] + g[1][j] for j in ends) + soft * sum(st)) / v for st, g, v in zip(sts, slim, ref))
+    ends = [j for j in range(n) if not back[j]]
+    value = lambda sts: sum(max(st[j] + g[1][j] for j in ends) / v for st, g, v in zip(sts, slim, ref))
     seq = best[1]; sts = run(seq, 0, [zero] * len(slim)); cur = value(sts); best = (cur, seq); chain = None
-    for it in range(OPT["steps"]):
+    for it in range(steps):
         if chain is None:
             pos = [0] * n; before = [None] * n; lastq = {}
             for k, j in enumerate(seq):
                 pos[j] = k; before[j] = lastq.get(eng[j]); lastq[eng[j]] = j
-            chain = {}
+            chain = {}; most = max(sts[0][j] + full0[j] for j in ends) + OPT["heat"] * ref[0]
         x = (x * 1103515245 + 12345) % 2147483648; v = (x >> 8) % len(slim)
         if v not in chain:
             st = sts[v]; d, full, lag = slim[v]; j = max(ends, key=lambda k: st[k] + full[k]); c = []
@@ -693,12 +898,34 @@ def schedule(ops, deps, prm):
             go = [k for k in mid if k == i or anc[k] >> i & 1]
             if go[-1] == j: continue
             new = seq[:pos[i]] + [k for k in mid if not (k == i or anc[k] >> i & 1)] + go + seq[pos[j] + 1:]
-        s2 = run(new, pos[i], sts); val = value(s2)
+        s2 = run(new, pos[i], sts, most)
+        if s2 is None: continue
+        val = value(s2)
         x = (x * 1103515245 + 12345) % 2147483648
-        if val <= cur + OPT["heat"] * (1.0 - it / OPT["steps"]) * (x / 2147483648.0) ** 2:
+        if val <= cur + OPT["heat"] * (1.0 - it / steps) * (x / 2147483648.0) ** 2:
             seq = new; sts = s2; cur = val; chain = None
             if cur < best[0]: best = (cur, seq)
-    return best[1]
+    return sum(span(best[1], gr) / (k + 1.0 if k < 2 else 2.0) for k, gr in enumerate(others)), best[1]
+
+
+def plan(ops, deps, prm):
+    cuts = [0] + [j + 1 for j, o in enumerate(ops) if o["kind"] == "recv"] + [len(ops)]
+    order = []
+    for u, v in zip(cuts, cuts[1:]):
+        part = [{i - u: need for i, need in d.items() if i >= u} for d in deps[u:v]]
+        tries = [schedule(ops[u:v], part, dict(prm, part=True), OPT["iters"], OPT["steps"], seed=k) for k in range(1, OPT["tries"] + 1)]
+        order += [u + j for j in min(tries)[1]]
+    return schedule(ops, deps, prm, 0, OPT["polish"], order)[1]
+
+
+def joint():
+    all_ops = [build(me) for me in range(NR)]
+    deps = link(all_ops[0])
+    for ops in all_ops[1:]:
+        for d, e in zip(deps, link(ops)):
+            for i, need in e.items():
+                if i not in d or (need and not d[i]): d[i] = need
+    return all_ops[0], deps
 
 
 _PLAN = {}
@@ -720,7 +947,8 @@ def rank_program(g, core, T, topo):
     cores = list(T.cores)
     ops = build(me); deps = link(ops)
     if "order" not in _PLAN:
-        _PLAN["order"] = schedule(ops, deps, PRM)
+        ops0, deps0 = joint()
+        _PLAN["order"] = plan(ops0, deps0, PRM)
     order = _PLAN["order"]
     Q = dict(V=g.vector, S=g.scalar, P=g.tensor, G=g, Y=g.sync)
     pos = {j: n for n, j in enumerate(order)}
@@ -785,16 +1013,16 @@ def rank_program(g, core, T, topo):
         elif k == "iota":
             if _SB[x[0][1]][1] == i32: ins = q.iota(ap(x[0]), x[1], x[2], x[3])
             else: ins = q.iota(ap(x[0]), x[1], x[2], x[3], allow_small_or_imprecise_dtypes=True)
-        elif k == "sel": ins = q.affine_select(ap(x[0]), ap(x[1]), x[2], x[3], 0.0, x[4], x[5])
+        elif k == "sel": ins = q.affine_select(ap(x[0]), ap(x[1]), x[2], x[3], x[6], x[4], x[5])
         elif k == "dma":
             for po, pi in x:
                 q.dma_start(ap(po), ap(pi)).then_inc(T.sem[mark[j][0]], 16)
         elif k == "send":
-            trs = []
-            for c, eng in masks(core, cores, topo).items():
-                b = cores.index(c); rid, pid = topo.addr(c, core)
-                trs.append(RemoteDMATransfer(dst_ids=[DstId(rid=rid, pnc=pid)], dma_engine_mask=sum(1 << n for n in eng), remote_sem=T.sem["arr%d" % x],
-                                             src=T.sb[:, S * x + 64 * b:S * x + 64 * b + 64], dst=T.Z[:, S * x + 64 * me:S * x + 64 * me + 64]))
+            trs = []; eng = masks(core, cores, topo)
+            for b, src, dst in transfers(o, me):
+                rid, pid = topo.addr(cores[b], core)
+                trs.append(RemoteDMATransfer(dst_ids=[DstId(rid=rid, pnc=pid)], dma_engine_mask=sum(1 << n for n in eng[cores[b]]),
+                                             remote_sem=T.sem["arr%d" % x], src=ap(src), dst=ap(dst)))
             q.remote_dma_fused(trs, local_sem=T.sem.sent)
         if ins is not None and j in mark:
             ins.then_inc(T.sem[mark[j][0]], 1)

@@ -1,39 +1,42 @@
 import math
 from concourse.bass import DstId, RemoteDMATransfer
-from concourse.mybir import AluOpType as ALU, ActivationFunctionType as AF, AxisListType as AX
+from concourse.mybir import AluOpType as ALU, ActivationFunctionType as AF
 
 W, S, R, CAP, ST, NR = 2048, 256, 3, 192, 467, 4
-OFF = 2 * CAP + 16
+OFF = 3 * CAP + 16
+Y0 = CAP
 W0 = OFF - 16
+D0 = OFF + 1024 - 16
 NW = OFF + W + R * S
 NA = S - S // NR
 BIG = 8192.0
 KD = 65536.0
+HS = 1600
 f32, b16, i32, u16 = "float32", "bfloat16", "int32", "uint16"
 
 _SB = dict(
-    X=(NW, b16), XJ=(NW, b16), C=(NW, f32), D=(NW, i32), CD=(16 + W + 2 * S, b16), cm=(768, b16),
-    blk=(160, i32), blkf=(160, f32), bti=(288, i32), bt=(288, f32),
+    X=(NW, b16), XJ=(NW, b16), C=(NW, i32), CF=(NW, f32), D=(NW, i32), CD=(16 + W + 2 * S, b16), cm=(768, b16),
+    blk=(160, i32), blkf=(128, f32), bti=(288, i32), Ei=(40, i32),
     ag=(32, i32), agf=(32, f32), agt=(32, f32), agr=(32, f32), thr=(160, f32), ahf=(16, f32),
-    ones=(160, b16), bow=(128, b16), bow0=(128, b16), gi=(9, b16), z1=(144, b16), zk=(144, b16), iw=(160, b16),
-    ni=(128, b16), ni32=(128, b16), i32=(128, b16), ih=(128, b16), rs=(9, f32),
+    ones=(160, b16), bow=(128, b16), bow0=(128, b16), z1=(144, b16), zk=(144, b16), iw=(160, b16),
+    ni=(128, b16), ni32=(128, b16), i32=(128, b16), ih=(128, b16), rs=(9, f32), nq=(256, b16),
     bom=(128, b16), bof=(128, f32), tri=(128, b16), tri2=(128, b16), iwe=(160, f32), iwo=(160, f32), nkr=(128, b16),
-    pi=(4, i32), pj=(8, i32), pc=(18, f32), j16=(192, f32), dm=(256, f32), kp=(192, b16), coef=(256, f32), cfm=(16, f32), kr=(192, b16),
-    Mh=(192, f32), idf=(128, f32), mk=(16, b16), wv=(16, b16), kc=(36, f32), ky=(12, f32), c32=(32, f32), kq=(16, f32),
-    pw0=(128, f32), pw=(128, f32), kw=(16, f32), l16=(16, u16), l12=(12, f32), l15=(12, u16), lc=(16, u16), lk=(16, u16),
-    lq=(16, u16), lr=(2, u16), ln=(2, u16), lo1=(2, u16), lid=(16, u16),
-    lm=(16, u16), bv=(512, b16), bk=(256, b16), onesf=(256, f32), U=(2048, b16),
-    xi=(256, i32), x2=(256, b16), xa=(512, b16), xb=(256, b16), wh=(128, i32), whm=(128, i32), who=(128, u16),
+    pi=(4, i32), pj=(9, i32), pc=(30, f32), kp2=(288, f32), lef2=(256, f32), lt2=(288, f32), lx=(2, u16), j16=(192, f32), dm=(192, f32), kp0=(192, f32), kp=(192, f32), ka=(192, f32), cfm=(16, f32), kr=(192, b16),
+    Mh=(192, f32), idf=(128, f32), mk=(16, b16), mb=(16, f32), tu=(128, f32), tq=(128, f32), ti=(128, i32), cw=(512, f32), cw0=(256, f32), wv=(16, b16), kc=(36, f32), c32=(32, f32), kq=(16, f32), c4=(12, f32),
+    pw=(128, f32), kw=(16, f32), l15=(12, u16), lk=(16, u16), l4=(24, u16),
+    lq=(16, u16), lr=(2, u16), ln=(2, u16), lo1=(2, u16),
+    lm=(16, u16), bv=(512, b16), bk=(256, b16), U=(2048, b16), onesf=(256, f32),
+    xi=(256, i32), x2=(256, b16), xa=(1024, b16), xb=(512, b16), wh=(128, i32), whm=(128, i32), who=(128, u16),
     g2=(1024, b16), sg=(144, b16), junk=(128, b16), acc=(16, f32), ar=(1, f32), acol=(3, f32),
     offp=(128, u16), pg=(2048, b16), F=(144, b16), Fp=(144, b16), Q=(144, b16), Lf=(144, b16), vb=(128, b16), M=(12 * 128, b16),
     cu=(12, u16), uf=(12, f32), uu=(12, f32), cmp2=(192, b16),
-    offo=(12, u16), offw=(192, u16), dp=(192, f32), y=(192, b16),
-    G=(3072, b16), cmpo=(3072, b16), left=(192, f32), lt=(192, f32), ls=(192, f32), bb=(192, f32), br=(192, f32),
-    w1=(12, f32), offx=(12, u16), xh=(192, f32), yn=(192, i32), dn=(192, i32),
-    tq=(128, f32), tu=(128, f32), ti=(128, i32), th=(128, f32), cu0=(256, f32), cu1=(256, f32), asq=(16, f32), au=(16, f32), ah=(16, i32), at=(256, f32), ati=(256, i32), atm=(256, i32), offa=(256, u16),
-    cmpa=(4096, b16), lfa=(256, f32), tr=(256, f32), a1=(16, f32), E=(256, f32), din=(288, f32), dout=(544, f32),
-    offh=(48, u16), H=(768, f32), hs=(1600, f32), q1=(80, f32), q2=(80, f32), offq=(16, u16),
-    sb=(512, b16), Z=(512, b16), aw=(128, f32), awt=(128, f32),
+    offo=(12, u16), offw=(192, u16), dp=(224, f32), dq=(192, f32), dt=(416, f32), yr=(768, b16),
+    G=(3072, b16), cmpo=(3072, b16), left=(192, f32), lt=(192, f32), ls=(480, f32), bb=(192, f32), br=(192, f32),
+    offx=(16, u16), xh=(192, f32), xw=(192, b16), yn=(192, i32),
+    asq=(16, f32), au=(16, f32), ati=(256, i32), atm=(256, i32), offa=(256, u16),
+    cmpa=(4096, b16), lfa=(256, f32), tr=(256, f32), top=(256, f32), E=(112, f32), offd=(12, u16), din=(288, f32), dout=(544, f32),
+    offh=(48, u16), H=(768, f32), hs=(2 * HS, f32), q1=(80, f32), q2=(80, f32), offq=(16, u16),
+    sb=(512, b16), Z=(512, b16), aw=(128, f32), awx=(128, b16),
 )
 _AT = {}
 SCRATCH = {}
@@ -50,38 +53,29 @@ for _k in range(8):
 NDMA = 40
 SEMAPHORES = ["cV", "cS", "cP", "cG", "sent", "arr0", "arr1"] + ["d%d" % k for k in range(NDMA)]
 
-PRM = dict(cyc=0.92, pe=0.46, g=1.56, sc=3.8, same=150.0, cross=160.0, dma=2000.0, comm=2400.0, pool=1.3)
-VARIANTS = [{}, dict(cyc=1.0, pe=0.5, same=100.0, cross=150.0, dma=1500.0, pool=1.0),
-            dict(cyc=0.85, pe=0.42, same=180.0, cross=190.0, dma=2500.0, comm=3800.0, pool=1.6), dict(g=1.2, sc=2.5), dict(cyc=1.2, pe=0.6, g=2.0, sc=5.5)]
+PRM = dict(cyc=0.88, pe=0.46, g=1.4, sc=3.2, same=195.0, cross=205.0, dma=2000.0, comm=2000.0, pool=1.5)
+VARIANTS = [{}, dict(cyc=1.0, pe=0.52, g=1.56, sc=3.8, same=110.0, cross=140.0, dma=1500.0, comm=1600.0, pool=1.0),
+            dict(cyc=0.85, pe=0.44, g=1.15, sc=2.2, same=235.0, cross=250.0, dma=2500.0, comm=2600.0, pool=1.8), dict(cyc=1.15, pe=0.6, g=1.9, sc=5.0, same=170.0, cross=180.0, comm=2400.0),
+            dict(cyc=1.05, pe=0.58, g=1.08, sc=4.5, same=170.0, cross=180.0, comm=3000.0)]
 
 
 def _pieces(text):
-    return tuple((e, int(w)) for e, w in text.split())
+    return tuple((e[0], int(e[1:])) for e in text.split())
 
 
 OPT = dict(
-    x_parts=((0, 32), (32, 64), (64, 96), (96, 128)), x2_s=1, one_m=0, late=0, both=[0] * 3, first=[()] * 3, t_e=["SS"] * 3, cut=[99] * 3, bkl=[(6, 7, 6, 7)] * 3, na=192, xj_s=[()] * 3, sg2=[7, 0, 0], bka=[(2, 3, 6, 7), (1, 2, 6, 7), (1, 4, 6, 7)], bkb=[(2, 3, 6, 7), (7, 6, 7, 7), (4, 7, 6, 6)],
-    die=[((0, 32, "V"), (32, 64, "V"), (64, 96, "V"), (96, 128, "V"))] * 2 + [((0, 32, "V"), (32, 64, "V"), (64, 104, "V"), (104, 128, "S"))],
-    par=[((0, 32, "S"), (32, 64, "S"), (64, 96, "S"), (96, 128, "S"))] + [((0, 16, "S"), (16, 48, "S"), (48, 96, "S"), (96, 128, "S"))] * 2,
-    sgp=[((0, 64), (64, 128))] * 3, parw=[(), (), (64,)],
-    sg_last=[0, 1, 0], dp_s=[0] * 3, e_s=[2, 2, 2], c_s=[1, 1, 1], cb_s=[1, 1, 1], f_s=[1, 1, 0], cnt_s=[(), (6, 7, 8, 9, 10, 11), (10, 11)], y_e=["S"] * 3,
-    arr=[_pieces("S2 S2 S2 V2 V2 V2 V2 V2"), _pieces("V2 V2 S2 S2 V2 V2 V2 V2"), _pieces("S2 S2 V2 V2 V2 V2 V2 V2")], cha=[(8, 16)] * 3,
-    brr=[_pieces("S8 S8")] * 3,
-    og=[((0, 32, "V"), (32, 64, "S"), (64, 128, "S"), (128, 192, "S")), ((0, 32, "S"), (32, 64, "V"), (64, 128, "S"), (128, 160, "S"), (160, 192, "S")),
-        ((0, 64, "S"), (64, 128, "S"), (128, 160, "S"), (160, 192, "V"))],
-    oc=[((0, 64, "V", 8, 1), (64, 128, "S", (2, 3), 5), (128, 192, "V", 8, 1))] + [((0, 64, "V", 4, 1), (64, 128, "V", 4, 5), (128, 192, "S", (2, 3), 1))] * 2,
-    bb_s=[(), (0,), (0, 128)],
-    ox=[((0, 192, (0, 64, 128, 192)),), ((0, 192, (0, 96, 192)),), ((0, 192, (0, 192)),)],
-    hop=[((0, 6, "SSS"), (6, 12, "SSS"), (12, 16, "SSS")), ((0, 6, "SVS"), (6, 12, "SSS"), (12, 16, "SSS"))],
-    snd=[((0, 6, "S"), (6, 12, "V"), (12, 16, "S")), ((0, 6, "S"), (6, 12, "V"), (12, 16, "S"))],
-    jit=1500.0, moves=4, tries=2, iters=100, steps=60000, polish=8000, heat=0.006)
-for _t, _d in enumerate((
-        dict(bb_s=(0, 128), sg_last=1, sgp=((0, 96), (96, 128))),
-        dict(),
-        dict(arr=_pieces("S2 V1 V1 V1 V1 V2 V2 V2 S2 S2"), cut=5, og=((0, 32, "V"), (32, 64, "S"), (64, 96, "V"), (96, 128, "S"), (128, 192, "S")),
-             oc=((0, 64, "V", 4, 1), (64, 128, "S", (2, 3), 5), (128, 192, "V", 4, 1)), c_s=0, bkb=(6, 7, 6, 7), cha=(16,), brr=_pieces("V4 V4 S8"), f_s=1))):
-    for _k, _v in _d.items():
-        OPT[_k][_t] = _v
+    x_parts=((0, 32), (32, 64), (64, 128)), cut=[99, 99, 12], bkl=[(0, 1, 6, 7)] * 3, sg2=[0, 0, 0],
+    bka=[(0, 1, 6, 7)] * 3, bkb=[(1, 6, 7, 7)] * 2,
+    die=[((0, 32, "V"), (32, 64, "V"), (64, 96, "V"), (96, 128, "V"))] + [((0, 16, "V"), (16, 40, "V"), (40, 64, "V"), (64, 96, "V"), (96, 112, "V"), (112, 128, "V"))] * 2,
+    par=[((0, 32), (32, 64), (64, 96), (96, 128))] + [((0, 16), (16, 40), (40, 64), (64, 96), (96, 112), (112, 128))] * 2,
+    sgp=[((0, 64), (64, 128))] * 3, parw=[(64,)] * 3, sg_last=[1, 1, 1], hpe=[0, 0, 0],
+    arr=[_pieces("S2 S2 V2 V2 V2 V2 V2 V2"), _pieces("S2 S2 V2 V2 V2 V2 V2 V2"), _pieces("S2 S2 V1 V1 V1 V1 V1 V1 V1 V1 V1 V1 S2")],
+    cha=[(8, 16), (8, 16), (12, 16)], brr=[_pieces("S8 S8")] * 2,
+    xju=[(), (), ()], yb=[4] * 3,
+    orp=[((0, 64, 5, (2, 3), ()), (64, 128, 4, (2, 3), _pieces("V4 V4 V4 V4")), (128, 192, k, (2, 3), _pieces("V4 V4 V4 V4"))) for k in (0, 0, 6)],
+    ox=[((0, 192, (0, 192)),)] * 3,
+    hop=[((0, 6), (6, 12), (12, 16))] * 2, snd=[((0, 6), (6, 12), (12, 16))] * 2,
+    jit=1500.0, moves=8, tries=6, iters=300, steps=18000, polish=2000, heat=0.02, flip=5, walk=0, stale=400, reach=20, blur=50.0, rest=45, kick=30.0, kicks=15, near=1.004, run=500, srow=[1] * 3, ynp=[1, 1, 0], csc=[(128, 192)] * 3, defer=[3, 3], two=[0, 0, 1], cm_at=1, hs_=[0] * 3, cool=0.001, more=15000, warm=0.004, walk2=0, fix=(), miles=(), mean=0.1, shy=300.0, slack=0.01)
 WAIT_ALL = True
 
 
@@ -102,7 +96,7 @@ def ext(name, idx):
 def n_of(d):
     if d[0] == "ind":
         return 16 * n_of(d[2])
-    return len(range(d[2], d[3], d[4]))
+    return len(range(d[2], d[3], abs(d[4])))
 
 
 def spans(d):
@@ -110,7 +104,7 @@ def spans(d):
         return []
     if d[0] == "ind":
         return spans(d[1]) + spans(d[2])
-    return [(d[1], d[2], d[3], d[4])]
+    return [(d[1], d[2], d[3], abs(d[4]))]
 
 
 def meet(x, y):
@@ -135,15 +129,15 @@ def transfers(o, me):
     return out
 
 
-def recv_needs(o, me):
-    return [(b, o["args"]) for b in range(NR) if b != me]
+def choose(o, e):
+    o.update(o["alts"][e]); o["eng"] = e
 
 
 def build(me):
     ops = []
     table = [1500.0]
 
-    def add(eng, kind, args, outs, ins, cost):
+    def add(eng, kind, args, outs, ins, cost, alts=None):
         rd, wr = [], []
         for o in outs:
             if o[0] == "ind":
@@ -153,6 +147,8 @@ def build(me):
         for i in ins:
             rd += spans(i)
         ops.append(dict(eng=eng, kind=kind, args=args, rd=rd, wr=wr, cost=cost))
+        if alts:
+            ops[-1]["alts"] = alts
 
     def vcost(out, in0, k):
         if out[0] == "ind":
@@ -160,6 +156,9 @@ def build(me):
         if in0[0] == "ind":
             return ("g", n_of(in0))
         return ("c", max(64, k * n_of(out)))
+
+    def scost(x, more=0):
+        return ("g", n_of(x) + 10) if x[0] == "ind" else ("c", max(64, n_of(x)) + more)
 
     def half(*aps):
         return 1.0 if any(wide(d) for d in aps) else 0.5
@@ -183,21 +182,45 @@ def build(me):
         add("V", "trn", (out, x), [out], [x], ("c", max(64, n_of(out))))
 
     def act(out, x, func=AF.Identity, bias=0.0, scale=1.0, accum=None):
-        c = ("g", n_of(x)) if x[0] == "ind" else ("c", max(64, n_of(x)) + (20 if accum else 0))
-        if func == AF.Sigmoid and table[0]:
-            c = ("c", c[1] + table[0]); table[0] = 0.0
-        add("S", "act", (out, x, func, bias, scale, accum), [out] + ([accum] if accum else []), [x, bias, scale], c)
+        add("S", "act", (out, x, func, bias, scale, accum), [out] + ([accum] if accum else []), [x, bias, scale], scost(x, 20 if accum else 0))
 
-    def step(out, x, at, sign=1.0):
-        act(out, x, AF.Sigmoid, bias=-256.0 * sign * at, scale=256.0 * sign)
-        if len(table) > 1:
-            ops[-1]["after"] = table[1]
-        else:
-            table.append(len(ops) - 1)
+    def either(on, forms, out, ins):
+        if out[1] in OPT["fix"] and "S" in on: on = on.replace("V", "")
+        alts = {e: dict(kind=k, args=x, cost=c) for e, (k, x, c) in forms.items() if e in on}
+        f = alts[on[0]]
+        add(on[0], f["kind"], f["args"], [out], ins, f["cost"], alts)
+
+    def lin(out, x, mul=1.0, plus=0.0, relu=False, on="SV"):
+        c = vcost(out, x, half(out, x))
+        if relu and _SB[out[1]][1] != u16: v = ("ts", (out, x, plus, 0.0, ALU.add, ALU.max), c)
+        elif mul == 1.0 and plus == 0.0: v = ("cp", (out, x), c)
+        elif mul == 1.0: v = ("ts", (out, x, plus, None, ALU.add, None), c)
+        elif plus == 0.0: v = ("ts", (out, x, mul, None, ALU.mult, None), c)
+        else: v = ("ts", (out, x, mul, plus, ALU.mult, ALU.add), c)
+        either(on, dict(V=v, S=("act", (out, x, AF.Relu if relu else AF.Identity, plus, mul, None), scost(x)),
+                        G=("sel", (out, x, [[0, n_of(x)]], ALU.is_ge, 0, 0, 0.0), ("c", 170 + 2 * n_of(out)))), out, [x, mul, plus])
+
+    def together(k):
+        some = ops[-k:]; del ops[-k:]
+        forms = [o.get("alts", {o["eng"]: o}) for o in some]
+        alts = {e: dict(kind="many", args=[(f[e]["kind"], f[e]["args"]) for f in forms], cost=("c", sum(f[e]["cost"][1] for f in forms)))
+                for e in forms[0] if all(e in f for f in forms)}
+        first = some[0]["eng"] if some[0]["eng"] in alts else "V"
+        ops.append(dict(alts[first], eng=first, alts=alts, rd=sum([o["rd"] for o in some], []), wr=sum([o["wr"] for o in some], [])))
+
+    def step(out, x, at, sign=1.0, on="SV"):
+        either(on, dict(V=("ts", (out, x, at, None, ALU.is_gt if sign > 0 else ALU.is_lt, None), vcost(out, x, half(out, x))),
+                        S=("act", (out, x, AF.Sigmoid, -256.0 * sign * at, 256.0 * sign, None), scost(x, table[0]))), out, [x])
+        if table[0]:
+            table[0] = 0.0; table.append(len(ops) - 1)
 
     def mm(lst, start=True, stop=True):
-        cyc = sum(max(min(64, n_of(l)), n_of(r)) * (4 if wide(r) else 1) for o, l, r in lst)
-        add("P", "mm", (lst, start, stop), [o for o, l, r in lst], [l for o, l, r in lst] + [r for o, l, r in lst], ("pe", cyc))
+        run = []; cyc = 0
+        for k, (o, l, r) in enumerate(lst):
+            run.append((o, l, r)); cyc += max(min(64, n_of(l)), n_of(r)) * (4 if wide(r) else 1)
+            if k == len(lst) - 1 or cyc >= OPT["run"]:
+                add("P", "mm", (run, start and k + 1 == len(run), stop and k == len(lst) - 1), [x[0] for x in run], [x[1] for x in run] + [x[2] for x in run], ("pe", cyc))
+                run = []; cyc = 0
 
     def iota(out, pat, base, cm=0):
         add("G", "iota", (out, pat, base, cm), [out], [], ("c", 130 + 2 * n_of(out)))
@@ -205,17 +228,11 @@ def build(me):
     def sel(out, x, pat, op, base, cm, other=0.0):
         add("G", "sel", (out, x, pat, op, base, cm, other), [out], [x], ("c", 170 + 2 * n_of(out)))
 
-    def move(out, x):
-        sel(out, x, [[0, n_of(x)]], ALU.is_ge, 0, 0)
+    def move(out, x, on="G"):
+        lin(out, x, on=on)
 
     def fill(out, v):
         iota(out, [[0, n_of(out)]], int(v))
-
-    def take(e, out, src):
-        if e == "S":
-            act(out, src)
-        else:
-            cp(out, src)
 
     def dma(q, pairs, extra=0.0):
         add(q, "dma", pairs, [o for o, i in pairs], [i for o, i in pairs], ("dma", len(pairs), extra))
@@ -223,151 +240,161 @@ def build(me):
     def wrap(out, z, src, c0, n, first=()):
         mm(list(first) + [(out, a(z, 15 - r, 143 - r), a(src, c0 + r, c0 + 16 * n, 16)) for r in range(16)])
 
+    def repeat(name, c0, n, d, on):
+        k = 1
+        while k < d:
+            j = min(k, d - k)
+            move(a(name, c0 + n * k, c0 + n * (k + j)), a(name, c0, c0 + n * j), on); k += j
+
     I = a("iw", 16, 144); BOW = a("bow", 0, 128)
-    pm, pr, pn, pm_, p32, p3, par, p8, pf, pm2, npar, pq, pm12, pm4, p16, pa, pb, pd = [a("pc", k, k + 1) for k in range(18)]
-    s4 = 4 * (me + 1); na = OPT["na"]
+    pm, pr, pn, pm_, p32, p3, par, p8, pgp, pm2, npar, pq, pm12, pm4, p16, pa, pb, pd, pn16, px, py, pz, n32, pt, pf, pf16, pu, pv, pw_, px2 = [a("pc", k, k + 1) for k in range(30)]
+    s4 = 4 * (me + 1); na = NA
     nat = [(q + me + 1) % NR for q in range(NR)]
+    y = lambda j0, j1: a("XJ", Y0 + j0, Y0 + j1)
 
     parts = OPT["x_parts"]
     for k, (c0, c1) in enumerate(parts):
-        dma("Y", [(a("X", OFF + 16 * c0, OFF + 16 * c1), ext("x0", (slice(None), slice(16 * c0, 16 * c1))))], 11.0 * c1 + (300.0 if k else 0.0))
-        if k == 0:
+        dma("Y", [(a("X", OFF + 16 * c0, OFF + 16 * c1), ext("x0", (slice(None), slice(16 * c0, 16 * c1))))], 11.0 * c1 + (300.0 if k > OPT["cm_at"] else 0.0))
+        if k == OPT["cm_at"]:
             dma("Y", [(a("cm", 0, S), ext("come", (slice(None), slice(0, S))))], 11.0 * c1 + 150.0)
             dma("Y", [(a("blk", 16, 144), ext("cd0", (slice(None), slice(None))))], 11.0 * c1 + 300.0)
     dma("Y", [(a("D", OFF + 1024, OFF + W), ext("dl0", (slice(None), slice(None))))], 3000.0)
     dma("Y", [(a("cm", S, 3 * S), ext("come", (slice(None), slice(S, 3 * S))))], 3300.0)
     dma("Y", [(a("ag", 16 * h, 16 * h + 16), ext("age", (slice(h, 8, 2), slice(None)))) for h in range(2)], 3300.0)
+    dma("Y", [(a("C", OFF, OFF + W, 1, slice(m, 128, 16)), ext("cd0", (slice(None), slice(None)))) for m in range(16)], 9000.0)
     for k in range(1, len(ops)):
         ops[k]["after"] = k - 1
-    ms(a("bv"), 21 * KD); ms(a("ones"), 1.0); ms(a("z1"), 0.0); ms(a("bk", 0, 128 if all(len(c) > 1 and c[0] * na <= 2048 for c in OPT["cha"]) else 256), -86016.0)
-    step(a("onesf"), a("bv", 0, S), 0.5)
+    ms(a("ones"), 1.0); ms(a("bv"), 21 * KD); ms(a("z1"), 0.0); ms(a("bk", 0, 192), -86016.0)
+    step(a("onesf", 0, 64), a("ones", 0, 64), 0.5, on="S")
+    fill(a("onesf", 64, S), 1.0)
     iota(a("pi"), [[16 - s4, 2], [s4, 2]], 0, 1)
-    sel(a("gi"), a("ones", 0, 9), [[-16, 9]], ALU.is_ge, 0, 1)
-    sel(a("z1", 15, 144, 16), a("gi"), [[16, 9]], ALU.is_ge, 15, -1)
-    sel(a("bow0"), a("ones", 0, 128), [[-16, 8], [0, 16]], ALU.is_ge, 0, 1)
-    sel(a("bow"), a("bow0"), [[16, 8], [0, 16]], ALU.is_ge, 15, -1)
-    iota(a("pw0"), [[0, 8], [32, 16]], 0)
-    sel(a("iw"), a("ones"), [[-1, 160]], ALU.is_equal, 16, 1)
-    iota(a("j16"), [[0, 12], [1, 16]], 0)
-    if not all(OPT["c_s"]) or 2 in OPT["c_s"]:
-        iota(a("coef", 0, na), [[61, 16], [0, na // 16]], 7)
-    if na < S and (not all(OPT["cb_s"]) or 2 in OPT["c_s"]):
-        iota(a("coef", NA, S), [[61, 16], [0, 4]], 7)
-    if 2 in OPT["c_s"]:
-        for u, v, k0 in ((0, na, 0), (na, S, 12))[:1 + (na < S)]:
-            for dst, src in (("cu1", "coef"), ("cu0", "onesf")):
-                sel(a(dst, u, v, 1, slice(0, 16)), a(src, u, v, 1, slice(0, 16)), [[0, 16], [1, (v - u) // 16]], ALU.is_equal, k0, -1)
     iota(a("c32"), [[0, 2], [32, 16]], 0)
-    sel(a("tri"), BOW, [[1, 128]], ALU.is_ge, 0, -1)
-    sel(a("tri2"), a("tri"), [[1, 128]], ALU.not_equal, 0, -1, 4096.0)
+    iota(a("j16"), [[0, 12], [1, 16]], 0)
     iota(a("kr"), [[1, 192]], 0)
+    iota(a("bow0"), [[1, 8], [0, 16]], 0)
     iota(a("rs", 0, 3), [[ST % 16, 3]], ST % 16)
     iota(a("rs", 3, 6), [[-(ST // 16), 3]], 127 - ST // 16)
-    n4 = (OFF + 1024) // 4
-    ms(a("D", 0, n4), -1)
-    dma("Y", [(a("D", n4 * k, n4 * k + n4), a("D", 0, n4)) for k in range(1, 4)], 3500.0)
+    iota(a("cfm"), [[122, 16]], 14)
+    iota(a("kp0"), [[-32, 6], [0, 2], [4096, 16]], Y0 - OFF)
+    iota(a("ka"), [[0, 12], [8192, 16]], -1)
+    iota(a("c4"), [[64, 3], [4, 4]], 0)
+    if any(OPT["hpe"]):
+        fill(a("tu"), 0.0)
+        for c0, k0, w in ((0, 0, NA // 16), (NA, NA // 16, (S - NA) // 16), (S, 0, S // 16)):
+            iota(a("cw0", 0, 16 * w), [[122, 16], [0, w]], 14)
+            sel(a("cw", c0, c0 + 16 * w), a("cw0", 0, 16 * w), [[0, 16], [1, w]], ALU.is_equal, k0, -1)
+            sel(a("cw", c0, c0 + 16 * w), a("cw", c0, c0 + 16 * w), [[0, 16], [1, w]], ALU.not_equal, k0 + 32, -1, 1.0)
+    fill(a("dp", 0, 16), 0.0); fill(a("dp", 144, 224), 0.0); fill(a("XJ", Y0 + CAP, W0), 0.0)
+    ms(a("D", D0, D0 + 16), -1)
     ts(a("pj", 0, 3), a("pi", 0, 3), 15, ALU.bitwise_and)
     ts(a("pj", 4, 5), a("pi", 0, 1), 31, ALU.bitwise_and)
     ts(a("pj", 5, 6), a("pi", 0, 1), 3, ALU.bitwise_and)
     ts(a("pj", 6, 7), a("pi", 0, 1), 4, ALU.arith_shift_right, 1, ALU.bitwise_and)
     ts(a("pj", 7, 8), a("pi", 0, 1), 3, ALU.arith_shift_right, 1, ALU.bitwise_and)
     ts(a("pj", 3, 4), a("pi", 0, 1), 1, ALU.bitwise_and)
-    cp(a("pc", 0, 8), a("pj"))
-    cp(pf, a("pi", 0, 1))
+    ts(a("pj", 8, 9), a("pi", 0, 1), 4, ALU.arith_shift_right)
+    together(7)
+    cp(a("pc", 0, 9), a("pj"))
+    cp(a("pc", 24, 26), a("pi", 0, 4, 3))
+    together(2)
+    ts(a("z1", 15, 144, 16), a("c32", 0, 9), 1.0 / 32, ALU.mult, pgp, ALU.is_equal)
+    ts(a("iw"), a("kr", 0, 160), pf16, ALU.is_equal)
+    ts(a("bow"), a("bow0"), pgp, ALU.is_equal)
+    sel(a("tri"), BOW, [[1, 128]], ALU.is_ge, 0, -1)
+    sel(a("tri2"), a("tri"), [[1, 128]], ALU.not_equal, 0, -1, 4096.0)
     ms(a("blk", 0, 16), 0); ms(a("blk", 144, 160), 0); ms(a("din", 0, 16), 0.0); ms(a("din", 272, 288), 0.0)
-    act(pm2, pm, scale=2.0, bias=2.0 * (S - 16 * s4) - 0.3125)
-    act(a("pw"), a("pw0"), bias=pm2)
+    together(4)
+    lin(pm2, pm, 2.0, 2.0 * (S - 16 * s4) - 0.3125, on="VS")
+    lin(a("pw"), a("j16", 0, 128), 32.0, pm2, on="VS")
     ts(p16, pm_, par, ALU.not_equal, 9.0, ALU.mult)
     ts(pa, p16, pm, ALU.add, 16.0, ALU.mult)
-    act(pq, p8, scale=-127.0, bias=pa)
-    act(npar, par, scale=-1.0, bias=1.0)
-    act(pb, par, scale=272.0, bias=pm)
-    act(pd, npar, scale=272.0, bias=pm)
-    act(pm12, pm, scale=na / 16.0)
-    if na < S:
-        act(pm4, pm, scale=4.0, bias=180.0)
-    ts(a("lq", 0, 8), a("c32", 0, 8), 1.0 / 16, ALU.mult, pq, ALU.add)
-    ts(a("lq", 8, 15), a("c32", 1, 8), 1.0 / 16, ALU.mult, pq, ALU.add)
-    ms(a("X", 0, OFF), 0.0); ms(a("XJ", W0, OFF), -1.0); ms(a("C", W0, OFF), -1.0); ms(a("CD", 0, 16), 0.0)
-    ms(a("Fp", 0, 1), 0.0); ms(a("acol", 0, 1), -0.375); ms(a("wv", 0, 6, 2), 1.0); ms(a("sg", 128, 144), -1.0); ms(a("thr", 0, 160, 5), 0.0)
-    nk = max(j1 - j0 for t in range(R) for j0, j1, e, by, bank in OPT["oc"][t])
-    ts(a("kp", 0, nk), a("j16", 0, nk), 0.5, ALU.is_lt, -16 * BIG, ALU.mult)
-    act(a("ni"), I, scale=-1.0)
-    act(a("ni32"), I, scale=-32.0)
-    act(a("i32"), I, scale=32.0)
-    act(a("ih"), I, scale=0.5)
-    act(a("bom"), BOW, scale=-2 * KD)
-    act(a("zk"), a("z1"), scale=8192.0)
-    act(a("nkr"), a("j16", 0, 128), scale=-1.0)
-    act(a("bof"), BOW)
-    act(a("iwe"), a("iw"), scale=npar)
-    act(a("iwo"), a("iw"), scale=par)
-    nh = 16 * max(c1 - c0 for c0, c1, e in OPT["hop"][0] + OPT["hop"][1])
-    nd = nh if all(OPT["e_s"][:2]) else S
-    ts(a("dm", 0, min(nd, NA)), a("j16", 0, min(nd, NA)), pm, ALU.is_equal)
-    if nd > NA:
-        move(a("dm", NA, S), a("dm", 0, S - NA))
+    lin(pq, p8, -127.0, pa)
+    lin(npar, par, -1.0, 1.0)
+    lin(pb, par, 272.0, pm)
+    lin(pm12, pm, na / 16.0)
+    lin(pm4, pm, 4.0, -12.0)
+    together(4)
+    lin(n32, p32, -1.0); lin(pn16, pn, 16.0, 15.0); lin(pt, par, float(S), BIG + W + S - 1); lin(pu, pm, 8.0, 208.0)
+    together(4)
+    lin(pd, npar, 272.0, pm); lin(py, pm, -15.75, pa); lin(pv, p3, -8.0, pu)
+    together(3)
+    lin(a("lq", 0, 8), a("c32", 0, 8), 1.0 / 16, pq)
+    lin(a("lq", 8, 15), a("c32", 1, 8), 1.0 / 16, pq)
+    together(2)
+    lin(pz, p3, 15.75, py)
+    lin(a("l4", 0, 12), a("c4"), plus=pz)
+    if any(OPT["two"]):
+        ts(px, pm_, par, ALU.not_equal, pv, ALU.mult)
+        lin(px2, pm, 16.0, px)
+        ts(a("lx", 0, 1), px2, 15.0, ALU.add, 479.0, ALU.min)
+        for k in range(3):
+            iota(a("lt2", 96 * k, 96 * k + 96), [[-32, 3], [0, 2], [4096, 16]], Y0 - OFF + 16 - 64 * k)
+        lin(a("kp2"), a("lt2"), plus=n32)
+        fill(a("lef2"), 0.0)
+    ms(a("X", 0, OFF), 0.0); ms(a("CD", 0, 16), 0.0); ms(a("acol", 0, 1), -0.75 * (1 - OPT["hpe"][0]))
+    together(3)
+    ms(a("XJ", W0, OFF), -1.0); ms(a("C", W0, OFF), -1); ms(a("Fp", 0, 1), 0.0); ms(a("wv", 0, 6, 2), 1.0)
+    together(4)
+    ms(a("sg", 128, 144), -1.0); ms(a("thr", 0, 160, 5), 0.0); ms(a("nq"), -0.25)
+    together(3)
+    lin(a("kp"), a("kp0"), plus=n32)
+    for some in ((("ni", I, -1.0), ("ni32", I, -32.0)), (("i32", I, 32.0), ("ih", I, 0.5)), (("bom", BOW, -2 * KD), ("zk", a("z1"), 8192.0)),
+                 (("nkr", a("j16", 0, 128), -1.0), ("idf", I, 1.0)), (("iwe", a("iw"), npar), ("iwo", a("iw"), par), ("bof", BOW, 1.0))):
+        for name, x, k in some:
+            lin(a(name), x, k)
+        together(len(some))
+    nh = 16 * max(c1 - c0 for c0, c1 in OPT["hop"][0] + OPT["hop"][1])
+    ts(a("dm", 0, nh), a("j16", 0, nh), pm, ALU.is_equal)
     ts(a("H", 0, nh), a("j16", 0, nh), pm, ALU.is_lt, BIG, ALU.mult)
-    act(a("H", S, S + nh), a("dm", 0, nh), scale=-BIG)
+    together(2)
+    for r in range(16 * any(OPT["xju"])):
+        lin(a("U", 128 * r, 128 * r + 128), a("bom"), a("dm", r, r + 1), on="VS")
+    lin(a("H", S, S + nh), a("dm", 0, nh), -BIG)
     tt(a("Mh", 0, nh), a("H", 0, nh), a("H", S, S + nh), ALU.add)
-    act(a("Mh", 15, nh, 16), a("Mh", 15, nh, 16), bias=2 * BIG)
-    act(a("idf"), I)
-    act(a("kw"), a("c32", 0, 16), scale=0.5, bias=pm)
-    act(a("ky"), a("kw", 0, 12), bias=float(CAP - OFF))
-    if na == S and not all(OPT["c_s"]):
-        ts(a("l16"), a("X", 0, 16), pm, ALU.add)
-    elif not all(OPT["c_s"]):
-        iota(a("l12"), [[0, 4], [4, 3]], 0)
-        act(a("uf"), a("l12"), bias=pm)
-        ts(a("uu"), a("uf"), 12.0, ALU.is_ge, -12.0, ALU.mult)
-        tt(a("l12"), a("uf"), a("uu"), ALU.add)
-        cp(a("l16", 0, 12), a("l12"))
-    if na < S and not all(OPT["cb_s"]):
-        ts(a("l16", 12, 16), a("bv", 0, 4), 4.0, ALU.min, p3, ALU.add)
-    if any(OPT["c_s"]) or any(OPT["cb_s"]):
-        iota(a("cfm"), [[61, 16]], 7)
-    if OPT["x2_s"] == 1:
-        cp(a("lid"), a("kw"))
-    ts(a("l15"), a("c32", 0, 12), 0.5, ALU.mult, 15.0, ALU.add)
-    if not all(OPT["e_s"][:2]):
-        ts(a("lc"), a("c32", 16 - s4, 32 - s4), 1.0 / 32, ALU.mult)
-    ts(a("lk", 0, na // 16), a("c32", 0, na // 16), 1.0 / 32, ALU.mult, pm12, ALU.add)
-    if na < S:
-        ts(a("lk", 12, 16), a("c32", 12, 16), 1.0 / 32, ALU.mult, pm4, ALU.add)
-    if any(OPT["xj_s"]):
-        for r in range(16):
-            ts(a("U", 128 * r, 128 * r + 128), a("bom"), a("dm", r, r + 1), ALU.mult, 0.5, ALU.mult)
-    ts(a("lm", 0, 16, 2), a("c32", 16 - s4, 32 - s4, 2), 0.5, ALU.mult, pb, ALU.add)
-    ts(a("lm", 1, 16, 2), a("c32", 17 - s4, 32 - s4, 2), 0.5, ALU.mult, pd, ALU.add)
-    ts(a("lr"), a("c32", 0, 2), 0.5, ALU.mult, pr, ALU.add)
-    ts(a("ln"), a("X", 0, 2), pn, ALU.add)
-    cp(a("lo1", 0, 1), p32)
-    act(a("kq"), a("c32", s4, s4 + 16), scale=0.5, bias=pm)
+    lin(a("Mh", 15, nh, 16), a("Mh", 15, nh, 16), plus=2 * BIG)
+    lin(a("kw"), a("c32", 0, 16), 0.5, pm)
+    lin(a("kq"), a("c32", s4, s4 + 16), 0.5, pm)
+    lin(a("l15"), a("c32", 0, 12), 0.5, 15.0)
+    lin(a("lr"), a("c32", 0, 2), 0.5, pr)
+    together(4)
+    lin(a("lk", 0, na // 16), a("c32", 0, na // 16), 1.0 / 32, pm12)
+    lin(a("lk", 12, 16), a("c32", 12, 16), 1.0 / 32, pm4)
+    lin(a("lm", 0, 16, 2), a("c32", 16 - s4, 32 - s4, 2), 0.5, pb)
+    together(3)
+    lin(a("lm", 1, 16, 2), a("c32", 17 - s4, 32 - s4, 2), 0.5, pd)
+    lin(a("ln"), a("X", 0, 2), plus=pn16)
+    lin(a("lo1", 0, 1), p32)
+    together(3)
     ts(a("mk", 0, 6, 2), a("rs", 0, 3), pm, ALU.is_gt, -64.0, ALU.mult)
     ts(a("mk", 1, 6, 2), a("rs", 0, 3), pm, ALU.is_le, -64.0, ALU.mult)
     ts(a("rs", 6, 9), a("rs", 3, 6), pf, ALU.is_equal, float(-W), ALU.mult)
-    act(a("wv", 1, 6, 2), a("rs", 6, 9), bias=16.0)
+    together(3)
+    lin(a("mb", 0, 6), a("mk", 0, 6), 256.0, -256 * 42.5)
+    lin(a("wv", 1, 6, 2), a("rs", 6, 9), plus=16.0)
+    together(2)
     for t in range(R):
-        act(a("kc", 12 * t, 12 * t + 12), a("kw", 0, 12), bias=float(-16 - OFF - S * t - 16 * ((ST * (t + 1)) // 16)))
-    cp(a("blkf"), a("blk"))
-    dma("Y", [(a("C", OFF, OFF + W, 1, slice(0, 128, 16)), a("blkf", 16, 144))], 1500.0)
-    dma("Y", [(a("C", OFF, OFF + W, 1, slice(m, 128, 16)), a("C", OFF, OFF + W, 1, slice(0, 128, 16))) for m in range(1, 16)], 7000.0)
-    cp(a("agf"), a("ag"))
-    trn(a("agt"), a("agf"))
-    act(a("agr"), ind(a("agt"), a("lr")))
+        lin(a("kc", 12 * t, 12 * t + 12), a("kw", 0, 12), plus=float(-16 - OFF - S * t - 16 * ((ST * (t + 1)) // 16)))
+    together(R)
+    bases = lambda t, pieces: {c0: HS * t + 80 * c0 + 64 * (c0 >= 6) + 64 * (c0 >= 12) for c0, c1 in pieces}
     for t in range(R - 1):
-        for k in range(1, 5):
-            act(a("thr", 80 * t + k, 80 * t + 80, 5), a("agr", 16 * t, 16 * t + 16), bias=BIG + W + S * t + S - 1, scale=-1.0)
+        for c0, c1 in OPT["hop"][t]:
+            h0 = bases(t, OPT["hop"][t])[c0]
+            lin(a("hs", h0 + 75, h0 + 80 * (c1 - c0), 80), a("kq", c0, c1), plus=BIG + W + S * t)
+        together(len(OPT["hop"][t]))
+    lin(a("agf"), a("ag"), -1.0, pt)
+    trn(a("agt"), a("agf"))
+    lin(a("agr"), ind(a("agt"), a("lr")))
+    for k in range(1, 5):
+        lin(a("thr", k, 160, 5), a("agr"))
+    together(4)
     trn(a("bti", 0, 128), a("blk", 16, 144))
     trn(a("bti", 128, 288), a("blk"))
-    ts(a("offp"), ind(a("bti"), a("lq", 0, 8)), 16.0, ALU.add)
-
-    for o in ops[table[1] + 1:]:
-        if o["eng"] == "S": o["after"] = table[1]
+    lin(a("offp"), ind(a("bti"), a("lq", 0, 8)), plus=16.0, on="VS")
 
     for t in range(R):
         lo = S * t; B = W + lo; L = OFF + lo; BB = OFF + B; K0 = 16 + lo
         last = t == R - 1
+        na = S if last else NA
         cs = (ST * (t + 1)) // 16; n1 = 128 - cs
 
         def turned(c0, c1, cs=cs):
@@ -380,24 +407,23 @@ def build(me):
             act(a(pn_, 128, 128 + c1 - c0), a(pn_, 0, c1 - c0), AF.Square, scale=0.25)
             tt(a("wh", c0, c1), a(pn_, 128, 128 + c1 - c0), a("pw", c0, c1), ALU.add)
             ts(a("whm", c0, c1), a("wh", c0, c1), 1, ALU.arith_shift_right, 255, ALU.bitwise_and)
-            cp(a("who", c0, c1), a("whm", c0, c1))
+            lin(a("who", c0, c1), a("whm", c0, c1), on="VS" if t == 0 else "SV")
         if t > 0:
-            for q in range(NR):
-                act(a("ps6", 64 * q, 64 * q + 64), a("cm", S * t + 64 * nat[q], S * t + 64 * nat[q] + 64), bias=-0.25, scale=0.5)
+            mm([(a("ps6", 0, S), I, a("nq"))] + [(a("ps6", 64 * q, 64 * q + 64), a("ih"), a("cm", S * t + 64 * nat[q], S * t + 64 * nat[q] + 64)) for q in range(NR)])
             fill(a("XJ", L - S, L), -1.0)
             fill(a("CD", K0 - S, K0), 1.0)
         for q in range(4):
             n = 512 if q < 3 else 512 - S
-            if q in OPT["xj_s"][t]:
-                mm([(a("ps%d" % q), I, a("X", L + 512 * q, L + 512 * q + 512))], True, False)
-            else:
-                mm([(a("ps%d" % q), I, a("bv"))] + [(a("ps%d" % q, 0, n), a("i32"), a("XJ", L + 512 * q, L + 512 * q + n))] * (t > 0), True, False)
+            if q // 2 in OPT["xju"][t]:
+                mm([(a("ps%d" % q, 64 * k, 64 * k + 64), I, a("X", L + 1024 * (q // 2) + 8 * (q % 2) + k, L + 1024 * (q // 2 + 1), 16)) for k in range(8)], True, False)
+                continue
+            mm([(a("ps%d" % q), I, a("bv"))] + [(a("ps%d" % q, 0, n), a("i32"), a("XJ", L + 512 * q, L + 512 * q + n))] * (t > 0), True, False)
         for c0, c1, e in OPT["die"][t]:
             if e == "S":
                 mm([(a("ps7", 0, 16 * (c1 - c0)), a("ni"), a("X", L + 16 * c0, L + 16 * c1))], True, False)
-        was = [] if t == 0 else [(a("ps5", w, w + v - u), a("i32"), a("Lf", w0 + u + 16 - u0, w0 + v + 16 - u0))
-                                 for u0, v0, w0 in turned(16, 128, (ST * t) // 16) for u, v, w in turned(u0 - 16, v0 - 16)]
-        mm([(a("ps5", 0, 129), I, a("X", CAP, CAP + 129)), (a("ps5", 0, 129, 128), I, a("mk", 2 * t, 2 * t + 2))] + was, True, False)
+        if t > 0:
+            mm([(a("ps5", 0, 128), I, a("X", CAP, CAP + 128))] +
+               [(a("ps5", u - 16, v - 16), a("i32"), a("Lf", w, w + v - u)) for u, v, w in turned(16, 128, (ST * t) // 16)], True, False)
         if t > 0 and OPT["sg2"][t]:
             for k, (c0, c1) in enumerate(OPT["sgp"][t]):
                 mm([(a("ps%d" % (OPT["sg2"][t] if k else 4), c0, c1), a("i32"), a("sg", 16 + c0, 16 + c1))], True, False)
@@ -405,51 +431,41 @@ def build(me):
             mm([(a("ps4", 0, 128), a("i32"), a("sg", 16, 144))], True, False)
         if t == 0:
             for q in range(NR):
-                ts(a("xi", 64 * q, 64 * q + 64), a("cm", 64 * nat[q], 64 * nat[q] + 64), 0.5, ALU.mult, -0.25, ALU.add)
+                lin(a("xi", 64 * q, 64 * q + 64), a("cm", 64 * nat[q], 64 * nat[q] + 64), 0.5, -0.25, on="VS")
         else:
             z = S * (t - 1)
             tt(a("xi", NA, S), a("Z", z + NA, z + S), a("ps6", NA, S), ALU.add)
             add("V", "recv", t - 1, [a("Z", z, z + NA)], [a("Z", z, z + NA)], ("c", 0))
             tt(a("xi", 0, NA), a("Z", z, z + NA), a("ps6", 0, NA), ALU.add)
-        if OPT["x2_s"] == 0:
-            cp(a("x2"), a("xi"))
-        elif OPT["x2_s"] == 1:
-            act(a("x2"), ind(a("xi"), a("lid")))
-        else:
-            act(a("x2"), a("xi"))
-        if OPT["c_s"][t] == 2:
-            low = slice(0, 16)
-            mm([(a("ps6", 256 + r, 384, 16, low), a("x2", r, S, 16), a("z1", 15, 143, 16)) for r in range(16)])
-            act(a("tq", 0, 128, 1, low), a("ps6", 256, 384, 1, low), AF.Square, scale=0.25)
+            ops.extend(held_back)
+        lin(a("x2"), a("xi"))
+        if OPT["hpe"][t]:
+            low, high, both = slice(0, 16), slice(32, 48), slice(0, 48)
+            for p in (high, low):
+                mm([(a("ps6", 256 + r, 384, 16, p), a("x2", r, S, 16), a("z1", 15, 143, 16)) for r in range(16)])
+            act(a("tq", 0, 128, 1, high), a("ps6", 256, 384, 1, high), AF.Square, scale=0.25)
             act(a("tu", 0, 128, 1, low), a("ps6", 256, 384, 1, low))
-            ts(a("ti", 0, 128, 1, low), a("tq", 0, 128, 1, low), 0.5, ALU.mult, -0.375, ALU.add)
-            cp(a("th", 0, 128, 1, low), a("ti", 0, 128, 1, low))
+            if OPT["hs_"][t]:
+                act(a("ti", 0, 128, 1, high), a("tq", 0, 128, 1, high), scale=0.5, bias=-0.375)
+                act(a("tu", 0, 128, 1, high), a("ti", 0, 128, 1, high), scale=2.0)
+            else:
+                ts(a("tu", 0, 128, 1, high), a("tq", 0, 128, 1, high), -0.75, ALU.add, 2.0 ** 24 + 2 * W, ALU.add)
+            mm([(a("ps6", 0, S), a("tu", 0, 128, 1, both), a("cw", S * last, S * last + S, 1, both))])
+            lin(a("ati"), a("ps6", 0, S), plus=a("acol", t, t + 1))
         else:
             wrap(a("ps6", 256, 272), "z1", "x2", 0, 16)
             act(a("asq"), a("ps6", 256, 272), AF.Square, scale=0.25)
             act(a("au"), a("ps6", 256, 272))
-            ts(a("ah"), a("asq"), 0.5, ALU.mult, a("acol", t, t + 1), ALU.add)
-            if OPT["c_s"][t] or OPT["cb_s"][t]:
-                cp(a("ahf"), a("ah"))
+            ts(a("ahf"), a("asq"), a("acol", t, t + 1), ALU.add, 2.0 ** 24 + 2 * W, ALU.add)
 
-        def hashes(i0, n, on_s):
+        def hashes(i0, n):
             w = n // 16; k0 = i0 // 16
-            if OPT["c_s"][t] == 2:
-                low = slice(0, 16); o = a("ps6", 0, n)
-                mm([(o, a("tu", 0, 128, 1, low), a("cu1", i0, i0 + n, 1, low)), (o, a("th", 0, 128, 1, low), a("cu0", i0, i0 + n, 1, low))])
-                ts(a("ati", i0, i0 + n), o, a("acol", t, t + 1), ALU.add, 0.375, ALU.add)
-            elif on_s:
-                for k in range(w):
-                    act(a("at", i0 + k, i0 + n, w), a("cfm"), bias=a("ahf", k0 + k, k0 + k + 1), scale=a("au", k0 + k, k0 + k + 1))
-                cp(a("ati", i0, i0 + n), a("at", i0, i0 + n))
-            else:
-                tt(a("at", i0, i0 + n), ind(a("au", k0 // 8 * 8, 16), a("l16", k0, k0 + w)), a("coef", i0, i0 + n), ALU.mult)
-                tt(a("ati", i0, i0 + n), ind(a("ah", k0 // 8 * 8, 16), a("l16", k0, k0 + w)), a("at", i0, i0 + n), ALU.add)
-            ts(a("atm", i0, i0 + n), a("ati", i0, i0 + n), W - 1, ALU.bitwise_and)
-            cp(a("offa", i0, i0 + n), a("atm", i0, i0 + n))
+            for k in range(w * (1 - OPT["hpe"][t])):
+                lin(a("ati", i0 + k, i0 + n, w), a("cfm"), a("au", k0 + k, k0 + k + 1), a("ahf", k0 + k, k0 + k + 1))
+            ts(a("atm", i0, i0 + n), a("ati", i0, i0 + n), 1, ALU.arith_shift_right, W - 1, ALU.bitwise_and)
+            lin(a("offa", i0, i0 + n), a("atm", i0, i0 + n))
 
-        both = OPT["c_s"][t] == 2 and OPT["both"][t]
-        hashes(0, S if both else na, OPT["c_s"][t])
+        hashes(0, na)
         for c0, c1, e in OPT["die"][t]:
             o = a("CD", K0 + 16 * c0, K0 + 16 * c1); n = 16 * (c1 - c0)
             if e == "S":
@@ -466,231 +482,274 @@ def build(me):
                 u = c0 if OPT["sg2"][t] else 0
                 act(a("sg", u, c1), a(pn2, u, c1), AF.Sign, bias=-10.5 if t == 0 else 21.5)
         for q in range(4):
-            if q in OPT["xj_s"][t]:
-                mm([(a("ps%d" % q, r, 512, 16), a("U", 128 * r, 128 * r + 128), a("sg", 32 * q, 32 * q + 32)) for r in range(16)], False, True)
-                act(a("XJ", L + 512 * q, L + 512 * q + 512), a("ps%d" % q), bias=-KD)
-            else:
-                mm([(a("ps%d" % q), a("bom"), a("CD", K0 + 512 * q, K0 + 512 * q + 512))], False, True)
-                tt(a("XJ", L + 512 * q, L + 512 * q + 512), a("ps%d" % q), a("X", L + 512 * q, L + 512 * q + 512), ALU.min)
-        for c0, c1, e in OPT["par"][t]:
-            take(e, a("pg", 16 * c0, 16 * c1), ind(a("CD", 0, K0 + 16 * c1), a("offp", c0, c1)))
-        cuts = [0] + [c for c in OPT["parw"][t] if c < cs - 8] + [cs + 1, cs] + [c for c in OPT["parw"][t] if c > cs + 8] + [128]
-        runs = [(u, v) for u, v in zip(cuts, cuts[1:]) if u < v]
-        own = [(a("ps5", w, w + v - u), a("ni32"), a("sg", u, v)) for u, v, w in turned(0, 128)]
+            if q // 2 in OPT["xju"][t]:
+                rows = range(8 * (q % 2), 8 * (q % 2) + 8); h = q // 2
+                mm([(a("ps%d" % q, 64 * (r % 8), 64 * (r % 8) + 64), a("U", 128 * r, 128 * r + 128), a("sg", 64 * h, 64 * h + 64)) for r in rows], False, True)
+                for r in rows:
+                    lin(a("XJ", L + 1024 * h + r, L + 1024 * (h + 1), 16), a("ps%d" % q, 64 * (r % 8), 64 * (r % 8) + 64), plus=-2 * KD)
+                together(8)
+                continue
+            mm([(a("ps%d" % q), a("bom"), a("CD", K0 + 512 * q, K0 + 512 * q + 512))], False, True)
+            tt(a("XJ", L + 512 * q, L + 512 * q + 512), a("ps%d" % q), a("X", L + 512 * q, L + 512 * q + 512), ALU.min)
+        for c0, c1 in OPT["par"][t]:
+            lin(a("pg", 16 * c0, 16 * c1), ind(a("CD", 0, K0 + 16 * c1), a("offp", c0, c1)))
+        cuts = [0] + list(OPT["parw"][t]) + [128]
+        runs = list(zip(cuts, cuts[1:]))
+        own = [(a("ps5", 0, 128), a("ni32"), a("sg", 0, 128))]
         for k, (u, v) in enumerate(runs):
-            end = k == len(runs) - 1; w = u - cs if u >= cs else n1 + u
+            end = k == len(runs) - 1
             if end and not OPT["sg_last"][t]:
                 mm(own, False, False)
-            mm([(a("ps5", w, w + v - u), a("z1", 15 - r, 143 - r), a("pg", 16 * u + r, 16 * v, 16)) for r in range(16)], False, end and not OPT["sg_last"][t])
+            mm([(a("ps5", u, v), a("z1", 15 - r, 143 - r), a("pg", 16 * u + r, 16 * v, 16)) for r in range(16)], t == 0 and k == 0, end and not OPT["sg_last"][t])
         if OPT["sg_last"][t]:
             mm(own, False, True)
-        if OPT["f_s"][t]:
-            step(a("F", 0, 129), a("ps5", 0, 129), 42.5)
-        else:
-            ts(a("F", 0, 129), a("ps5", 0, 129), 42.5, ALU.is_ge)
+        step(a("F", 1, n1), a("ps5", cs + 1, 128), 42.5)
+        step(a("F", n1, 128), a("ps5", 0, cs), 42.5)
+        for k in range(2):
+            o = a("F", 128 * k, 128 * k + 1); x = a("ps5", cs, cs + 1); mk, mb = a("mk", 2 * t + k, 2 * t + k + 1), a("mb", 2 * t + k, 2 * t + k + 1)
+            either("SV", dict(V=("ts", (o, x, mk, 42.5, ALU.add, ALU.is_gt), ("c", 64)), S=("act", (o, x, AF.Sigmoid, mb, 256.0, None), ("c", 64))), o, [x, mk, mb])
+        together(4)
         mm([(a("ps4", 0, 128), I, a("nkr"))], True, False)
         scan(a("Fp", 1, 130), a("ones", 0, 129), a("F", 0, 129), ALU.mult, ALU.add)
         mm([(a("ps4", 0, 128), a("Fp", 1, 129), BOW)], False, True)
         mm([(a("ps5", 256, 386), BOW, a("Fp", 0, 130)), (a("ps5", 256, 385), a("tri"), a("F", 0, 129))])
-        act(a("Q", 0, 130), a("ps5", 256, 386))
+        lin(a("Q", 0, 130), a("ps5", 256, 386))
         ts(a("uf"), a("kw", 0, 12), a("Q", 129, 130), ALU.is_ge, -4096.0, ALU.mult)
         tt(a("uu"), a("uf"), a("kc", 12 * t, 12 * t + 12), ALU.max)
-        cs_ = OPT["cnt_s"][t]
-        if len(cs_) < 12:
-            cp(a("vb"), a("ps4", 0, 128))
+        lin(a("vb"), a("ps4", 0, 128), on="VS")
         for k in range(12):
-            if k in cs_:
-                step(a("M", 128 * k, 128 * k + 128), a("vb") if len(cs_) < 12 else a("ps4", 0, 128), 16 * k + 0.5, -1.0)
-            else:
-                ts(a("M", 128 * k, 128 * k + 128), a("vb"), 16 * k + 0.5, ALU.is_lt)
-        if OPT["one_m"]:
-            for k in range(12):
-                mm([(a("ps5", k, k + 17, 16), a("M", 128 * k, 128 * k + 128), a("wv", 2 * t, 2 * t + 2))], k == 0, False)
-            cp(a("cu"), a("ps5", 0, 12))
-            o = a("ps5", 16, 28)
-        else:
-            for k in range(12):
-                mm([(a("ps5", k, k + 1), a("M", 128 * k, 128 * k + 128), a("wv", 2 * t, 2 * t + 1))], k == 0, k == 11)
-            cp(a("cu"), a("ps5", 0, 12))
-            o = a("ps4", 0, 12)
-            mm([(a("ps4", k, k + 1), a("M", 128 * k, 128 * k + 128), a("wv", 2 * t + 1, 2 * t + 2)) for k in range(12)], True, False)
-        mm([(o, a("idf"), a("uu"))], False, False)
+            step(a("M", 128 * k, 128 * k + 128), a("vb"), 16 * k + 0.5, -1.0, on="VS" if k < 8 else "SV")
+        for k in range(12):
+            mm([(a("ps5", k, k + 17, 16), a("M", 128 * k, 128 * k + 128), a("wv", 2 * t, 2 * t + 2))], k == 0, k == 11)
+        lin(a("cu"), a("ps5", 0, 12), on="VS")
+        tt(a("uf"), a("uu"), a("ps5", 16, 28), ALU.add)
+        o = a("ps4", 0, 12)
+        mm([(o, a("idf"), a("uf"))], True, False)
         tt(a("cmp2"), ind(a("Q", 0, 130), a("cu")), a("kr"), ALU.is_le)
         mm([(o, a("z1", 15 - r, 143 - r), a("cmp2", r, CAP, 16)) for r in range(16)], False, True)
-        ts(a("offo"), o, float(L + 16 * cs), ALU.add)
+        lin(a("offd"), o, plus=float(L + 16 * cs - D0), relu=True, on="VS")
+        lin(a("offo"), o, plus=float(L + 16 * cs), on="VS")
+        together(2)
 
-        def arrivals(i0, n, pieces, ends, rep, on_s, t0, banks, cut=99):
+        def judge(e, o, src, rec, many, d, k, banks):
+            n = n_of(rec)
+            if e == "S":
+                gq = a("g2", 512 * k, 512 * k + n * d); pn2 = "ps%d" % banks[k]
+                mm([(a(pn2, n * j, n * j + n), a("ni"), rec) for j in range(d)], True, False)
+                act(gq, src)
+                mm([(a(pn2, 0, n * d), I, gq)], False, True)
+                step(o, a(pn2, 0, n * d), -0.5)
+            else:
+                tt(o, src, rec if d == 1 else many, ALU.is_ge)
+
+        def arrivals(i0, n, pieces, ends, rep, t0, banks, cut=99):
             w = n // 16; k0 = i0 // 16; g0 = 16 * i0
             m0 = 0; k = 0; done = 0
             for p, (e, d) in enumerate(pieces):
                 if p == cut:
                     yield
                     banks = OPT["bkl"][t]
-                src = ind(a("XJ", L, BB), a("offa", i0 + w * m0, i0 + w * (m0 + d))); o = a("cmpa", g0 + n * m0, g0 + n * (m0 + d))
-                if e == "S":
-                    gq = a("g2", 512 * k, 512 * k + n * d); pn2 = "ps%d" % banks[k]; k = 1 - k
-                    mm([(a(pn2, n * j, n * j + n), a("ni"), a("x2", i0, i0 + n)) for j in range(d)], True, False)
-                    act(gq, src)
-                    mm([(a(pn2, 0, n * d), I, gq)], False, True)
-                    step(o, a(pn2, 0, n * d), -0.5)
-                else:
-                    tt(o, src, a("xi", i0, i0 + n) if d == 1 else a(rep, 0, n * d), ALU.is_ge)
+                judge(e, a("cmpa", g0 + n * m0, g0 + n * (m0 + d)), ind(a("XJ", L, BB), a("offa", i0 + w * m0, i0 + w * (m0 + d))),
+                      a("x2", i0, i0 + n), a(rep, 0, n * d), d, k, banks)
+                k = 1 - k if e == "S" else k
                 m0 += d
                 if m0 in ends:
                     o = a("ps%d" % banks[2 + ends.index(m0) % 2], 0, w * (m0 - done))
                     wrap(o, "zk", "cmpa", g0 + n * done, w * (m0 - done), [(o, I, a("bk", 0, w * (m0 - done)))])
                     tt(a("lfa", i0 + w * done, i0 + w * m0), o, a("atm", i0 + w * done, i0 + w * m0), ALU.min)
                     done = m0
-            src = ("lfa", i0); h = n // 2
-            while h >= w:
-                tt(a("tr", t0, t0 + h), a(src[0], src[1], src[1] + h), a(src[0], src[1] + h, src[1] + 2 * h), ALU.max)
-                src = ("tr", t0); t0 += h; h //= 2
-            top = a("tr", src[1], src[1] + w)
-            ts(a("a1", k0, k0 + w), top, float(lo), ALU.add, -1.0, ALU.max)
+            top = a("top", i0 + 15, i0 + n, 16)
+            if last:
+                src = ("lfa", i0); h = n // 2
+                while h >= w:
+                    tt(a("tr", t0, t0 + h), a(src[0], src[1], src[1] + h), a(src[0], src[1] + h, src[1] + 2 * h), ALU.max)
+                    src = ("tr", t0); t0 += h; h //= 2
+                for k in range(3):
+                    lin(a("E", s4 % 16 + 16 * k, s4 % 16 + 16 * k + 16), a("tr", src[1], src[1] + w), plus=lo + 1.0, relu=True, on="VS")
+                together(3)
+                trn(a("E", 64, 96), a("E", 16, 48))
+                lin(a("E", 96, 112), ind(a("E", 64, 96), a("lo1", 0, 1)), plus=-1.0)
+                dma("Y", [(ext("yc", (slice(None), slice(W, W + S))), a("E", 96, 112))])
+            else:
+                lin(a("din", 16 + i0, 16 + i0 + n), ind(a("lfa", i0, i0 + n), a("lk", k0, k0 + w)), plus=float(lo))
+                scan(a("top", i0, i0 + n), a("ka", 0, n), a("din", 16 + i0, 16 + i0 + n), ALU.min, ALU.max)
             if not last:
-                ts(a("offh", k0, k0 + w), top, float(K0), ALU.add, 15.0, ALU.max)
+                lin(a("offh", k0, k0 + w), top, plus=16.0)
 
-        if any(e == "V" and d > 1 for e, d in OPT["arr"][t]):
-            move(a("xa", 0, na), a("x2", 0, na)); move(a("xa", na, 2 * na), a("x2", 0, na))
+        def copies(name, i0, n, pieces, on="GVS"):
+            d = max([d for e, d in pieces if e == "V"] + [1])
+            if d > 1:
+                move(a(name, 0, n), a("x2", i0, i0 + n), on); move(a(name, n, 2 * n), a("x2", i0, i0 + n), on)
+                repeat(name, 0, 2 * n, (d + 1) // 2, on)
+
+        copies("xa", 0, na, OPT["arr"][t])
         for q in range(NR):
             move(a("X", BB + 64 * nat[q], BB + 64 * nat[q] + 64), a("x2", 64 * q, 64 * q + 64))
-        leaving = arrivals(0, na, OPT["arr"][t], OPT["cha"][t], "xa", OPT["c_s"][t], 0, OPT["bka"][t], OPT["cut"][t])
+        leaving = arrivals(0, na, OPT["arr"][t], OPT["cha"][t], "xa", 0, OPT["bka"][t], OPT["cut"][t])
         next(leaving, None)
 
         def rest():
-            if na < S and any(e == "V" for e, d in OPT["brr"][t]):
-                move(a("xb", 0, 64), a("x2", NA, S)); move(a("xb", 64, 128), a("x2", NA, S)); move(a("xb", 128, S), a("xb", 0, 128))
-            if na < S:
-                if not both:
-                    hashes(NA, S - NA, OPT["cb_s"][t])
-                next(arrivals(NA, S - NA, OPT["brr"][t], (16,), "xb", OPT["cb_s"][t], 180, OPT["bkb"][t]), None)
-            if last or OPT["e_s"][t] == 2:
-                take(OPT["t_e"][t][0], a("E", 0, 32), ind(a("a1"), a("ln")))
-                trn(a("E", 32, 64), a("E", 0, 32))
-                take(OPT["t_e"][t][1], a("E", 64, 80), ind(a("E", 32, 64), a("lo1", 0, 1)))
-                if last:
-                    dma("Y", [(ext("yc", (slice(None), slice(W, W + S))), a("E", 64, 80))])
-                else:
-                    row = lambda m: a("C", BB, BB + S, 1, slice(m, 128, 16))
-                    dma("Y", [(row(0), a("E", 64, 80))], 500.0)
-                    ops[-1]["behind"] = sent[0]
-                    dma("Y", [(row(m), row(0)) for m in range(1, 16)], 2000.0)
-                    ops[-1]["later"] = ops[-2]["later"] = True
-                return
-            if OPT["e_s"][t]:
-                for k in range(16):
-                    kk = (k - s4) % 16
-                    act(a("E", 16 * k, 16 * k + 16), a("dm", 0, 16), scale=a("a1", kk, kk + 1))
-            else:
-                tt(a("E"), ind(a("a1"), a("lc")), a("dm"), ALU.mult)
-            mm([(a("ps6", 0, S), a("bof"), a("E"))])
-            act(a("C", BB, BB + S), a("ps6", 0, S))
+            copies("xb", NA, S - NA, OPT["brr"][t])
+            hashes(NA, S - NA)
+            next(arrivals(NA, S - NA, OPT["brr"][t], (16,), "xb", 180, OPT["bkb"][t]), None)
+            lin(a("E", 0, 32), ind(a("top"), a("ln")))
+            trn(a("E", 32, 64), a("E", 0, 32))
+            o = a("Ei", 0, 16) if t < R - 2 else a("E", 64, 80)
+            lin(o, ind(a("E", 32, 64), a("lo1", 0, 1)))
+            row = lambda m: a("C" if t < R - 2 else "CF", BB, BB + S, 1, slice(m, 128, 16))
+            dma("Y", [(row(0), o)], 500.0)
+            ops[-1]["behind"] = sent[0]; ops[-1]["later"] = True
+            if t < R - 2:
+                dma("Y", [(row(m), row(0)) for m in range(1, 16)], 2000.0)
+                ops[-1]["later"] = True
 
         if last:
-            if not (OPT["late"] or OPT["cut"][t] < 99):
-                rest()
             dma("Y", [(ext("yx", (slice(None), slice(W, W + S))), a("X", BB, BB + S)),
                       (ext("ya", (slice(None), slice(W, W + S))), a("onesf", 0, S, 1, slice(0, 8)))], 10000.0)
-            act(a("aw"), a("sg", 0, 128), bias=0.5, scale=-0.5)
-            trn(a("awt"), a("aw"))
-            dma("Y", [(ext("ya", (slice(h, 8, 2), slice(512 * b, 512 * b + 512))), a("awt", 32 * b + 16 * h, 32 * b + 16 * h + 16))
-                      for b in range(4) for h in range(2)], 10000.0)
-        ts(a("offw"), ind(a("D", 0, BB), a("offo")), 16.0, ALU.add)
-        take(OPT["y_e"][t], a("y"), ind(a("X", 0, BB), a("offo")))
-        mm([(a("ps0", 0, CAP), I, a("y")), (a("ps0", 256, 256 + CAP), a("ih"), a("y"))])
-        move(a("XJ", CAP, 2 * CAP), a("y"))
-        if OPT["dp_s"][t]:
-            act(a("dp"), ind(a("D", 0, BB), a("offo")))
-        else:
-            ts(a("dp"), a("offw"), -16.0, ALU.add)
-        for j0, j1, e in OPT["og"][t]:
-            take(e, a("G", 16 * j0, 16 * j1), ind(a("XJ", W0, BB), a("offw", j0, j1)))
-        for j0, j1, e, by, bank in OPT["oc"][t]:
+            dma("Y", [(a("awx"), a("XJ", L, BB, 1, slice(0, 128, 16)))], 1500.0)
+            step(a("aw"), a("awx"), -0.5)
+            dma("Y", [(ext("ya", (slice(None), slice(0, W))), a("aw"))], 8000.0)
+        orp = OPT["orp"][t]
+        s1 = min([p[0] for p in orp if p[4]] + [CAP]); fw = CAP - s1
+        if s1:
+            lin(a("offw", 0, s1), ind(a("D", D0, BB), a("offd", 0, s1 // 16)), plus=16.0, relu=True)
+            lin(a("dq", 0, s1), a("offw", 0, s1), plus=-16.0, on="VS")
+        if fw:
+            lin(a("dp", 16, 16 + fw), ind(a("D", D0, BB), a("offd", s1 // 16, 12)), on="VS")
+            trn(a("dt", 0, fw), a("dp", 16, 16 + fw))
+            trn(a("dt", fw, 2 * fw + 32), a("dp", 0, fw + 32))
+        lin(y(0, CAP), ind(a("X", 0, BB), a("offo")))
+        yb = "ps%d" % OPT["yb"][t]
+        if not OPT["ynp"][t]:
+            mm([(a(yb, 256, 256 + CAP), a("ih"), y(0, CAP))])
+        for j0, j1, bank, by, pieces in orp:
             n = j1 - j0; o = a("ps%d" % bank, j0, j1)
-            if e == "S":
+            if not pieces and OPT["srow"][t]:
+                for h in range(2):
+                    mm([(a("ps%d" % by[h], n * m, n * m + n), a("ni"), y(j0, j1)) for m in range(8)], True, False)
+                for h in range(n // 32):
+                    act(a("G", 16 * j0 + 512 * h, 16 * j0 + 512 * h + 512), ind(a("XJ", W0, BB), a("offw", j0 + 32 * h, j0 + 32 * h + 32)))
+                mm([(o, I, a("bk", 0, n))], True, False)
+                for h in range(2):
+                    k = 16 * j0 + 8 * n * h
+                    mm([(a("ps%d" % by[h], n * m, n * m + n), I, a("G", 16 * j0 + 8 * h + m, 16 * j1, 16)) for m in range(8)], False, True)
+                    step(a("cmpo", k, k + 8 * n), a("ps%d" % by[h], 0, 8 * n), -0.5)
+                    mm([(o, a("zk", 15 - m - 8 * h, 143 - m - 8 * h), a("cmpo", k + n * m, k + n * m + n)) for m in range(8)], False, h == 1)
+                dv = a("dq", j0, j1)
+            elif not pieces:
                 for h in range(n // 32):
                     k = 16 * j0 + 512 * h; pn2 = "ps%d" % by[h % len(by)]
-                    mm([(a(pn2, m, 512, 16), a("ni"), a("y", j0 + 32 * h, j0 + 32 * h + 32)) for m in range(16)], True, False)
+                    mm([(a(pn2, m, 512, 16), a("ni"), y(j0 + 32 * h, j0 + 32 * h + 32)) for m in range(16)], True, False)
+                    act(a("G", k, k + 512), ind(a("XJ", W0, BB), a("offw", j0 + 32 * h, j0 + 32 * h + 32)))
                     mm([(a(pn2), I, a("G", k, k + 512))], False, True)
                     step(a("cmpo", k, k + 512), a(pn2), -0.5)
                 mm([(o, I, a("bk", 0, n))] + [(o, a("zk", 15 - m, 143 - m), a("cmpo", 16 * j0 + m, 16 * j1, 16)) for m in range(16)])
+                dv = a("dq", j0, j1)
             else:
+                k = (j0 - s1) // 16; w = n // 16
+                pick = a("lq", 0, 8) if n == 128 else a("l4", k, k + w)
+                lin(a("offw", j0, j1), ind(a("dt", 0, 2 * fw + 32), pick), plus=16.0, relu=True, on="VS")
+                d = max([d for e, d in pieces if e == "V"] + [1]); rep = ("XJ", Y0 + j0)
+                if j1 < CAP and d > 1:
+                    rep = ("yr", 4 * (j0 - s1)); move(a("yr", rep[1], rep[1] + n), y(j0, j1), "VSG"); move(a("yr", rep[1] + n, rep[1] + 2 * n), y(j0, j1), "VSG")
+                    repeat("yr", rep[1], 2 * n, (d + 1) // 2, "VSG")
+                else:
+                    repeat("XJ", rep[1], n, d, "GVS")
                 mm([(o, I, a("bk", 0, n))], True, False)
-                for h in range(0, 16, by):
-                    for m in range(h, h + by):
-                        tt(a("cmpo", 16 * j0 + n * m, 16 * j0 + n * m + n), a("G", 16 * j0 + m, 16 * j1, 16), a("ps0", j0, j1), ALU.is_ge)
-                    mm([(o, a("zk", 15 - m, 143 - m), a("cmpo", 16 * j0 + n * m, 16 * j0 + n * m + n)) for m in range(h, h + by)], False, h + by == 16)
-            tt(a("left", j0, j1), o, a("dp", j0, j1), ALU.min)
-            trn(a("lt", j0, j1), a("left", j0, j1))
-            scan(a("ls", j0, j1), a("kp", 0, n), a("lt", j0, j1), ALU.add, ALU.max)
-            src = ind(a("ls", j0, j1), a("l15", 0, n // 16))
-            if j0 in OPT["bb_s"][t]:
-                act(a("bb", j0, j1), src, AF.Relu, bias=1.0)
-            else:
-                ts(a("bb", j0, j1), src, 1.0, ALU.add, 0.0, ALU.max)
+                m0 = 0; k = 0
+                for e, d in pieces:
+                    g0 = 16 * j0 + n * m0
+                    judge(e, a("cmpo", g0, g0 + n * d), ind(a("XJ", W0, BB), a("offw", j0 + w * m0, j0 + w * (m0 + d))),
+                          y(j0, j1), a(rep[0], rep[1], rep[1] + n * d), d, k, by)
+                    k = 1 - k if e == "S" else k
+                    mm([(o, a("zk", 15 - m, 143 - m), a("cmpo", 16 * j0 + n * m, 16 * j0 + n * m + n)) for m in range(m0, m0 + d)], False, m0 + d == 16)
+                    m0 += d
+                dv = a("dp", 16 + j0 - s1, 16 + j1 - s1)
+            k = j0 // 64; lf = a("lef2", 16 + 80 * k, 80 + 80 * k) if OPT["two"][t] else a("left", j0, j1)
+            tt(lf, o, dv, ALU.min)
+            trn(a("lt", j0, j1), lf)
+            if OPT["two"][t]:
+                trn(a("lt2", 96 * k, 96 * k + 96), a("lef2", 80 * k, 80 * k + 96))
+                together(2)
+            scan(a("ls", j0, j1), a("kp", j0, j1), a("lt", j0, j1), ALU.min, ALU.max)
+            if OPT["two"][t]:
+                scan(a("ls", CAP + 96 * k, CAP + 96 * k + 96), a("kp2", 96 * k, 96 * k + 96), a("lt2", 96 * k, 96 * k + 96), ALU.min, ALU.max)
+                together(2)
+            lin(a("bb", j0, j1), ind(a("ls", j0, j1), a("l15", 0, n // 16)), plus=1.0 * last, relu=last)
             trn(a("br", j0, j1), a("bb", j0, j1))
-            ts(ind(a("C", 0, BB), a("offo", j0 // 16, j1 // 16)), a("br", j0, j1), 1.0, ALU.mult, -1.0, ALU.add)
+            if j1 not in OPT["csc"][t]:
+                continue
+            j0 = ([0] + list(OPT["csc"][t]))[OPT["csc"][t].index(j1)]
+            if last:
+                ts(ind(a("CF", 0, BB), a("offo", j0 // 16, j1 // 16)), a("br", j0, j1), 1.0, ALU.mult, -1.0, ALU.add)
+            else:
+                cp(ind(a("C", 0, BB), a("offo", j0 // 16, j1 // 16)), a("br", j0, j1))
         for j0, j1, k0 in OPT["ox"][t]:
             c0, c1 = j0 // 16, j1 // 16
-            mm([(a("ps4", c0 + ih, c1, 2), a("iwo" if ih else "iwe", 16 + 16 * (ih - gh), 144 + 16 * (ih - gh)), a("ls", j0 + 16 * gh + 15, j1, 32))
-                for ih in range(2) for gh in range(2)])
-            tt(a("w1", c0, c1), a("ps4", c0, c1), a("ky", c0, c1), ALU.max)
-            ts(a("offx", c0, c1), a("w1", c0, c1), float(OFF - CAP), ALU.add)
-            act(a("xh", j0, j1), ind(a("XJ", CAP, BB), a("offx", c0, c1)), bias=-0.25, scale=0.5)
-            tt(a("yn", j0, j1), a("xh", j0, j1), a("ps0", 256 + j0, 256 + j1), ALU.add)
+            if OPT["two"][t]:
+                act(a("offx"), ind(a("ls"), a("lx", 0, 1)), AF.Abs, bias=float(OFF - Y0))
+            else:
+                mm([(a("ps4", c0 + ih, c1, 2), a("iwo" if ih else "iwe", 16 + 16 * (ih - gh), 144 + 16 * (ih - gh)), a("ls", j0 + 16 * gh + 15, j1, 32))
+                    for ih in range(2) for gh in range(2)])
+                act(a("offx", c0, c1), a("ps4", c0, c1), AF.Abs, bias=float(OFF - Y0))
+            if OPT["ynp"][t]:
+                lin(a("xw", j0, j1), ind(a("XJ", Y0, BB), a("offx", c0, c1)))
+                mm([(a(yb, 256 + j0, 256 + j1), a("ih"), x) for x in (y(j0, j1), a("xw", j0, j1))])
+                lin(a("yn", j0, j1), a(yb, 256 + j0, 256 + j1), plus=-0.25)
+            else:
+                lin(a("xh", j0, j1), ind(a("XJ", Y0, BB), a("offx", c0, c1)), 0.5, -0.25)
+                tt(a("yn", j0, j1), a("xh", j0, j1), a(yb, 256 + j0, 256 + j1), ALU.add)
             for k in range(len(k0) - 1):
                 cp(ind(a("X", 0, BB), a("offo", k0[k] // 16, k0[k + 1] // 16)), a("yn", k0[k], k0[k + 1]))
         next(leaving, None)
         if last:
-            if OPT["late"] or OPT["cut"][t] < 99:
-                rest()
-            dma("Y", [(ext("yc", (slice(None), slice(0, W))), a("C", L, BB, 1, slice(0, 128, 16)))], 300.0)
+            dma("Y", [(ext("yc", (slice(None), slice(0, W))), a("CF", L, BB, 1, slice(0, 128, 16)))], 300.0)
             dma("Y", [(ext("yx", (slice(None), slice(0, 1024))), a("X", L, L + 1024))], 700.0)
             dma("S", [(ext("yx", (slice(None), slice(1024, W))), a("X", L + 1024, BB))], 700.0)
             break
-        dma("Y", [(a("blkf", 16, 144), a("C", L, BB, 1, slice(0, 128, 16)))], 200.0)
-        trn(a("bt", 0, 128), a("blkf", 16, 144))
-        trn(a("bt", 128, 288), a("blkf"))
-        ts(a("offp", 0, 112), ind(a("bt"), a("lq", 8, 15)), 16.0, ALU.add)
+        dma("Y", [(a("blk", 16, 144), a("C", L, BB, 1, slice(0, 128, 16)))], 200.0)
+        trn(a("bti", 0, 128), a("blk", 16, 144))
+        trn(a("bti", 128, 288), a("blk"))
+        lin(a("offp", 0, 112), ind(a("bti"), a("lq", 8, 15)), plus=16.0, relu=True)
 
         def queries(pieces, snd):
-            base = {c0: 80 * c0 + 64 * k + (128 if c0 == 12 else 0) for k, (c0, c1, e) in enumerate(pieces)}
-            for c0, c1, e in pieces:
+            base = bases(t, pieces)
+            for c0, c1 in pieces:
                 h0 = base[c0]; n = 80 * (c1 - c0)
-                act(a("hs", h0 + 75, h0 + n, 80), a("kq", c0, c1), bias=BIG + B)
-                act(a("hs", h0 + 91, h0 + n + 16, 80), a("a1", c0, c1), bias=BIG)
+                lin(a("hs", h0 + 91, h0 + n + 16, 80), a("top", 16 * c0 + 15, 16 * c1, 16), plus=BIG)
             for k in range(3):
-                for c0, c1, e in pieces:
+                for c0, c1 in pieces:
                     p0, p1 = S * k + 16 * c0, S * k + 16 * c1; h0 = base[c0] + 16 * (k + 2); n = 80 * (c1 - c0)
-                    take(e[k], a("H", p0, p1), ind(a("C", W0, BB), a("offh", 16 * k + c0, 16 * k + c1)))
+                    lin(a("H", p0, p1), ind(a("C", W0, BB), a("offh", 16 * k + c0, 16 * k + c1)))
                     scan(a("hs", h0, h0 + n, 5), a("H", p0, p1), a("Mh", 0, p1 - p0), ALU.min, ALU.add, BIG)
                     if k < 2:
-                        ts(a("offh", 16 * k + 16 + c0, 16 * k + 16 + c1), a("hs", h0 + 75, h0 + n, 80), 16 - BIG, ALU.add)
-            for c0, c1, e in pieces:
+                        lin(a("offh", 16 * k + 16 + c0, 16 * k + 16 + c1), a("hs", h0 + 75, h0 + n, 80), plus=16 - BIG, relu=True)
+            for c0, c1 in pieces:
                 five = a("hs", base[c0] + 75, base[c0] + 80 * (c1 - c0) + 60, 16)
                 tt(a("q1", 5 * c0, 5 * c1), five, a("thr", 80 * t + 5 * c0, 80 * t + 5 * c1), ALU.is_lt)
                 scan(a("q2", 5 * c0, 5 * c1), a("q1", 5 * c0, 5 * c1), five, ALU.mult, ALU.max)
-                ts(a("offq", c0, c1), a("q2", 5 * c0 + 4, 5 * c1, 5), 16 - BIG, ALU.add)
-            for c0, c1, e in snd:
-                o = a("sb" if c0 < 12 else "Z", S * t + 16 * c0, S * t + 16 * c1); src = ind(a("X", W0, BB + S), a("offq", c0, c1))
-                if e == "S":
-                    act(o, src, scale=0.5)
-                else:
-                    ts(o, src, 0.5, ALU.mult)
+                lin(a("offq", c0, c1), a("q2", 5 * c0 + 4, 5 * c1, 5), plus=16 - BIG)
+            for c0, c1 in snd:
+                lin(a("sb" if c0 < 12 else "Z", S * t + 16 * c0, S * t + 16 * c1), ind(a("X", W0, BB + S), a("offq", c0, c1)), 0.5)
 
         queries([p for p in OPT["hop"][t] if p[0] < 12], [p for p in OPT["snd"][t] if p[0] < 12])
         add("G", "send", t, [], [a("sb", S * t, S * t + NA)], ("c", 300))
         sent = [len(ops) - 1]
+        if t == R - 2:
+            ts(a("blkf"), a("blk", 16, 144), -1.0, ALU.max)
+            dma("Y", [(a("CF", L, BB, 1, slice(0, 128, 16)), a("blkf"))], 500.0)
+            ops[-1]["later"] = True; ops[-1]["behind"] = sent[0]
         rest()
         queries([p for p in OPT["hop"][t] if p[0] >= 12], [p for p in OPT["snd"][t] if p[0] >= 12])
-        ts(a("offp", 112, 128), ind(a("a1"), a("ln", 0, 1)), 16.0, ALU.add)
+        lin(a("offp", 112, 128), ind(a("top"), a("ln", 0, 1)), plus=16.0)
         mm([(a("ps5", 0, 129), BOW, a("Fp", 0, 129)), (a("ps5", 0, 129), a("tri2"), a("F", 0, 129))])
         step(a("Lf", 0, 129), a("ps5", 0, 129), 4096 + CAP - 0.5)
+        k0 = len(ops)
         cp(ind(a("D", 0, BB), a("offo")), a("left"))
-        act(a("din", 16, 272), ind(a("lfa"), a("lk")))
         trn(a("dout", 0, 256), a("din", 16, 272))
         trn(a("dout", 256, 544), a("din"))
-        ts(a("D", BB, BB + S), ind(a("dout"), a("lm")), float(lo), ALU.add, -1.0, ALU.max)
+        lin(a("D", BB, BB + S), ind(a("dout"), a("lm")))
+        held_back = ops[k0 + OPT["defer"][t]:]; del ops[k0 + OPT["defer"][t]:]
         if t == 0:
             act(a("junk", 0, 16), a("sg", 0, 16), accum=a("acc", 0, 1))
             act(a("junk", 16, 128), a("sg", 16, 128), accum=a("acc", 1, 2))
@@ -699,16 +758,15 @@ def build(me):
             act(a("junk"), a("sg", 0, 128), accum=a("acc", 2, 3))
             tt(a("ar"), a("acc", 2, 3), a("acc", 1, 2), ALU.subtract)
         mm([(a("ps7", 0, 1), a("bof"), a("ar"))])
-        ts(a("acol", t + 1, t + 2), a("ps7", 0, 1), 0.5, ALU.mult, (1024.0 if t == 0 else 128.0) - 0.375, ALU.add)
-    cuts = [0] + [j for j, o in enumerate(ops) if o["kind"] == "recv"] + [len(ops)]
-    for t in range(R):
-        for x, m, y, n in OPT["first"][t]:
-            nth = lambda name, k: [j for j in range(cuts[t], cuts[t + 1]) if ops[j]["wr"] and ops[j]["wr"][0][0] == name and ops[j]["eng"] in "VS"][k]
-            ops[nth(y, n)]["after"] = nth(x, m)
+        lin(a("acol", t + 1, t + 2), a("ps7", 0, 1), plus=(2048.0 if t == 0 else 256.0) - 0.75 * (1 - OPT["hpe"][t + 1]))
+    for o in ops[table[1] + 1:]:
+        f = o.get("alts", {}).get("S", o)
+        if any(x[2] in (AF.Sigmoid, AF.Square) for k, x in (f["args"] if f["kind"] == "many" else [(f["kind"], f["args"])]) if k == "act"):
+            o.setdefault("after", table[1])
     return ops
 
 
-def link(ops):
+def link(ops, loose=False):
     hist = {}
     deps = []
     sends = {}
@@ -723,6 +781,8 @@ def link(ops):
                         continue
                     p = ops[i]
                     same = p["eng"] == o["eng"] and p["kind"] not in ("dma", "send") and o["kind"] not in ("dma", "send")
+                    if loose and (len(p.get("alts", ())) > 1 or len(o.get("alts", ())) > 1):
+                        same = False
                     if bank and same and o["eng"] != "P" and not hit:
                         continue
                     need = (not same) or (hit and w and not acc_w) or (WAIT_ALL and o["eng"] != "P" and hit)
@@ -744,15 +804,18 @@ def link(ops):
     return deps
 
 
+def held(c, e, prm):
+    if c[0] == "c": return max(c[1] * prm["cyc"] * (prm["pool"] if e == "G" else 1.0), 1e-3)
+    if c[0] == "g": return 50 + c[1] * prm["cyc"] * prm["g"]
+    if c[0] == "sc": return 50 + c[1] * prm["cyc"] * prm["sc"]
+    if c[0] == "pe": return c[1] * prm["pe"]
+    return 60.0 * c[1]
+
+
 def sizes(ops, prm):
     out = []
     for o in ops:
-        c = o["cost"]
-        if c[0] == "c": v = c[1] * prm["cyc"] * (prm["pool"] if o["eng"] == "G" else 1.0)
-        elif c[0] == "g": v = 60 + c[1] * prm["cyc"] * prm["g"]
-        elif c[0] == "sc": v = 60 + c[1] * prm["cyc"] * prm["sc"]
-        elif c[0] == "pe": v = c[1] * prm["pe"]
-        else: v = 60.0 * c[1]
+        c = o["cost"]; v = held(c, o["eng"], prm)
         out.append((v, v + (prm["dma"] + c[2] if c[0] == "dma" and not ("later" in o and prm.get("part")) else 0.0)))
     return out
 
@@ -763,8 +826,8 @@ def gap(ops, i, j, need, prm):
     return prm["same"] if ops[i]["eng"] == ops[j]["eng"] else prm["cross"]
 
 
-def schedule(ops, deps, prm, iters, steps, start=None, seed=7):
-    n = len(ops); eng = [o["eng"] for o in ops]
+def schedule(ops, deps, prm, iters, steps, start=None, seed=7, moves=0, heat=None):
+    n = len(ops); eng = [o["eng"] for o in ops]; heat = heat or OPT["heat"]
     anc = [0] * n; keep = []
     for j in range(n):
         up = 0
@@ -774,69 +837,34 @@ def schedule(ops, deps, prm, iters, steps, start=None, seed=7):
         anc[j] = up
 
     def graph(p):
-        sz = sizes(ops, p); d = [max(s[0], 1e-3) for s in sz]
-        lag = [[(i, (sz[i][1] if deps[j][i] is not False else d[i]) + gap(ops, i, j, deps[j][i], p) + 1e-3) for i in keep[j]] for j in range(n)]
-        return d, [s[1] for s in sz], lag
+        sz = sizes(ops, p); more = [s[1] - s[0] for s in sz]
+        lag = [[(i, (more[i] if deps[j][i] is not False else 0.0) + gap(ops, i, j, deps[j][i], p) + 1e-3) for i in keep[j]] for j in range(n)]
+        return [s[0] for s in sz], more, lag, [{e: held(f["cost"], e, p) for e, f in o.get("alts", {}).items()} for o in ops]
 
-    def place(seq, pred, first, d):
+    def place(seq, pred, first, pick=None):
         busy = {e: ([], []) for e in "VSPGY"}
-        start = [0.0] * n
+        fin = [0.0] * n
         for j in seq:
-            t = first[j]
+            t0 = first[j]
             for i, l in pred[j]:
-                if start[i] + l > t: t = start[i] + l
-            bs, be = busy[eng[j]]; k = len(be)
-            while k > 0 and be[k - 1] > t: k -= 1
-            while k < len(bs) and t + d[j] > bs[k]:
-                if be[k] > t: t = be[k]
-                k += 1
-            start[j] = t; bs.insert(k, t); be.insert(k, t + d[j])
-        return start
+                if fin[i] + l > t0: t0 = fin[i] + l
+            got = None
+            for e, dj in (alt0[j].items() if pick and alt0[j] else ((eng[j], d0[j]),)):
+                t = t0; bs, be = busy[e]; k = len(be)
+                while k > 0 and be[k - 1] > t: k -= 1
+                while k < len(bs) and t + dj > bs[k]:
+                    if be[k] > t: t = be[k]
+                    k += 1
+                v = t + dj + (pick[j] if pick and e == "V" else 0.0)
+                if got is None or v < got[0]: got = (v, e, t, dj, k)
+            v, e, t, dj, k = got
+            if e != eng[j]: put(j, e)
+            fin[j] = t + dj; busy[e][0].insert(k, t); busy[e][1].insert(k, t + dj)
+        return fin
 
-    def span(seq, gr):
-        d, full, lag = gr; free = {e: 0.0 for e in "VSPGY"}; st = [0.0] * n; end = 0.0
-        for j in seq:
-            t = free[eng[j]]
-            for i, l in lag[j]:
-                if st[i] + l > t: t = st[i] + l
-            st[j] = t; free[eng[j]] = t + d[j]
-            if t + full[j] > end: end = t + full[j]
-        return end
-
-    others = [graph(dict(prm, **v)) for v in VARIANTS]
-    d, full, lag = others[0]
-    back = [[] for j in range(n)]
-    for j in range(n):
-        for i, l in lag[j]: back[i].append((j, d[j] + l - d[i]))
-    tail = [full[j] - d[j] for j in range(n)]; zero = [0.0] * n
-    level = list(full)
-    for j in range(n - 1, -1, -1):
-        for i, l in lag[j]: level[i] = max(level[i], l + level[j])
-    key = [-v for v in level]
-    x = seed; best = None; ref = None
-    if start:
-        ref = [span(start, gr) for gr in others]; best = (0.0, start)
-    for it in range(iters):
-        st = place(sorted(range(n), key=lambda k: (key[k], k)), lag, zero, d)
-        for rep in range(2):
-            sb = place(sorted(range(n), key=lambda k: (-st[k], -k)), back, tail, d)
-            st = place(sorted(range(n), key=lambda k: (-sb[k] - d[k], k)), lag, zero, d)
-        seq = sorted(range(n), key=lambda k: (st[k], k))
-        first = span(seq, others[0])
-        if best is None or first < 1.01 * best[3]:
-            tm = [first] + [span(seq, gr) for gr in others[1:]]
-            if ref is None: ref = tm
-            score = sum(u / v for u, v in zip(tm, ref))
-            if best is None or score < best[0]: best = (score, seq, st, first)
-        key = list(best[2])
-        for k in range(OPT["moves"]):
-            x = (x * 1103515245 + 12345) % 2147483648; j = (x >> 8) % n
-            x = (x * 1103515245 + 12345) % 2147483648
-            key[j] += OPT["jit"] * (x / 1073741824.0 - 1.0)
-        for j in range(n):
-            for i, l in lag[j]:
-                if key[j] <= key[i]: key[j] = key[i] + 1e-3
-    slim = others; full0 = others[0][1]
+    def put(j, e):
+        eng[j] = e
+        for g in graphs: g[0][j] = g[3][j][e]
 
     def run(seq, p0, old, most=None):
         lastop = {}
@@ -845,45 +873,210 @@ def schedule(ops, deps, prm, iters, steps, start=None, seed=7):
                 lastop[eng[seq[k]]] = seq[k]
                 if len(lastop) == 5: break
         out = []; tail_seq = seq[p0:]
-        for (d, full, lag), o in zip(slim, old):
-            st = list(o); free = {e: (st[lastop[e]] + d[lastop[e]] if e in lastop else 0.0) for e in "VSPGY"}
+        for (d, more, lag, alt), o in zip(graphs, old):
+            fin = list(o); free = {e: (fin[lastop[e]] if e in lastop else 0.0) for e in "VSPGY"}
             for j in tail_seq:
                 e = eng[j]; t = free[e]
                 for i, l in lag[j]:
-                    u = st[i] + l
+                    u = fin[i] + l
                     if u > t: t = u
-                st[j] = t; free[e] = t + d[j]
-            if most and not out and max(st[j] + full[j] for j in ends) > most:
+                free[e] = fin[j] = t + d[j]
+            if most and not out and max(fin[j] + more[j] for j in ends) > most:
                 return None
-            out.append(st)
+            out.append(fin)
         return out
 
+    graphs = [graph(dict(prm, **v)) for v in VARIANTS]
+    d0, more0, lag0, alt0 = graphs[0]
+    back = [[] for j in range(n)]
+    for j in range(n):
+        for i, l in lag0[j]: back[i].append((j, l))
     ends = [j for j in range(n) if not back[j]]
-    value = lambda sts: sum(max(st[j] + g[1][j] for j in ends) / v for st, g, v in zip(sts, slim, ref))
-    seq = best[1]; sts = run(seq, 0, [zero] * len(slim)); cur = value(sts); best = (cur, seq); chain = None
+    zero = [0.0] * n
+    spans_of = lambda fins: [max(f[j] + g[1][j] for j in ends) + OPT["mean"] * sum(f) / n + sum(w * max(f[j] for j in js) for w, js in miles)
+                             for f, g in zip(fins, graphs)]
+    cut = [j for j, o in enumerate(ops) if o["kind"] == "recv"] + [n]
+    miles = [(w, [j for j in range(u, v) if ops[j]["wr"] and ops[j]["wr"][0][0] == name and ops[j]["eng"] != "G"])
+             for name, w in OPT["miles"] for u, v in zip([0] + cut, cut)]
+    miles = [m for m in miles if m[1]]
+    level = [d0[j] + more0[j] for j in range(n)]
+    for j in range(n - 1, -1, -1):
+        for i, l in lag0[j]: level[i] = max(level[i], d0[i] + l + level[j])
+    key = [-v for v in level]
+    x = seed; best = None; ref = None; now = None; shy = [OPT["shy"]] * n
+    if start:
+        ref = spans_of(run(start, 0, [zero] * len(graphs))); best = (0.0, start, list(eng))
+    for it in range(iters):
+        fin = place(sorted(range(n), key=lambda k: (key[k], k)), lag0, zero, shy)
+        for rep in range(2):
+            sb = place(sorted(range(n), key=lambda k: (d0[k] - fin[k], -k)), back, more0)
+            fin = place(sorted(range(n), key=lambda k: (-sb[k], k)), lag0, zero, shy)
+        seq = sorted(range(n), key=lambda k: (fin[k] - d0[k], k))
+        fins = run(seq, 0, [zero] * len(graphs), now and 1.015 * now[3])
+        if fins:
+            tm = spans_of(fins)
+            if ref is None: ref = tm
+            score = sum(u / v for u, v in zip(tm, ref))
+            if now is None or score < now[0] + OPT["slack"] * (1.0 - it / iters): now = (score, [fin[k] - d0[k] for k in range(n)], list(shy), tm[0])
+            if best is None or score < best[0]: best = (score, seq, list(eng))
+        key = list(now[1]); shy = list(now[2])
+        for k in range(OPT["moves"]):
+            x = (x * 1103515245 + 12345) % 2147483648; j = (x >> 8) % n
+            x = (x * 1103515245 + 12345) % 2147483648
+            key[j] += OPT["jit"] * (x / 1073741824.0 - 1.0)
+            x = (x * 1103515245 + 12345) % 2147483648; j = (x >> 8) % n
+            x = (x * 1103515245 + 12345) % 2147483648
+            shy[j] = OPT["shy"] + OPT["jit"] * (x / 1073741824.0 - 1.0)
+        for j in range(n):
+            for i, l in lag0[j]:
+                if key[j] <= key[i]: key[j] = key[i] + 1e-3
+    for j, e in enumerate(best[2]):
+        if e != eng[j]: put(j, e)
+
+    def lines(seq):
+        prv = [-1] * n; nxt = [-1] * n; lastq = {}
+        for j in seq:
+            if eng[j] in lastq: prv[j] = lastq[eng[j]]; nxt[prv[j]] = j
+            lastq[eng[j]] = j
+        return prv, nxt
+
+    def walk(prv, nxt):
+        need = [len(lag0[j]) + (prv[j] >= 0) for j in range(n)]
+        seq = [j for j in range(n) if not need[j]]; r = [0.0] * n; rj = [0.0] * n
+        for j in seq:
+            f = r[j] + d0[j]
+            for k, l in back[j]:
+                if f + l > rj[k]:
+                    rj[k] = f + l
+                    if f + l > r[k]: r[k] = f + l
+                need[k] -= 1
+                if not need[k]: seq.append(k)
+            k = nxt[j]
+            if k >= 0:
+                if f > r[k]: r[k] = f
+                need[k] -= 1
+                if not need[k]: seq.append(k)
+        q = list(more0); qj = list(more0)
+        for j in reversed(seq):
+            f = q[j] + d0[j]
+            for i, l in lag0[j]:
+                if f + l > qj[i]:
+                    qj[i] = f + l
+                    if f + l > q[i]: q[i] = f + l
+            i = prv[j]
+            if i >= 0 and f > q[i]: q[i] = f
+        return seq, r, rj, q, qj
+
+    if moves:
+        prv, nxt = lines(best[1])
+        rest = [0] * n; top = None; vi = 0
+        backs = [[[] for j in range(n)] for g in graphs]
+        for g, bk in zip(graphs, backs):
+            for j in range(n):
+                for i, l in g[2][j]: bk[i].append((j, l))
+        for it in range(moves):
+            seq, r, rj, q, qj = walk(prv, nxt)
+            span = max(r[j] + d0[j] + q[j] for j in ends)
+            if top is None or span < top[5][vi] * OPT["near"]:
+                tm = [max(f[j] + g[1][j] for j in ends) for f, g in zip(run(seq, 0, [zero] * len(graphs)), graphs)]
+                score = sum(u / v for u, v in zip(tm, ref))
+                if top is None or score < top[0] - 1e-9: top = (score, seq, list(eng), it, False, tm)
+            if it - top[3] > OPT["stale"]:
+                for j, e in enumerate(top[2]):
+                    if e != eng[j]: put(j, e)
+                prv, nxt = lines(top[1])
+                top = top[:3] + (it, True, top[5])
+                vi = (vi + 1) % len(graphs)
+                d0, more0, lag0, alt0 = graphs[vi]; back = backs[vi]
+                continue
+            line = {e: [] for e in "VSPGY"}
+            for j in seq: line[eng[j]].append(j)
+            pick = None
+            for v in seq:
+                if r[v] + d0[v] + q[v] < span - 1e-6: continue
+                a0, b0 = prv[v], nxt[v]
+                if not ((a0 >= 0 and r[a0] + d0[a0] >= r[v] - 1e-6) or (b0 >= 0 and d0[b0] + q[b0] >= q[v] - 1e-6)): continue
+                qs = max([q[s] for s, l in back[v]] + [-1.0]); rp = max([r[p] for p, l in lag0[v]] + [-1.0])
+                found = []
+                t = r[a0] + d0[a0] if a0 >= 0 else 0.0; w = b0; mid = []
+                while w >= 0 and len(mid) < OPT["reach"] and qs < d0[w] + q[w] and not anc[w] >> v & 1:
+                    s = rj[w] if rj[w] > t else t; t = s + d0[w]; mid.append((w, t))
+                    b = nxt[w]; u = max(qj[v], d0[b] + q[b] if b >= 0 else 0.0); est = max(rj[v], t) + d0[v] + u; u += d0[v]
+                    for k, f in reversed(mid):
+                        if qj[k] > u: u = qj[k]
+                        if f + u > est: est = f + u
+                        u += d0[k]
+                    found.append((est, eng[v], w, b)); w = b
+                t = d0[b0] + q[b0] if b0 >= 0 else 0.0; w = a0; mid = []
+                while w >= 0 and len(mid) < OPT["reach"] and rp < r[w] + d0[w] and not anc[v] >> w & 1:
+                    s = qj[w] if qj[w] > t else t; t = s + d0[w]; mid.append((w, t))
+                    b = prv[w]; u = max(rj[v], r[b] + d0[b] if b >= 0 else 0.0); est = max(qj[v], t) + d0[v] + u; u += d0[v]
+                    for k, f in reversed(mid):
+                        if rj[k] > u: u = rj[k]
+                        if f + u > est: est = f + u
+                        u += d0[k]
+                    found.append((est, eng[v], b, w)); w = b
+                for e, dv in alt0[v].items():
+                    if e == eng[v]: continue
+                    b = -1
+                    for w in line[e] + [-1]:
+                        if b >= 0 and (qs >= d0[b] + q[b] or anc[b] >> v & 1): break
+                        if w < 0 or (rp < r[w] + d0[w] and not anc[v] >> w & 1):
+                            found.append((max(rj[v], r[b] + d0[b] if b >= 0 else 0.0) + dv + max(qj[v], d0[w] + q[w] if w >= 0 else 0.0), e, b, w))
+                        b = w
+                for m in found:
+                    x = (x * 1103515245 + 12345) % 2147483648
+                    val = m[0] + OPT["blur"] * (OPT["kick"] if it - top[3] < OPT["kicks"] and top[4] else 1.0) * x / 2147483648.0
+                    if (rest[v] <= it or m[0] < top[5][vi] - 1e-6) and (pick is None or val < pick[0]): pick = (val, v) + m[1:]
+            if pick is None:
+                rest = [0] * n
+                continue
+            val, v, e, a1, b1 = pick
+            if prv[v] >= 0: nxt[prv[v]] = nxt[v]
+            if nxt[v] >= 0: prv[nxt[v]] = prv[v]
+            if e != eng[v]: put(v, e)
+            prv[v] = a1; nxt[v] = b1
+            if a1 >= 0: nxt[a1] = v
+            if b1 >= 0: prv[b1] = v
+            x = (x * 1103515245 + 12345) % 2147483648
+            rest[v] = it + OPT["rest"] + (x >> 8) % OPT["rest"]
+        for j, e in enumerate(top[2]):
+            if e != eng[j]: put(j, e)
+        d0, more0, lag0, alt0 = graphs[0]; back = backs[0]
+        seq, r, rj, q, qj = walk(*lines(top[1]))
+        at = {j: k for k, j in enumerate(seq)}
+        best = (0.0, sorted(range(n), key=lambda k: (r[k], at[k])), list(eng))
+    value = lambda fins: sum(u / v for u, v in zip(spans_of(fins), ref))
+    seq = best[1]; fins = run(seq, 0, [zero] * len(graphs)); cur = value(fins); best = (cur, seq, list(eng)); chain = None
     for it in range(steps):
         if chain is None:
             pos = [0] * n; before = [None] * n; lastq = {}
             for k, j in enumerate(seq):
                 pos[j] = k; before[j] = lastq.get(eng[j]); lastq[eng[j]] = j
-            chain = {}; most = max(sts[0][j] + full0[j] for j in ends) + OPT["heat"] * ref[0]
-        x = (x * 1103515245 + 12345) % 2147483648; v = (x >> 8) % len(slim)
+            chain = {}; most = max(fins[0][j] + more0[j] for j in ends) + heat * ref[0]
+        x = (x * 1103515245 + 12345) % 2147483648; v = (x >> 8) % len(graphs)
         if v not in chain:
-            st = sts[v]; d, full, lag = slim[v]; j = max(ends, key=lambda k: st[k] + full[k]); c = []
+            fin = fins[v]; d, more, lag, alt = graphs[v]; j = max(ends, key=lambda k: fin[k] + more[k]); c = []
             while j is not None:
                 b = before[j]
-                if b is not None and st[b] + d[b] >= st[j] - 1e-6:
+                if b is not None and fin[b] >= fin[j] - d[j] - 1e-6:
                     if not anc[j] >> b & 1: c.append(j)
                     j = b
                 else:
-                    j = next((i for i, l in lag[j] if st[i] + l >= st[j] - 1e-6), None)
+                    j = next((i for i, l in lag[j] if fin[i] + l >= fin[j] - d[j] - 1e-6), None)
             chain[v] = c
         x = (x * 1103515245 + 12345) % 2147483648
         j = chain[v][(x >> 8) % len(chain[v])] if chain[v] and x % 8 else (x >> 8) % n
         i = before[j]
-        if i is None: continue
         x = (x * 1103515245 + 12345) % 2147483648; far = (0, 0, 0, 1, 2, 4, 8, 16)[(x >> 8) % 8]
-        if x >> 20 & 1:
+        undo = None
+        if (x >> 12) % OPT["flip"] == 0:
+            if i is not None and x >> 21 & 1: j = i
+            if len(alt0[j]) < 2: continue
+            others = [e for e in alt0[j] if e != eng[j]]
+            undo = (j, eng[j]); put(j, others[(x >> 22) % len(others)]); new = seq; i = j
+        elif i is None: continue
+        elif x >> 20 & 1:
             while far and before[i] is not None: i = before[i]; far -= 1
             mid = seq[pos[i]:pos[j] + 1]
             go = [k for k in mid if k == j or anc[j] >> k & 1]
@@ -898,14 +1091,18 @@ def schedule(ops, deps, prm, iters, steps, start=None, seed=7):
             go = [k for k in mid if k == i or anc[k] >> i & 1]
             if go[-1] == j: continue
             new = seq[:pos[i]] + [k for k in mid if not (k == i or anc[k] >> i & 1)] + go + seq[pos[j] + 1:]
-        s2 = run(new, pos[i], sts, most)
-        if s2 is None: continue
-        val = value(s2)
-        x = (x * 1103515245 + 12345) % 2147483648
-        if val <= cur + OPT["heat"] * (1.0 - it / steps) * (x / 2147483648.0) ** 2:
-            seq = new; sts = s2; cur = val; chain = None
-            if cur < best[0]: best = (cur, seq)
-    return sum(span(best[1], gr) / (k + 1.0 if k < 2 else 2.0) for k, gr in enumerate(others)), best[1]
+        s2 = run(new, pos[i], fins, most)
+        if s2 is not None:
+            val = value(s2)
+            x = (x * 1103515245 + 12345) % 2147483648
+            if val <= cur + heat * (1.0 - it / steps) * (x / 2147483648.0) ** 2:
+                seq = new; fins = s2; cur = val; chain = None; undo = None
+                if cur < best[0]: best = (cur, seq, list(eng))
+        if undo: put(*undo)
+    for j, e in enumerate(best[2]):
+        if e != eng[j]: put(j, e)
+    tm = spans_of(run(best[1], 0, [zero] * len(graphs)))
+    return sum(v / (k + 1.0 if k < 2 else 2.0) for k, v in enumerate(tm)), best[1], best[2]
 
 
 def plan(ops, deps, prm):
@@ -913,16 +1110,24 @@ def plan(ops, deps, prm):
     order = []
     for u, v in zip(cuts, cuts[1:]):
         part = [{i - u: need for i, need in d.items() if i >= u} for d in deps[u:v]]
-        tries = [schedule(ops[u:v], part, dict(prm, part=True), OPT["iters"], OPT["steps"], seed=k) for k in range(1, OPT["tries"] + 1)]
-        order += [u + j for j in min(tries)[1]]
-    return schedule(ops, deps, prm, 0, OPT["polish"], order)[1]
+        val, seq, eng = min(schedule(ops[u:v], part, dict(prm, part=True), OPT["iters"], OPT["steps"], seed=k, moves=OPT["walk"]) for k in range(1, OPT["tries"] + 1))
+        for o, e in zip(ops[u:v], eng):
+            if "alts" in o: choose(o, e)
+        val, seq, eng = schedule(ops[u:v], part, dict(prm, part=True), 0, OPT["more"], seq, moves=OPT["walk2"], heat=OPT["warm"])
+        for o, e in zip(ops[u:v], eng):
+            if "alts" in o: choose(o, e)
+        order += [u + j for j in seq]
+    val, order, eng = schedule(ops, deps, prm, 0, OPT["polish"], order, heat=OPT["cool"])
+    for o, e in zip(ops, eng):
+        if "alts" in o: choose(o, e)
+    return order, eng
 
 
 def joint():
     all_ops = [build(me) for me in range(NR)]
-    deps = link(all_ops[0])
+    deps = link(all_ops[0], True)
     for ops in all_ops[1:]:
-        for d, e in zip(deps, link(ops)):
+        for d, e in zip(deps, link(ops, True)):
             for i, need in e.items():
                 if i not in d or (need and not d[i]): d[i] = need
     return all_ops[0], deps
@@ -945,11 +1150,14 @@ def rank_program(g, core, T, topo):
     if me is None:
         return
     cores = list(T.cores)
-    ops = build(me); deps = link(ops)
     if "order" not in _PLAN:
         ops0, deps0 = joint()
-        _PLAN["order"] = plan(ops0, deps0, PRM)
+        _PLAN["order"], _PLAN["eng"] = plan(ops0, deps0, PRM)
     order = _PLAN["order"]
+    ops = build(me)
+    for o, e in zip(ops, _PLAN["eng"]):
+        if "alts" in o: choose(o, e)
+    deps = link(ops)
     Q = dict(V=g.vector, S=g.scalar, P=g.tensor, G=g, Y=g.sync)
     pos = {j: n for n, j in enumerate(order)}
     key = lambda i: ops[i]["eng"] if ops[i]["kind"] not in ("dma", "send", "recv") else i
@@ -983,6 +1191,23 @@ def rank_program(g, core, T, topo):
         nm, o0 = _AT.get(d[1], (d[1], 0))
         return T[nm][p, o0 + d[2]:o0 + d[3]] if d[4] == 1 else T[nm][p, o0 + d[2]:o0 + d[3]:d[4]]
 
+    def issue(q, k, x):
+        if k == "tt": return q.tensor_tensor(ap(x[0]), ap(x[1]), ap(x[2]), x[3])
+        if k == "ts":
+            if x[5] is None: return q.tensor_scalar(ap(x[0]), ap(x[1]), ap(x[2]), None, x[4])
+            return q.tensor_scalar(ap(x[0]), ap(x[1]), ap(x[2]), ap(x[3]), x[4], x[5])
+        if k == "cp": return q.tensor_copy(ap(x[0]), ap(x[1]))
+        if k == "ms": return q.memset(ap(x[0]), x[1])
+        if k == "scan": return q.tensor_tensor_scan(ap(x[0]), ap(x[1]), ap(x[2]), x[3], x[4], x[5])
+        if k == "trn": return q.transpose(ap(x[0]), ap(x[1]))
+        if k == "act": return q.activation(ap(x[0]), ap(x[1]), x[2], bias=ap(x[3]), scale=ap(x[4]), accum_out=ap(x[5]))
+        if k == "mm":
+            return [q.matmul(ap(po), ap(l), ap(r), x[1] and n == 0, x[2] and n == len(x[0]) - 1) for n, (po, l, r) in enumerate(x[0])][-1]
+        if k == "iota":
+            if _SB[x[0][1]][1] == i32: return q.iota(ap(x[0]), x[1], x[2], x[3])
+            return q.iota(ap(x[0]), x[1], x[2], x[3], allow_small_or_imprecise_dtypes=True)
+        return q.affine_select(ap(x[0]), ap(x[1]), x[2], x[3], x[6], x[4], x[5])
+
     seen = {e: {} for e in Q}
     for j in order:
         o = ops[j]; e = o["eng"]; q = Q[e]; k = o["kind"]; x = o["args"]
@@ -998,22 +1223,9 @@ def rank_program(g, core, T, topo):
             if seen[e].get(s, 0) < v:
                 q.wait_ge(T.sem[s], v); seen[e][s] = v
         ins = None
-        if k == "tt": ins = q.tensor_tensor(ap(x[0]), ap(x[1]), ap(x[2]), x[3])
-        elif k == "ts":
-            if x[5] is None: ins = q.tensor_scalar(ap(x[0]), ap(x[1]), ap(x[2]), None, x[4])
-            else: ins = q.tensor_scalar(ap(x[0]), ap(x[1]), ap(x[2]), ap(x[3]), x[4], x[5])
-        elif k == "cp": ins = q.tensor_copy(ap(x[0]), ap(x[1]))
-        elif k == "ms": ins = q.memset(ap(x[0]), x[1])
-        elif k == "scan": ins = q.tensor_tensor_scan(ap(x[0]), ap(x[1]), ap(x[2]), x[3], x[4], x[5])
-        elif k == "trn": ins = q.transpose(ap(x[0]), ap(x[1]))
-        elif k == "act": ins = q.activation(ap(x[0]), ap(x[1]), x[2], bias=ap(x[3]), scale=ap(x[4]), accum_out=ap(x[5]))
-        elif k == "mm":
-            for n, (po, l, r) in enumerate(x[0]):
-                ins = q.matmul(ap(po), ap(l), ap(r), x[1] and n == 0, x[2] and n == len(x[0]) - 1)
-        elif k == "iota":
-            if _SB[x[0][1]][1] == i32: ins = q.iota(ap(x[0]), x[1], x[2], x[3])
-            else: ins = q.iota(ap(x[0]), x[1], x[2], x[3], allow_small_or_imprecise_dtypes=True)
-        elif k == "sel": ins = q.affine_select(ap(x[0]), ap(x[1]), x[2], x[3], x[6], x[4], x[5])
+        if k == "many":
+            for k2, x2 in x: ins = issue(q, k2, x2)
+        elif k not in ("dma", "send", "recv"): ins = issue(q, k, x)
         elif k == "dma":
             for po, pi in x:
                 q.dma_start(ap(po), ap(pi)).then_inc(T.sem[mark[j][0]], 16)

import math
from concourse.bass import DstId, RemoteDMATransfer
from concourse.mybir import AluOpType as ALU, ActivationFunctionType as AF

W, S, R, CAP, ST, NR = 2048, 256, 3, 192, 467, 4
OFF = 3 * CAP + 16
Y0 = CAP
W0 = OFF - 16
D0 = OFF + 1024 - 16
NW = OFF + W + R * S
NA = S - S // NR
BIG = 8192.0
KD = 65536.0
HS = 1600
f32, b16, i32, u16 = "float32", "bfloat16", "int32", "uint16"

_SB = dict(
    X=(NW, b16), XJ=(NW, b16), C=(NW, i32), CF=(NW, f32), D=(NW, i32), CD=(16 + W + 2 * S, b16), cm=(768, b16),
    blk=(160, i32), blkf=(128, f32), bti=(288, i32), Ei=(40, i32),
    ag=(32, i32), agf=(32, f32), agt=(32, f32), agr=(32, f32), thr=(160, f32), ahf=(16, f32),
    ones=(160, b16), bow=(128, b16), bow0=(128, b16), z1=(144, b16), zk=(144, b16), iw=(160, b16),
    ni=(128, b16), ni32=(128, b16), i32=(128, b16), ih=(128, b16), rs=(9, f32), nq=(256, b16),
    bom=(128, b16), bof=(128, f32), tri=(128, b16), tri2=(128, b16), iwe=(160, f32), iwo=(160, f32), nkr=(128, b16),
    pi=(4, i32), pj=(9, i32), pc=(30, f32), kp2=(288, f32), lef2=(256, f32), lt2=(288, f32), lx=(2, u16), j16=(192, f32), dm=(192, f32), kp0=(192, f32), kp=(192, f32), ka=(192, f32), cfm=(16, f32), kr=(192, b16),
    Mh=(192, f32), idf=(128, f32), mk=(16, b16), mb=(16, f32), tu=(128, f32), tq=(128, f32), ti=(128, i32), cw=(512, f32), cw0=(256, f32), wv=(16, b16), kc=(36, f32), c32=(32, f32), kq=(16, f32), c4=(12, f32),
    pw=(128, f32), kw=(16, f32), l15=(12, u16), lk=(16, u16), l4=(24, u16),
    lq=(16, u16), lr=(2, u16), ln=(2, u16), lo1=(2, u16),
    lm=(16, u16), bv=(512, b16), bk=(256, b16), U=(2048, b16), onesf=(256, f32),
    xi=(256, i32), x2=(256, b16), xa=(1024, b16), xb=(512, b16), wh=(128, i32), whm=(128, i32), who=(128, u16),
    g2=(1024, b16), sg=(144, b16), junk=(128, b16), acc=(16, f32), ar=(1, f32), acol=(3, f32),
    offp=(128, u16), pg=(2048, b16), F=(144, b16), Fp=(144, b16), Q=(144, b16), Lf=(144, b16), vb=(128, b16), M=(12 * 128, b16),
    cu=(12, u16), uf=(12, f32), uu=(12, f32), cmp2=(192, b16),
    offo=(12, u16), offw=(192, u16), dp=(224, f32), dq=(192, f32), dt=(416, f32), yr=(768, b16),
    G=(3072, b16), cmpo=(3072, b16), left=(192, f32), lt=(192, f32), ls=(480, f32), bb=(192, f32), br=(192, f32),
    offx=(16, u16), xh=(192, f32), xw=(192, b16), yn=(192, i32),
    asq=(16, f32), au=(16, f32), ati=(256, i32), atm=(256, i32), offa=(256, u16),
    cmpa=(4096, b16), lfa=(256, f32), tr=(256, f32), top=(256, f32), E=(112, f32), offd=(12, u16), din=(288, f32), dout=(544, f32),
    offh=(48, u16), H=(768, f32), hs=(2 * HS, f32), q1=(80, f32), q2=(80, f32), offq=(16, u16),
    sb=(512, b16), Z=(512, b16), aw=(128, f32), awx=(128, b16),
)
_AT = {}
SCRATCH = {}
for _k, (_n, _d) in _SB.items():
    if _n <= 36 and _d in (f32, u16, b16):
        _w = SCRATCH.get("pack_" + _d, (0, [0, 0]))[1][1]
        _AT[_k] = ("pack_" + _d, _w)
        SCRATCH["pack_" + _d] = ("sbuf", [128, _w + (_n + 15) // 16 * 16], _d)
    else:
        _AT[_k] = (_k, 0)
        SCRATCH[_k] = ("sbuf", [128, _n], _d)
for _k in range(8):
    SCRATCH["ps%d" % _k] = ("psum", [128, 512], f32)
NDMA = 40
SEMAPHORES = ["cV", "cS", "cP", "cG", "sent", "arr0", "arr1"] + ["d%d" % k for k in range(NDMA)]

PRM = dict(cyc=0.88, pe=0.46, g=1.4, sc=3.2, same=195.0, cross=205.0, dma=2000.0, comm=2000.0, pool=1.5)
VARIANTS = [{}, dict(cyc=1.0, pe=0.52, g=1.56, sc=3.8, same=110.0, cross=140.0, dma=1500.0, comm=1600.0, pool=1.0),
            dict(cyc=0.85, pe=0.44, g=1.15, sc=2.2, same=235.0, cross=250.0, dma=2500.0, comm=2600.0, pool=1.8), dict(cyc=1.15, pe=0.6, g=1.9, sc=5.0, same=170.0, cross=180.0, comm=2400.0),
            dict(cyc=1.05, pe=0.58, g=1.08, sc=4.5, same=170.0, cross=180.0, comm=3000.0)]


def _pieces(text):
    return tuple((e[0], int(e[1:])) for e in text.split())


OPT = dict(
    x_parts=((0, 32), (32, 64), (64, 128)), cut=[99, 99, 12], bkl=[(0, 1, 6, 7)] * 3, sg2=[0, 0, 0],
    bka=[(0, 1, 6, 7)] * 3, bkb=[(1, 6, 7, 7)] * 2,
    die=[((0, 32, "V"), (32, 64, "V"), (64, 96, "V"), (96, 128, "V"))] + [((0, 16, "V"), (16, 40, "V"), (40, 64, "V"), (64, 96, "V"), (96, 112, "V"), (112, 128, "V"))] * 2,
    par=[((0, 32), (32, 64), (64, 96), (96, 128))] + [((0, 16), (16, 40), (40, 64), (64, 96), (96, 112), (112, 128))] * 2,
    sgp=[((0, 64), (64, 128))] * 3, parw=[(64,)] * 3, sg_last=[1, 1, 1], hpe=[0, 0, 0],
    arr=[_pieces("S2 S2 V2 V2 V2 V2 V2 V2"), _pieces("S2 S2 V2 V2 V2 V2 V2 V2"), _pieces("S2 S2 V1 V1 V1 V1 V1 V1 V1 V1 V1 V1 S2")],
    cha=[(8, 16), (8, 16), (12, 16)], brr=[_pieces("S8 S8")] * 2,
    xju=[(), (), ()], yb=[4] * 3,
    orp=[((0, 64, 5, (2, 3), ()), (64, 128, 4, (2, 3), _pieces("V4 V4 V4 V4")), (128, 192, k, (2, 3), _pieces("V4 V4 V4 V4"))) for k in (0, 0, 6)],
    ox=[((0, 192, (0, 192)),)] * 3,
    hop=[((0, 6), (6, 12), (12, 16))] * 2, snd=[((0, 6), (6, 12), (12, 16))] * 2,
    jit=1500.0, moves=8, tries=6, iters=300, steps=18000, polish=2000, heat=0.02, flip=5, walk=0, stale=400, reach=20, blur=50.0, rest=45, kick=30.0, kicks=15, near=1.004, run=500, srow=[1] * 3, ynp=[1, 1, 0], csc=[(128, 192)] * 3, defer=[3, 3], two=[0, 0, 1], cm_at=1, hs_=[0] * 3, cool=0.001, more=15000, warm=0.004, walk2=0, fix=(), miles=(), mean=0.1, shy=300.0, slack=0.01)
WAIT_ALL = True


def a(name, c0=0, c1=None, st=1, p=None):
    if c1 is None:
        c1 = _SB[name][0] if name in _SB else 512
    return ("ap", name, c0, c1, st, p)


def ind(win, off):
    return ("ind", win, off)


def ext(name, idx):
    return ("ext", name, idx)


def n_of(d):
    if d[0] == "ind":
        return 16 * n_of(d[2])
    return len(range(d[2], d[3], abs(d[4])))


def spans(d):
    if not isinstance(d, tuple) or d[0] == "ext":
        return []
    if d[0] == "ind":
        return spans(d[1]) + spans(d[2])
    return [(d[1], d[2], d[3], abs(d[4]))]


def meet(x, y):
    if (x[0] - y[0]) % math.gcd(x[2], y[2]):
        return False
    return x[0] < y[1] and y[0] < x[1]


def wide(d):
    return d[0] == "ap" and (d[1] not in _SB or _SB[d[1]][1] in (f32, i32))


def psum(d):
    return d[0] == "ap" and d[1] not in _SB


def transfers(o, me):
    t = o["args"]; out = []
    for q in range(NR - 1):
        b = (q + me + 1) % NR; z = S * t + 64 * ((me - b - 1) % NR)
        out.append((b, a("sb", S * t + 64 * q, S * t + 64 * q + 64), a("Z", z, z + 64)))
    return out


def choose(o, e):
    o.update(o["alts"][e]); o["eng"] = e


def build(me):
    ops = []
    table = [1500.0]

    def add(eng, kind, args, outs, ins, cost, alts=None):
        rd, wr = [], []
        for o in outs:
            if o[0] == "ind":
                wr += spans(o[1]); rd += spans(o[2])
            else:
                wr += spans(o)
        for i in ins:
            rd += spans(i)
        ops.append(dict(eng=eng, kind=kind, args=args, rd=rd, wr=wr, cost=cost))
        if alts:
            ops[-1]["alts"] = alts

    def vcost(out, in0, k):
        if out[0] == "ind":
            return ("sc", n_of(out))
        if in0[0] == "ind":
            return ("g", n_of(in0))
        return ("c", max(64, k * n_of(out)))

    def scost(x, more=0):
        return ("g", n_of(x) + 10) if x[0] == "ind" else ("c", max(64, n_of(x)) + more)

    def half(*aps):
        return 1.0 if any(wide(d) for d in aps) else 0.5

    def tt(out, x, y, op):
        add("V", "tt", (out, x, y, op), [out], [x, y], vcost(out, x, 1 if psum(x) or psum(y) else 2))

    def ts(out, x, s1, op0, s2=None, op1=None):
        add("V", "ts", (out, x, s1, s2, op0, op1), [out], [x, s1, s2], vcost(out, x, half(out, x)))

    def cp(out, x):
        add("V", "cp", (out, x), [out], [x], vcost(out, x, half(out, x)))

    def ms(out, v):
        add("V", "ms", (out, v), [out], [], ("c", max(64, n_of(out) * half(out))))

    def scan(out, d0, d1, op0, op1, first=0.0):
        add("V", "scan", (out, d0, d1, first, op0, op1), [out], [d0, d1], ("c", max(64, n_of(out) * half(out, d0, d1))))

    def trn(out, x):
        add("V", "trn", (out, x), [out], [x], ("c", max(64, n_of(out))))

    def act(out, x, func=AF.Identity, bias=0.0, scale=1.0, accum=None):
        add("S", "act", (out, x, func, bias, scale, accum), [out] + ([accum] if accum else []), [x, bias, scale], scost(x, 20 if accum else 0))

    def either(on, forms, out, ins):
        if out[1] in OPT["fix"] and "S" in on: on = on.replace("V", "")
        alts = {e: dict(kind=k, args=x, cost=c) for e, (k, x, c) in forms.items() if e in on}
        f = alts[on[0]]
        add(on[0], f["kind"], f["args"], [out], ins, f["cost"], alts)

    def lin(out, x, mul=1.0, plus=0.0, relu=False, on="SV"):
        c = vcost(out, x, half(out, x))
        if relu and _SB[out[1]][1] != u16: v = ("ts", (out, x, plus, 0.0, ALU.add, ALU.max), c)
        elif mul == 1.0 and plus == 0.0: v = ("cp", (out, x), c)
        elif mul == 1.0: v = ("ts", (out, x, plus, None, ALU.add, None), c)
        elif plus == 0.0: v = ("ts", (out, x, mul, None, ALU.mult, None), c)
        else: v = ("ts", (out, x, mul, plus, ALU.mult, ALU.add), c)
        either(on, dict(V=v, S=("act", (out, x, AF.Relu if relu else AF.Identity, plus, mul, None), scost(x)),
                        G=("sel", (out, x, [[0, n_of(x)]], ALU.is_ge, 0, 0, 0.0), ("c", 170 + 2 * n_of(out)))), out, [x, mul, plus])

    def together(k):
        some = ops[-k:]; del ops[-k:]
        forms = [o.get("alts", {o["eng"]: o}) for o in some]
        alts = {e: dict(kind="many", args=[(f[e]["kind"], f[e]["args"]) for f in forms], cost=("c", sum(f[e]["cost"][1] for f in forms)))
                for e in forms[0] if all(e in f for f in forms)}
        first = some[0]["eng"] if some[0]["eng"] in alts else "V"
        ops.append(dict(alts[first], eng=first, alts=alts, rd=sum([o["rd"] for o in some], []), wr=sum([o["wr"] for o in some], [])))

    def step(out, x, at, sign=1.0, on="SV"):
        either(on, dict(V=("ts", (out, x, at, None, ALU.is_gt if sign > 0 else ALU.is_lt, None), vcost(out, x, half(out, x))),
                        S=("act", (out, x, AF.Sigmoid, -256.0 * sign * at, 256.0 * sign, None), scost(x, table[0]))), out, [x])
        if table[0]:
            table[0] = 0.0; table.append(len(ops) - 1)

    def mm(lst, start=True, stop=True):
        run = []; cyc = 0
        for k, (o, l, r) in enumerate(lst):
            run.append((o, l, r)); cyc += max(min(64, n_of(l)), n_of(r)) * (4 if wide(r) else 1)
            if k == len(lst) - 1 or cyc >= OPT["run"]:
                add("P", "mm", (run, start and k + 1 == len(run), stop and k == len(lst) - 1), [x[0] for x in run], [x[1] for x in run] + [x[2] for x in run], ("pe", cyc))
                run = []; cyc = 0

    def iota(out, pat, base, cm=0):
        add("G", "iota", (out, pat, base, cm), [out], [], ("c", 130 + 2 * n_of(out)))

    def sel(out, x, pat, op, base, cm, other=0.0):
        add("G", "sel", (out, x, pat, op, base, cm, other), [out], [x], ("c", 170 + 2 * n_of(out)))

    def move(out, x, on="G"):
        lin(out, x, on=on)

    def fill(out, v):
        iota(out, [[0, n_of(out)]], int(v))

    def dma(q, pairs, extra=0.0):
        add(q, "dma", pairs, [o for o, i in pairs], [i for o, i in pairs], ("dma", len(pairs), extra))

    def wrap(out, z, src, c0, n, first=()):
        mm(list(first) + [(out, a(z, 15 - r, 143 - r), a(src, c0 + r, c0 + 16 * n, 16)) for r in range(16)])

    def repeat(name, c0, n, d, on):
        k = 1
        while k < d:
            j = min(k, d - k)
            move(a(name, c0 + n * k, c0 + n * (k + j)), a(name, c0, c0 + n * j), on); k += j

    I = a("iw", 16, 144); BOW = a("bow", 0, 128)
    pm, pr, pn, pm_, p32, p3, par, p8, pgp, pm2, npar, pq, pm12, pm4, p16, pa, pb, pd, pn16, px, py, pz, n32, pt, pf, pf16, pu, pv, pw_, px2 = [a("pc", k, k + 1) for k in range(30)]
    s4 = 4 * (me + 1); na = NA
    nat = [(q + me + 1) % NR for q in range(NR)]
    y = lambda j0, j1: a("XJ", Y0 + j0, Y0 + j1)

    parts = OPT["x_parts"]
    for k, (c0, c1) in enumerate(parts):
        dma("Y", [(a("X", OFF + 16 * c0, OFF + 16 * c1), ext("x0", (slice(None), slice(16 * c0, 16 * c1))))], 11.0 * c1 + (300.0 if k > OPT["cm_at"] else 0.0))
        if k == OPT["cm_at"]:
            dma("Y", [(a("cm", 0, S), ext("come", (slice(None), slice(0, S))))], 11.0 * c1 + 150.0)
            dma("Y", [(a("blk", 16, 144), ext("cd0", (slice(None), slice(None))))], 11.0 * c1 + 300.0)
    dma("Y", [(a("D", OFF + 1024, OFF + W), ext("dl0", (slice(None), slice(None))))], 3000.0)
    dma("Y", [(a("cm", S, 3 * S), ext("come", (slice(None), slice(S, 3 * S))))], 3300.0)
    dma("Y", [(a("ag", 16 * h, 16 * h + 16), ext("age", (slice(h, 8, 2), slice(None)))) for h in range(2)], 3300.0)
    dma("Y", [(a("C", OFF, OFF + W, 1, slice(m, 128, 16)), ext("cd0", (slice(None), slice(None)))) for m in range(16)], 9000.0)
    for k in range(1, len(ops)):
        ops[k]["after"] = k - 1
    ms(a("ones"), 1.0); ms(a("bv"), 21 * KD); ms(a("z1"), 0.0); ms(a("bk", 0, 192), -86016.0)
    step(a("onesf", 0, 64), a("ones", 0, 64), 0.5, on="S")
    fill(a("onesf", 64, S), 1.0)
    iota(a("pi"), [[16 - s4, 2], [s4, 2]], 0, 1)
    iota(a("c32"), [[0, 2], [32, 16]], 0)
    iota(a("j16"), [[0, 12], [1, 16]], 0)
    iota(a("kr"), [[1, 192]], 0)
    iota(a("bow0"), [[1, 8], [0, 16]], 0)
    iota(a("rs", 0, 3), [[ST % 16, 3]], ST % 16)
    iota(a("rs", 3, 6), [[-(ST // 16), 3]], 127 - ST // 16)
    iota(a("cfm"), [[122, 16]], 14)
    iota(a("kp0"), [[-32, 6], [0, 2], [4096, 16]], Y0 - OFF)
    iota(a("ka"), [[0, 12], [8192, 16]], -1)
    iota(a("c4"), [[64, 3], [4, 4]], 0)
    if any(OPT["hpe"]):
        fill(a("tu"), 0.0)
        for c0, k0, w in ((0, 0, NA // 16), (NA, NA // 16, (S - NA) // 16), (S, 0, S // 16)):
            iota(a("cw0", 0, 16 * w), [[122, 16], [0, w]], 14)
            sel(a("cw", c0, c0 + 16 * w), a("cw0", 0, 16 * w), [[0, 16], [1, w]], ALU.is_equal, k0, -1)
            sel(a("cw", c0, c0 + 16 * w), a("cw", c0, c0 + 16 * w), [[0, 16], [1, w]], ALU.not_equal, k0 + 32, -1, 1.0)
    fill(a("dp", 0, 16), 0.0); fill(a("dp", 144, 224), 0.0); fill(a("XJ", Y0 + CAP, W0), 0.0)
    ms(a("D", D0, D0 + 16), -1)
    ts(a("pj", 0, 3), a("pi", 0, 3), 15, ALU.bitwise_and)
    ts(a("pj", 4, 5), a("pi", 0, 1), 31, ALU.bitwise_and)
    ts(a("pj", 5, 6), a("pi", 0, 1), 3, ALU.bitwise_and)
    ts(a("pj", 6, 7), a("pi", 0, 1), 4, ALU.arith_shift_right, 1, ALU.bitwise_and)
    ts(a("pj", 7, 8), a("pi", 0, 1), 3, ALU.arith_shift_right, 1, ALU.bitwise_and)
    ts(a("pj", 3, 4), a("pi", 0, 1), 1, ALU.bitwise_and)
    ts(a("pj", 8, 9), a("pi", 0, 1), 4, ALU.arith_shift_right)
    together(7)
    cp(a("pc", 0, 9), a("pj"))
    cp(a("pc", 24, 26), a("pi", 0, 4, 3))
    together(2)
    ts(a("z1", 15, 144, 16), a("c32", 0, 9), 1.0 / 32, ALU.mult, pgp, ALU.is_equal)
    ts(a("iw"), a("kr", 0, 160), pf16, ALU.is_equal)
    ts(a("bow"), a("bow0"), pgp, ALU.is_equal)
    sel(a("tri"), BOW, [[1, 128]], ALU.is_ge, 0, -1)
    sel(a("tri2"), a("tri"), [[1, 128]], ALU.not_equal, 0, -1, 4096.0)
    ms(a("blk", 0, 16), 0); ms(a("blk", 144, 160), 0); ms(a("din", 0, 16), 0.0); ms(a("din", 272, 288), 0.0)
    together(4)
    lin(pm2, pm, 2.0, 2.0 * (S - 16 * s4) - 0.3125, on="VS")
    lin(a("pw"), a("j16", 0, 128), 32.0, pm2, on="VS")
    ts(p16, pm_, par, ALU.not_equal, 9.0, ALU.mult)
    ts(pa, p16, pm, ALU.add, 16.0, ALU.mult)
    lin(pq, p8, -127.0, pa)
    lin(npar, par, -1.0, 1.0)
    lin(pb, par, 272.0, pm)
    lin(pm12, pm, na / 16.0)
    lin(pm4, pm, 4.0, -12.0)
    together(4)
    lin(n32, p32, -1.0); lin(pn16, pn, 16.0, 15.0); lin(pt, par, float(S), BIG + W + S - 1); lin(pu, pm, 8.0, 208.0)
    together(4)
    lin(pd, npar, 272.0, pm); lin(py, pm, -15.75, pa); lin(pv, p3, -8.0, pu)
    together(3)
    lin(a("lq", 0, 8), a("c32", 0, 8), 1.0 / 16, pq)
    lin(a("lq", 8, 15), a("c32", 1, 8), 1.0 / 16, pq)
    together(2)
    lin(pz, p3, 15.75, py)
    lin(a("l4", 0, 12), a("c4"), plus=pz)
    if any(OPT["two"]):
        ts(px, pm_, par, ALU.not_equal, pv, ALU.mult)
        lin(px2, pm, 16.0, px)
        ts(a("lx", 0, 1), px2, 15.0, ALU.add, 479.0, ALU.min)
        for k in range(3):
            iota(a("lt2", 96 * k, 96 * k + 96), [[-32, 3], [0, 2], [4096, 16]], Y0 - OFF + 16 - 64 * k)
        lin(a("kp2"), a("lt2"), plus=n32)
        fill(a("lef2"), 0.0)
    ms(a("X", 0, OFF), 0.0); ms(a("CD", 0, 16), 0.0); ms(a("acol", 0, 1), -0.75 * (1 - OPT["hpe"][0]))
    together(3)
    ms(a("XJ", W0, OFF), -1.0); ms(a("C", W0, OFF), -1); ms(a("Fp", 0, 1), 0.0); ms(a("wv", 0, 6, 2), 1.0)
    together(4)
    ms(a("sg", 128, 144), -1.0); ms(a("thr", 0, 160, 5), 0.0); ms(a("nq"), -0.25)
    together(3)
    lin(a("kp"), a("kp0"), plus=n32)
    for some in ((("ni", I, -1.0), ("ni32", I, -32.0)), (("i32", I, 32.0), ("ih", I, 0.5)), (("bom", BOW, -2 * KD), ("zk", a("z1"), 8192.0)),
                 (("nkr", a("j16", 0, 128), -1.0), ("idf", I, 1.0)), (("iwe", a("iw"), npar), ("iwo", a("iw"), par), ("bof", BOW, 1.0))):
        for name, x, k in some:
            lin(a(name), x, k)
        together(len(some))
    nh = 16 * max(c1 - c0 for c0, c1 in OPT["hop"][0] + OPT["hop"][1])
    ts(a("dm", 0, nh), a("j16", 0, nh), pm, ALU.is_equal)
    ts(a("H", 0, nh), a("j16", 0, nh), pm, ALU.is_lt, BIG, ALU.mult)
    together(2)
    for r in range(16 * any(OPT["xju"])):
        lin(a("U", 128 * r, 128 * r + 128), a("bom"), a("dm", r, r + 1), on="VS")
    lin(a("H", S, S + nh), a("dm", 0, nh), -BIG)
    tt(a("Mh", 0, nh), a("H", 0, nh), a("H", S, S + nh), ALU.add)
    lin(a("Mh", 15, nh, 16), a("Mh", 15, nh, 16), plus=2 * BIG)
    lin(a("kw"), a("c32", 0, 16), 0.5, pm)
    lin(a("kq"), a("c32", s4, s4 + 16), 0.5, pm)
    lin(a("l15"), a("c32", 0, 12), 0.5, 15.0)
    lin(a("lr"), a("c32", 0, 2), 0.5, pr)
    together(4)
    lin(a("lk", 0, na // 16), a("c32", 0, na // 16), 1.0 / 32, pm12)
    lin(a("lk", 12, 16), a("c32", 12, 16), 1.0 / 32, pm4)
    lin(a("lm", 0, 16, 2), a("c32", 16 - s4, 32 - s4, 2), 0.5, pb)
    together(3)
    lin(a("lm", 1, 16, 2), a("c32", 17 - s4, 32 - s4, 2), 0.5, pd)
    lin(a("ln"), a("X", 0, 2), plus=pn16)
    lin(a("lo1", 0, 1), p32)
    together(3)
    ts(a("mk", 0, 6, 2), a("rs", 0, 3), pm, ALU.is_gt, -64.0, ALU.mult)
    ts(a("mk", 1, 6, 2), a("rs", 0, 3), pm, ALU.is_le, -64.0, ALU.mult)
    ts(a("rs", 6, 9), a("rs", 3, 6), pf, ALU.is_equal, float(-W), ALU.mult)
    together(3)
    lin(a("mb", 0, 6), a("mk", 0, 6), 256.0, -256 * 42.5)
    lin(a("wv", 1, 6, 2), a("rs", 6, 9), plus=16.0)
    together(2)
    for t in range(R):
        lin(a("kc", 12 * t, 12 * t + 12), a("kw", 0, 12), plus=float(-16 - OFF - S * t - 16 * ((ST * (t + 1)) // 16)))
    together(R)
    bases = lambda t, pieces: {c0: HS * t + 80 * c0 + 64 * (c0 >= 6) + 64 * (c0 >= 12) for c0, c1 in pieces}
    for t in range(R - 1):
        for c0, c1 in OPT["hop"][t]:
            h0 = bases(t, OPT["hop"][t])[c0]
            lin(a("hs", h0 + 75, h0 + 80 * (c1 - c0), 80), a("kq", c0, c1), plus=BIG + W + S * t)
        together(len(OPT["hop"][t]))
    lin(a("agf"), a("ag"), -1.0, pt)
    trn(a("agt"), a("agf"))
    lin(a("agr"), ind(a("agt"), a("lr")))
    for k in range(1, 5):
        lin(a("thr", k, 160, 5), a("agr"))
    together(4)
    trn(a("bti", 0, 128), a("blk", 16, 144))
    trn(a("bti", 128, 288), a("blk"))
    lin(a("offp"), ind(a("bti"), a("lq", 0, 8)), plus=16.0, on="VS")

    for t in range(R):
        lo = S * t; B = W + lo; L = OFF + lo; BB = OFF + B; K0 = 16 + lo
        last = t == R - 1
        na = S if last else NA
        cs = (ST * (t + 1)) // 16; n1 = 128 - cs

        def turned(c0, c1, cs=cs):
            runs = [(max(c0, cs), c1, max(c0, cs) - cs), (c0, min(c1, cs + 1), 128 - cs + c0)]
            return [x for x in runs if x[0] < x[1]]

        for k, (c0, c1) in enumerate(parts if t == 0 else ((0, 128),)):
            pn_ = "ps%d" % (4 + k % 2)
            wrap(a(pn_, 0, c1 - c0), "z1", "X", L + 16 * c0, c1 - c0)
            act(a(pn_, 128, 128 + c1 - c0), a(pn_, 0, c1 - c0), AF.Square, scale=0.25)
            tt(a("wh", c0, c1), a(pn_, 128, 128 + c1 - c0), a("pw", c0, c1), ALU.add)
            ts(a("whm", c0, c1), a("wh", c0, c1), 1, ALU.arith_shift_right, 255, ALU.bitwise_and)
            lin(a("who", c0, c1), a("whm", c0, c1), on="VS" if t == 0 else "SV")
        if t > 0:
            mm([(a("ps6", 0, S), I, a("nq"))] + [(a("ps6", 64 * q, 64 * q + 64), a("ih"), a("cm", S * t + 64 * nat[q], S * t + 64 * nat[q] + 64)) for q in range(NR)])
            fill(a("XJ", L - S, L), -1.0)
            fill(a("CD", K0 - S, K0), 1.0)
        for q in range(4):
            n = 512 if q < 3 else 512 - S
            if q // 2 in OPT["xju"][t]:
                mm([(a("ps%d" % q, 64 * k, 64 * k + 64), I, a("X", L + 1024 * (q // 2) + 8 * (q % 2) + k, L + 1024 * (q // 2 + 1), 16)) for k in range(8)], True, False)
                continue
            mm([(a("ps%d" % q), I, a("bv"))] + [(a("ps%d" % q, 0, n), a("i32"), a("XJ", L + 512 * q, L + 512 * q + n))] * (t > 0), True, False)
        for c0, c1, e in OPT["die"][t]:
            if e == "S":
                mm([(a("ps7", 0, 16 * (c1 - c0)), a("ni"), a("X", L + 16 * c0, L + 16 * c1))], True, False)
        if t > 0:
            mm([(a("ps5", 0, 128), I, a("X", CAP, CAP + 128))] +
               [(a("ps5", u - 16, v - 16), a("i32"), a("Lf", w, w + v - u)) for u, v, w in turned(16, 128, (ST * t) // 16)], True, False)
        if t > 0 and OPT["sg2"][t]:
            for k, (c0, c1) in enumerate(OPT["sgp"][t]):
                mm([(a("ps%d" % (OPT["sg2"][t] if k else 4), c0, c1), a("i32"), a("sg", 16 + c0, 16 + c1))], True, False)
        elif t > 0:
            mm([(a("ps4", 0, 128), a("i32"), a("sg", 16, 144))], True, False)
        if t == 0:
            for q in range(NR):
                lin(a("xi", 64 * q, 64 * q + 64), a("cm", 64 * nat[q], 64 * nat[q] + 64), 0.5, -0.25, on="VS")
        else:
            z = S * (t - 1)
            tt(a("xi", NA, S), a("Z", z + NA, z + S), a("ps6", NA, S), ALU.add)
            add("V", "recv", t - 1, [a("Z", z, z + NA)], [a("Z", z, z + NA)], ("c", 0))
            tt(a("xi", 0, NA), a("Z", z, z + NA), a("ps6", 0, NA), ALU.add)
            ops.extend(held_back)
        lin(a("x2"), a("xi"))
        if OPT["hpe"][t]:
            low, high, both = slice(0, 16), slice(32, 48), slice(0, 48)
            for p in (high, low):
                mm([(a("ps6", 256 + r, 384, 16, p), a("x2", r, S, 16), a("z1", 15, 143, 16)) for r in range(16)])
            act(a("tq", 0, 128, 1, high), a("ps6", 256, 384, 1, high), AF.Square, scale=0.25)
            act(a("tu", 0, 128, 1, low), a("ps6", 256, 384, 1, low))
            if OPT["hs_"][t]:
                act(a("ti", 0, 128, 1, high), a("tq", 0, 128, 1, high), scale=0.5, bias=-0.375)
                act(a("tu", 0, 128, 1, high), a("ti", 0, 128, 1, high), scale=2.0)
            else:
                ts(a("tu", 0, 128, 1, high), a("tq", 0, 128, 1, high), -0.75, ALU.add, 2.0 ** 24 + 2 * W, ALU.add)
            mm([(a("ps6", 0, S), a("tu", 0, 128, 1, both), a("cw", S * last, S * last + S, 1, both))])
            lin(a("ati"), a("ps6", 0, S), plus=a("acol", t, t + 1))
        else:
            wrap(a("ps6", 256, 272), "z1", "x2", 0, 16)
            act(a("asq"), a("ps6", 256, 272), AF.Square, scale=0.25)
            act(a("au"), a("ps6", 256, 272))
            ts(a("ahf"), a("asq"), a("acol", t, t + 1), ALU.add, 2.0 ** 24 + 2 * W, ALU.add)

        def hashes(i0, n):
            w = n // 16; k0 = i0 // 16
            for k in range(w * (1 - OPT["hpe"][t])):
                lin(a("ati", i0 + k, i0 + n, w), a("cfm"), a("au", k0 + k, k0 + k + 1), a("ahf", k0 + k, k0 + k + 1))
            ts(a("atm", i0, i0 + n), a("ati", i0, i0 + n), 1, ALU.arith_shift_right, W - 1, ALU.bitwise_and)
            lin(a("offa", i0, i0 + n), a("atm", i0, i0 + n))

        hashes(0, na)
        for c0, c1, e in OPT["die"][t]:
            o = a("CD", K0 + 16 * c0, K0 + 16 * c1); n = 16 * (c1 - c0)
            if e == "S":
                act(a("g2", 0, n), ind(a("xi"), a("who", c0, c1)))
                mm([(a("ps7", 0, n), I, a("g2", 0, n))], False, True)
                step(o, a("ps7", 0, n), -0.5)
            else:
                tt(o, ind(a("xi"), a("who", c0, c1)), a("X", L + 16 * c0, L + 16 * c1), ALU.is_ge)
        for k, (c0, c1) in enumerate(OPT["sgp"][t]):
            pn2 = "ps%d" % (4 if k == 0 or not OPT["sg2"][t] else OPT["sg2"][t]); end = OPT["sg2"][t] or k == len(OPT["sgp"][t]) - 1
            mm([(a(pn2, c0, c1), a("z1", 15 - r, 143 - r), a("CD", K0 + 16 * c0 + r, K0 + 16 * c1, 16)) for r in range(16)],
               t == 0 and (k == 0 or bool(OPT["sg2"][t])), bool(end))
            if end:
                u = c0 if OPT["sg2"][t] else 0
                act(a("sg", u, c1), a(pn2, u, c1), AF.Sign, bias=-10.5 if t == 0 else 21.5)
        for q in range(4):
            if q // 2 in OPT["xju"][t]:
                rows = range(8 * (q % 2), 8 * (q % 2) + 8); h = q // 2
                mm([(a("ps%d" % q, 64 * (r % 8), 64 * (r % 8) + 64), a("U", 128 * r, 128 * r + 128), a("sg", 64 * h, 64 * h + 64)) for r in rows], False, True)
                for r in rows:
                    lin(a("XJ", L + 1024 * h + r, L + 1024 * (h + 1), 16), a("ps%d" % q, 64 * (r % 8), 64 * (r % 8) + 64), plus=-2 * KD)
                together(8)
                continue
            mm([(a("ps%d" % q), a("bom"), a("CD", K0 + 512 * q, K0 + 512 * q + 512))], False, True)
            tt(a("XJ", L + 512 * q, L + 512 * q + 512), a("ps%d" % q), a("X", L + 512 * q, L + 512 * q + 512), ALU.min)
        for c0, c1 in OPT["par"][t]:
            lin(a("pg", 16 * c0, 16 * c1), ind(a("CD", 0, K0 + 16 * c1), a("offp", c0, c1)))
        cuts = [0] + list(OPT["parw"][t]) + [128]
        runs = list(zip(cuts, cuts[1:]))
        own = [(a("ps5", 0, 128), a("ni32"), a("sg", 0, 128))]
        for k, (u, v) in enumerate(runs):
            end = k == len(runs) - 1
            if end and not OPT["sg_last"][t]:
                mm(own, False, False)
            mm([(a("ps5", u, v), a("z1", 15 - r, 143 - r), a("pg", 16 * u + r, 16 * v, 16)) for r in range(16)], t == 0 and k == 0, end and not OPT["sg_last"][t])
        if OPT["sg_last"][t]:
            mm(own, False, True)
        step(a("F", 1, n1), a("ps5", cs + 1, 128), 42.5)
        step(a("F", n1, 128), a("ps5", 0, cs), 42.5)
        for k in range(2):
            o = a("F", 128 * k, 128 * k + 1); x = a("ps5", cs, cs + 1); mk, mb = a("mk", 2 * t + k, 2 * t + k + 1), a("mb", 2 * t + k, 2 * t + k + 1)
            either("SV", dict(V=("ts", (o, x, mk, 42.5, ALU.add, ALU.is_gt), ("c", 64)), S=("act", (o, x, AF.Sigmoid, mb, 256.0, None), ("c", 64))), o, [x, mk, mb])
        together(4)
        mm([(a("ps4", 0, 128), I, a("nkr"))], True, False)
        scan(a("Fp", 1, 130), a("ones", 0, 129), a("F", 0, 129), ALU.mult, ALU.add)
        mm([(a("ps4", 0, 128), a("Fp", 1, 129), BOW)], False, True)
        mm([(a("ps5", 256, 386), BOW, a("Fp", 0, 130)), (a("ps5", 256, 385), a("tri"), a("F", 0, 129))])
        lin(a("Q", 0, 130), a("ps5", 256, 386))
        ts(a("uf"), a("kw", 0, 12), a("Q", 129, 130), ALU.is_ge, -4096.0, ALU.mult)
        tt(a("uu"), a("uf"), a("kc", 12 * t, 12 * t + 12), ALU.max)
        lin(a("vb"), a("ps4", 0, 128), on="VS")
        for k in range(12):
            step(a("M", 128 * k, 128 * k + 128), a("vb"), 16 * k + 0.5, -1.0, on="VS" if k < 8 else "SV")
        for k in range(12):
            mm([(a("ps5", k, k + 17, 16), a("M", 128 * k, 128 * k + 128), a("wv", 2 * t, 2 * t + 2))], k == 0, k == 11)
        lin(a("cu"), a("ps5", 0, 12), on="VS")
        tt(a("uf"), a("uu"), a("ps5", 16, 28), ALU.add)
        o = a("ps4", 0, 12)
        mm([(o, a("idf"), a("uf"))], True, False)
        tt(a("cmp2"), ind(a("Q", 0, 130), a("cu")), a("kr"), ALU.is_le)
        mm([(o, a("z1", 15 - r, 143 - r), a("cmp2", r, CAP, 16)) for r in range(16)], False, True)
        lin(a("offd"), o, plus=float(L + 16 * cs - D0), relu=True, on="VS")
        lin(a("offo"), o, plus=float(L + 16 * cs), on="VS")
        together(2)

        def judge(e, o, src, rec, many, d, k, banks):
            n = n_of(rec)
            if e == "S":
                gq = a("g2", 512 * k, 512 * k + n * d); pn2 = "ps%d" % banks[k]
                mm([(a(pn2, n * j, n * j + n), a("ni"), rec) for j in range(d)], True, False)
                act(gq, src)
                mm([(a(pn2, 0, n * d), I, gq)], False, True)
                step(o, a(pn2, 0, n * d), -0.5)
            else:
                tt(o, src, rec if d == 1 else many, ALU.is_ge)

        def arrivals(i0, n, pieces, ends, rep, t0, banks, cut=99):
            w = n // 16; k0 = i0 // 16; g0 = 16 * i0
            m0 = 0; k = 0; done = 0
            for p, (e, d) in enumerate(pieces):
                if p == cut:
                    yield
                    banks = OPT["bkl"][t]
                judge(e, a("cmpa", g0 + n * m0, g0 + n * (m0 + d)), ind(a("XJ", L, BB), a("offa", i0 + w * m0, i0 + w * (m0 + d))),
                      a("x2", i0, i0 + n), a(rep, 0, n * d), d, k, banks)
                k = 1 - k if e == "S" else k
                m0 += d
                if m0 in ends:
                    o = a("ps%d" % banks[2 + ends.index(m0) % 2], 0, w * (m0 - done))
                    wrap(o, "zk", "cmpa", g0 + n * done, w * (m0 - done), [(o, I, a("bk", 0, w * (m0 - done)))])
                    tt(a("lfa", i0 + w * done, i0 + w * m0), o, a("atm", i0 + w * done, i0 + w * m0), ALU.min)
                    done = m0
            top = a("top", i0 + 15, i0 + n, 16)
            if last:
                src = ("lfa", i0); h = n // 2
                while h >= w:
                    tt(a("tr", t0, t0 + h), a(src[0], src[1], src[1] + h), a(src[0], src[1] + h, src[1] + 2 * h), ALU.max)
                    src = ("tr", t0); t0 += h; h //= 2
                for k in range(3):
                    lin(a("E", s4 % 16 + 16 * k, s4 % 16 + 16 * k + 16), a("tr", src[1], src[1] + w), plus=lo + 1.0, relu=True, on="VS")
                together(3)
                trn(a("E", 64, 96), a("E", 16, 48))
                lin(a("E", 96, 112), ind(a("E", 64, 96), a("lo1", 0, 1)), plus=-1.0)
                dma("Y", [(ext("yc", (slice(None), slice(W, W + S))), a("E", 96, 112))])
            else:
                lin(a("din", 16 + i0, 16 + i0 + n), ind(a("lfa", i0, i0 + n), a("lk", k0, k0 + w)), plus=float(lo))
                scan(a("top", i0, i0 + n), a("ka", 0, n), a("din", 16 + i0, 16 + i0 + n), ALU.min, ALU.max)
            if not last:
                lin(a("offh", k0, k0 + w), top, plus=16.0)

        def copies(name, i0, n, pieces, on="GVS"):
            d = max([d for e, d in pieces if e == "V"] + [1])
            if d > 1:
                move(a(name, 0, n), a("x2", i0, i0 + n), on); move(a(name, n, 2 * n), a("x2", i0, i0 + n), on)
                repeat(name, 0, 2 * n, (d + 1) // 2, on)

        copies("xa", 0, na, OPT["arr"][t])
        for q in range(NR):
            move(a("X", BB + 64 * nat[q], BB + 64 * nat[q] + 64), a("x2", 64 * q, 64 * q + 64))
        leaving = arrivals(0, na, OPT["arr"][t], OPT["cha"][t], "xa", 0, OPT["bka"][t], OPT["cut"][t])
        next(leaving, None)

        def rest():
            copies("xb", NA, S - NA, OPT["brr"][t])
            hashes(NA, S - NA)
            next(arrivals(NA, S - NA, OPT["brr"][t], (16,), "xb", 180, OPT["bkb"][t]), None)
            lin(a("E", 0, 32), ind(a("top"), a("ln")))
            trn(a("E", 32, 64), a("E", 0, 32))
            o = a("Ei", 0, 16) if t < R - 2 else a("E", 64, 80)
            lin(o, ind(a("E", 32, 64), a("lo1", 0, 1)))
            row = lambda m: a("C" if t < R - 2 else "CF", BB, BB + S, 1, slice(m, 128, 16))
            dma("Y", [(row(0), o)], 500.0)
            ops[-1]["behind"] = sent[0]; ops[-1]["later"] = True
            if t < R - 2:
                dma("Y", [(row(m), row(0)) for m in range(1, 16)], 2000.0)
                ops[-1]["later"] = True

        if last:
            dma("Y", [(ext("yx", (slice(None), slice(W, W + S))), a("X", BB, BB + S)),
                      (ext("ya", (slice(None), slice(W, W + S))), a("onesf", 0, S, 1, slice(0, 8)))], 10000.0)
            dma("Y", [(a("awx"), a("XJ", L, BB, 1, slice(0, 128, 16)))], 1500.0)
            step(a("aw"), a("awx"), -0.5)
            dma("Y", [(ext("ya", (slice(None), slice(0, W))), a("aw"))], 8000.0)
        orp = OPT["orp"][t]
        s1 = min([p[0] for p in orp if p[4]] + [CAP]); fw = CAP - s1
        if s1:
            lin(a("offw", 0, s1), ind(a("D", D0, BB), a("offd", 0, s1 // 16)), plus=16.0, relu=True)
            lin(a("dq", 0, s1), a("offw", 0, s1), plus=-16.0, on="VS")
        if fw:
            lin(a("dp", 16, 16 + fw), ind(a("D", D0, BB), a("offd", s1 // 16, 12)), on="VS")
            trn(a("dt", 0, fw), a("dp", 16, 16 + fw))
            trn(a("dt", fw, 2 * fw + 32), a("dp", 0, fw + 32))
        lin(y(0, CAP), ind(a("X", 0, BB), a("offo")))
        yb = "ps%d" % OPT["yb"][t]
        if not OPT["ynp"][t]:
            mm([(a(yb, 256, 256 + CAP), a("ih"), y(0, CAP))])
        for j0, j1, bank, by, pieces in orp:
            n = j1 - j0; o = a("ps%d" % bank, j0, j1)
            if not pieces and OPT["srow"][t]:
                for h in range(2):
                    mm([(a("ps%d" % by[h], n * m, n * m + n), a("ni"), y(j0, j1)) for m in range(8)], True, False)
                for h in range(n // 32):
                    act(a("G", 16 * j0 + 512 * h, 16 * j0 + 512 * h + 512), ind(a("XJ", W0, BB), a("offw", j0 + 32 * h, j0 + 32 * h + 32)))
                mm([(o, I, a("bk", 0, n))], True, False)
                for h in range(2):
                    k = 16 * j0 + 8 * n * h
                    mm([(a("ps%d" % by[h], n * m, n * m + n), I, a("G", 16 * j0 + 8 * h + m, 16 * j1, 16)) for m in range(8)], False, True)
                    step(a("cmpo", k, k + 8 * n), a("ps%d" % by[h], 0, 8 * n), -0.5)
                    mm([(o, a("zk", 15 - m - 8 * h, 143 - m - 8 * h), a("cmpo", k + n * m, k + n * m + n)) for m in range(8)], False, h == 1)
                dv = a("dq", j0, j1)
            elif not pieces:
                for h in range(n // 32):
                    k = 16 * j0 + 512 * h; pn2 = "ps%d" % by[h % len(by)]
                    mm([(a(pn2, m, 512, 16), a("ni"), y(j0 + 32 * h, j0 + 32 * h + 32)) for m in range(16)], True, False)
                    act(a("G", k, k + 512), ind(a("XJ", W0, BB), a("offw", j0 + 32 * h, j0 + 32 * h + 32)))
                    mm([(a(pn2), I, a("G", k, k + 512))], False, True)
                    step(a("cmpo", k, k + 512), a(pn2), -0.5)
                mm([(o, I, a("bk", 0, n))] + [(o, a("zk", 15 - m, 143 - m), a("cmpo", 16 * j0 + m, 16 * j1, 16)) for m in range(16)])
                dv = a("dq", j0, j1)
            else:
                k = (j0 - s1) // 16; w = n // 16
                pick = a("lq", 0, 8) if n == 128 else a("l4", k, k + w)
                lin(a("offw", j0, j1), ind(a("dt", 0, 2 * fw + 32), pick), plus=16.0, relu=True, on="VS")
                d = max([d for e, d in pieces if e == "V"] + [1]); rep = ("XJ", Y0 + j0)
                if j1 < CAP and d > 1:
                    rep = ("yr", 4 * (j0 - s1)); move(a("yr", rep[1], rep[1] + n), y(j0, j1), "VSG"); move(a("yr", rep[1] + n, rep[1] + 2 * n), y(j0, j1), "VSG")
                    repeat("yr", rep[1], 2 * n, (d + 1) // 2, "VSG")
                else:
                    repeat("XJ", rep[1], n, d, "GVS")
                mm([(o, I, a("bk", 0, n))], True, False)
                m0 = 0; k = 0
                for e, d in pieces:
                    g0 = 16 * j0 + n * m0
                    judge(e, a("cmpo", g0, g0 + n * d), ind(a("XJ", W0, BB), a("offw", j0 + w * m0, j0 + w * (m0 + d))),
                          y(j0, j1), a(rep[0], rep[1], rep[1] + n * d), d, k, by)
                    k = 1 - k if e == "S" else k
                    mm([(o, a("zk", 15 - m, 143 - m), a("cmpo", 16 * j0 + n * m, 16 * j0 + n * m + n)) for m in range(m0, m0 + d)], False, m0 + d == 16)
                    m0 += d
                dv = a("dp", 16 + j0 - s1, 16 + j1 - s1)
            k = j0 // 64; lf = a("lef2", 16 + 80 * k, 80 + 80 * k) if OPT["two"][t] else a("left", j0, j1)
            tt(lf, o, dv, ALU.min)
            trn(a("lt", j0, j1), lf)
            if OPT["two"][t]:
                trn(a("lt2", 96 * k, 96 * k + 96), a("lef2", 80 * k, 80 * k + 96))
                together(2)
            scan(a("ls", j0, j1), a("kp", j0, j1), a("lt", j0, j1), ALU.min, ALU.max)
            if OPT["two"][t]:
                scan(a("ls", CAP + 96 * k, CAP + 96 * k + 96), a("kp2", 96 * k, 96 * k + 96), a("lt2", 96 * k, 96 * k + 96), ALU.min, ALU.max)
                together(2)
            lin(a("bb", j0, j1), ind(a("ls", j0, j1), a("l15", 0, n // 16)), plus=1.0 * last, relu=last)
            trn(a("br", j0, j1), a("bb", j0, j1))
            if j1 not in OPT["csc"][t]:
                continue
            j0 = ([0] + list(OPT["csc"][t]))[OPT["csc"][t].index(j1)]
            if last:
                ts(ind(a("CF", 0, BB), a("offo", j0 // 16, j1 // 16)), a("br", j0, j1), 1.0, ALU.mult, -1.0, ALU.add)
            else:
                cp(ind(a("C", 0, BB), a("offo", j0 // 16, j1 // 16)), a("br", j0, j1))
        for j0, j1, k0 in OPT["ox"][t]:
            c0, c1 = j0 // 16, j1 // 16
            if OPT["two"][t]:
                act(a("offx"), ind(a("ls"), a("lx", 0, 1)), AF.Abs, bias=float(OFF - Y0))
            else:
                mm([(a("ps4", c0 + ih, c1, 2), a("iwo" if ih else "iwe", 16 + 16 * (ih - gh), 144 + 16 * (ih - gh)), a("ls", j0 + 16 * gh + 15, j1, 32))
                    for ih in range(2) for gh in range(2)])
                act(a("offx", c0, c1), a("ps4", c0, c1), AF.Abs, bias=float(OFF - Y0))
            if OPT["ynp"][t]:
                lin(a("xw", j0, j1), ind(a("XJ", Y0, BB), a("offx", c0, c1)))
                mm([(a(yb, 256 + j0, 256 + j1), a("ih"), x) for x in (y(j0, j1), a("xw", j0, j1))])
                lin(a("yn", j0, j1), a(yb, 256 + j0, 256 + j1), plus=-0.25)
            else:
                lin(a("xh", j0, j1), ind(a("XJ", Y0, BB), a("offx", c0, c1)), 0.5, -0.25)
                tt(a("yn", j0, j1), a("xh", j0, j1), a(yb, 256 + j0, 256 + j1), ALU.add)
            for k in range(len(k0) - 1):
                cp(ind(a("X", 0, BB), a("offo", k0[k] // 16, k0[k + 1] // 16)), a("yn", k0[k], k0[k + 1]))
        next(leaving, None)
        if last:
            dma("Y", [(ext("yc", (slice(None), slice(0, W))), a("CF", L, BB, 1, slice(0, 128, 16)))], 300.0)
            dma("Y", [(ext("yx", (slice(None), slice(0, 1024))), a("X", L, L + 1024))], 700.0)
            dma("S", [(ext("yx", (slice(None), slice(1024, W))), a("X", L + 1024, BB))], 700.0)
            break
        dma("Y", [(a("blk", 16, 144), a("C", L, BB, 1, slice(0, 128, 16)))], 200.0)
        trn(a("bti", 0, 128), a("blk", 16, 144))
        trn(a("bti", 128, 288), a("blk"))
        lin(a("offp", 0, 112), ind(a("bti"), a("lq", 8, 15)), plus=16.0, relu=True)

        def queries(pieces, snd):
            base = bases(t, pieces)
            for c0, c1 in pieces:
                h0 = base[c0]; n = 80 * (c1 - c0)
                lin(a("hs", h0 + 91, h0 + n + 16, 80), a("top", 16 * c0 + 15, 16 * c1, 16), plus=BIG)
            for k in range(3):
                for c0, c1 in pieces:
                    p0, p1 = S * k + 16 * c0, S * k + 16 * c1; h0 = base[c0] + 16 * (k + 2); n = 80 * (c1 - c0)
                    lin(a("H", p0, p1), ind(a("C", W0, BB), a("offh", 16 * k + c0, 16 * k + c1)))
                    scan(a("hs", h0, h0 + n, 5), a("H", p0, p1), a("Mh", 0, p1 - p0), ALU.min, ALU.add, BIG)
                    if k < 2:
                        lin(a("offh", 16 * k + 16 + c0, 16 * k + 16 + c1), a("hs", h0 + 75, h0 + n, 80), plus=16 - BIG, relu=True)
            for c0, c1 in pieces:
                five = a("hs", base[c0] + 75, base[c0] + 80 * (c1 - c0) + 60, 16)
                tt(a("q1", 5 * c0, 5 * c1), five, a("thr", 80 * t + 5 * c0, 80 * t + 5 * c1), ALU.is_lt)
                scan(a("q2", 5 * c0, 5 * c1), a("q1", 5 * c0, 5 * c1), five, ALU.mult, ALU.max)
                lin(a("offq", c0, c1), a("q2", 5 * c0 + 4, 5 * c1, 5), plus=16 - BIG)
            for c0, c1 in snd:
                lin(a("sb" if c0 < 12 else "Z", S * t + 16 * c0, S * t + 16 * c1), ind(a("X", W0, BB + S), a("offq", c0, c1)), 0.5)

        queries([p for p in OPT["hop"][t] if p[0] < 12], [p for p in OPT["snd"][t] if p[0] < 12])
        add("G", "send", t, [], [a("sb", S * t, S * t + NA)], ("c", 300))
        sent = [len(ops) - 1]
        if t == R - 2:
            ts(a("blkf"), a("blk", 16, 144), -1.0, ALU.max)
            dma("Y", [(a("CF", L, BB, 1, slice(0, 128, 16)), a("blkf"))], 500.0)
            ops[-1]["later"] = True; ops[-1]["behind"] = sent[0]
        rest()
        queries([p for p in OPT["hop"][t] if p[0] >= 12], [p for p in OPT["snd"][t] if p[0] >= 12])
        lin(a("offp", 112, 128), ind(a("top"), a("ln", 0, 1)), plus=16.0)
        mm([(a("ps5", 0, 129), BOW, a("Fp", 0, 129)), (a("ps5", 0, 129), a("tri2"), a("F", 0, 129))])
        step(a("Lf", 0, 129), a("ps5", 0, 129), 4096 + CAP - 0.5)
        k0 = len(ops)
        cp(ind(a("D", 0, BB), a("offo")), a("left"))
        trn(a("dout", 0, 256), a("din", 16, 272))
        trn(a("dout", 256, 544), a("din"))
        lin(a("D", BB, BB + S), ind(a("dout"), a("lm")))
        held_back = ops[k0 + OPT["defer"][t]:]; del ops[k0 + OPT["defer"][t]:]
        if t == 0:
            act(a("junk", 0, 16), a("sg", 0, 16), accum=a("acc", 0, 1))
            act(a("junk", 16, 128), a("sg", 16, 128), accum=a("acc", 1, 2))
            tt(a("ar"), a("acc", 0, 1), a("acc", 1, 2), ALU.add)
        else:
            act(a("junk"), a("sg", 0, 128), accum=a("acc", 2, 3))
            tt(a("ar"), a("acc", 2, 3), a("acc", 1, 2), ALU.subtract)
        mm([(a("ps7", 0, 1), a("bof"), a("ar"))])
        lin(a("acol", t + 1, t + 2), a("ps7", 0, 1), plus=(2048.0 if t == 0 else 256.0) - 0.75 * (1 - OPT["hpe"][t + 1]))
    for o in ops[table[1] + 1:]:
        f = o.get("alts", {}).get("S", o)
        if any(x[2] in (AF.Sigmoid, AF.Square) for k, x in (f["args"] if f["kind"] == "many" else [(f["kind"], f["args"])]) if k == "act"):
            o.setdefault("after", table[1])
    return ops


def link(ops, loose=False):
    hist = {}
    deps = []
    sends = {}
    for j, o in enumerate(ops):
        d = {}
        for acc_w, lst in ((False, o["rd"]), (True, o["wr"])):
            for sp in lst:
                bank = sp[0] not in _SB
                for i, w, run in hist.get(sp[0], []):
                    hit = (w or acc_w) and meet(run, sp[1:])
                    if i == j or not (bank or hit):
                        continue
                    p = ops[i]
                    same = p["eng"] == o["eng"] and p["kind"] not in ("dma", "send") and o["kind"] not in ("dma", "send")
                    if loose and (len(p.get("alts", ())) > 1 or len(o.get("alts", ())) > 1):
                        same = False
                    if bank and same and o["eng"] != "P" and not hit:
                        continue
                    need = (not same) or (hit and w and not acc_w) or (WAIT_ALL and o["eng"] != "P" and hit)
                    if p["kind"] == "recv" and same:
                        need = False
                    d[i] = d.get(i, False) or need
        for acc_w, lst in ((False, o["rd"]), (True, o["wr"])):
            for sp in lst:
                hist.setdefault(sp[0], []).append((j, acc_w, sp[1:]))
        if "after" in o:
            d.setdefault(o["after"], False)
        if "behind" in o:
            d[o["behind"]] = True
        if o["kind"] == "send":
            sends[o["args"]] = j
        if o["kind"] == "recv":
            d[sends[o["args"]]] = None
        deps.append(d)
    return deps


def held(c, e, prm):
    if c[0] == "c": return max(c[1] * prm["cyc"] * (prm["pool"] if e == "G" else 1.0), 1e-3)
    if c[0] == "g": return 50 + c[1] * prm["cyc"] * prm["g"]
    if c[0] == "sc": return 50 + c[1] * prm["cyc"] * prm["sc"]
    if c[0] == "pe": return c[1] * prm["pe"]
    return 60.0 * c[1]


def sizes(ops, prm):
    out = []
    for o in ops:
        c = o["cost"]; v = held(c, o["eng"], prm)
        out.append((v, v + (prm["dma"] + c[2] if c[0] == "dma" and not ("later" in o and prm.get("part")) else 0.0)))
    return out


def gap(ops, i, j, need, prm):
    if need is None: return prm["comm"]
    if not need: return 0.0
    return prm["same"] if ops[i]["eng"] == ops[j]["eng"] else prm["cross"]


def schedule(ops, deps, prm, iters, steps, start=None, seed=7, moves=0, heat=None):
    n = len(ops); eng = [o["eng"] for o in ops]; heat = heat or OPT["heat"]
    anc = [0] * n; keep = []
    for j in range(n):
        up = 0
        for i in deps[j]: up |= anc[i]
        keep.append([i for i in deps[j] if not up >> i & 1 or ops[i]["kind"] in ("dma", "send")])
        for i in deps[j]: up |= 1 << i
        anc[j] = up

    def graph(p):
        sz = sizes(ops, p); more = [s[1] - s[0] for s in sz]
        lag = [[(i, (more[i] if deps[j][i] is not False else 0.0) + gap(ops, i, j, deps[j][i], p) + 1e-3) for i in keep[j]] for j in range(n)]
        return [s[0] for s in sz], more, lag, [{e: held(f["cost"], e, p) for e, f in o.get("alts", {}).items()} for o in ops]

    def place(seq, pred, first, pick=None):
        busy = {e: ([], []) for e in "VSPGY"}
        fin = [0.0] * n
        for j in seq:
            t0 = first[j]
            for i, l in pred[j]:
                if fin[i] + l > t0: t0 = fin[i] + l
            got = None
            for e, dj in (alt0[j].items() if pick and alt0[j] else ((eng[j], d0[j]),)):
                t = t0; bs, be = busy[e]; k = len(be)
                while k > 0 and be[k - 1] > t: k -= 1
                while k < len(bs) and t + dj > bs[k]:
                    if be[k] > t: t = be[k]
                    k += 1
                v = t + dj + (pick[j] if pick and e == "V" else 0.0)
                if got is None or v < got[0]: got = (v, e, t, dj, k)
            v, e, t, dj, k = got
            if e != eng[j]: put(j, e)
            fin[j] = t + dj; busy[e][0].insert(k, t); busy[e][1].insert(k, t + dj)
        return fin

    def put(j, e):
        eng[j] = e
        for g in graphs: g[0][j] = g[3][j][e]

    def run(seq, p0, old, most=None):
        lastop = {}
        for k in range(p0 - 1, -1, -1):
            if eng[seq[k]] not in lastop:
                lastop[eng[seq[k]]] = seq[k]
                if len(lastop) == 5: break
        out = []; tail_seq = seq[p0:]
        for (d, more, lag, alt), o in zip(graphs, old):
            fin = list(o); free = {e: (fin[lastop[e]] if e in lastop else 0.0) for e in "VSPGY"}
            for j in tail_seq:
                e = eng[j]; t = free[e]
                for i, l in lag[j]:
                    u = fin[i] + l
                    if u > t: t = u
                free[e] = fin[j] = t + d[j]
            if most and not out and max(fin[j] + more[j] for j in ends) > most:
                return None
            out.append(fin)
        return out

    graphs = [graph(dict(prm, **v)) for v in VARIANTS]
    d0, more0, lag0, alt0 = graphs[0]
    back = [[] for j in range(n)]
    for j in range(n):
        for i, l in lag0[j]: back[i].append((j, l))
    ends = [j for j in range(n) if not back[j]]
    zero = [0.0] * n
    spans_of = lambda fins: [max(f[j] + g[1][j] for j in ends) + OPT["mean"] * sum(f) / n + sum(w * max(f[j] for j in js) for w, js in miles)
                             for f, g in zip(fins, graphs)]
    cut = [j for j, o in enumerate(ops) if o["kind"] == "recv"] + [n]
    miles = [(w, [j for j in range(u, v) if ops[j]["wr"] and ops[j]["wr"][0][0] == name and ops[j]["eng"] != "G"])
             for name, w in OPT["miles"] for u, v in zip([0] + cut, cut)]
    miles = [m for m in miles if m[1]]
    level = [d0[j] + more0[j] for j in range(n)]
    for j in range(n - 1, -1, -1):
        for i, l in lag0[j]: level[i] = max(level[i], d0[i] + l + level[j])
    key = [-v for v in level]
    x = seed; best = None; ref = None; now = None; shy = [OPT["shy"]] * n
    if start:
        ref = spans_of(run(start, 0, [zero] * len(graphs))); best = (0.0, start, list(eng))
    for it in range(iters):
        fin = place(sorted(range(n), key=lambda k: (key[k], k)), lag0, zero, shy)
        for rep in range(2):
            sb = place(sorted(range(n), key=lambda k: (d0[k] - fin[k], -k)), back, more0)
            fin = place(sorted(range(n), key=lambda k: (-sb[k], k)), lag0, zero, shy)
        seq = sorted(range(n), key=lambda k: (fin[k] - d0[k], k))
        fins = run(seq, 0, [zero] * len(graphs), now and 1.015 * now[3])
        if fins:
            tm = spans_of(fins)
            if ref is None: ref = tm
            score = sum(u / v for u, v in zip(tm, ref))
            if now is None or score < now[0] + OPT["slack"] * (1.0 - it / iters): now = (score, [fin[k] - d0[k] for k in range(n)], list(shy), tm[0])
            if best is None or score < best[0]: best = (score, seq, list(eng))
        key = list(now[1]); shy = list(now[2])
        for k in range(OPT["moves"]):
            x = (x * 1103515245 + 12345) % 2147483648; j = (x >> 8) % n
            x = (x * 1103515245 + 12345) % 2147483648
            key[j] += OPT["jit"] * (x / 1073741824.0 - 1.0)
            x = (x * 1103515245 + 12345) % 2147483648; j = (x >> 8) % n
            x = (x * 1103515245 + 12345) % 2147483648
            shy[j] = OPT["shy"] + OPT["jit"] * (x / 1073741824.0 - 1.0)
        for j in range(n):
            for i, l in lag0[j]:
                if key[j] <= key[i]: key[j] = key[i] + 1e-3
    for j, e in enumerate(best[2]):
        if e != eng[j]: put(j, e)

    def lines(seq):
        prv = [-1] * n; nxt = [-1] * n; lastq = {}
        for j in seq:
            if eng[j] in lastq: prv[j] = lastq[eng[j]]; nxt[prv[j]] = j
            lastq[eng[j]] = j
        return prv, nxt

    def walk(prv, nxt):
        need = [len(lag0[j]) + (prv[j] >= 0) for j in range(n)]
        seq = [j for j in range(n) if not need[j]]; r = [0.0] * n; rj = [0.0] * n
        for j in seq:
            f = r[j] + d0[j]
            for k, l in back[j]:
                if f + l > rj[k]:
                    rj[k] = f + l
                    if f + l > r[k]: r[k] = f + l
                need[k] -= 1
                if not need[k]: seq.append(k)
            k = nxt[j]
            if k >= 0:
                if f > r[k]: r[k] = f
                need[k] -= 1
                if not need[k]: seq.append(k)
        q = list(more0); qj = list(more0)
        for j in reversed(seq):
            f = q[j] + d0[j]
            for i, l in lag0[j]:
                if f + l > qj[i]:
                    qj[i] = f + l
                    if f + l > q[i]: q[i] = f + l
            i = prv[j]
            if i >= 0 and f > q[i]: q[i] = f
        return seq, r, rj, q, qj

    if moves:
        prv, nxt = lines(best[1])
        rest = [0] * n; top = None; vi = 0
        backs = [[[] for j in range(n)] for g in graphs]
        for g, bk in zip(graphs, backs):
            for j in range(n):
                for i, l in g[2][j]: bk[i].append((j, l))
        for it in range(moves):
            seq, r, rj, q, qj = walk(prv, nxt)
            span = max(r[j] + d0[j] + q[j] for j in ends)
            if top is None or span < top[5][vi] * OPT["near"]:
                tm = [max(f[j] + g[1][j] for j in ends) for f, g in zip(run(seq, 0, [zero] * len(graphs)), graphs)]
                score = sum(u / v for u, v in zip(tm, ref))
                if top is None or score < top[0] - 1e-9: top = (score, seq, list(eng), it, False, tm)
            if it - top[3] > OPT["stale"]:
                for j, e in enumerate(top[2]):
                    if e != eng[j]: put(j, e)
                prv, nxt = lines(top[1])
                top = top[:3] + (it, True, top[5])
                vi = (vi + 1) % len(graphs)
                d0, more0, lag0, alt0 = graphs[vi]; back = backs[vi]
                continue
            line = {e: [] for e in "VSPGY"}
            for j in seq: line[eng[j]].append(j)
            pick = None
            for v in seq:
                if r[v] + d0[v] + q[v] < span - 1e-6: continue
                a0, b0 = prv[v], nxt[v]
                if not ((a0 >= 0 and r[a0] + d0[a0] >= r[v] - 1e-6) or (b0 >= 0 and d0[b0] + q[b0] >= q[v] - 1e-6)): continue
                qs = max([q[s] for s, l in back[v]] + [-1.0]); rp = max([r[p] for p, l in lag0[v]] + [-1.0])
                found = []
                t = r[a0] + d0[a0] if a0 >= 0 else 0.0; w = b0; mid = []
                while w >= 0 and len(mid) < OPT["reach"] and qs < d0[w] + q[w] and not anc[w] >> v & 1:
                    s = rj[w] if rj[w] > t else t; t = s + d0[w]; mid.append((w, t))
                    b = nxt[w]; u = max(qj[v], d0[b] + q[b] if b >= 0 else 0.0); est = max(rj[v], t) + d0[v] + u; u += d0[v]
                    for k, f in reversed(mid):
                        if qj[k] > u: u = qj[k]
                        if f + u > est: est = f + u
                        u += d0[k]
                    found.append((est, eng[v], w, b)); w = b
                t = d0[b0] + q[b0] if b0 >= 0 else 0.0; w = a0; mid = []
                while w >= 0 and len(mid) < OPT["reach"] and rp < r[w] + d0[w] and not anc[v] >> w & 1:
                    s = qj[w] if qj[w] > t else t; t = s + d0[w]; mid.append((w, t))
                    b = prv[w]; u = max(rj[v], r[b] + d0[b] if b >= 0 else 0.0); est = max(qj[v], t) + d0[v] + u; u += d0[v]
                    for k, f in reversed(mid):
                        if rj[k] > u: u = rj[k]
                        if f + u > est: est = f + u
                        u += d0[k]
                    found.append((est, eng[v], b, w)); w = b
                for e, dv in alt0[v].items():
                    if e == eng[v]: continue
                    b = -1
                    for w in line[e] + [-1]:
                        if b >= 0 and (qs >= d0[b] + q[b] or anc[b] >> v & 1): break
                        if w < 0 or (rp < r[w] + d0[w] and not anc[v] >> w & 1):
                            found.append((max(rj[v], r[b] + d0[b] if b >= 0 else 0.0) + dv + max(qj[v], d0[w] + q[w] if w >= 0 else 0.0), e, b, w))
                        b = w
                for m in found:
                    x = (x * 1103515245 + 12345) % 2147483648
                    val = m[0] + OPT["blur"] * (OPT["kick"] if it - top[3] < OPT["kicks"] and top[4] else 1.0) * x / 2147483648.0
                    if (rest[v] <= it or m[0] < top[5][vi] - 1e-6) and (pick is None or val < pick[0]): pick = (val, v) + m[1:]
            if pick is None:
                rest = [0] * n
                continue
            val, v, e, a1, b1 = pick
            if prv[v] >= 0: nxt[prv[v]] = nxt[v]
            if nxt[v] >= 0: prv[nxt[v]] = prv[v]
            if e != eng[v]: put(v, e)
            prv[v] = a1; nxt[v] = b1
            if a1 >= 0: nxt[a1] = v
            if b1 >= 0: prv[b1] = v
            x = (x * 1103515245 + 12345) % 2147483648
            rest[v] = it + OPT["rest"] + (x >> 8) % OPT["rest"]
        for j, e in enumerate(top[2]):
            if e != eng[j]: put(j, e)
        d0, more0, lag0, alt0 = graphs[0]; back = backs[0]
        seq, r, rj, q, qj = walk(*lines(top[1]))
        at = {j: k for k, j in enumerate(seq)}
        best = (0.0, sorted(range(n), key=lambda k: (r[k], at[k])), list(eng))
    value = lambda fins: sum(u / v for u, v in zip(spans_of(fins), ref))
    seq = best[1]; fins = run(seq, 0, [zero] * len(graphs)); cur = value(fins); best = (cur, seq, list(eng)); chain = None
    for it in range(steps):
        if chain is None:
            pos = [0] * n; before = [None] * n; lastq = {}
            for k, j in enumerate(seq):
                pos[j] = k; before[j] = lastq.get(eng[j]); lastq[eng[j]] = j
            chain = {}; most = max(fins[0][j] + more0[j] for j in ends) + heat * ref[0]
        x = (x * 1103515245 + 12345) % 2147483648; v = (x >> 8) % len(graphs)
        if v not in chain:
            fin = fins[v]; d, more, lag, alt = graphs[v]; j = max(ends, key=lambda k: fin[k] + more[k]); c = []
            while j is not None:
                b = before[j]
                if b is not None and fin[b] >= fin[j] - d[j] - 1e-6:
                    if not anc[j] >> b & 1: c.append(j)
                    j = b
                else:
                    j = next((i for i, l in lag[j] if fin[i] + l >= fin[j] - d[j] - 1e-6), None)
            chain[v] = c
        x = (x * 1103515245 + 12345) % 2147483648
        j = chain[v][(x >> 8) % len(chain[v])] if chain[v] and x % 8 else (x >> 8) % n
        i = before[j]
        x = (x * 1103515245 + 12345) % 2147483648; far = (0, 0, 0, 1, 2, 4, 8, 16)[(x >> 8) % 8]
        undo = None
        if (x >> 12) % OPT["flip"] == 0:
            if i is not None and x >> 21 & 1: j = i
            if len(alt0[j]) < 2: continue
            others = [e for e in alt0[j] if e != eng[j]]
            undo = (j, eng[j]); put(j, others[(x >> 22) % len(others)]); new = seq; i = j
        elif i is None: continue
        elif x >> 20 & 1:
            while far and before[i] is not None: i = before[i]; far -= 1
            mid = seq[pos[i]:pos[j] + 1]
            go = [k for k in mid if k == j or anc[j] >> k & 1]
            if go[0] == i: continue
            new = seq[:pos[i]] + go + [k for k in mid if not (k == j or anc[j] >> k & 1)] + seq[pos[j] + 1:]
        else:
            k = pos[j] + 1
            while far and k < n:
                if eng[seq[k]] == eng[j]: j = seq[k]; far -= 1
                k += 1
            mid = seq[pos[i]:pos[j] + 1]
            go = [k for k in mid if k == i or anc[k] >> i & 1]
            if go[-1] == j: continue
            new = seq[:pos[i]] + [k for k in mid if not (k == i or anc[k] >> i & 1)] + go + seq[pos[j] + 1:]
        s2 = run(new, pos[i], fins, most)
        if s2 is not None:
            val = value(s2)
            x = (x * 1103515245 + 12345) % 2147483648
            if val <= cur + heat * (1.0 - it / steps) * (x / 2147483648.0) ** 2:
                seq = new; fins = s2; cur = val; chain = None; undo = None
                if cur < best[0]: best = (cur, seq, list(eng))
        if undo: put(*undo)
    for j, e in enumerate(best[2]):
        if e != eng[j]: put(j, e)
    tm = spans_of(run(best[1], 0, [zero] * len(graphs)))
    return sum(v / (k + 1.0 if k < 2 else 2.0) for k, v in enumerate(tm)), best[1], best[2]


def plan(ops, deps, prm):
    cuts = [0] + [j + 1 for j, o in enumerate(ops) if o["kind"] == "recv"] + [len(ops)]
    order = []
    for u, v in zip(cuts, cuts[1:]):
        part = [{i - u: need for i, need in d.items() if i >= u} for d in deps[u:v]]
        val, seq, eng = min(schedule(ops[u:v], part, dict(prm, part=True), OPT["iters"], OPT["steps"], seed=k, moves=OPT["walk"]) for k in range(1, OPT["tries"] + 1))
        for o, e in zip(ops[u:v], eng):
            if "alts" in o: choose(o, e)
        val, seq, eng = schedule(ops[u:v], part, dict(prm, part=True), 0, OPT["more"], seq, moves=OPT["walk2"], heat=OPT["warm"])
        for o, e in zip(ops[u:v], eng):
            if "alts" in o: choose(o, e)
        order += [u + j for j in seq]
    val, order, eng = schedule(ops, deps, prm, 0, OPT["polish"], order, heat=OPT["cool"])
    for o, e in zip(ops, eng):
        if "alts" in o: choose(o, e)
    return order, eng


def joint():
    all_ops = [build(me) for me in range(NR)]
    deps = link(all_ops[0], True)
    for ops in all_ops[1:]:
        for d, e in zip(deps, link(ops, True)):
            for i, need in e.items():
                if i not in d or (need and not d[i]): d[i] = need
    return all_ops[0], deps


_PLAN = {}


def masks(src, cores, topo):
    peers = sorted([c for c in cores if c != src], key=lambda c: len(topo.engines(src, c)))
    used = []; out = {}
    for c in peers:
        e = [k for k in topo.engines(src, c) if k not in used][:4]
        used += e; out[c] = e
    return out


def rank_program(g, core, T, topo):
    me = T.rank_of(core)
    if me is None:
        return
    cores = list(T.cores)
    if "order" not in _PLAN:
        ops0, deps0 = joint()
        _PLAN["order"], _PLAN["eng"] = plan(ops0, deps0, PRM)
    order = _PLAN["order"]
    ops = build(me)
    for o, e in zip(ops, _PLAN["eng"]):
        if "alts" in o: choose(o, e)
    deps = link(ops)
    Q = dict(V=g.vector, S=g.scalar, P=g.tensor, G=g, Y=g.sync)
    pos = {j: n for n, j in enumerate(order)}
    key = lambda i: ops[i]["eng"] if ops[i]["kind"] not in ("dma", "send", "recv") else i
    know = {e: {} for e in Q}; clock = {}; needed = set()
    for j in order:
        kn = know[ops[j]["eng"]]
        for i in sorted([i for i, need in deps[j].items() if need], key=lambda i: -pos[i]):
            if kn.get(key(i), -1) >= pos[i]:
                deps[j][i] = False
                continue
            needed.add(i)
            for k2, v in clock[i].items(): kn[k2] = max(kn.get(k2, -1), v)
            kn[key(i)] = pos[i]
        if ops[j]["kind"] == "recv": kn[j] = pos[j]
        clock[j] = dict(kn)
    mark = {}; cnt = dict(V=0, S=0, P=0, G=0); nd = 0
    for j in order:
        o = ops[j]
        if o["kind"] == "dma":
            mark[j] = ("d%d" % nd, 16 * len(o["args"])); nd += 1
        elif o["kind"] == "send":
            mark[j] = ("sent", (o["args"] + 1) * sum(len(e) for e in masks(core, cores, topo).values()))
        elif j in needed and o["kind"] != "recv":
            cnt[o["eng"]] += 1; mark[j] = ("c" + o["eng"], cnt[o["eng"]])

    def ap(d):
        if not isinstance(d, tuple): return d
        if d[0] == "ind": return ap(d[1]).indirect(ap(d[2]))
        if d[0] == "ext": return T[d[1]][d[2]]
        p = slice(None) if d[5] is None else d[5]
        nm, o0 = _AT.get(d[1], (d[1], 0))
        return T[nm][p, o0 + d[2]:o0 + d[3]] if d[4] == 1 else T[nm][p, o0 + d[2]:o0 + d[3]:d[4]]

    def issue(q, k, x):
        if k == "tt": return q.tensor_tensor(ap(x[0]), ap(x[1]), ap(x[2]), x[3])
        if k == "ts":
            if x[5] is None: return q.tensor_scalar(ap(x[0]), ap(x[1]), ap(x[2]), None, x[4])
            return q.tensor_scalar(ap(x[0]), ap(x[1]), ap(x[2]), ap(x[3]), x[4], x[5])
        if k == "cp": return q.tensor_copy(ap(x[0]), ap(x[1]))
        if k == "ms": return q.memset(ap(x[0]), x[1])
        if k == "scan": return q.tensor_tensor_scan(ap(x[0]), ap(x[1]), ap(x[2]), x[3], x[4], x[5])
        if k == "trn": return q.transpose(ap(x[0]), ap(x[1]))
        if k == "act": return q.activation(ap(x[0]), ap(x[1]), x[2], bias=ap(x[3]), scale=ap(x[4]), accum_out=ap(x[5]))
        if k == "mm":
            return [q.matmul(ap(po), ap(l), ap(r), x[1] and n == 0, x[2] and n == len(x[0]) - 1) for n, (po, l, r) in enumerate(x[0])][-1]
        if k == "iota":
            if _SB[x[0][1]][1] == i32: return q.iota(ap(x[0]), x[1], x[2], x[3])
            return q.iota(ap(x[0]), x[1], x[2], x[3], allow_small_or_imprecise_dtypes=True)
        return q.affine_select(ap(x[0]), ap(x[1]), x[2], x[3], x[6], x[4], x[5])

    seen = {e: {} for e in Q}
    for j in order:
        o = ops[j]; e = o["eng"]; q = Q[e]; k = o["kind"]; x = o["args"]
        want = {}
        for i, need in deps[j].items():
            if need and i in mark:
                s, v = mark[i]; want[s] = max(want.get(s, 0), v)
            if need and ops[i]["kind"] == "recv":
                want["arr%d" % ops[i]["args"]] = sum(len(masks(c, cores, topo)[core]) for c in cores if c != core)
        if k == "recv":
            want["arr%d" % x] = sum(len(masks(c, cores, topo)[core]) for c in cores if c != core)
        for s, v in want.items():
            if seen[e].get(s, 0) < v:
                q.wait_ge(T.sem[s], v); seen[e][s] = v
        ins = None
        if k == "many":
            for k2, x2 in x: ins = issue(q, k2, x2)
        elif k not in ("dma", "send", "recv"): ins = issue(q, k, x)
        elif k == "dma":
            for po, pi in x:
                q.dma_start(ap(po), ap(pi)).then_inc(T.sem[mark[j][0]], 16)
        elif k == "send":
            trs = []; eng = masks(core, cores, topo)
            for b, src, dst in transfers(o, me):
                rid, pid = topo.addr(cores[b], core)
                trs.append(RemoteDMATransfer(dst_ids=[DstId(rid=rid, pnc=pid)], dma_engine_mask=sum(1 << n for n in eng[cores[b]]),
                                             remote_sem=T.sem["arr%d" % x], src=ap(src), dst=ap(dst)))
            q.remote_dma_fused(trs, local_sem=T.sem.sent)
        if ins is not None and j in mark:
            ins.then_inc(T.sem[mark[j][0]], 1)
    last = {}
    for s, v in mark.values():
        last[s] = max(last.get(s, 0), v)
    for s, v in last.items():
        if not any(seen[e].get(s, 0) >= v for e in Q):
            g.wait_ge(T.sem[s], v)
